import numpy as np, ml_dtypes
CORES = [10,34,74,98]
N = 4
import mx_ref
BF = ml_dtypes.bfloat16
def gcols(t, e):
    v = np.concatenate([t.reshape(8, 16, -1, 4), np.zeros((8, 16, 1, 4), BF)], axis=2)
    return np.ascontiguousarray(np.stack([v[g][:, e[g]] for g in range(8)])).reshape(128, -1)
def tile(rs):
    return np.stack(rs, axis=2).reshape(128, -1).astype(BF)
def pick(q, e):
    c = np.concatenate([q[0].reshape(128, -1, 4), np.zeros((128, 1, 4), np.uint8)], axis=1); s = np.concatenate([q[1], np.ones((16, 1), np.uint8)], axis=1)
    return (np.ascontiguousarray(c[:, e].reshape(128, -1)), np.ascontiguousarray(s[:, e]))
def join(*qs):
    return (np.concatenate([q[0] for q in qs], axis=1), np.concatenate([q[1] for q in qs], axis=1))
def put(q, e, v):
    c, s = q[0].reshape(128, -1, 4).copy(), q[1].copy(); c[:, e] = v[0].reshape(128, -1, 4); s[:, e] = v[1]
    return (c.reshape(128, -1), s)
def pk(c, s):
    return (np.ascontiguousarray(c), mx_ref.live(s))
def emit(q):
    return q[0], q[1]
def packed(v, rng):
    q = [mx_ref.quantize(np.ascontiguousarray(v[r])) for r in range(N)]
    return np.stack([a for a, b in q]), np.stack([mx_ref.plane(b, rng) for a, b in q])
def values_of_codes():
    e, c = np.zeros((128, 128, 4), np.float32), np.zeros((128, 2, 4), np.uint8)
    e[np.arange(128), np.arange(128), 0] = 1
    c[:127, :, 0] = np.arange(256).reshape(2, 128).T[:127]
    return mx_ref.matmul(mx_ref.quantize(e.reshape(128, 512).astype(BF)), (c.reshape(128, 8), np.full((16, 2), 127, np.uint8))).T.reshape(-1).astype(np.float64)
CODE_VALUE, SCALE_VALUE = values_of_codes(), 2.0 ** (np.arange(256) - 127.0)
def decode(q):
    return (CODE_VALUE[q[0]].reshape(16, 8, -1, 4) * SCALE_VALUE[q[1]][:, None, :, None] + 0.0).reshape(128, -1).astype(np.float32)
def f(rng, *shape):
    return mx_ref.flush((rng.standard_normal(shape, dtype=np.float32) * np.exp2(rng.integers(-2, 3, shape[:-1] + (1,)))).astype(BF))
def wide(rng, *shape, cols=0):
    v = rng.standard_normal(shape, dtype=np.float32) * np.exp2(rng.integers(-12, 13, shape)).astype(np.float32)
    if cols: v *= np.repeat(np.exp2(rng.integers(-cols, cols + 1, shape[:-2] + (1, shape[-1] // 4))) * (rng.random(shape[:-2] + (1, shape[-1] // 4)) > 0.0625), 4, axis=-1).astype(np.float32)
    return mx_ref.flush(v.astype(BF))
C, K, E, R = 416, 96, 512, 3
def numbers_of(rng):
    return {"x": np.array(f(rng, N, 128, 4 * E)), "u": np.array(f(rng, N, 128, 512)), "v": np.array(f(rng, N, 128, 512))}
def layers(rng, still=[]):
    w = np.array(f(rng, N, 128, 2048)).reshape(N, 8, 16, 4, 8, 16, 4)
    for i in still:
        w[:, :, i] = 0
        w[:, :, :, :, :, i] = 0
    return w
def weights(rng, w):
    c, s = packed(np.ascontiguousarray(w).reshape(N, 128, 2048), rng)
    return {"wc": c, "ws": s}
def setup_inputs(rng):
    return {**numbers_of(rng), **weights(rng, layers(rng))}
def setup_inputs_ties(rng):
    d = numbers_of(rng)
    x = d["x"].reshape(N, 8, 16, E, 4)
    k = rng.integers(0, 4, (N, 8, E))
    k[:, :, C:] = rng.integers(-1, 5, (N, 8, K))
    x[:, :, 0] = 0
    x[:, :, 0, :, 0] = k.astype(np.float32).astype(BF)
    u = d["u"].reshape(N, 128, 128, 4)
    u[:, :, ::16] = 0
    o = rng.permutation(N)
    for r in range(N):
        for h in range(0, 128, 16): u[r, h, h, 0] = 0.0 if r == o[0] else -1.0 if r == o[1] else 1.0
    return {"x": x.reshape(N, 128, 4 * E), "u": u.reshape(N, 128, 512), "v": d["v"], **weights(rng, layers(rng, [0]))}
def close():
    t = np.zeros((128, 40, 4), np.float32)
    t[8, :, 0] = 1.96875
    t[9, :, 0] = (np.arange(8, 16) * np.exp2(-np.arange(14.0, 19.0))[:, None]).reshape(-1)
    once = decode(mx_ref.quantize(t.reshape(128, 160).astype(BF)))
    twice = decode(mx_ref.quantize(once.astype(BF)))[9, ::4]
    return max([np.unique(once[9, ::4][twice == k]) for k in twice], key=len)
def setup_inputs_edges(rng):
    d = numbers_of(rng)
    x = d["x"].astype(np.float32).reshape(N, 8, 16, E, 4)
    k = rng.integers(64, 192, (N, 8, E))
    k[:, :, :K // 2] = 200
    k[:, :, :C] = rng.permuted(k[:, :, :C], axis=2)
    for r in range(N):
        h = rng.permutation(8)
        for i in range(5): k[r, h[i], C:] = [255, 0, 199, 200, 128][i]
        k[r, h[5], C:] = rng.permutation(K) % 2 * 255
    b = np.arange(4)
    x[:, :, 0] = ((k[:, :, :, None] >> b) & 1) * np.exp2(b)
    x[:, :, 1] = ((k[:, :, :, None] >> (b + 4)) & 1) * np.exp2(b + 4)
    a = np.exp2(rng.integers(-14, -7, (N, 4, 8, E, 4))) * (1.0 + (2 * rng.integers(0, 64, (N, 4, 8, E, 4)) + 1) * 2.0 ** -7) * rng.choice([-1.0, 1.0], (N, 4, 8, E, 4))
    a[:, :, 0, :, 0] = 1.96875
    a[:, :, 1] = 0
    a[:, :, 1, :, 0] = rng.choice(close(), (N, 4, E))
    x[:, 4:, 8:] = a
    x[:, 0, 9] = 0
    u = d["u"].reshape(N, 128, 128, 4)
    u[:, :, ::16] = 0
    for h in range(0, 128, 16):
        u[:, h, h] = 1.0
        u[:, h + 1, h] = 1.0
    u[:, 9, 0, 0] = 2.0 ** 8
    w = layers(rng, [0, 1, 9])
    w[:, :, :, :, 4:, 8:] = 0
    return {"x": x.reshape(N, 128, 4 * E).astype(BF), "u": u.reshape(N, 128, 512), "v": d["v"], **weights(rng, w)}
def setup_inputs_near(rng):
    d = numbers_of(rng)
    x = d["x"].astype(np.float32).reshape(N, 8, 16, E, 4)
    x[:, :, 0] = 0
    x[:, :, 8:] = 0
    s = rng.integers(0, 256, (N, 8, E))
    b = np.arange(4)
    u = d["u"].reshape(N, 128, 128, 4)
    u[:, :, ::16] = 0
    o = rng.permutation(N) % 4
    for r in range(N):
        sign = rng.choice([-1.0, 1.0], (8, E))
        if o[r] < 2:
            x[r, :, 0, :, 0] = sign
            x[r, :, 11, :, 0] = 2.0 ** -10
            sign = np.ones((8, E))
        else:
            for g in rng.permutation(8)[:4]: x[r, g, 0, rng.integers(E), 0] = rng.choice([-1.0, 1.0]) * 2.0 ** 29
        least = -30.0 if o[r] == 2 else -23.0
        x[r, :, 8] = ((s[r, :, :, None] >> b) & 1) * np.exp2(b + least) * sign[:, :, None]
        x[r, :, 9] = ((s[r, :, :, None] >> (b + 4)) & 1) * np.exp2(b + 4 + least) * sign[:, :, None]
        k = 1.0 if o[r] == 0 else 2.0 ** -30
        for h in range(0, 128, 16):
            u[r, h, h, 0] = k
            u[r, h + 8, h] = k
            u[r, h + 9, h] = k
            u[r, h + 11, h, 0] = k
    return {"x": x.reshape(N, 128, 4 * E).astype(BF), "u": u.reshape(N, 128, 512), "v": d["v"], **weights(rng, layers(rng, [0, 8, 9, 10, 11, 12, 13, 14, 15]))}
def setup_inputs_huge(rng):
    d = numbers_of(rng)
    o = rng.permutation(N)
    c = rng.choice([-1.0, 1.0], (N, 8, 1, E, 1))
    u = d["u"].reshape(N, 128, 128, 4)
    u[:, :, ::16] = 0
    for r in range(N):
        a = (2.0 ** 30 * (1.0 - 0.1 * rng.random((128, 8, 4)))).astype(np.float32).astype(BF)
        if o[r] < N // 2:
            c[r] = c[r, :1].copy()
            u[r, :, ::16] = a
        else:
            c[r, rng.permutation(8)[:4]] = -1.0
            for g in range(8): u[r, 16 * g:16 * g + 16, 16 * g] = a[16 * g:16 * g + 16, g]
    x = c * (0.8 + 0.2 * rng.random((N, 8, 16, E, 4))) * 2.0 ** 30
    w = np.zeros((N, 128, 4, 128, 4), np.float32)
    i = np.arange(128)
    for b in range(4): w[:, i, b, i, b] = -2
    return {"x": x.astype(np.float32).reshape(N, 128, 4 * E).astype(BF), "u": u.reshape(N, 128, 512), "v": d["v"], **weights(rng, w.astype(BF))}
def setup_inputs_spread(rng):
    d = setup_inputs(rng)
    d["x"] = wide(rng, N, 128, 4 * E, cols=6)
    return d
def check_inputs(d):
    b = []
    for k in ("x", "u", "v"):
        a = np.abs(d[k].astype(np.float32))
        if not (np.isfinite(a).all() and ((a == 0) | (a >= 2.0 ** -30) & (a <= 2.0 ** 30)).all()): b.append("a value of " + k)
    none, least, most = [emit(mx_ref.quantize(np.full((128, 16), k, np.float32).astype(BF)))[1][0, 0] for k in (0.0, 2.0 ** -30, 2.0 ** 30)]
    for r in range(N):
        if ((d["wc"][r] == 0x7F) | (d["wc"][r] == 0xFF)).any(): b.append("wc: a code that is no number")
        s = mx_ref.live(d["ws"][r])
        if ((s != none) & ((s < least) | (s > most))).any(): b.append("ws: a scale out of range")
    return b
def reference(x, u, v, wc, ws):
    qu = [mx_ref.quantize(u[r]) for r in range(N)]
    lay = [pk(wc[r], ws[r]) for r in range(N)]
    now = [x[r] for r in range(N)]
    le = np.zeros((N, 8, E), np.float32)
    for t in range(R):
        made, sent = [], []
        for r in range(N):
            s = mx_ref.matmul(qu[r], mx_ref.quantize(now[r]))[::16] + np.float32(0.0)
            o = np.argsort(s[:, :C], axis=1, kind="stable")
            b = C + np.argsort(s[:, C:], axis=1, kind="stable")
            e = np.concatenate([o, b], axis=1)
            for g in range(8):
                k = np.searchsorted(s[g, o[g]], s[g, b[g]], side="right")
                p = np.maximum.accumulate(k - np.arange(K)) + np.arange(K)
                j = np.flatnonzero(p < C)
                e[g, p[j]] = b[g, j]
                e[g, C + j] = o[g, p[j]]
            le[r] = e
            z = gcols(now[r], e)
            q = mx_ref.quantize(z)
            m = tile([mx_ref.matmul(pick(lay[r], np.arange(128 * a, 128 * a + 128)), q) * np.float32(0.015625) + z[:, a::4].astype(np.float32) for a in range(4)]).reshape(8, 16, E, 4)
            made.append(m)
            sent.append(mx_ref.quantize(np.ascontiguousarray(m[7, :, C:].reshape(16, K // 8, 8, 4).transpose(2, 0, 1, 3)).reshape(128, -1)))
        now = []
        for r in range(N):
            came = decode(sent[(r - t - 1) % N]).astype(BF).reshape(8, 16, K // 8, 4).transpose(1, 2, 0, 3).reshape(1, 16, K, 4)
            wait = np.concatenate([came, made[r][:7, :, C:]])
            now.append(np.ascontiguousarray(np.concatenate([made[r][:, :, :C], wait], axis=2)).reshape(128, -1))
    y = np.zeros((N, 128, E), np.float32)
    oc, osc = np.zeros((N, 128, 4 * E), np.uint8), np.zeros((N, 16, E), np.uint8)
    for r in range(N):
        q = mx_ref.quantize(now[r])
        y[r] = mx_ref.matmul(mx_ref.quantize(v[r]), q)
        oc[r], osc[r] = emit(q)
    return {"y": y, "le": le, "oc": oc, "osc": osc}

@@ -1,0 +1,572 @@
+from concourse.mybir import dt, AluOpType, ActivationFunctionType
+
+ALU = AluOpType
+ACT = ActivationFunctionType
+BF, F32, I32, U16, U8, X4 = "bfloat16", "float32", "int32", "uint16", "uint8", "float8_e4m3fn_x4"
+NR = 3
+CFG = {"LOOK": 2, "UNP": 2, "SP": 3, "WS": 96, "SPLIT": 288, "ZV": 1, "XA": 3}
+
+SCRATCH = {}
+for _d, _l in (
+        (BF, "UU:512 VV:512 XX:2048 ZZ:2048 Z64:2048 T64:2048 MW:384 MR:384 BT:512 ZT:512 ONE:512 F512:384 MLT:128 "
+             "CC:1664 C2:512 CS:96 CS4:512 CR:96 CR4:512 CT:96 CT4:512 EE:4096 TG:512 JK:6144 "
+             "TA0:1536 TA1:1536 TD0:1536 TD1:1536 TB0:2048 TB1:2048"),
+        (F32, "KS:32 KA:32 KE:32 TH:4096 RR:40 RB:40 TOT:40 DD:88 VS:512 W1:512 W2:512 E2:96 KC:96 NK:96 PP:96 PS:96 "
+              "SC:512 F6:8 G6:8 H6:8 YY:512"),
+        (I32, "PI:16 UBI:64"), (U16, "UBL:64 GL:32 PKL:16 BL:4 OF:32 PW:6 LL:128")):
+    for _e in _l.split():
+        SCRATCH[_e.split(":")[0]] = ("sbuf", [128, int(_e.split(":")[1])], _d)
+for _e in ("U:128 V:128 UB:1024 W:512 X:512 Z:512 CC:416 C2:128 E:1024 TG:128 TA0:384 TA1:384 TD0:384 TD1:384 TB0:512 "
+           "TB1:512 B0:128 B1:128 B2:128 LD0:144 LD1:144 LD2:144 PK0:240 PK1:240 PK2:240").split():
+    SCRATCH["q" + _e.split(":")[0]] = ("sbuf", [128, int(_e.split(":")[1])], X4)
+    SCRATCH["s" + _e.split(":")[0]] = ("sbuf", [128, int(_e.split(":")[1])], U8)
+for _k in range(8):
+    SCRATCH["P%d" % _k] = ("psum", [128, 512], F32)
+POOL = {}
+_at = 0
+for _n, _w in (("R16", 2), ("B1", 32), ("B2", 32), ("B3", 32), ("B4", 32), ("B5", 32), ("PKI", 16), ("PKJ", 16),
+               ("BLI", 4), ("S6", 6), ("SR", 6), ("PF", 16), ("PG", 16), ("CE", 2), ("BASE", 40), ("WC", 96)):
+    POOL[_n] = (_at, _w)
+    _at += (_w + 7) // 8 * 8
+SCRATCH["KF"] = ("sbuf", [128, _at], F32)
+
+SEMAPHORES = ("sv sa st sg ldu ldx0 ldx1 ldw ldv loc ole oa ob oy0 oy1 zl "
+              "rep0 rep1 rep2 shf0 shf1 shf2 arr0 arr1 arr2").split()
+
+BIG = 1.5 * 2.0 ** 23
+BIG32 = 1.5 * 2.0 ** 28
+PHI = 2.0 ** -24 * (1.0 + 2.0 ** -23)
+ETA = 2.0 ** -110
+
+
+def rank_program(g, core, T, topo):
+    rank = T.rank_of(core)
+    if rank is None:
+        return
+    LOOK = CFG["LOOK"]
+    n_ranks = len(T.cores)
+    eng = {"v": g.vector, "a": g.scalar, "t": g.tensor, "g": g, "s": g.sync}
+    own = {"v": "sv", "a": "sa", "t": "st", "g": "sg"}
+    total = {}
+    known = {q: {} for q in eng}
+    log = {}
+    serial = [0]
+    part = [False]
+
+    def A(name, c0=0, c1=None, step=1, p0=0, p1=128):
+        if name in POOL:
+            at, w = POOL[name]
+            name, c0, c1 = "KF", at + c0, at + (w if c1 is None else c1)
+        t = T[name]
+        if c1 is None:
+            c1 = t.shape[1]
+        ap = t[p0:p1, c0:c1] if step == 1 else t[p0:p1, c0:c1:step]
+        return (ap, (name, p0, p1, c0, c1, step))
+
+    def meets(a, b):
+        if a[0][0] == "P" and a[0][1:].isdigit():
+            return True
+        if a[2] <= b[1] or b[2] <= a[1] or a[4] <= b[3] or b[4] <= a[3]:
+            return False
+        s = min(a[5], b[5])
+        if s > 1 and a[5] % s == 0 and b[5] % s == 0 and a[3] % s != b[3] % s:
+            return False
+        return True
+
+    def need(q, deps):
+        for h in sorted(deps, key=lambda h: -h["n"]):
+            if known[q].get(h["sem"], 0) < h["cnt"]:
+                eng[q].wait_ge(T.sem[h["sem"]], h["cnt"])
+                known[q][h["sem"]] = h["cnt"]
+                for s, c in h["clock"].items():
+                    if known[q].get(s, 0) < c:
+                        known[q][s] = c
+
+    def collect(q, reads, writes, dma, me=None):
+        deps = {}
+        for keys, wr in ((reads, False), (writes, True)):
+            for k in keys:
+                bank = k[0][0] == "P" and k[0][1:].isdigit()
+                for (k2, wr2, q2, h) in log.get(k[0], []):
+                    if h is me or not meets(k, k2):
+                        continue
+                    if bank:
+                        if q2 == q:
+                            continue
+                    elif not (wr or wr2):
+                        continue
+                    elif q2 == q and not dma and not h["dma"] and not wr2:
+                        continue
+                    old = deps.get(h["sem"])
+                    if old is None or old["cnt"] < h["cnt"]:
+                        deps[h["sem"]] = h
+        return list(deps.values())
+
+    def record(q, reads, writes, h):
+        for k in reads:
+            log.setdefault(k[0], []).append((k, False, q, h))
+        for k in writes:
+            log.setdefault(k[0], []).append((k, True, q, h))
+
+    def op(q, fn, reads, writes):
+        reads = [r[1] for r in reads if isinstance(r, tuple)]
+        writes = [w[1] for w in writes]
+        need(q, collect(q, reads, writes, False))
+        s = own[q]
+        if q == "g":
+            now = writes[0][2] - writes[0][1] < 128
+            if now or part[0]:
+                need(q, [{"sem": s, "cnt": total[s], "clock": {}, "n": 0}])
+            part[0] = now
+        ins = fn()
+        total[s] = total.get(s, 0) + 1
+        ins.then_inc(T.sem[s], 1)
+        serial[0] += 1
+        record(q, reads, writes, {"sem": s, "cnt": total[s], "clock": dict(known[q]), "dma": False, "n": serial[0]})
+
+    def group(sem):
+        serial[0] += 1
+        return {"sem": sem, "cnt": total.get(sem, 0), "clock": {}, "dma": True, "n": serial[0]}
+
+    def dma(q, h, out, in_):
+        reads = [in_[1]] if in_[1] else []
+        writes = [out[1]] if out[1] else []
+        need(q, collect(q, reads, writes, True, h))
+        eng[q].dma_start(out[0], in_[0]).then_inc(T.sem[h["sem"]], 16)
+        total[h["sem"]] = total.get(h["sem"], 0) + 16
+        h["cnt"] = total[h["sem"]]
+        serial[0] += 1
+        h["n"] = serial[0]
+        for s, c in known[q].items():
+            if h["clock"].get(s, 0) < c:
+                h["clock"][s] = c
+        record(q, reads, writes, h)
+
+    def ap(x):
+        return x[0] if isinstance(x, tuple) else x
+
+    def bytes_of(x):
+        return (x[0].bitcast(dt.uint8), x[1])
+
+    def memset(out, c):
+        op("v", lambda: g.vector.memset(out[0], c), [], [out])
+
+    def copy(out, in_):
+        op("v", lambda: g.vector.tensor_copy(out[0], in_[0]), [in_], [out])
+
+    def ts(out, in0, s1, s2, o0, o1=None):
+        if o1 is None:
+            op("v", lambda: g.vector.tensor_scalar(out[0], in0[0], ap(s1), None, o0), [in0, s1], [out])
+        else:
+            op("v", lambda: g.vector.tensor_scalar(out[0], in0[0], ap(s1), ap(s2), o0, o1), [in0, s1, s2], [out])
+
+    def tt(out, in0, in1, o):
+        op("v", lambda: g.vector.tensor_tensor(out[0], in0[0], in1[0], o), [in0, in1], [out])
+
+    def scan(out, d0, d1, init, o0=ALU.add, o1=ALU.max):
+        op("v", lambda: g.vector.tensor_tensor_scan(out[0], d0[0], d1[0], init, o0, o1), [d0, d1], [out])
+
+    def gather(out, win, off):
+        op("v", lambda: g.vector.tensor_copy(out[0], win[0].indirect(off[0])), [win, off], [out])
+
+    def scatter(win, off, in_):
+        op("v", lambda: g.vector.tensor_copy(win[0].indirect(off[0]), in_[0]), [in_, off], [win])
+
+    def act(out, in_, func=ACT.Copy, bias=None, scale=None, accum=None, off=None):
+        src = in_[0] if off is None else in_[0].indirect(off[0])
+        kw = {}
+        if bias is not None:
+            kw["bias"] = ap(bias)
+        if scale is not None:
+            kw["scale"] = ap(scale)
+        if accum is not None:
+            kw["accum_out"] = accum[0]
+        op("a", lambda: g.scalar.activation(out[0], src, func, **kw), [in_, bias, scale, off],
+           [out] + ([accum] if accum is not None else []))
+
+    def lin(out, in_, scale, bias):
+        act(out, in_, ACT.Identity, bias, scale)
+
+    def quant(name, c0, c1, src=None):
+        qq, ss, in_ = A("q" + name, c0, c1), A("s" + name, c0, c1), A(src or name, 4 * c0, 4 * c1)
+        op("v", lambda: g.vector.quantize_mx(qq[0], ss[0], in_[0]), [in_], [qq, ss])
+
+    def pick(dst, d0, d1, src, off):
+        qo, qi, so, si = A("q" + dst, d0, d1), A("q" + src), A("s" + dst, d0, d1), A("s" + src)
+        op("v", lambda: g.vector.tensor_copy(qo[0].bitcast(dt.uint32), qi[0].bitcast(dt.uint32).indirect(off[0])),
+           [qi, off], [qo])
+        op("a", lambda: g.scalar.activation(so[0], si[0].indirect(off[0]), ACT.Copy), [si, off], [so])
+
+    def mm(bank, st, s0, mv, m0, n, start=True, stop=True):
+        out = A("P%d" % bank, 0, n)
+        a, b = A("q" + st, s0, s0 + 128), A("s" + st, s0, s0 + 128)
+        c, d = A("q" + mv, m0, m0 + n), A("s" + mv, m0, m0 + n)
+        op("t", lambda: g.tensor.matmul_mx(out[0], a[0], b[0], c[0], d[0], start, stop), [a, b, c, d], [out])
+
+    def iota(out, pattern, base, cm=0, real=True):
+        if real:
+            op("g", lambda: g.iota(out[0], pattern, base, cm, allow_small_or_imprecise_dtypes=True), [], [out])
+        else:
+            op("g", lambda: g.iota(out[0], pattern, base, cm), [], [out])
+
+    def select(out, in_, pattern, cmp, base, cm):
+        op("g", lambda: g.affine_select(out[0], in_[0], pattern, cmp, 0.0, base, cm), [in_], [out])
+
+    def col(name, c):
+        return A(name, c, c + 1)
+
+    dma("s", group("ldu"), A("UU"), (T.u[:], None))
+    dma("a", group("ldx0"), A("XX", 0, 1536), (T.x[:, 0:1536], None))
+    dma("s", group("ldx1"), A("XX", 1536, 2048), (T.x[:, 1536:2048], None))
+    h = group("ldw")
+    dma("s", h, bytes_of(A("qW")), (T.wc[:], None))
+    dma("s", h, A("sW"), (T.ws[:], None))
+    dma("s", group("ldv"), A("VV"), (T.v[:], None))
+
+    memset(A("ONE"), 1.0)
+    iota(A("UBI"), [[16, 8], [0, 8]], 0, 0, False)
+    iota(col("PI", 0), [[0, 1]], 0, 1, False)
+    select(A("MLT"), A("ONE", 0, 128), [[-1, 128]], ALU.is_gt, 0, 1)
+    memset(A("CE"), ETA)
+    memset(A("CC", 1536, 1664), 0.0)
+    for c0 in range(0, 1536, 512):
+        act(A("CC", c0, c0 + 512), A("ONE"), scale=0.0)
+    act(A("F512"), A("ONE", 0, 384), scale=512.0)
+    for c0, val in ((0, 415.0), (8, 287.0), (16, 159.0), (32, 511.0)):
+        memset(A("BASE", c0, c0 + 8), val)
+    for p0, p1, val in ((0, 32, 31.0), (32, 64, 32.0), (64, 128, 32.0)):
+        memset(A("BASE", 24, 32, 1, p0, p1), val)
+    memset(A("RR", 0, 8), 0.0)
+    memset(A("RR", 32, 40), 0.0)
+    memset(A("DD", 80, 88), 0.0)
+    copy(A("UBL"), A("UBI"))
+    for c, (sh, msk) in enumerate(((0, 15), (0, 1), (1, 1), (2, 3), (4, 7), (0, 3), (3, 1), (0, 7), (5, 3))):
+        ts(col("PI", c + 1), col("PI", 0), sh, msk, ALU.logical_shift_right, ALU.bitwise_and)
+    c_q, c_a0, c_a1, c_q4, c_g, c_t, c_h, c_8, c_k = [col("PF", c) for c in range(1, 10)]
+    c_eta = col("CE", 0)
+    iota(A("R16"), [[1, 2]], 0)
+    iota(A("B1"), [[1, 8], [8, 4]], 0)
+    iota(A("B1", 3, 32, 4, 32, 64), [[1, 8]], 32)
+    iota(A("B1", 3, 32, 4, 64, 128), [[1, 8]], 32)
+    iota(A("B2"), [[1, 8], [0, 4]], 24)
+    iota(A("S6"), [[16, 6]], 416)
+    iota(A("BLI", 0, 3), [[128, 3]], 0)
+    iota(A("PKI", 0, 7), [[2, 7]], 127)
+    iota(A("PKI", 7, 15), [[2, 8]], 128)
+    iota(A("ZT"), [[0, 512]], 0)
+    iota(A("CR"), [[0, 6], [1, 16]], 0)
+    iota(A("CR4"), [[0, 128], [1, 4]], 0)
+    for k in range(4):
+        select(A("C2", 0, 128, 1, 32 * k, 32 * k + 32), A("ONE", 0, 128, 1, 32 * k, 32 * k + 32),
+               [[-1, 32], [1000, 2], [0, 2]], ALU.is_equal, 0, 1)
+    select(A("C2", 128, 512), A("F512"), [[-1, 96], [1000, 2], [0, 2]], ALU.is_equal, -1032, 1)
+    iota(A("WC"), [[1, 96]], 416)
+    iota(A("VS"), [[1, 32], [32, 16]], 0)
+    iota(A("BT"), [[0, 512]], 0)
+    for k in range(8):
+        select(A("EE", 512 * k, 512 * k + 512), A("ONE"), [[-1000, 4], [-1, 32], [1000, 4]], ALU.is_equal, -16 * k, 1)
+
+    g_off, g_thr, g_sub, g_o4, g_na1, g_a40, g_b0, g_b1, g_i0, g_i1, g_eq, g_m, g_sc, g_bi, g_lt = [
+        col("PG", c) for c in range(15)]
+
+    def late0():
+        for c0, p0, p1 in ((128, 0, 128), (640, 0, 32), (1152, 0, 32), (1184, 32, 64), (1184, 64, 128)):
+            memset(A("CC", c0, c0 + 20, 5, p0, p1), -1.0)
+        copy(A("PF", 0, 10), A("PI", 0, 10))
+        quant("CC", 0, 416)
+
+    def late1():
+        ts(g_off, c_q, -1024.0, 15360.0, ALU.mult, ALU.add)
+        ts(g_o4, c_q4, 4096.0, -12288.0, ALU.mult, ALU.add)
+        lin(g_na1, c_a1, -1.0, 1.0)
+        ts(g_a40, c_a0, 40.0, -80.0, ALU.mult, ALU.add)
+        lin(g_b0, c_q4, 32.0, c_t)
+        ts(A("PG", 8, 10), A("R16"), c_8, None, ALU.is_equal)
+        ts(A("PKJ", 0, 15), A("PKI", 0, 15), c_h, 139.0, ALU.add, ALU.min)
+        ts(g_eq, c_q4, c_k, None, ALU.is_equal)
+
+    def late2():
+        ts(g_thr, g_off, 417.0 + BIG, None, ALU.add)
+        ts(g_sub, g_off, 1.0 + BIG, None, ALU.add)
+        lin(g_b1, c_g, 4.0, g_b0)
+        lin(g_lt, g_o4, None, c_t)
+        lin(g_sc, g_eq, g_na1, None)
+        ts(g_m, g_eq, c_a1, None, ALU.max)
+        ts(A("PKL", 0, 7), A("PKJ", 0, 7), g_i0, None, ALU.mult)
+        ts(A("PKL", 7, 15), A("PKJ", 7, 15), g_i1, None, ALU.mult)
+
+    def late3():
+        ts(A("SR"), A("S6"), c_q, g_sub, ALU.add, ALU.add)
+        lin(g_bi, g_m, g_a40, 80.0)
+        lin(A("B4"), A("B2"), c_a1, None)
+        ts(A("BL", 0, 3), A("BLI", 0, 3), g_b1, None, ALU.add)
+
+    def late4():
+        lin(A("B3"), A("B1"), g_sc, g_bi)
+        ts(A("CT"), A("CR"), c_q, 32768.0, ALU.is_gt, ALU.mult)
+        ts(A("CT4"), A("CR4"), c_q4, 32768.0, ALU.is_gt, ALU.mult)
+        quant("LD0", 0, 128, "ZT")
+        hz = group("zl")
+        for k in range(1, NR):
+            dma("s", hz, bytes_of(A("qLD%d" % k, 0, 128)), bytes_of(A("qLD0", 0, 128)))
+            dma("s", hz, A("sLD%d" % k, 0, 128), A("sLD0", 0, 128))
+
+    def late5():
+        tt(A("B5"), A("B3"), A("B4"), ALU.add)
+
+    def late6():
+        copy(A("GL"), A("B5"))
+        lin(A("CS"), A("CT"), None, -31744.0)
+        lin(A("CS4"), A("CT4"), None, -31744.0)
+        quant("C2", 0, 128)
+
+    late = [late0, late1, late2, late3, late4, late5, late6]
+    epieces = list(range(8))
+
+    def quant_e(n):
+        for k in range(min(n, len(epieces))):
+            e = epieces.pop(0)
+            quant("E", 128 * e, 128 * e + 128, "EE")
+
+    quant("U", 0, 128, "UU")
+    pick("UB", 0, 384, "U", A("UBL", 0, 24))
+    quant("X", 0, 384, "XX")
+
+    arrivals = {}
+
+    def unpack_pick(t):
+        land = [A("qLD%d" % t, 128, 140)[1], A("sLD%d" % t, 128, 140)[1]]
+        record("r", [], land, arrivals[t])
+        pick("PK%d" % t, 0, 240, "LD%d" % t, A("PKL", 0, 15))
+        for k in range(8):
+            mm(6, "E", 128 * k, "PK%d" % t, (8 - k) if k % 2 == 0 else (113 - k), 128, k == 0, k == 7)
+
+    def unpack_copy(f):
+        for b in range(4):
+            f(A("XX", 1664 + b, 2048, 4, 0, 16), A("P6", 0, 96, 1, 32 * b, 32 * b + 16))
+
+    def thresholds(c0, c1):
+        act(A("KA", c0, c1), A("KS", c0, c1), ACT.Abs, scale=PHI)
+        lin(A("KE", c0, c1), A("KA", c0, c1), None, c_eta)
+
+    def send(t):
+        gather(A("BT", 0, 48), A("MR"), A("BL", 0, 3))
+        quant("B%d" % t, 0, 128, "BT")
+        dst = T.cores[(rank + t + 1) % n_ranks]
+        src = T.cores[(rank - t - 1) % n_ranks]
+        rid, pid, _ = topo.addr(dst)
+        qb, sb = A("qB%d" % t, 0, 12), A("sB%d" % t, 0, 12)
+        need("g", collect("g", [qb[1], sb[1]], [], True))
+        g.remote_dma(T["qLD%d" % t][:, 128:140].bitcast(dt.uint8), qb[0].bitcast(dt.uint8), T.sem["arr%d" % t],
+                     T.sem.loc, pid, rid, topo.mask(core, dst))
+        g.remote_dma(T["sLD%d" % t][:, 128:140], sb[0], T.sem["arr%d" % t], T.sem.loc, pid, rid, topo.mask(core, dst))
+        total["loc"] = total.get("loc", 0) + 2 * len(topo.engines(core, dst))
+        total["arr%d" % t] = 2 * len(topo.engines(src, core))
+        serial[0] += 1
+        arrivals[t] = {"sem": "arr%d" % t, "cnt": total["arr%d" % t], "clock": {}, "dma": True, "n": serial[0]}
+
+    for t in range(NR):
+        first = [True]
+
+        def colsum(tile, w0, blk, gq, pos, last=False):
+            mm(5, tile, w0, "CC", pos - (8 * blk + 4 * gq), 128, first[0], last)
+            first[0] = False
+
+        def sums_one(gq):
+            quant("TA%d" % gq, 0, 384)
+            quant("TD%d" % gq, 0, 384)
+            for w0, blk in ((0, 0), (128, 0), (256, 1)):
+                colsum("TA%d" % gq, w0, blk, gq, 32)
+            for blk in range(3):
+                colsum("TD%d" % gq, 128 * blk, blk, gq, 32)
+
+        def sums_two(gq):
+            quant("TB%d" % gq, 0, 384)
+            for blk in range(3):
+                colsum("TB%d" % gq, 128 * blk, blk, gq, 160)
+            quant("TB%d" % gq, 384, 512)
+            colsum("TB%d" % gq, 384, 3, gq, 288, gq == 1)
+
+        def off_tile(gr, blk):
+            gq, lane = gr // 4, gr % 4
+            if blk == 3:
+                return A("TB%d" % gq, lane, 1536, 4)
+            return A("TA%d" % gq, lane, 512, 4) if blk == 1 else A("TA%d" % gq, 512 + lane, 1536, 4)
+
+        def diag_tile(gr, b0):
+            gq, lane = gr // 4, gr % 4
+            if b0 == 3:
+                return A("TB%d" % gq, 1536 + lane, 2048, 4)
+            return A("TD%d" % gq, lane, 1536, 4)
+
+        def unit(gr, blks):
+            bk, top = gr % 4, 128 * (blks[-1] + 1)
+
+            def z0():
+                mm(bk, "UB", 128 * gr, "X", 0, top)
+                for blk in blks:
+                    c0 = 512 * gr + 128 * blk
+                    lin(A("TH", c0, c0 + 128), A("MLT"), col("KE", 8 * blk + gr), col("KS", 8 * blk + gr))
+
+            def z1():
+                for blk in blks:
+                    if blk > 0:
+                        ts(off_tile(gr, blk), A("P%d" % bk, 0, 128 * blk), col("KS", 8 * blk + gr), None, ALU.is_le)
+                tt(diag_tile(gr, blks[0]), A("P%d" % bk, 128 * blks[0], top),
+                   A("TH", 512 * gr + 128 * blks[0], 512 * gr + top), ALU.is_lt)
+
+            def z2():
+                for blk in blks:
+                    if blk > 0:
+                        c0 = 768 * gr + 64 * blk * (blk - 1)
+                        act(A("JK", c0, c0 + 128 * blk), off_tile(gr, blk), accum=col("RR", 8 * blk + gr))
+            return [z0, z1, z2]
+
+        for blk in (1, 2, 0):
+            mm(4 + blk, "X", 128 * blk, "U", 0, 128)
+        for blk in (1, 2, 0):
+            act(A("KS", 8 * blk, 8 * blk + 8), A("P%d" % (4 + blk), 0, 128, 16))
+        thresholds(0, 24)
+        units = [unit(gr, [0, 1, 2]) for gr in range(8)] + [unit(gr, [3]) for gr in range(8)]
+        hooks = {}
+
+        def hook(n, f):
+            hooks.setdefault(n, []).append(f)
+
+        def block3():
+            quant("X", 384, 512, "XX")
+            mm(6, "X", 384, "U", 0, 128)
+            act(A("KS", 24, 32), A("P6", 0, 128, 16))
+            thresholds(24, 32)
+
+        if t > 0:
+            hook(7 - LOOK - CFG["UNP"], lambda: unpack_pick(t - 1))
+            hook(8 - LOOK - CFG["UNP"], lambda: unpack_copy(act))
+        else:
+            hook(0, lambda: pick("UB", 384, 640, "U", A("UBL", 24, 40)))
+            hook(1, lambda: pick("UB", 640, 1024, "U", A("UBL", 40, 64)))
+            for n, f in enumerate(late):
+                hook(n + 2, f)
+        hook(7 - LOOK, block3)
+        hook(4, lambda: sums_one(0))
+        hook(8, lambda: sums_one(1))
+        hook(12, lambda: sums_two(0))
+        issued = 0
+        for n in range(16):
+            while issued < min(16, n + LOOK + 1):
+                units[issued][0]()
+                issued += 1
+            units[n][1]()
+            if n > 0:
+                units[n - 1][2]()
+            for f in hooks.get(n, []):
+                f()
+        units[-1][2]()
+        sums_two(1)
+
+        tt(A("RB"), A("RR"), A("BASE"), ALU.add)
+        quant_e(2)
+        tt(A("TOT"), A("P5", 0, 40), A("RB"), ALU.add)
+        ts(A("DD", 0, 40), A("TOT"), BIG32, BIG32, ALU.add, ALU.subtract)
+        tt(A("DD", 40, 80), A("TOT"), A("DD", 0, 40), ALU.subtract)
+        act(A("TG", 256, 512), A("DD"), off=A("GL", 16, 32))
+        gather(A("TG", 0, 256), A("DD"), A("GL", 0, 16))
+        quant("TG", 0, 128)
+        mm(4, "TG", 0, "C2", 0, 128)
+        quant_e(2)
+        copy(A("OF"), A("P4", 0, 32))
+        for k in range(3):
+            tt(A("VS", 13 + k, 512, 16), A("P4", 32 + 32 * k, 64 + 32 * k), A("WC", 32 * k, 32 * k + 32), ALU.add)
+        scatter(A("W1"), A("OF"), A("VS"))
+
+        ts(A("KC"), A("W1", 416, 512), 2.0 ** -9, BIG, ALU.mult, ALU.add)
+        lin(A("NK"), A("KC"), -512.0, 512.0 * (BIG + 1.0))
+        act(A("W2", 0, 416), A("W1", 0, 416))
+        scan(A("PP"), A("ONE", 0, 96), A("KC"), BIG)
+        scan(A("PS"), A("CS"), A("PP"), 0.0)
+        raw = A("PS", 15, 96, 16)
+        ts(A("F6", 0, 6), raw, g_thr, 2.0 ** 25, ALU.is_ge, ALU.mult)
+        tt(A("W1", 416, 512), A("W1", 416, 512), A("NK"), ALU.add)
+        tt(A("G6", 0, 6), A("F6", 0, 6), A("SR"), ALU.min)
+        tt(A("H6", 0, 6), A("G6", 0, 6), raw, ALU.max)
+        ts(A("PW"), A("H6", 0, 6), g_sub, None, ALU.subtract)
+        act(A("E2"), A("W1"), off=A("PW"))
+        scatter(A("W2"), A("PW"), A("W1", 416, 512))
+        scan(A("SC", 416, 512), A("CS4", 0, 96), A("E2"), 0.0)
+        scan(A("SC", 384, 416), A("CS4", 0, 32), A("W2", 384, 416), 0.0)
+        ts(A("LL", 96, 128), A("SC", 387, 512, 4), 4.0, g_lt, ALU.mult, ALU.add)
+
+        def take(on, c0, c1):
+            o, off = A("ZZ", 4 * c0, 4 * c1), A("LL", c0 // 4, c1 // 4)
+            if on == "a":
+                act(o, A("XX"), off=off)
+            else:
+                gather(o, A("XX"), off)
+
+        def scaled(on, dst, src, c, *view):
+            if on == "a":
+                act(A(dst, *view), A(src, *view), scale=c)
+            else:
+                ts(A(dst, *view), A(src, *view), c, None, ALU.mult)
+
+        take("a", 384, 384 + CFG["WS"])
+        if CFG["WS"] < 128:
+            take("v", 384 + CFG["WS"], 512)
+        scan(A("SC", 0, 384), A("CS4", 0, 384), A("W2", 0, 384), 0.0)
+        ts(A("LL", 0, 96), A("SC", 3, 384, 4), 4.0, g_lt, ALU.mult, ALU.add)
+        if t == NR - 1:
+            h = group("ole")
+            dma("s", h, (T.le[:, 0:416], None), (T.W2[0:128:16, 0:416], A("W2", 0, 416)[1]))
+            dma("s", h, (T.le[:, 416:512], None), (T.E2[0:128:16, 0:96], A("E2")[1]))
+        take("a", 0, CFG["SPLIT"])
+        quant("Z", 384, 512, "ZZ")
+        for b in range(4):
+            mm(4 + b, "W", 128 * b, "Z", 384, 128)
+        scaled("v", "Z64", "ZZ", 64.0, 1536, 2048)
+        for b in range(4):
+            tt(A("T64", 1536 + b, 2048, 4), A("P%d" % (4 + b), 0, 128), A("Z64", 1536 + b, 2048, 4), ALU.add)
+        ts(A("MW"), A("T64", 1664, 2048), 0.015625, None, ALU.mult)
+        h = group("rep%d" % t)
+        for k in range(8):
+            dma("s", h, A("MR", 0, 384, 1, 16 * k, 16 * k + 16), A("MW", 0, 384, 1, 112, 128))
+        take("v", CFG["SPLIT"], 384)
+        quant("Z", 0, 384, "ZZ")
+        dma("s", group("shf%d" % t), A("XX", 1664, 2048, 1, 16, 128), A("MW", 0, 384, 1, 0, 112))
+        for b in range(4):
+            mm(b, "W", 128 * b, "Z", 0, 384)
+            scaled("v" if b < CFG["ZV"] else "a", "Z64", "ZZ", 64.0, b, 1536, 4)
+        scaled("a", "XX", "T64", 0.015625, 1536, 1664)
+        if t == NR - 1:
+            quant("V", 0, 128, "VV")
+            send(t)
+        for b in range(4):
+            tt(A("T64", b, 1536, 4), A("P%d" % b, 0, 384), A("Z64", b, 1536, 4), ALU.add)
+            if b == CFG["SP"] and t < NR - 1:
+                send(t)
+            if b < CFG["XA"]:
+                scaled("a", "XX", "T64", 0.015625, b, 1536, 4)
+        for b in range(CFG["XA"], 4):
+            scaled("v", "XX", "T64", 0.015625, b, 1536, 4)
+        quant("X", 0, 384, "XX")
+        quant_e(4)
+
+    mm(0, "V", 0, "X", 0, 384)
+    h = group("oa")
+    dma("s", h, (T.oc[:, 0:1536], None), bytes_of(A("qX", 0, 384)))
+    for k in range(4):
+        dma("s", h, (T.osc[4 * k:4 * k + 4, 0:384], None), A("sX", 0, 384, 1, 32 * k, 32 * k + 4))
+    act(A("YY", 0, 384), A("P0", 0, 384))
+    dma("s", group("oy0"), (T.y[:, 0:384], None), A("YY", 0, 384))
+    unpack_pick(NR - 1)
+    unpack_copy(copy)
+    quant("X", 384, 512, "XX")
+    mm(7, "V", 0, "X", 384, 128)
+    h = group("ob")
+    dma("s", h, (T.oc[:, 1536:2048], None), bytes_of(A("qX", 384, 512)))
+    for k in range(4):
+        dma("a" if k < 2 else "s", h, (T.osc[4 * k:4 * k + 4, 384:512], None), A("sX", 384, 512, 1, 32 * k, 32 * k + 4))
+    copy(A("YY", 384, 512), A("P7", 0, 128))
+    dma("a", group("oy1"), (T.y[:, 384:512], None), A("YY", 384, 512))
+    for s, c in total.items():
+        if known["g"].get(s, 0) < c:
+            g.wait_ge(T.sem[s], c)

@@ -4,46 +4,63 @@ ALU = AluOpType
 ACT = ActivationFunctionType
 BF, F32, I32, U16, U8, X4 = "bfloat16", "float32", "int32", "uint16", "uint8", "float8_e4m3fn_x4"
 NR = 3
-CFG = {"LOOK": 2, "UNP": 2, "SP": 3, "WS": 96, "SPLIT": 288, "ZV": 1, "XA": 3}
+C, K = 416, 96
+M = C // 16
+S = 200
+CFG = {"TOP": 3, "LOW": 2, "CROSS": "vvvaaaa", "WW": "a", "GW": 96, "GA": (144, 144), "XA": (208, 104), "ZA": (0, 0),
+       "CP": "a", "SP": "a", "KSPLIT": 288}
+
+LANES = [["A", "B", M - 1, M - 2]] + [[m for m in range(top, top - 4, -1) if m > 0] for top in range(M - 3, 0, -4)]
+RANGES = (("H", 240, 416, 3), ("M", 112, 240, 7), ("L", 0, 112, 4))
+TILES = []
+_at = 0
+for _l in LANES:
+    _w = C if _l[0] == "A" else 16 * _l[0]
+    _p = max([_w, 128] + [min(a + 128, b) for (_n, a, b, _k) in RANGES if a < _w])
+    TILES.append((_l, _at, _w, _p))
+    _at += _p
+TRW = _at
+NB = 9
+TCW = NB * K + 32
 
 SCRATCH = {}
 for _d, _l in (
-        (BF, "UU:512 VV:512 XX:2048 ZZ:2048 Z64:2048 T64:2048 MW:384 MR:384 BT:512 ZT:512 ONE:512 F512:384 MLT:128 "
-             "CC:1664 C2:512 CS:96 CS4:512 CR:96 CR4:512 CT:96 CT4:512 EE:4096 TG:512 JK:6144 "
-             "TA0:1536 TA1:1536 TD0:1536 TD1:1536 TB0:2048 TB1:2048"),
-        (F32, "KS:32 KA:32 KE:32 TH:4096 RR:40 RB:40 TOT:40 DD:88 VS:512 W1:512 W2:512 E2:96 KC:96 NK:96 PP:96 PS:96 "
-              "SC:512 F6:8 G6:8 H6:8 YY:512"),
-        (I32, "PI:16 UBI:64"), (U16, "UBL:64 GL:32 PKL:16 BL:4 OF:32 PW:6 LL:128")):
+        (BF, "UU:512 VV:512 X0:2048 X1:2048 ZZ:1664 ZW:512 Z64:1664 W64:384 T64:1664 U64:384 MW:384 MR:384 BT:512 "
+             "ZT:512 ONE:512 CR:416 CR4:416 CG:512 MK:416 RS:416 C2:128 CT:416 CT4:416 CS:416 CS4:416 SR1:512 SX:512 "
+             "SK:512 EE:4096 TR:%d TC:%d" % (4 * TRW, 4 * TCW)),
+        (F32, "KM:512 KS:416 KW:96 KSW:96 KB:416 KBW:96 AC:%d HS:512 TOT:32 VS:416 VW:96 W1:512 BV:96 E2:96 KC:96 NK:96 "
+              "PP:96 PS:96 SC:512 F6:8 G6:8 H6:8 YY:512" % (32 * S)),
+        (I32, "PI:16 UBI:8 KLI:26"), (U16, "UBL:8 KL:26 PKL:16 BL:4 OFH:12 OFM:8 OFL:8 OFW:6 PW:6 LL:104 LW:24")):
     for _e in _l.split():
         SCRATCH[_e.split(":")[0]] = ("sbuf", [128, int(_e.split(":")[1])], _d)
-for _e in ("U:128 V:128 UB:1024 W:512 X:512 Z:512 CC:416 C2:128 E:1024 TG:128 TA0:384 TA1:384 TD0:384 TD1:384 TB0:512 "
-           "TB1:512 B0:128 B1:128 B2:128 LD0:144 LD1:144 LD2:144 PK0:240 PK1:240 PK2:240").split():
+for _e in ("U:128 V:128 UB:128 W:512 X:512 ZZ:416 ZW:128 SR1:128 SX:128 SK:128 E:1024 TR:%d TC:%d B0:128 B1:128 B2:128 "
+           "LD0:144 LD1:144 LD2:144 PK0:240 PK1:240 PK2:240" % (TRW, TCW)).split():
     SCRATCH["q" + _e.split(":")[0]] = ("sbuf", [128, int(_e.split(":")[1])], X4)
     SCRATCH["s" + _e.split(":")[0]] = ("sbuf", [128, int(_e.split(":")[1])], U8)
 for _k in range(8):
     SCRATCH["P%d" % _k] = ("psum", [128, 512], F32)
 POOL = {}
 _at = 0
-for _n, _w in (("R16", 2), ("B1", 32), ("B2", 32), ("B3", 32), ("B4", 32), ("B5", 32), ("PKI", 16), ("PKJ", 16),
-               ("BLI", 4), ("S6", 6), ("SR", 6), ("PF", 16), ("PG", 16), ("CE", 2), ("BASE", 40), ("WC", 96)):
+for _n, _w in (("R16", 2), ("PKI", 16), ("PKJ", 16), ("BLI", 4), ("S6", 6), ("SR", 6), ("PF", 16), ("PG", 16),
+               ("WC", 96)):
     POOL[_n] = (_at, _w)
     _at += (_w + 7) // 8 * 8
 SCRATCH["KF"] = ("sbuf", [128, _at], F32)
 
-SEMAPHORES = ("sv sa st sg ldu ldx0 ldx1 ldw ldv loc ole oa ob oy0 oy1 zl "
+SEMAPHORES = ("sv sa st sg ldu ldx0 ldx1 ldw ldv loc ole oa ob oc oy0 oy1 zl "
               "rep0 rep1 rep2 shf0 shf1 shf2 arr0 arr1 arr2").split()
 
 BIG = 1.5 * 2.0 ** 23
-BIG32 = 1.5 * 2.0 ** 28
-PHI = 2.0 ** -24 * (1.0 + 2.0 ** -23)
 ETA = 2.0 ** -110
+STEP = 2048.0
+CYC, WAKE, LOCAL, REMOTE, GAT, SCA = 0.83, 80.0, 2000.0, 3000.0, 1.56, 3.8
 
 
 def rank_program(g, core, T, topo):
     rank = T.rank_of(core)
     if rank is None:
         return
-    LOOK = CFG["LOOK"]
+    TOP, LOW = CFG["TOP"], CFG["LOW"]
     n_ranks = len(T.cores)
     eng = {"v": g.vector, "a": g.scalar, "t": g.tensor, "g": g, "s": g.sync}
     own = {"v": "sv", "a": "sa", "t": "st", "g": "sg"}
@@ -52,6 +69,8 @@ def rank_program(g, core, T, topo):
     log = {}
     serial = [0]
     part = [False]
+    calls = []
+    touched = {}
 
     def A(name, c0=0, c1=None, step=1, p0=0, p1=128):
         if name in POOL:
@@ -63,8 +82,11 @@ def rank_program(g, core, T, topo):
         ap = t[p0:p1, c0:c1] if step == 1 else t[p0:p1, c0:c1:step]
         return (ap, (name, p0, p1, c0, c1, step))
 
+    def is_bank(k):
+        return k[0][0] == "P" and k[0][1:].isdigit()
+
     def meets(a, b):
-        if a[0][0] == "P" and a[0][1:].isdigit():
+        if is_bank(a):
             return True
         if a[2] <= b[1] or b[2] <= a[1] or a[4] <= b[3] or b[4] <= a[3]:
             return False
@@ -72,6 +94,42 @@ def rank_program(g, core, T, topo):
         if s > 1 and a[5] % s == 0 and b[5] % s == 0 and a[3] % s != b[3] % s:
             return False
         return True
+
+    def note(q, run, reads, writes, busy, late=0.0):
+        c = {"q": q, "run": run, "busy": busy, "late": late, "after": {}, "next": [], "i": len(calls)}
+        for keys, wr in ((reads, False), (writes, True)):
+            for k in keys:
+                for (k2, wr2, d) in touched.get(k[0], []):
+                    if (wr or wr2) and d is not c and meets(k, k2):
+                        free = d["q"] == q and not d["late"] and (not wr2 or q == "t")
+                        c["after"][d["i"]] = max(c["after"].get(d["i"], 0.0), 0.0 if free else WAKE + d["late"])
+        for keys, wr in ((reads, False), (writes, True)):
+            for k in keys:
+                touched.setdefault(k[0], []).append((k, wr, c))
+        for i in c["after"]:
+            calls[i]["next"].append(c)
+        calls.append(c)
+
+    def issue():
+        for c in reversed(calls):
+            c["way"] = c["busy"] + max([c["late"]] + [d["way"] + d["after"][c["i"]] for d in c["next"]])
+            c["left"] = len(c["after"])
+            c["at"] = 0.0
+        ready = [c for c in calls if not c["left"]]
+        free = {q: 0.0 for q in eng}
+        while ready:
+            first = min(ready, key=lambda c: (max(c["at"], free[c["q"]]), c["i"]))
+            t0 = max(first["at"], free[first["q"]])
+            c = max([c for c in ready if c["q"] == first["q"] and c["at"] <= t0 + WAKE], key=lambda c: (c["way"], -c["i"]))
+            ready.remove(c)
+            end = max(c["at"], free[c["q"]]) + c["busy"]
+            free[c["q"]] = end
+            c["run"]()
+            for d in c["next"]:
+                d["at"] = max(d["at"], end + d["after"][c["i"]])
+                d["left"] -= 1
+                if not d["left"]:
+                    ready.append(d)
 
     def need(q, deps):
         for h in sorted(deps, key=lambda h: -h["n"]):
@@ -82,13 +140,13 @@ def rank_program(g, core, T, topo):
                     if known[q].get(s, 0) < c:
                         known[q][s] = c
 
-    def collect(q, reads, writes, dma, me=None):
+    def collect(q, reads, writes, dma):
         deps = {}
         for keys, wr in ((reads, False), (writes, True)):
             for k in keys:
-                bank = k[0][0] == "P" and k[0][1:].isdigit()
+                bank = is_bank(k)
                 for (k2, wr2, q2, h) in log.get(k[0], []):
-                    if h is me or not meets(k, k2):
+                    if not meets(k, k2):
                         continue
                     if bank:
                         if q2 == q:
@@ -102,45 +160,42 @@ def rank_program(g, core, T, topo):
                         deps[h["sem"]] = h
         return list(deps.values())
 
-    def record(q, reads, writes, h):
+    def record(q, reads, writes, sem, dma):
+        serial[0] += 1
+        h = {"sem": sem, "cnt": total[sem], "clock": dict(known[q]) if q in known else {}, "dma": dma, "n": serial[0]}
         for k in reads:
             log.setdefault(k[0], []).append((k, False, q, h))
         for k in writes:
             log.setdefault(k[0], []).append((k, True, q, h))
 
-    def op(q, fn, reads, writes):
+    def op(q, fn, reads, writes, busy):
         reads = [r[1] for r in reads if isinstance(r, tuple)]
         writes = [w[1] for w in writes]
-        need(q, collect(q, reads, writes, False))
-        s = own[q]
-        if q == "g":
-            now = writes[0][2] - writes[0][1] < 128
-            if now or part[0]:
-                need(q, [{"sem": s, "cnt": total[s], "clock": {}, "n": 0}])
-            part[0] = now
-        ins = fn()
-        total[s] = total.get(s, 0) + 1
-        ins.then_inc(T.sem[s], 1)
-        serial[0] += 1
-        record(q, reads, writes, {"sem": s, "cnt": total[s], "clock": dict(known[q]), "dma": False, "n": serial[0]})
 
-    def group(sem):
-        serial[0] += 1
-        return {"sem": sem, "cnt": total.get(sem, 0), "clock": {}, "dma": True, "n": serial[0]}
+        def run():
+            need(q, collect(q, reads, writes, False))
+            s = own[q]
+            if q == "g":
+                now = writes[0][2] - writes[0][1] < 128
+                if now or part[0]:
+                    need(q, [{"sem": s, "cnt": total[s], "clock": {}, "n": 0}])
+                part[0] = now
+            total[s] = total.get(s, 0) + 1
+            fn().then_inc(T.sem[s], 1)
+            record(q, reads, writes, s, False)
+        note(q, run, reads, writes, busy)
 
-    def dma(q, h, out, in_):
-        reads = [in_[1]] if in_[1] else []
-        writes = [out[1]] if out[1] else []
-        need(q, collect(q, reads, writes, True, h))
-        eng[q].dma_start(out[0], in_[0]).then_inc(T.sem[h["sem"]], 16)
-        total[h["sem"]] = total.get(h["sem"], 0) + 16
-        h["cnt"] = total[h["sem"]]
-        serial[0] += 1
-        h["n"] = serial[0]
-        for s, c in known[q].items():
-            if h["clock"].get(s, 0) < c:
-                h["clock"][s] = c
-        record(q, reads, writes, h)
+    def dmas(q, sem, pairs, late=LOCAL):
+        reads = [i[1] for (o, i) in pairs if i[1]]
+        writes = [o[1] for (o, i) in pairs if o[1]]
+
+        def run():
+            need(q, collect(q, reads, writes, True))
+            for (o, i) in pairs:
+                eng[q].dma_start(o[0], i[0]).then_inc(T.sem[sem], 16)
+            total[sem] = 16 * len(pairs)
+            record(q, reads, writes, sem, True)
+        note(q, run, reads, writes, 60.0 * len(pairs), late)
 
     def ap(x):
         return x[0] if isinstance(x, tuple) else x
@@ -148,29 +203,44 @@ def rank_program(g, core, T, topo):
     def bytes_of(x):
         return (x[0].bitcast(dt.uint8), x[1])
 
+    def count(x):
+        return len(range(x[1][3], x[1][4], x[1][5]))
+
+    def span(out, *ins, both=False):
+        sides = [out] + list(ins)
+        c = 0.5 if all(SCRATCH[x[1][0]][2] in (BF, U16) for x in sides) else 1.0
+        if both and not any(is_bank(x[1]) for x in ins):
+            c *= 2
+        return CYC * max(64, c * count(out))
+
     def memset(out, c):
-        op("v", lambda: g.vector.memset(out[0], c), [], [out])
+        op("v", lambda: g.vector.memset(out[0], c), [], [out], span(out))
 
     def copy(out, in_):
-        op("v", lambda: g.vector.tensor_copy(out[0], in_[0]), [in_], [out])
+        op("v", lambda: g.vector.tensor_copy(out[0], in_[0]), [in_], [out], span(out, in_))
 
     def ts(out, in0, s1, s2, o0, o1=None):
         if o1 is None:
-            op("v", lambda: g.vector.tensor_scalar(out[0], in0[0], ap(s1), None, o0), [in0, s1], [out])
+            fn = lambda: g.vector.tensor_scalar(out[0], in0[0], ap(s1), None, o0)
         else:
-            op("v", lambda: g.vector.tensor_scalar(out[0], in0[0], ap(s1), ap(s2), o0, o1), [in0, s1, s2], [out])
+            fn = lambda: g.vector.tensor_scalar(out[0], in0[0], ap(s1), ap(s2), o0, o1)
+        op("v", fn, [in0, s1, s2], [out], span(out, in0))
 
     def tt(out, in0, in1, o):
-        op("v", lambda: g.vector.tensor_tensor(out[0], in0[0], in1[0], o), [in0, in1], [out])
+        op("v", lambda: g.vector.tensor_tensor(out[0], in0[0], in1[0], o), [in0, in1], [out],
+           span(out, in0, in1, both=True))
 
     def scan(out, d0, d1, init, o0=ALU.add, o1=ALU.max):
-        op("v", lambda: g.vector.tensor_tensor_scan(out[0], d0[0], d1[0], init, o0, o1), [d0, d1], [out])
+        op("v", lambda: g.vector.tensor_tensor_scan(out[0], d0[0], d1[0], init, o0, o1), [d0, d1], [out],
+           span(out, d0, d1))
 
     def gather(out, win, off):
-        op("v", lambda: g.vector.tensor_copy(out[0], win[0].indirect(off[0])), [win, off], [out])
+        op("v", lambda: g.vector.tensor_copy(out[0], win[0].indirect(off[0])), [win, off], [out],
+           50 + GAT * CYC * count(out))
 
     def scatter(win, off, in_):
-        op("v", lambda: g.vector.tensor_copy(win[0].indirect(off[0]), in_[0]), [in_, off], [win])
+        op("v", lambda: g.vector.tensor_copy(win[0].indirect(off[0]), in_[0]), [in_, off], [win],
+           50 + SCA * CYC * count(in_))
 
     def act(out, in_, func=ACT.Copy, bias=None, scale=None, accum=None, off=None):
         src = in_[0] if off is None else in_[0].indirect(off[0])
@@ -181,173 +251,133 @@ def rank_program(g, core, T, topo):
             kw["scale"] = ap(scale)
         if accum is not None:
             kw["accum_out"] = accum[0]
+        busy = CYC * max(64, count(out)) if off is None else 65 + GAT * CYC * count(out)
         op("a", lambda: g.scalar.activation(out[0], src, func, **kw), [in_, bias, scale, off],
-           [out] + ([accum] if accum is not None else []))
+           [out] + ([accum] if accum is not None else []), busy + (20 if accum is not None else 0))
 
     def lin(out, in_, scale, bias):
         act(out, in_, ACT.Identity, bias, scale)
 
     def quant(name, c0, c1, src=None):
         qq, ss, in_ = A("q" + name, c0, c1), A("s" + name, c0, c1), A(src or name, 4 * c0, 4 * c1)
-        op("v", lambda: g.vector.quantize_mx(qq[0], ss[0], in_[0]), [in_], [qq, ss])
+        op("v", lambda: g.vector.quantize_mx(qq[0], ss[0], in_[0]), [in_], [qq, ss], 12 + 0.88 * (c1 - c0))
 
-    def pick(dst, d0, d1, src, off):
+    def pick(dst, d0, d1, src, off, on="a"):
         qo, qi, so, si = A("q" + dst, d0, d1), A("q" + src), A("s" + dst, d0, d1), A("s" + src)
         op("v", lambda: g.vector.tensor_copy(qo[0].bitcast(dt.uint32), qi[0].bitcast(dt.uint32).indirect(off[0])),
-           [qi, off], [qo])
-        op("a", lambda: g.scalar.activation(so[0], si[0].indirect(off[0]), ACT.Copy), [si, off], [so])
+           [qi, off], [qo], 50 + GAT * CYC * (d1 - d0))
+        (act if on == "a" else gather)(so, si, off=off)
 
     def mm(bank, st, s0, mv, m0, n, start=True, stop=True):
         out = A("P%d" % bank, 0, n)
         a, b = A("q" + st, s0, s0 + 128), A("s" + st, s0, s0 + 128)
         c, d = A("q" + mv, m0, m0 + n), A("s" + mv, m0, m0 + n)
-        op("t", lambda: g.tensor.matmul_mx(out[0], a[0], b[0], c[0], d[0], start, stop), [a, b, c, d], [out])
+        op("t", lambda: g.tensor.matmul_mx(out[0], a[0], b[0], c[0], d[0], start, stop), [a, b, c, d], [out],
+           CYC * (n + 16))
 
     def iota(out, pattern, base, cm=0, real=True):
-        if real:
-            op("g", lambda: g.iota(out[0], pattern, base, cm, allow_small_or_imprecise_dtypes=True), [], [out])
-        else:
-            op("g", lambda: g.iota(out[0], pattern, base, cm), [], [out])
+        kw = {"allow_small_or_imprecise_dtypes": True} if real else {}
+        op("g", lambda: g.iota(out[0], pattern, base, cm, **kw), [], [out], 130 + 2 * CYC * count(out))
 
     def select(out, in_, pattern, cmp, base, cm):
-        op("g", lambda: g.affine_select(out[0], in_[0], pattern, cmp, 0.0, base, cm), [in_], [out])
+        op("g", lambda: g.affine_select(out[0], in_[0], pattern, cmp, 0.0, base, cm), [in_], [out],
+           170 + 2 * CYC * count(out))
 
     def col(name, c):
         return A(name, c, c + 1)
 
-    dma("s", group("ldu"), A("UU"), (T.u[:], None))
-    dma("a", group("ldx0"), A("XX", 0, 1536), (T.x[:, 0:1536], None))
-    dma("s", group("ldx1"), A("XX", 1536, 2048), (T.x[:, 1536:2048], None))
-    h = group("ldw")
-    dma("s", h, bytes_of(A("qW")), (T.wc[:], None))
-    dma("s", h, A("sW"), (T.ws[:], None))
-    dma("s", group("ldv"), A("VV"), (T.v[:], None))
+    def scaled(dst, d0, src, s0, n, on_scalar, c):
+        if on_scalar > 0:
+            act(A(dst, d0, d0 + on_scalar), A(src, s0, s0 + on_scalar), scale=c)
+        if on_scalar < n:
+            ts(A(dst, d0 + on_scalar, d0 + n), A(src, s0 + on_scalar, s0 + n), c, None, ALU.mult)
 
-    memset(A("ONE"), 1.0)
-    iota(A("UBI"), [[16, 8], [0, 8]], 0, 0, False)
+    def blk(b):
+        return 32 + K * b
+
+    def hbm(x):
+        return (x, None)
+
+    dmas("s", "ldu", [(A("UU"), hbm(T.u[:]))])
+    dmas("a", "ldx0", [(A("X0", 0, 4 * C), hbm(T.x[:, 0:4 * C]))], 3000.0)
+    dmas("s", "ldx1", [(A("X0", 4 * C, 2048), hbm(T.x[:, 4 * C:2048]))], 3500.0)
+    dmas("s", "ldw", [(bytes_of(A("qW")), hbm(T.wc[:])), (A("sW"), hbm(T.ws[:]))], 4500.0)
+    dmas("s", "ldv", [(A("VV"), hbm(T.v[:]))], 5000.0)
+
     iota(col("PI", 0), [[0, 1]], 0, 1, False)
-    select(A("MLT"), A("ONE", 0, 128), [[-1, 128]], ALU.is_gt, 0, 1)
-    memset(A("CE"), ETA)
-    memset(A("CC", 1536, 1664), 0.0)
-    for c0 in range(0, 1536, 512):
-        act(A("CC", c0, c0 + 512), A("ONE"), scale=0.0)
-    act(A("F512"), A("ONE", 0, 384), scale=512.0)
-    for c0, val in ((0, 415.0), (8, 287.0), (16, 159.0), (32, 511.0)):
-        memset(A("BASE", c0, c0 + 8), val)
-    for p0, p1, val in ((0, 32, 31.0), (32, 64, 32.0), (64, 128, 32.0)):
-        memset(A("BASE", 24, 32, 1, p0, p1), val)
-    memset(A("RR", 0, 8), 0.0)
-    memset(A("RR", 32, 40), 0.0)
-    memset(A("DD", 80, 88), 0.0)
-    copy(A("UBL"), A("UBI"))
-    for c, (sh, msk) in enumerate(((0, 15), (0, 1), (1, 1), (2, 3), (4, 7), (0, 3), (3, 1), (0, 7), (5, 3))):
-        ts(col("PI", c + 1), col("PI", 0), sh, msk, ALU.logical_shift_right, ALU.bitwise_and)
-    c_q, c_a0, c_a1, c_q4, c_g, c_t, c_h, c_8, c_k = [col("PF", c) for c in range(1, 10)]
-    c_eta = col("CE", 0)
+    iota(A("UBI"), [[16, 8]], 0, 0, False)
+    iota(A("CR"), [[0, M], [1, 16]], 0)
+    iota(A("KLI"), [[16, M]], 15, 0, False)
+    iota(A("CG"), [[1, 8], [0, 64]], 0)
     iota(A("R16"), [[1, 2]], 0)
-    iota(A("B1"), [[1, 8], [8, 4]], 0)
-    iota(A("B1", 3, 32, 4, 32, 64), [[1, 8]], 32)
-    iota(A("B1", 3, 32, 4, 64, 128), [[1, 8]], 32)
-    iota(A("B2"), [[1, 8], [0, 4]], 24)
-    iota(A("S6"), [[16, 6]], 416)
+    iota(A("S6"), [[16, 6]], C)
     iota(A("BLI", 0, 3), [[128, 3]], 0)
     iota(A("PKI", 0, 7), [[2, 7]], 127)
     iota(A("PKI", 7, 15), [[2, 8]], 128)
-    iota(A("ZT"), [[0, 512]], 0)
-    iota(A("CR"), [[0, 6], [1, 16]], 0)
-    iota(A("CR4"), [[0, 128], [1, 4]], 0)
-    for k in range(4):
-        select(A("C2", 0, 128, 1, 32 * k, 32 * k + 32), A("ONE", 0, 128, 1, 32 * k, 32 * k + 32),
-               [[-1, 32], [1000, 2], [0, 2]], ALU.is_equal, 0, 1)
-    select(A("C2", 128, 512), A("F512"), [[-1, 96], [1000, 2], [0, 2]], ALU.is_equal, -1032, 1)
-    iota(A("WC"), [[1, 96]], 416)
-    iota(A("VS"), [[1, 32], [32, 16]], 0)
-    iota(A("BT"), [[0, 512]], 0)
+    signs = sum(min(4, M - 4 * b) for b, on in enumerate(CFG["CROSS"]) if on == "a")
+    iota(A("WC"), [[1, K]], C + 16 * 256 * signs)
+    iota(A("VS"), [[1, C]], 0)
+    iota(A("CR4"), [[0, C // 4], [1, 4]], 0)
+    for (lanes, at, w, pad) in TILES:
+        lo = min([16 * m for m in lanes if m not in ("A", "B")]) if len(lanes) == 4 else 0
+        memset(A("TR", 4 * (at + lo), 4 * (at + pad)), 0.0)
+    memset(A("TC", 0, 4 * blk(2)), 0.0)
+    memset(A("TC", 4 * blk(NB - 1), 4 * blk(NB)), 0.0)
+    memset(A("ZW", 0, 128), 0.0)
+    memset(A("BT"), 0.0)
+    memset(A("ZT"), 0.0)
+    memset(A("ONE"), 1.0)
+    copy(A("UBL"), A("UBI"))
+    copy(A("KL"), A("KLI"))
+    for c, (sh, msk) in enumerate(((0, 15), (2, 3), (4, 7), (0, 3), (3, 1), (0, 7))):
+        ts(col("PI", c + 1), col("PI", 0), sh, msk, ALU.logical_shift_right, ALU.bitwise_and)
+    copy(A("PF", 0, 7), A("PI", 0, 7))
+    c_q, c_q4, c_g, c_t, c_h, c_8 = [col("PF", c) for c in range(1, 7)]
+    g_off, g_thr, g_sub, g_o4, g_b0, g_b1, g_i0, g_i1, g_lt, g_row, g_wt = [col("PG", c) for c in range(11)]
+    ts(A("MK"), A("CR"), c_q, None, ALU.is_equal)
+    ts(A("RS"), A("CR"), 0.0, None, ALU.is_gt)
+    quant("LD0", 0, 128, "ZT")
+    dmas("s", "zl", [p for k in range(1, NR) for p in (
+        (bytes_of(A("qLD%d" % k, 0, 128)), bytes_of(A("qLD0", 0, 128))), (A("sLD%d" % k, 0, 128), A("sLD0", 0, 128)))])
+    ts(A("SR1"), A("CG"), c_g, -1.0, ALU.is_equal, ALU.mult)
+    act(A("SK"), A("SR1"), scale=-256.0)
+    act(A("SX", 2, 512, 4), A("SR1", 2, 512, 4))
+    act(A("SX", 3, 512, 4), A("SR1", 3, 512, 4))
+    act(A("C2"), A("SR1", 0, 512, 4), scale=-2.0)
+    select(A("SX", 0, 512, 4), A("C2"), [[1, 128]], ALU.is_gt, 0, -1)
+    select(A("SX", 1, 512, 4), A("C2"), [[-1, 128]], ALU.is_gt, 0, 1)
+    for name in ("SR1", "SX", "SK"):
+        quant(name, 0, 128)
     for k in range(8):
         select(A("EE", 512 * k, 512 * k + 512), A("ONE"), [[-1000, 4], [-1, 32], [1000, 4]], ALU.is_equal, -16 * k, 1)
-
-    g_off, g_thr, g_sub, g_o4, g_na1, g_a40, g_b0, g_b1, g_i0, g_i1, g_eq, g_m, g_sc, g_bi, g_lt = [
-        col("PG", c) for c in range(15)]
-
-    def late0():
-        for c0, p0, p1 in ((128, 0, 128), (640, 0, 32), (1152, 0, 32), (1184, 32, 64), (1184, 64, 128)):
-            memset(A("CC", c0, c0 + 20, 5, p0, p1), -1.0)
-        copy(A("PF", 0, 10), A("PI", 0, 10))
-        quant("CC", 0, 416)
-
-    def late1():
-        ts(g_off, c_q, -1024.0, 15360.0, ALU.mult, ALU.add)
-        ts(g_o4, c_q4, 4096.0, -12288.0, ALU.mult, ALU.add)
-        lin(g_na1, c_a1, -1.0, 1.0)
-        ts(g_a40, c_a0, 40.0, -80.0, ALU.mult, ALU.add)
-        lin(g_b0, c_q4, 32.0, c_t)
-        ts(A("PG", 8, 10), A("R16"), c_8, None, ALU.is_equal)
-        ts(A("PKJ", 0, 15), A("PKI", 0, 15), c_h, 139.0, ALU.add, ALU.min)
-        ts(g_eq, c_q4, c_k, None, ALU.is_equal)
-
-    def late2():
-        ts(g_thr, g_off, 417.0 + BIG, None, ALU.add)
-        ts(g_sub, g_off, 1.0 + BIG, None, ALU.add)
-        lin(g_b1, c_g, 4.0, g_b0)
-        lin(g_lt, g_o4, None, c_t)
-        lin(g_sc, g_eq, g_na1, None)
-        ts(g_m, g_eq, c_a1, None, ALU.max)
-        ts(A("PKL", 0, 7), A("PKJ", 0, 7), g_i0, None, ALU.mult)
-        ts(A("PKL", 7, 15), A("PKJ", 7, 15), g_i1, None, ALU.mult)
-
-    def late3():
-        ts(A("SR"), A("S6"), c_q, g_sub, ALU.add, ALU.add)
-        lin(g_bi, g_m, g_a40, 80.0)
-        lin(A("B4"), A("B2"), c_a1, None)
-        ts(A("BL", 0, 3), A("BLI", 0, 3), g_b1, None, ALU.add)
-
-    def late4():
-        lin(A("B3"), A("B1"), g_sc, g_bi)
-        ts(A("CT"), A("CR"), c_q, 32768.0, ALU.is_gt, ALU.mult)
-        ts(A("CT4"), A("CR4"), c_q4, 32768.0, ALU.is_gt, ALU.mult)
-        quant("LD0", 0, 128, "ZT")
-        hz = group("zl")
-        for k in range(1, NR):
-            dma("s", hz, bytes_of(A("qLD%d" % k, 0, 128)), bytes_of(A("qLD0", 0, 128)))
-            dma("s", hz, A("sLD%d" % k, 0, 128), A("sLD0", 0, 128))
-
-    def late5():
-        tt(A("B5"), A("B3"), A("B4"), ALU.add)
-
-    def late6():
-        copy(A("GL"), A("B5"))
-        lin(A("CS"), A("CT"), None, -31744.0)
-        lin(A("CS4"), A("CT4"), None, -31744.0)
-        quant("C2", 0, 128)
-
-    late = [late0, late1, late2, late3, late4, late5, late6]
-    epieces = list(range(8))
-
-    def quant_e(n):
-        for k in range(min(n, len(epieces))):
-            e = epieces.pop(0)
-            quant("E", 128 * e, 128 * e + 128, "EE")
+        quant("E", 128 * k, 128 * k + 128, "EE")
+    wv = 5 if CFG["WW"] == "v" else 0
+    memset(col("AC", S - 1), 16.0 * LOW)
+    memset(col("AC", S * M + S - 1), 16.0 * wv)
+    lin(g_off, c_q, -STEP, 15 * STEP)
+    lin(g_o4, c_q4, 4096.0, -12288.0)
+    lin(g_b0, c_q4, 32.0, c_t)
+    lin(g_thr, g_off, None, C + 1.0 + BIG)
+    lin(g_sub, g_off, None, 1.0 + BIG)
+    lin(g_row, g_off, -1.0, 16.0 * (M - 1 + TOP))
+    lin(g_wt, g_off, -1.0, 16.0 * (K // 16 - 1))
+    lin(g_b1, c_g, 4.0, g_b0)
+    lin(g_lt, g_o4, None, c_t)
+    ts(A("CT"), A("CR"), c_q, 32 * STEP, ALU.is_gt, ALU.mult)
+    ts(A("CT4"), A("CR4"), c_q4, 32768.0, ALU.is_gt, ALU.mult)
+    lin(A("CS"), A("CT"), None, -31 * STEP)
+    lin(A("CS4"), A("CT4"), None, -31744.0)
+    ts(A("PG", 6, 8), A("R16"), c_8, None, ALU.is_equal)
+    ts(A("PKJ", 0, 15), A("PKI", 0, 15), c_h, 139.0, ALU.add, ALU.min)
+    ts(A("SR"), A("S6"), c_q, g_sub, ALU.add, ALU.add)
+    ts(A("BL", 0, 3), A("BLI", 0, 3), g_b1, None, ALU.add)
+    ts(A("PKL", 0, 7), A("PKJ", 0, 7), g_i0, None, ALU.mult)
+    ts(A("PKL", 7, 15), A("PKJ", 7, 15), g_i1, None, ALU.mult)
 
     quant("U", 0, 128, "UU")
-    pick("UB", 0, 384, "U", A("UBL", 0, 24))
-    quant("X", 0, 384, "XX")
-
-    arrivals = {}
-
-    def unpack_pick(t):
-        land = [A("qLD%d" % t, 128, 140)[1], A("sLD%d" % t, 128, 140)[1]]
-        record("r", [], land, arrivals[t])
-        pick("PK%d" % t, 0, 240, "LD%d" % t, A("PKL", 0, 15))
-        for k in range(8):
-            mm(6, "E", 128 * k, "PK%d" % t, (8 - k) if k % 2 == 0 else (113 - k), 128, k == 0, k == 7)
-
-    def unpack_copy(f):
-        for b in range(4):
-            f(A("XX", 1664 + b, 2048, 4, 0, 16), A("P6", 0, 96, 1, 32 * b, 32 * b + 16))
-
-    def thresholds(c0, c1):
-        act(A("KA", c0, c1), A("KS", c0, c1), ACT.Abs, scale=PHI)
-        lin(A("KE", c0, c1), A("KA", c0, c1), None, c_eta)
+    pick("UB", 0, 128, "U", A("UBL"))
+    quant("V", 0, 128, "VV")
+    quant("X", 0, C, "X0")
 
     def send(t):
         gather(A("BT", 0, 48), A("MR"), A("BL", 0, 3))
@@ -356,217 +386,185 @@ def rank_program(g, core, T, topo):
         src = T.cores[(rank - t - 1) % n_ranks]
         rid, pid, _ = topo.addr(dst)
         qb, sb = A("qB%d" % t, 0, 12), A("sB%d" % t, 0, 12)
-        need("g", collect("g", [qb[1], sb[1]], [], True))
-        g.remote_dma(T["qLD%d" % t][:, 128:140].bitcast(dt.uint8), qb[0].bitcast(dt.uint8), T.sem["arr%d" % t],
-                     T.sem.loc, pid, rid, topo.mask(core, dst))
-        g.remote_dma(T["sLD%d" % t][:, 128:140], sb[0], T.sem["arr%d" % t], T.sem.loc, pid, rid, topo.mask(core, dst))
-        total["loc"] = total.get("loc", 0) + 2 * len(topo.engines(core, dst))
-        total["arr%d" % t] = 2 * len(topo.engines(src, core))
-        serial[0] += 1
-        arrivals[t] = {"sem": "arr%d" % t, "cnt": total["arr%d" % t], "clock": {}, "dma": True, "n": serial[0]}
+        ql, sl = A("qLD%d" % t, 128, 140), A("sLD%d" % t, 128, 140)
+        arr = "arr%d" % t
+
+        def run():
+            need("g", collect("g", [qb[1], sb[1]], [], True))
+            g.remote_dma(ql[0].bitcast(dt.uint8), qb[0].bitcast(dt.uint8), T.sem[arr], T.sem.loc, pid, rid,
+                         topo.mask(core, dst))
+            g.remote_dma(sl[0], sb[0], T.sem[arr], T.sem.loc, pid, rid, topo.mask(core, dst))
+            total["loc"] = total.get("loc", 0) + 2 * len(topo.engines(core, dst))
+            total[arr] = 2 * len(topo.engines(src, core))
+            record("r", [], [ql[1], sl[1]], arr, True)
+        note("g", run, [qb[1], sb[1]], [ql[1], sl[1]], 200.0, REMOTE)
+
+    def unpack(t, xx, f):
+        pick("PK%d" % t, 0, 240, "LD%d" % t, A("PKL", 0, 15), CFG["SP"])
+        for k in range(8):
+            mm(5, "E", 128 * k, "PK%d" % t, (8 - k) if k % 2 == 0 else (113 - k), 128, k == 0, k == 7)
+        for b in range(4):
+            f(A(xx, 4 * C + b, 2048, 4, 0, 16), A("P5", 0, K, 1, 32 * b, 32 * b + 16))
+
+    where = {m: (at, ln) for (lanes, at, w, pad) in TILES for ln, m in enumerate(lanes)}
+
+    def lane(buf, at, ln, c0, c1):
+        return A(buf, 4 * (at + c0) + ln, 4 * (at + c1), 4)
+
+    def own_keys(dst, bank, c0, c1, p0=0, k0=0):
+        tt(A("KM", k0 + c0, k0 + c1), A(bank, p0 + c0, p0 + c1), A("MK", c0, c1), ALU.mult)
+        scan(A(dst, c0, c1), A("RS", c0, c1), A("KM", k0 + c0, k0 + c1), 0.0, ALU.mult, ALU.add)
+
+    def step(on, buf, at, ln, src, p0, keys, m, slot, start):
+        out, own_key, end = lane(buf, at, ln, 0, 16 * m), col(keys, 16 * m + 15), S * slot + S
+        if on == "a":
+            lin(out, A(src, p0, p0 + 16 * m), -1.0, own_key)
+            act(out, out, ACT.Sign, bias=ETA, accum=col("AC", end - 1))
+        else:
+            ts(out, A(src, p0, p0 + 16 * m), own_key, 2.0, ALU.is_le, ALU.mult)
+            scan(A("AC", end - 8 * m, end), lane(buf, at, ln, 0, 8 * m), lane(buf, at, ln, 8 * m, 16 * m),
+                 start - 16.0 * m, ALU.add, ALU.add)
+
+    def place(name, bank, c0, n, slot, off, win, vals, p0=0):
+        k = n // 16
+        scan(A("HS", c0, c0 + n), A("CS", 0, n), A("P%d" % bank, p0, p0 + n), 0.0)
+        tt(A("TOT", slot, slot + k), A("HS", c0 + 15, c0 + n, 16), A("AC", S * slot + S - 1, S * (slot + k), S), ALU.add)
+        ts(A("OF" + name, 0, k), A("TOT", slot, slot + k), off, 0.5, ALU.add, ALU.mult)
+        scatter(win, A("OF" + name, 0, k), vals)
 
     for t in range(NR):
-        first = [True]
+        xx, xn = "X%d" % (t % 2), "X%d" % ((t + 1) % 2)
 
-        def colsum(tile, w0, blk, gq, pos, last=False):
-            mm(5, tile, w0, "CC", pos - (8 * blk + 4 * gq), 128, first[0], last)
-            first[0] = False
-
-        def sums_one(gq):
-            quant("TA%d" % gq, 0, 384)
-            quant("TD%d" % gq, 0, 384)
-            for w0, blk in ((0, 0), (128, 0), (256, 1)):
-                colsum("TA%d" % gq, w0, blk, gq, 32)
-            for blk in range(3):
-                colsum("TD%d" % gq, 128 * blk, blk, gq, 32)
-
-        def sums_two(gq):
-            quant("TB%d" % gq, 0, 384)
-            for blk in range(3):
-                colsum("TB%d" % gq, 128 * blk, blk, gq, 160)
-            quant("TB%d" % gq, 384, 512)
-            colsum("TB%d" % gq, 384, 3, gq, 288, gq == 1)
-
-        def off_tile(gr, blk):
-            gq, lane = gr // 4, gr % 4
-            if blk == 3:
-                return A("TB%d" % gq, lane, 1536, 4)
-            return A("TA%d" % gq, lane, 512, 4) if blk == 1 else A("TA%d" % gq, 512 + lane, 1536, 4)
-
-        def diag_tile(gr, b0):
-            gq, lane = gr // 4, gr % 4
-            if b0 == 3:
-                return A("TB%d" % gq, 1536 + lane, 2048, 4)
-            return A("TD%d" % gq, lane, 1536, 4)
-
-        def unit(gr, blks):
-            bk, top = gr % 4, 128 * (blks[-1] + 1)
-
-            def z0():
-                mm(bk, "UB", 128 * gr, "X", 0, top)
-                for blk in blks:
-                    c0 = 512 * gr + 128 * blk
-                    lin(A("TH", c0, c0 + 128), A("MLT"), col("KE", 8 * blk + gr), col("KS", 8 * blk + gr))
-
-            def z1():
-                for blk in blks:
-                    if blk > 0:
-                        ts(off_tile(gr, blk), A("P%d" % bk, 0, 128 * blk), col("KS", 8 * blk + gr), None, ALU.is_le)
-                tt(diag_tile(gr, blks[0]), A("P%d" % bk, 128 * blks[0], top),
-                   A("TH", 512 * gr + 128 * blks[0], 512 * gr + top), ALU.is_lt)
-
-            def z2():
-                for blk in blks:
-                    if blk > 0:
-                        c0 = 768 * gr + 64 * blk * (blk - 1)
-                        act(A("JK", c0, c0 + 128 * blk), off_tile(gr, blk), accum=col("RR", 8 * blk + gr))
-            return [z0, z1, z2]
-
-        for blk in (1, 2, 0):
-            mm(4 + blk, "X", 128 * blk, "U", 0, 128)
-        for blk in (1, 2, 0):
-            act(A("KS", 8 * blk, 8 * blk + 8), A("P%d" % (4 + blk), 0, 128, 16))
-        thresholds(0, 24)
-        units = [unit(gr, [0, 1, 2]) for gr in range(8)] + [unit(gr, [3]) for gr in range(8)]
-        hooks = {}
-
-        def hook(n, f):
-            hooks.setdefault(n, []).append(f)
-
-        def block3():
-            quant("X", 384, 512, "XX")
-            mm(6, "X", 384, "U", 0, 128)
-            act(A("KS", 24, 32), A("P6", 0, 128, 16))
-            thresholds(24, 32)
+        mm(1, "UB", 0, "X", 0, C)
+        mm(0, "UB", 0, "X", 0, C)
+        own_keys("KS", "P1", CFG["KSPLIT"], C)
+        own_keys("KS", "P1", 0, CFG["KSPLIT"])
+        act(A("KB"), A("KS"), off=A("KL"))
+        tt(lane("TR", 0, 0, 0, C), A("P1", 0, C), A("KB"), ALU.is_ge)
+        tt(lane("TR", 0, 1, 0, C), A("P1", 0, C), A("KB"), ALU.is_gt)
+        for m in range(M - 1, 0, -1):
+            at, ln = where[m]
+            if m >= M - TOP:
+                step("v", "TR", at, ln, "P1", 0, "KS", m, m, 16.0 * (M - 1 - m - TOP))
+            elif m <= LOW:
+                step("v", "TR", at, ln, "P1", 0, "KS", m, m, 16.0 * (LOW - m))
+            else:
+                step("a", "TR", at, ln, "P0", 0, "KS", m, m, 0.0)
 
         if t > 0:
-            hook(7 - LOOK - CFG["UNP"], lambda: unpack_pick(t - 1))
-            hook(8 - LOOK - CFG["UNP"], lambda: unpack_copy(act))
-        else:
-            hook(0, lambda: pick("UB", 384, 640, "U", A("UBL", 24, 40)))
-            hook(1, lambda: pick("UB", 640, 1024, "U", A("UBL", 40, 64)))
-            for n, f in enumerate(late):
-                hook(n + 2, f)
-        hook(7 - LOOK, block3)
-        hook(4, lambda: sums_one(0))
-        hook(8, lambda: sums_one(1))
-        hook(12, lambda: sums_two(0))
-        issued = 0
-        for n in range(16):
-            while issued < min(16, n + LOOK + 1):
-                units[issued][0]()
-                issued += 1
-            units[n][1]()
-            if n > 0:
-                units[n - 1][2]()
-            for f in hooks.get(n, []):
-                f()
-        units[-1][2]()
-        sums_two(1)
+            unpack(t - 1, xx, act if CFG["CP"] == "a" else copy)
+        quant("X", 384, 512, xx)
+        mm(2, "UB", 0, "X", 384, 128)
+        act(A("KW"), A("P2", 32, 128))
+        own_keys("KSW", "P2", 0, K, 32, C)
+        act(A("KBW"), A("KSW"), off=A("KL", 0, 6))
+        tt(lane("TC", blk(0), 0, 0, K), A("P2", 32, 128), A("KBW"), ALU.is_ge)
+        tt(lane("TC", blk(0), 1, 0, K), A("P2", 32, 128), A("KBW"), ALU.is_gt)
+        for m in range(5, 0, -1):
+            step(CFG["WW"], "TC", blk(0 if m > 3 else 1), (7 - m) % 4, "KW", 0, "KSW", m, M + m, 16.0 * (5 - m))
+        quant("TC", 0, blk(2))
+        mm(6, "SX", 0, "TC", blk(0) - 32, 128, True, False)
+        mm(6, "SR1", 0, "TC", blk(1) - 32, 128, False, True)
+        for b, on in enumerate(CFG["CROSS"]):
+            ms = range(4 * b, min(4 * b + 4, M))
+            for m in ms:
+                out = lane("TC", blk(2 + b), m % 4, 0, K)
+                if on == "v":
+                    ts(out, A("KW"), col("KS", 16 * m + 15), 2.0, ALU.is_ge, ALU.mult)
+                else:
+                    lin(out, A("KW"), -1.0, col("KS", 16 * m + 15))
+            outs = [A("TC", 4 * blk(2 + b), 4 * blk(3 + b))] if len(ms) == 4 else [
+                lane("TC", blk(2 + b), m % 4, 0, K) for m in ms]
+            for out in outs:
+                if on == "a":
+                    act(out, out, ACT.Sign, bias=ETA, scale=-1.0)
+                elif on == "m":
+                    ts(out, out, 0.0, 2.0, ALU.is_le, ALU.mult)
+        for b0, b1 in ((0, 2), (2, 4), (4, 7)):
+            quant("TC", blk(2 + b0), blk(2 + b1))
+            for b in range(b0, b1):
+                mm(5, "SK", 0, "TC", blk(2 + b) - 32, 128, b == 0, b == 6)
 
-        tt(A("RB"), A("RR"), A("BASE"), ALU.add)
-        quant_e(2)
-        tt(A("TOT"), A("P5", 0, 40), A("RB"), ALU.add)
-        ts(A("DD", 0, 40), A("TOT"), BIG32, BIG32, ALU.add, ALU.subtract)
-        tt(A("DD", 40, 80), A("TOT"), A("DD", 0, 40), ALU.subtract)
-        act(A("TG", 256, 512), A("DD"), off=A("GL", 16, 32))
-        gather(A("TG", 0, 256), A("DD"), A("GL", 0, 16))
-        quant("TG", 0, 128)
-        mm(4, "TG", 0, "C2", 0, 128)
-        quant_e(2)
-        copy(A("OF"), A("P4", 0, 32))
-        for k in range(3):
-            tt(A("VS", 13 + k, 512, 16), A("P4", 32 + 32 * k, 64 + 32 * k), A("WC", 32 * k, 32 * k + 32), ALU.add)
-        scatter(A("W1"), A("OF"), A("VS"))
+        for i, (lanes, at, w, pad) in enumerate(TILES):
+            quant("TR", at, at + (pad if t == 0 else max(w, 128)))
+            for (name, a, b, bank) in RANGES:
+                if a < w:
+                    last = i + 1 == len(TILES) or TILES[i + 1][2] <= a
+                    mm(bank, "SX" if i == 0 else "SR1", 0, "TR", at + a, max(128, min(b, w) - a), i == 0, last)
+        for (name, a, b, bank) in RANGES:
+            place(name, bank, a, b - a, a // 16, g_row, A("W1", 0, C), A("VS", a, b))
 
-        ts(A("KC"), A("W1", 416, 512), 2.0 ** -9, BIG, ALU.mult, ALU.add)
+        tt(A("VW"), A("P5", 32, 128), A("WC"), ALU.add)
+        place("W", 6, C, K, M, g_wt, A("W1", C, 512), A("VW"), 32)
+        ts(A("KC"), A("W1", C, 512), 2.0 ** -9, BIG, ALU.mult, ALU.add)
         lin(A("NK"), A("KC"), -512.0, 512.0 * (BIG + 1.0))
-        act(A("W2", 0, 416), A("W1", 0, 416))
-        scan(A("PP"), A("ONE", 0, 96), A("KC"), BIG)
-        scan(A("PS"), A("CS"), A("PP"), 0.0)
-        raw = A("PS", 15, 96, 16)
+        scan(A("PP"), A("ONE", 0, K), A("KC"), BIG)
+        scan(A("PS"), A("CS", 0, K), A("PP"), 0.0)
+        raw = A("PS", 15, K, 16)
         ts(A("F6", 0, 6), raw, g_thr, 2.0 ** 25, ALU.is_ge, ALU.mult)
-        tt(A("W1", 416, 512), A("W1", 416, 512), A("NK"), ALU.add)
         tt(A("G6", 0, 6), A("F6", 0, 6), A("SR"), ALU.min)
         tt(A("H6", 0, 6), A("G6", 0, 6), raw, ALU.max)
         ts(A("PW"), A("H6", 0, 6), g_sub, None, ALU.subtract)
-        act(A("E2"), A("W1"), off=A("PW"))
-        scatter(A("W2"), A("PW"), A("W1", 416, 512))
-        scan(A("SC", 416, 512), A("CS4", 0, 96), A("E2"), 0.0)
-        scan(A("SC", 384, 416), A("CS4", 0, 32), A("W2", 384, 416), 0.0)
-        ts(A("LL", 96, 128), A("SC", 387, 512, 4), 4.0, g_lt, ALU.mult, ALU.add)
-
-        def take(on, c0, c1):
-            o, off = A("ZZ", 4 * c0, 4 * c1), A("LL", c0 // 4, c1 // 4)
-            if on == "a":
-                act(o, A("XX"), off=off)
-            else:
-                gather(o, A("XX"), off)
-
-        def scaled(on, dst, src, c, *view):
-            if on == "a":
-                act(A(dst, *view), A(src, *view), scale=c)
-            else:
-                ts(A(dst, *view), A(src, *view), c, None, ALU.mult)
-
-        take("a", 384, 384 + CFG["WS"])
-        if CFG["WS"] < 128:
-            take("v", 384 + CFG["WS"], 512)
-        scan(A("SC", 0, 384), A("CS4", 0, 384), A("W2", 0, 384), 0.0)
-        ts(A("LL", 0, 96), A("SC", 3, 384, 4), 4.0, g_lt, ALU.mult, ALU.add)
+        tt(A("BV"), A("W1", C, 512), A("NK"), ALU.add)
+        act(A("W1", C, 512), A("BV"))
+        gather(A("E2"), A("W1"), A("PW"))
+        scatter(A("W1"), A("PW"), A("BV"))
         if t == NR - 1:
-            h = group("ole")
-            dma("s", h, (T.le[:, 0:416], None), (T.W2[0:128:16, 0:416], A("W2", 0, 416)[1]))
-            dma("s", h, (T.le[:, 416:512], None), (T.E2[0:128:16, 0:96], A("E2")[1]))
-        take("a", 0, CFG["SPLIT"])
-        quant("Z", 384, 512, "ZZ")
-        for b in range(4):
-            mm(4 + b, "W", 128 * b, "Z", 384, 128)
-        scaled("v", "Z64", "ZZ", 64.0, 1536, 2048)
-        for b in range(4):
-            tt(A("T64", 1536 + b, 2048, 4), A("P%d" % (4 + b), 0, 128), A("Z64", 1536 + b, 2048, 4), ALU.add)
-        ts(A("MW"), A("T64", 1664, 2048), 0.015625, None, ALU.mult)
-        h = group("rep%d" % t)
-        for k in range(8):
-            dma("s", h, A("MR", 0, 384, 1, 16 * k, 16 * k + 16), A("MW", 0, 384, 1, 112, 128))
-        take("v", CFG["SPLIT"], 384)
-        quant("Z", 0, 384, "ZZ")
-        dma("s", group("shf%d" % t), A("XX", 1664, 2048, 1, 16, 128), A("MW", 0, 384, 1, 0, 112))
-        for b in range(4):
-            mm(b, "W", 128 * b, "Z", 0, 384)
-            scaled("v" if b < CFG["ZV"] else "a", "Z64", "ZZ", 64.0, b, 1536, 4)
-        scaled("a", "XX", "T64", 0.015625, 1536, 1664)
-        if t == NR - 1:
-            quant("V", 0, 128, "VV")
-            send(t)
-        for b in range(4):
-            tt(A("T64", b, 1536, 4), A("P%d" % b, 0, 384), A("Z64", b, 1536, 4), ALU.add)
-            if b == CFG["SP"] and t < NR - 1:
-                send(t)
-            if b < CFG["XA"]:
-                scaled("a", "XX", "T64", 0.015625, b, 1536, 4)
-        for b in range(CFG["XA"], 4):
-            scaled("v", "XX", "T64", 0.015625, b, 1536, 4)
-        quant("X", 0, 384, "XX")
-        quant_e(4)
+            dmas("s", "ole", [(hbm(T.le[:, 0:C]), (T.W1[0:128:16, 0:C], A("W1", 0, C)[1])),
+                              (hbm(T.le[:, C:512]), (T.E2[0:128:16, 0:K], A("E2")[1]))])
 
+        def take(dst, lst, c0, c1, on_scalar, at=0):
+            mid = c0 + on_scalar
+            if mid > c0:
+                act(A(dst, at + 4 * c0, at + 4 * mid), A(xx), off=A(lst, c0 // 4, mid // 4))
+            if mid < c1:
+                gather(A(dst, at + 4 * mid, at + 4 * c1), A(xx), A(lst, mid // 4, c1 // 4))
+
+        scan(A("SC", C, 512), A("CS4", 0, K), A("E2"), 0.0)
+        ts(A("LW"), A("SC", C + 3, 512, 4), 4.0, g_lt, ALU.mult, ALU.add)
+        take("ZW", "LW", 0, K, CFG["GW"], 128)
+        quant("ZW", 0, 128)
+        wb = (0, 1, 2, 7)
+        for b in range(4):
+            mm(wb[b], "W", 128 * b, "ZW", 0, 128)
+        scaled("W64", 0, "ZW", 128, 4 * K, 0, 64.0)
+        for b in range(4):
+            tt(A("U64", b, 4 * K, 4), A("P%d" % wb[b], 32, 128), A("W64", b, 4 * K, 4), ALU.add)
+        scaled("MW", 0, "U64", 0, 4 * K, 0, 0.015625)
+        dmas("s", "rep%d" % t, [(A("MR", 0, 384, 1, 16 * k, 16 * k + 16), A("MW", 0, 384, 1, 112, 128)) for k in range(8)])
+        dmas("s", "shf%d" % t, [(A(xn, 4 * C, 2048, 1, 16, 128), A("MW", 0, 384, 1, 0, 112))])
+        send(t)
+        H = C // 2
+        for i, banks in enumerate(((3, 4, 5, 6), wb)):
+            c0, c1 = i * H, i * H + H
+            scan(A("SC", c0, c1), A("CS4", 0, H), A("W1", c0, c1), 0.0)
+            ts(A("LL", c0 // 4, c1 // 4), A("SC", c0 + 3, c1, 4), 4.0, g_lt, ALU.mult, ALU.add)
+            take("ZZ", "LL", c0, c1, CFG["GA"][i])
+            quant("ZZ", c0, c1)
+            for b in range(4):
+                mm(banks[b], "W", 128 * b, "ZZ", c0, H)
+            scaled("Z64", 4 * c0, "ZZ", 4 * c0, 4 * H, 4 * CFG["ZA"][i], 64.0)
+            for b in range(4):
+                tt(A("T64", 4 * c0 + b, 4 * c1, 4), A("P%d" % banks[b], 0, H), A("Z64", 4 * c0 + b, 4 * c1, 4), ALU.add)
+            scaled(xn, 4 * c0, "T64", 4 * c0, 4 * H, 4 * CFG["XA"][i], 0.015625)
+            quant("X", c0, c1, xn)
+
+    xx = "X%d" % (NR % 2)
     mm(0, "V", 0, "X", 0, 384)
-    h = group("oa")
-    dma("s", h, (T.oc[:, 0:1536], None), bytes_of(A("qX", 0, 384)))
-    for k in range(4):
-        dma("s", h, (T.osc[4 * k:4 * k + 4, 0:384], None), A("sX", 0, 384, 1, 32 * k, 32 * k + 4))
+    dmas("s", "oa", [(hbm(T.oc[:, 0:1536]), bytes_of(A("qX", 0, 384)))] + [
+        (hbm(T.osc[4 * k:4 * k + 4, 0:384]), A("sX", 0, 384, 1, 32 * k, 32 * k + 4)) for k in range(4)])
     act(A("YY", 0, 384), A("P0", 0, 384))
-    dma("s", group("oy0"), (T.y[:, 0:384], None), A("YY", 0, 384))
-    unpack_pick(NR - 1)
-    unpack_copy(copy)
-    quant("X", 384, 512, "XX")
+    dmas("s", "oy0", [(hbm(T.y[:, 0:384]), A("YY", 0, 384))])
+    unpack(NR - 1, xx, copy)
+    quant("X", 384, 512, xx)
     mm(7, "V", 0, "X", 384, 128)
-    h = group("ob")
-    dma("s", h, (T.oc[:, 1536:2048], None), bytes_of(A("qX", 384, 512)))
-    for k in range(4):
-        dma("a" if k < 2 else "s", h, (T.osc[4 * k:4 * k + 4, 384:512], None), A("sX", 384, 512, 1, 32 * k, 32 * k + 4))
+    scales = [(hbm(T.osc[4 * k:4 * k + 4, 384:512]), A("sX", 384, 512, 1, 32 * k, 32 * k + 4)) for k in range(4)]
+    dmas("s", "ob", [(hbm(T.oc[:, 1536:2048]), bytes_of(A("qX", 384, 512)))] + scales[2:])
+    dmas("a", "oc", scales[:2])
     copy(A("YY", 384, 512), A("P7", 0, 128))
-    dma("a", group("oy1"), (T.y[:, 384:512], None), A("YY", 384, 512))
+    dmas("a", "oy1", [(hbm(T.y[:, 384:512]), A("YY", 384, 512))])
+
+    issue()
     for s, c in total.items():
         if known["g"].get(s, 0) < c:
             g.wait_ge(T.sem[s], c)

@@ -7,8 +7,8 @@ NR = 3
 C, K = 416, 96
 M = C // 16
 S = 200
-CFG = {"TOP": 3, "LOW": 2, "CROSS": "vvvaaaa", "WW": "a", "GW": 96, "GA": (144, 144), "XA": (208, 104), "ZA": (0, 0),
-       "CP": "a", "SP": "a", "KSPLIT": 288}
+CFG = {"TOP": 3, "LOW": 0, "CROSS": "vvvvvvv", "WW": "v", "GW": 96, "GA": (128, 208), "XA": (104, 208), "ZA": (104, 104),
+       "CP": "v", "SP": "a", "KSPLIT": 160, "DG": "v"}
 
 LANES = [["A", "B", M - 1, M - 2]] + [[m for m in range(top, top - 4, -1) if m > 0] for top in range(M - 3, 0, -4)]
 RANGES = (("H", 240, 416, 3), ("M", 112, 240, 7), ("L", 0, 112, 4))
@@ -253,7 +253,7 @@ def rank_program(g, core, T, topo):
             kw["accum_out"] = accum[0]
         busy = CYC * max(64, count(out)) if off is None else 65 + GAT * CYC * count(out)
         op("a", lambda: g.scalar.activation(out[0], src, func, **kw), [in_, bias, scale, off],
-           [out] + ([accum] if accum is not None else []), busy + (20 if accum is not None else 0))
+           [out] + ([accum] if accum is not None else []), busy + (45 if accum is not None else 25))
 
     def lin(out, in_, scale, bias):
         act(out, in_, ACT.Identity, bias, scale)
@@ -397,7 +397,7 @@ def rank_program(g, core, T, topo):
             total["loc"] = total.get("loc", 0) + 2 * len(topo.engines(core, dst))
             total[arr] = 2 * len(topo.engines(src, core))
             record("r", [], [ql[1], sl[1]], arr, True)
-        note("g", run, [qb[1], sb[1]], [ql[1], sl[1]], 200.0, REMOTE)
+        note("g", run, [qb[1], sb[1]], [ql[1], sl[1]], 200.0, REMOTE * (1.5 if t == 0 else 1.0))
 
     def unpack(t, xx, f):
         pick("PK%d" % t, 0, 240, "LD%d" % t, A("PKL", 0, 15), CFG["SP"])
@@ -440,8 +440,13 @@ def rank_program(g, core, T, topo):
         own_keys("KS", "P1", CFG["KSPLIT"], C)
         own_keys("KS", "P1", 0, CFG["KSPLIT"])
         act(A("KB"), A("KS"), off=A("KL"))
-        tt(lane("TR", 0, 0, 0, C), A("P1", 0, C), A("KB"), ALU.is_ge)
-        tt(lane("TR", 0, 1, 0, C), A("P1", 0, C), A("KB"), ALU.is_gt)
+        if CFG["DG"] == "v":
+            tt(lane("TR", 0, 0, 0, C), A("P1", 0, C), A("KB"), ALU.is_ge)
+            tt(lane("TR", 0, 1, 0, C), A("P1", 0, C), A("KB"), ALU.is_gt)
+        else:
+            tt(lane("TR", 0, 0, 0, C), A("P1", 0, C), A("KB"), ALU.subtract)
+            ts(lane("TR", 0, 1, 0, C), lane("TR", 0, 0, 0, C), 0.0, None, ALU.is_gt)
+            ts(lane("TR", 0, 0, 0, C), lane("TR", 0, 0, 0, C), 0.0, None, ALU.is_ge)
         for m in range(M - 1, 0, -1):
             at, ln = where[m]
             if m >= M - TOP:

@@ -7,21 +7,32 @@ NR = 3
 C, K = 416, 96
 M = C // 16
 S = 200
-CFG = {"TOP": 3, "LOW": 0, "CROSS": "vvvvvvv", "WW": "v", "GW": 96, "GA": (128, 208), "XA": (104, 208), "ZA": (104, 104),
-       "CP": "v", "SP": "a", "KSPLIT": 160, "DG": "v"}
+CFG = {"TOP": 3, "LOW": 0, "CROSS": "vvvvvvv", "WW": "v", "GW": 96, "GA": (0.62, 1), "XA": (0.5, 1), "ZA": (0.5, 0.5),
+       "CP": "v", "SP": "a", "KSPLIT": 160, "DG": "v", "CUTS": (240, 112), "HALF": 208, "L2": 1, "XL": 0,
+       "QT": ((0,), (1,), (2,), (3,), (4,), (5, 6)), "QC": ((0, 2), (2, 4), (4, 7)), "WA": (1, 0), "KC": "v", "ZM": "v",
+       "LOOK": 70.0, "PASS": 4, "EARLY": 5, "X2": 0, "LQ": "sassss", "SHORT": 0.0, "SB": 120.0, "BWT": 0.0, "B0": 1000.0, "BW": (1000.0, 3000.0)}
+CFG.update({"CUTS": (240, 112), "WW": "a", "ZA": (0.62, 0.62), "KC": "a", "CROSS": "avvvvvv", "TOP": 4, "CP": "a",
+            "ZM": "a", 'QC': ((0, 4), (4, 7)), 'WA': (0, 0), 'XL': 1, 'XA': (0.62, 0.75), 'KSPLIT': 288,
+            "BWT": 1000.0, "EARLY": 3, "B0": 0.0})
+CFG.update({'LQ': 'ssssss', 'EARLY': 0, 'ZA': (0.5, 0.5)})
 
 LANES = [["A", "B", M - 1, M - 2]] + [[m for m in range(top, top - 4, -1) if m > 0] for top in range(M - 3, 0, -4)]
-RANGES = (("H", 240, 416, 3), ("M", 112, 240, 7), ("L", 0, 112, 4))
-TILES = []
-_at = 0
-for _l in LANES:
-    _w = C if _l[0] == "A" else 16 * _l[0]
-    _p = max([_w, 128] + [min(a + 128, b) for (_n, a, b, _k) in RANGES if a < _w])
-    TILES.append((_l, _at, _w, _p))
-    _at += _p
-TRW = _at
+
+
+def layout(cuts):
+    ranges = [(n, a, b, k) for n, a, b, k in zip("HML", cuts + (0,), (C,) + cuts, (3, 7, 4))]
+    tiles, at = [], 0
+    for lanes in LANES:
+        w = C if lanes[0] == "A" else 16 * lanes[0]
+        pad = max([w] + [min(a + 128, b) for (n, a, b, k) in ranges if a < w])
+        tiles.append((lanes, at, w, pad))
+        at += pad
+    return ranges, tiles
+
+
+TRW = 2176
 NB = 9
-TCW = NB * K + 32
+TCW = NB * K + 64
 
 SCRATCH = {}
 for _d, _l in (
@@ -29,8 +40,8 @@ for _d, _l in (
              "ZT:512 ONE:512 CR:416 CR4:416 CG:512 MK:416 RS:416 C2:128 CT:416 CT4:416 CS:416 CS4:416 SR1:512 SX:512 "
              "SK:512 EE:4096 TR:%d TC:%d" % (4 * TRW, 4 * TCW)),
         (F32, "KM:512 KS:416 KW:96 KSW:96 KB:416 KBW:96 AC:%d HS:512 TOT:32 VS:416 VW:96 W1:512 BV:96 E2:96 KC:96 NK:96 "
-              "PP:96 PS:96 SC:512 F6:8 G6:8 H6:8 YY:512" % (32 * S)),
-        (I32, "PI:16 UBI:8 KLI:26"), (U16, "UBL:8 KL:26 PKL:16 BL:4 OFH:12 OFM:8 OFL:8 OFW:6 PW:6 LL:104 LW:24")):
+              "PP:96 PS:96 SC:512 WV:96 YY:512" % (32 * S)),
+        (I32, "PI:16 UBI:8 KLI:26"), (U16, "UBL:8 KL:26 PKL:16 BL:4 OFH:26 OFM:26 OFL:26 OFW:6 PW:6 LL:104 LW:24")):
     for _e in _l.split():
         SCRATCH[_e.split(":")[0]] = ("sbuf", [128, int(_e.split(":")[1])], _d)
 for _e in ("U:128 V:128 UB:128 W:512 X:512 ZZ:416 ZW:128 SR1:128 SX:128 SK:128 E:1024 TR:%d TC:%d B0:128 B1:128 B2:128 "
@@ -47,20 +58,23 @@ for _n, _w in (("R16", 2), ("PKI", 16), ("PKJ", 16), ("BLI", 4), ("S6", 6), ("SR
     _at += (_w + 7) // 8 * 8
 SCRATCH["KF"] = ("sbuf", [128, _at], F32)
 
-SEMAPHORES = ("sv sa st sg ldu ldx0 ldx1 ldw ldv loc ole oa ob oc oy0 oy1 zl "
+SEMAPHORES = ("sv sa st sg ldu ldx0 ldx1 ldx2 ldw ldv loc ole oa ob oc oy0 oy1 zl "
               "rep0 rep1 rep2 shf0 shf1 shf2 arr0 arr1 arr2").split()
 
 BIG = 1.5 * 2.0 ** 23
 ETA = 2.0 ** -110
 STEP = 2048.0
-CYC, WAKE, LOCAL, REMOTE, GAT, SCA = 0.83, 80.0, 2000.0, 3000.0, 1.56, 3.8
+CFG["T"] = (0.83, 0.0, 10.0, 90.0, 1600.0, 2500.0, 1.56, 3.8, 0.83)
+CFG["PS"] = 83.0
 
 
 def rank_program(g, core, T, topo):
     rank = T.rank_of(core)
     if rank is None:
         return
+    CYC, CALL, ACALL, WAKE, LOCAL, REMOTE, GAT, SCA, PE = CFG["T"]
     TOP, LOW = CFG["TOP"], CFG["LOW"]
+    RANGES, TILES = layout(CFG["CUTS"])
     n_ranks = len(T.cores)
     eng = {"v": g.vector, "a": g.scalar, "t": g.tensor, "g": g, "s": g.sync}
     own = {"v": "sv", "a": "sa", "t": "st", "g": "sg"}
@@ -71,6 +85,7 @@ def rank_program(g, core, T, topo):
     part = [False]
     calls = []
     touched = {}
+    boost = [0.0]
 
     def A(name, c0=0, c1=None, step=1, p0=0, p1=128):
         if name in POOL:
@@ -96,12 +111,14 @@ def rank_program(g, core, T, topo):
         return True
 
     def note(q, run, reads, writes, busy, late=0.0):
-        c = {"q": q, "run": run, "busy": busy, "late": late, "after": {}, "next": [], "i": len(calls)}
+        c = {"q": q, "run": run, "busy": busy, "late": late, "after": {}, "next": [], "i": len(calls),
+             "list": any(SCRATCH[k[0]][2] == U16 for k in reads),
+             "boost": boost[0] + (CFG["SHORT"] if q == "a" and busy < CFG["SB"] else 0.0)}
         for keys, wr in ((reads, False), (writes, True)):
             for k in keys:
                 for (k2, wr2, d) in touched.get(k[0], []):
                     if (wr or wr2) and d is not c and meets(k, k2):
-                        free = d["q"] == q and not d["late"] and (not wr2 or q == "t")
+                        free = d["q"] == q and not d["late"] and (not wr2 and not d["list"] or q == "t")
                         c["after"][d["i"]] = max(c["after"].get(d["i"], 0.0), 0.0 if free else WAKE + d["late"])
         for keys, wr in ((reads, False), (writes, True)):
             for k in keys:
@@ -110,26 +127,39 @@ def rank_program(g, core, T, topo):
             calls[i]["next"].append(c)
         calls.append(c)
 
-    def issue():
-        for c in reversed(calls):
-            c["way"] = c["busy"] + max([c["late"]] + [d["way"] + d["after"][c["i"]] for d in c["next"]])
-            c["left"] = len(c["after"])
-            c["at"] = 0.0
-        ready = [c for c in calls if not c["left"]]
+    def plan(way, links, waits, lead):
+        left, at, ends, order = list(waits), list(lead), [0.0] * len(calls), []
+        ready = {q: [c["i"] for c in calls if c["q"] == q and not left[c["i"]]] for q in eng}
         free = {q: 0.0 for q in eng}
-        while ready:
-            first = min(ready, key=lambda c: (max(c["at"], free[c["q"]]), c["i"]))
-            t0 = max(first["at"], free[first["q"]])
-            c = max([c for c in ready if c["q"] == first["q"] and c["at"] <= t0 + WAKE], key=lambda c: (c["way"], -c["i"]))
-            ready.remove(c)
-            end = max(c["at"], free[c["q"]]) + c["busy"]
-            free[c["q"]] = end
-            c["run"]()
-            for d in c["next"]:
-                d["at"] = max(d["at"], end + d["after"][c["i"]])
-                d["left"] -= 1
-                if not d["left"]:
-                    ready.append(d)
+        while len(order) < len(calls):
+            t0, q = min((max(min(at[i] for i in ready[q]), free[q]), q) for q in eng if ready[q])
+            i = max((i for i in ready[q] if at[i] <= t0 + CFG["LOOK"]), key=lambda i: (way[i], -i))
+            ready[q].remove(i)
+            order.append(i)
+            ends[i] = free[q] = max(at[i], free[q]) + calls[i]["busy"]
+            for (j, gap) in links[i]:
+                at[j] = max(at[j], ends[i] + gap)
+                left[j] -= 1
+                if not left[j]:
+                    ready[calls[j]["q"]].append(j)
+        return order, ends
+
+    def issue():
+        ahead = [[(d["i"], d["after"][c["i"]]) for d in c["next"]] for c in calls]
+        behind = [list(c["after"].items()) for c in calls]
+        way = [0.0] * len(calls)
+        for c in reversed(calls):
+            way[c["i"]] = c["busy"] + max([c["late"]] + [way[j] + gap for (j, gap) in ahead[c["i"]]])
+        best = None
+        for k in range(CFG["PASS"]):
+            way = [c.get("first", way[c["i"]] + c["boost"]) for c in calls]
+            order, ends = plan(way, ahead, [len(b) for b in behind], [0.0] * len(calls))
+            length = max(ends[c["i"]] + c["late"] for c in calls)
+            if best is None or length < best[0]:
+                best = (length, order)
+            way = plan(ends, behind, [len(a) for a in ahead], [c["late"] for c in calls])[1]
+        for i in best[1]:
+            calls[i]["run"]()
 
     def need(q, deps):
         for h in sorted(deps, key=lambda h: -h["n"]):
@@ -153,7 +183,7 @@ def rank_program(g, core, T, topo):
                             continue
                     elif not (wr or wr2):
                         continue
-                    elif q2 == q and not dma and not h["dma"] and not wr2:
+                    elif q2 == q and not dma and not h["dma"] and not wr2 and not h["list"]:
                         continue
                     old = deps.get(h["sem"])
                     if old is None or old["cnt"] < h["cnt"]:
@@ -162,7 +192,8 @@ def rank_program(g, core, T, topo):
 
     def record(q, reads, writes, sem, dma):
         serial[0] += 1
-        h = {"sem": sem, "cnt": total[sem], "clock": dict(known[q]) if q in known else {}, "dma": dma, "n": serial[0]}
+        h = {"sem": sem, "cnt": total[sem], "clock": dict(known[q]) if q in known else {}, "dma": dma, "n": serial[0],
+             "list": any(SCRATCH[k[0]][2] == U16 for k in reads)}
         for k in reads:
             log.setdefault(k[0], []).append((k, False, q, h))
         for k in writes:
@@ -195,7 +226,7 @@ def rank_program(g, core, T, topo):
                 eng[q].dma_start(o[0], i[0]).then_inc(T.sem[sem], 16)
             total[sem] = 16 * len(pairs)
             record(q, reads, writes, sem, True)
-        note(q, run, reads, writes, 60.0 * len(pairs), late)
+        note(q, run, reads, writes, 120.0 * len(pairs), late)
 
     def ap(x):
         return x[0] if isinstance(x, tuple) else x
@@ -211,7 +242,7 @@ def rank_program(g, core, T, topo):
         c = 0.5 if all(SCRATCH[x[1][0]][2] in (BF, U16) for x in sides) else 1.0
         if both and not any(is_bank(x[1]) for x in ins):
             c *= 2
-        return CYC * max(64, c * count(out))
+        return CALL + CYC * max(64, c * count(out)) + (CFG["PS"] if any(is_bank(x[1]) for x in ins) else 0.0)
 
     def memset(out, c):
         op("v", lambda: g.vector.memset(out[0], c), [], [out], span(out))
@@ -253,7 +284,7 @@ def rank_program(g, core, T, topo):
             kw["accum_out"] = accum[0]
         busy = CYC * max(64, count(out)) if off is None else 65 + GAT * CYC * count(out)
         op("a", lambda: g.scalar.activation(out[0], src, func, **kw), [in_, bias, scale, off],
-           [out] + ([accum] if accum is not None else []), busy + (45 if accum is not None else 25))
+           [out] + ([accum] if accum is not None else []), busy + ACALL + (min(CALL, 20.0) if accum is not None else 0))
 
     def lin(out, in_, scale, bias):
         act(out, in_, ACT.Identity, bias, scale)
@@ -273,7 +304,7 @@ def rank_program(g, core, T, topo):
         a, b = A("q" + st, s0, s0 + 128), A("s" + st, s0, s0 + 128)
         c, d = A("q" + mv, m0, m0 + n), A("s" + mv, m0, m0 + n)
         op("t", lambda: g.tensor.matmul_mx(out[0], a[0], b[0], c[0], d[0], start, stop), [a, b, c, d], [out],
-           CYC * (n + 16))
+           PE * (n + 16))
 
     def iota(out, pattern, base, cm=0, real=True):
         kw = {"allow_small_or_imprecise_dtypes": True} if real else {}
@@ -293,16 +324,22 @@ def rank_program(g, core, T, topo):
             ts(A(dst, d0 + on_scalar, d0 + n), A(src, s0 + on_scalar, s0 + n), c, None, ALU.mult)
 
     def blk(b):
-        return 32 + K * b
+        return 32 + K * b + (32 if b >= 2 else 0)
 
     def hbm(x):
         return (x, None)
 
-    dmas("s", "ldu", [(A("UU"), hbm(T.u[:]))])
-    dmas("a", "ldx0", [(A("X0", 0, 4 * C), hbm(T.x[:, 0:4 * C]))], 3000.0)
-    dmas("s", "ldx1", [(A("X0", 4 * C, 2048), hbm(T.x[:, 4 * C:2048]))], 3500.0)
-    dmas("s", "ldw", [(bytes_of(A("qW")), hbm(T.wc[:])), (A("sW"), hbm(T.ws[:]))], 4500.0)
-    dmas("s", "ldv", [(A("VV"), hbm(T.v[:]))], 5000.0)
+    cut = 4 * CFG["HALF"] if CFG["X2"] else 4 * C
+    loads = (("ldu", 2800.0, [(A("UU"), hbm(T.u[:]))]),
+             ("ldx0", 3900.0, [(A("X0", 0, cut), hbm(T.x[:, 0:cut]))]),
+             ("ldx2", 5000.0, [(A("X0", cut, 4 * C), hbm(T.x[:, cut:4 * C]))] if cut < 4 * C else []),
+             ("ldx1", 5600.0, [(A("X0", 4 * C, 2048), hbm(T.x[:, 4 * C:2048]))]),
+             ("ldw", 7500.0, [(bytes_of(A("qW")), hbm(T.wc[:])), (A("sW"), hbm(T.ws[:]))]),
+             ("ldv", 8500.0, [(A("VV"), hbm(T.v[:]))]))
+    for q, (sem, late, pairs) in zip(CFG["LQ"], loads):
+        if pairs:
+            dmas(q, sem, pairs, late)
+            calls[-1]["first"] = 1e6 - late
 
     iota(col("PI", 0), [[0, 1]], 0, 1, False)
     iota(A("UBI"), [[16, 8]], 0, 0, False)
@@ -310,7 +347,6 @@ def rank_program(g, core, T, topo):
     iota(A("KLI"), [[16, M]], 15, 0, False)
     iota(A("CG"), [[1, 8], [0, 64]], 0)
     iota(A("R16"), [[1, 2]], 0)
-    iota(A("S6"), [[16, 6]], C)
     iota(A("BLI", 0, 3), [[128, 3]], 0)
     iota(A("PKI", 0, 7), [[2, 7]], 127)
     iota(A("PKI", 7, 15), [[2, 8]], 128)
@@ -318,14 +354,21 @@ def rank_program(g, core, T, topo):
     iota(A("WC"), [[1, K]], C + 16 * 256 * signs)
     iota(A("VS"), [[1, C]], 0)
     iota(A("CR4"), [[0, C // 4], [1, 4]], 0)
+    memset(A("ZT"), 0.0)
+
+    def zero(name, c0, c1, on):
+        for c in range(c0, c1, 512):
+            if on == "a":
+                act(A(name, c, min(c1, c + 512)), A("ZT", 0, min(c1, c + 512) - c))
+            else:
+                memset(A(name, c, min(c1, c + 512)), 0.0)
     for (lanes, at, w, pad) in TILES:
         lo = min([16 * m for m in lanes if m not in ("A", "B")]) if len(lanes) == 4 else 0
-        memset(A("TR", 4 * (at + lo), 4 * (at + pad)), 0.0)
-    memset(A("TC", 0, 4 * blk(2)), 0.0)
-    memset(A("TC", 4 * blk(NB - 1), 4 * blk(NB)), 0.0)
-    memset(A("ZW", 0, 128), 0.0)
-    memset(A("BT"), 0.0)
-    memset(A("ZT"), 0.0)
+        zero("TR", 4 * (at + lo), 4 * (at + max(pad, 128 * (len(lanes) < 4))), CFG["ZM"])
+    zero("TC", 0, 4 * blk(2), "v")
+    zero("TC", 4 * blk(NB - 1), 4 * blk(NB), CFG["ZM"])
+    zero("ZW", 0, 128, CFG["ZM"])
+    zero("BT", 0, 512, "v")
     memset(A("ONE"), 1.0)
     copy(A("UBL"), A("UBI"))
     copy(A("KL"), A("KLI"))
@@ -357,7 +400,6 @@ def rank_program(g, core, T, topo):
     lin(g_off, c_q, -STEP, 15 * STEP)
     lin(g_o4, c_q4, 4096.0, -12288.0)
     lin(g_b0, c_q4, 32.0, c_t)
-    lin(g_thr, g_off, None, C + 1.0 + BIG)
     lin(g_sub, g_off, None, 1.0 + BIG)
     lin(g_row, g_off, -1.0, 16.0 * (M - 1 + TOP))
     lin(g_wt, g_off, -1.0, 16.0 * (K // 16 - 1))
@@ -369,7 +411,6 @@ def rank_program(g, core, T, topo):
     lin(A("CS4"), A("CT4"), None, -31744.0)
     ts(A("PG", 6, 8), A("R16"), c_8, None, ALU.is_equal)
     ts(A("PKJ", 0, 15), A("PKI", 0, 15), c_h, 139.0, ALU.add, ALU.min)
-    ts(A("SR"), A("S6"), c_q, g_sub, ALU.add, ALU.add)
     ts(A("BL", 0, 3), A("BLI", 0, 3), g_b1, None, ALU.add)
     ts(A("PKL", 0, 7), A("PKJ", 0, 7), g_i0, None, ALU.mult)
     ts(A("PKL", 7, 15), A("PKJ", 7, 15), g_i1, None, ALU.mult)
@@ -377,7 +418,8 @@ def rank_program(g, core, T, topo):
     quant("U", 0, 128, "UU")
     pick("UB", 0, 128, "U", A("UBL"))
     quant("V", 0, 128, "VV")
-    quant("X", 0, C, "X0")
+    quant("X", 0, CFG["HALF"], "X0")
+    quant("X", CFG["HALF"], C, "X0")
 
     def send(t):
         gather(A("BT", 0, 48), A("MR"), A("BL", 0, 3))
@@ -435,10 +477,18 @@ def rank_program(g, core, T, topo):
     for t in range(NR):
         xx, xn = "X%d" % (t % 2), "X%d" % ((t + 1) % 2)
 
+        half = CFG["HALF"] if CFG["EARLY"] else 0
+        if half:
+            boost[0] = CFG["B0"]
+            mm(4, "UB", 0, "X", 0, half)
+            mm(6, "UB", 0, "X", 0, half)
+            own_keys("KS", "P4", 0, half)
+            boost[0] = 0.0
         mm(1, "UB", 0, "X", 0, C)
         mm(0, "UB", 0, "X", 0, C)
-        own_keys("KS", "P1", CFG["KSPLIT"], C)
-        own_keys("KS", "P1", 0, CFG["KSPLIT"])
+        own_keys("KS", "P1", max(half, CFG["KSPLIT"]), C)
+        if CFG["KSPLIT"] > half:
+            own_keys("KS", "P1", half, CFG["KSPLIT"])
         act(A("KB"), A("KS"), off=A("KL"))
         if CFG["DG"] == "v":
             tt(lane("TR", 0, 0, 0, C), A("P1", 0, C), A("KB"), ALU.is_ge)
@@ -454,8 +504,9 @@ def rank_program(g, core, T, topo):
             elif m <= LOW:
                 step("v", "TR", at, ln, "P1", 0, "KS", m, m, 16.0 * (LOW - m))
             else:
-                step("a", "TR", at, ln, "P0", 0, "KS", m, m, 0.0)
+                step("a", "TR", at, ln, "P6" if half // 16 - CFG["EARLY"] <= m < half // 16 else "P0", 0, "KS", m, m, 0.0)
 
+        boost[0] = CFG["BWT"]
         if t > 0:
             unpack(t - 1, xx, act if CFG["CP"] == "a" else copy)
         quant("X", 384, 512, xx)
@@ -467,7 +518,7 @@ def rank_program(g, core, T, topo):
         tt(lane("TC", blk(0), 1, 0, K), A("P2", 32, 128), A("KBW"), ALU.is_gt)
         for m in range(5, 0, -1):
             step(CFG["WW"], "TC", blk(0 if m > 3 else 1), (7 - m) % 4, "KW", 0, "KSW", m, M + m, 16.0 * (5 - m))
-        quant("TC", 0, blk(2))
+        quant("TC", 0 if t == 0 else 32, blk(2) - 32)
         mm(6, "SX", 0, "TC", blk(0) - 32, 128, True, False)
         mm(6, "SR1", 0, "TC", blk(1) - 32, 128, False, True)
         for b, on in enumerate(CFG["CROSS"]):
@@ -475,7 +526,7 @@ def rank_program(g, core, T, topo):
             for m in ms:
                 out = lane("TC", blk(2 + b), m % 4, 0, K)
                 if on == "v":
-                    ts(out, A("KW"), col("KS", 16 * m + 15), 2.0, ALU.is_ge, ALU.mult)
+                    ts(out, A("P2", 32, 128) if CFG.get("XP") else A("KW"), col("KS", 16 * m + 15), 2.0, ALU.is_ge, ALU.mult)
                 else:
                     lin(out, A("KW"), -1.0, col("KS", 16 * m + 15))
             outs = [A("TC", 4 * blk(2 + b), 4 * blk(3 + b))] if len(ms) == 4 else [
@@ -485,35 +536,44 @@ def rank_program(g, core, T, topo):
                     act(out, out, ACT.Sign, bias=ETA, scale=-1.0)
                 elif on == "m":
                     ts(out, out, 0.0, 2.0, ALU.is_le, ALU.mult)
-        for b0, b1 in ((0, 2), (2, 4), (4, 7)):
-            quant("TC", blk(2 + b0), blk(2 + b1))
+        for b0, b1 in CFG["QC"]:
+            quant("TC", blk(2 + b0) - (32 if t == 0 and b0 == 0 else 0), blk(2 + b1))
             for b in range(b0, b1):
                 mm(5, "SK", 0, "TC", blk(2 + b) - 32, 128, b == 0, b == 6)
 
-        for i, (lanes, at, w, pad) in enumerate(TILES):
-            quant("TR", at, at + (pad if t == 0 else max(w, 128)))
-            for (name, a, b, bank) in RANGES:
-                if a < w:
-                    last = i + 1 == len(TILES) or TILES[i + 1][2] <= a
-                    mm(bank, "SX" if i == 0 else "SR1", 0, "TR", at + a, max(128, min(b, w) - a), i == 0, last)
+        boost[0] = 0.0
+        for run in CFG["QT"]:
+            (_, at, w, pad) = TILES[run[-1]]
+            end = max(at + (pad if t == 0 else w), TILES[run[0]][1] + 128)
+            if run[-1] == len(TILES) - 1 and t == 0:
+                end = at + 128
+            quant("TR", TILES[run[0]][1], end)
+            for i in run:
+                (lanes, at, w, pad) = TILES[i]
+                for (name, a, b, bank) in RANGES:
+                    if a < w:
+                        last = i + 1 == len(TILES) or TILES[i + 1][2] <= a
+                        mm(bank, "SX" if i == 0 else "SR1", 0, "TR", at + a, max(128, min(b, w) - a), i == 0, last)
         for (name, a, b, bank) in RANGES:
             place(name, bank, a, b - a, a // 16, g_row, A("W1", 0, C), A("VS", a, b))
 
+        boost[0] = CFG["BWT"]
         tt(A("VW"), A("P5", 32, 128), A("WC"), ALU.add)
-        place("W", 6, C, K, M, g_wt, A("W1", C, 512), A("VW"), 32)
-        ts(A("KC"), A("W1", C, 512), 2.0 ** -9, BIG, ALU.mult, ALU.add)
+        place("W", 6, C, K, M, g_wt, A("WV"), A("VW"), 32)
+        if CFG["KC"] == "a":
+            lin(A("KC"), A("WV"), 2.0 ** -9, BIG)
+        else:
+            ts(A("KC"), A("WV"), 2.0 ** -9, BIG, ALU.mult, ALU.add)
         lin(A("NK"), A("KC"), -512.0, 512.0 * (BIG + 1.0))
         scan(A("PP"), A("ONE", 0, K), A("KC"), BIG)
         scan(A("PS"), A("CS", 0, K), A("PP"), 0.0)
-        raw = A("PS", 15, K, 16)
-        ts(A("F6", 0, 6), raw, g_thr, 2.0 ** 25, ALU.is_ge, ALU.mult)
-        tt(A("G6", 0, 6), A("F6", 0, 6), A("SR"), ALU.min)
-        tt(A("H6", 0, 6), A("G6", 0, 6), raw, ALU.max)
-        ts(A("PW"), A("H6", 0, 6), g_sub, None, ALU.subtract)
-        tt(A("BV"), A("W1", C, 512), A("NK"), ALU.add)
-        act(A("W1", C, 512), A("BV"))
-        gather(A("E2"), A("W1"), A("PW"))
-        scatter(A("W1"), A("PW"), A("BV"))
+        ts(A("PW"), A("PS", 15, K, 16), g_sub, None, ALU.subtract)
+        tt(A("BV"), A("WV"), A("NK"), ALU.add)
+        act(A("W1", C, 512), A("ONE", 0, K), scale=1024.0)
+        win, off, own_id, out = A("W1"), A("PW"), A("BV"), A("E2")
+        op("v", lambda win=win, off=off, own_id=own_id, out=out: g.vector.tensor_tensor(
+            out[0], win[0].indirect(off[0]), own_id[0], ALU.min), [win, off, own_id], [out], 50 + GAT * CYC * K)
+        scatter(win, off, own_id)
         if t == NR - 1:
             dmas("s", "ole", [(hbm(T.le[:, 0:C]), (T.W1[0:128:16, 0:C], A("W1", 0, C)[1])),
                               (hbm(T.le[:, C:512]), (T.E2[0:128:16, 0:K], A("E2")[1]))])
@@ -525,6 +585,7 @@ def rank_program(g, core, T, topo):
             if mid < c1:
                 gather(A(dst, at + 4 * mid, at + 4 * c1), A(xx), A(lst, mid // 4, c1 // 4))
 
+        boost[0] = CFG["BW"][t == NR - 1]
         scan(A("SC", C, 512), A("CS4", 0, K), A("E2"), 0.0)
         ts(A("LW"), A("SC", C + 3, 512, 4), 4.0, g_lt, ALU.mult, ALU.add)
         take("ZW", "LW", 0, K, CFG["GW"], 128)
@@ -532,26 +593,38 @@ def rank_program(g, core, T, topo):
         wb = (0, 1, 2, 7)
         for b in range(4):
             mm(wb[b], "W", 128 * b, "ZW", 0, 128)
-        scaled("W64", 0, "ZW", 128, 4 * K, 0, 64.0)
+        scaled("W64", 0, "ZW", 128, 4 * K, 4 * K * CFG["WA"][0], 64.0)
         for b in range(4):
             tt(A("U64", b, 4 * K, 4), A("P%d" % wb[b], 32, 128), A("W64", b, 4 * K, 4), ALU.add)
-        scaled("MW", 0, "U64", 0, 4 * K, 0, 0.015625)
+        scaled("MW", 0, "U64", 0, 4 * K, 4 * K * CFG["WA"][1], 0.015625)
         dmas("s", "rep%d" % t, [(A("MR", 0, 384, 1, 16 * k, 16 * k + 16), A("MW", 0, 384, 1, 112, 128)) for k in range(8)])
         dmas("s", "shf%d" % t, [(A(xn, 4 * C, 2048, 1, 16, 128), A("MW", 0, 384, 1, 0, 112))])
         send(t)
-        H = C // 2
-        for i, banks in enumerate(((3, 4, 5, 6), wb)):
-            c0, c1 = i * H, i * H + H
-            scan(A("SC", c0, c1), A("CS4", 0, H), A("W1", c0, c1), 0.0)
-            ts(A("LL", c0 // 4, c1 // 4), A("SC", c0 + 3, c1, 4), 4.0, g_lt, ALU.mult, ALU.add)
-            take("ZZ", "LL", c0, c1, CFG["GA"][i])
+        for i, (c0, c1, banks) in enumerate(((0, CFG["HALF"], (3, 4, 5, 6)), (CFG["HALF"], C, wb))):
+            H = c1 - c0
+            boost[0] = CFG["B0"] if i == 0 and t < NR - 1 else 0.0
+
+            def share(key):
+                return min(H, int(CFG[key][i] * H) // 8 * 8)
+            if i == 0 or CFG["L2"]:
+                l1 = c1 if CFG["L2"] else C
+                scan(A("SC", c0, l1), A("CS4", 0, l1 - c0), A("W1", c0, l1), 0.0)
+                ts(A("LL", c0 // 4, l1 // 4), A("SC", c0 + 3, l1, 4), 4.0, g_lt, ALU.mult, ALU.add)
+            take("ZZ", "LL", c0, c1, share("GA"))
             quant("ZZ", c0, c1)
             for b in range(4):
                 mm(banks[b], "W", 128 * b, "ZZ", c0, H)
-            scaled("Z64", 4 * c0, "ZZ", 4 * c0, 4 * H, 4 * CFG["ZA"][i], 64.0)
+            scaled("Z64", 4 * c0, "ZZ", 4 * c0, 4 * H, 4 * share("ZA"), 64.0)
             for b in range(4):
                 tt(A("T64", 4 * c0 + b, 4 * c1, 4), A("P%d" % banks[b], 0, H), A("Z64", 4 * c0 + b, 4 * c1, 4), ALU.add)
-            scaled(xn, 4 * c0, "T64", 4 * c0, 4 * H, 4 * CFG["XA"][i], 0.015625)
+            if CFG["XL"]:
+                for b in range(4):
+                    if b < 4 * CFG["XA"][i]:
+                        act(A(xn, 4 * c0 + b, 4 * c1, 4), A("T64", 4 * c0 + b, 4 * c1, 4), scale=0.015625)
+                    else:
+                        ts(A(xn, 4 * c0 + b, 4 * c1, 4), A("T64", 4 * c0 + b, 4 * c1, 4), 0.015625, None, ALU.mult)
+            else:
+                scaled(xn, 4 * c0, "T64", 4 * c0, 4 * H, 4 * share("XA"), 0.015625)
             quant("X", c0, c1, xn)
 
     xx = "X%d" % (NR % 2)

@@ -14,7 +14,12 @@ CFG = {"TOP": 3, "LOW": 0, "CROSS": "vvvvvvv", "WW": "v", "GW": 96, "GA": (0.62,
 CFG.update({"CUTS": (240, 112), "WW": "a", "ZA": (0.62, 0.62), "KC": "a", "CROSS": "avvvvvv", "TOP": 4, "CP": "a",
             "ZM": "a", 'QC': ((0, 4), (4, 7)), 'WA': (0, 0), 'XL': 1, 'XA': (0.62, 0.75), 'KSPLIT': 288,
             "BWT": 1000.0, "EARLY": 3, "B0": 0.0})
-CFG.update({'LQ': 'ssssss', 'EARLY': 0, 'ZA': (0.5, 0.5)})
+CFG.update({'LQ': 'ssssss', 'EARLY': 0, 'ZA': (0, 0.5, 0.5), "GA": (1, 0.62, 1), "XA": (0.5, 0.62, 0.75), "WA": 0,
+            "CH": ((0, 208, 416), (0, 208, 416)), "RA": (0, 0), "CP": "aa"})
+CFG.update({'CH': ((0, 160, 416), (0, 160, 416)), 'KSPLIT': 160, 'CROSS': 'vvvvvva', 'RA': (0, 2), 'BWT': 0, "XL": 0,
+            "BK": 3000.0})
+CFG.update({'CH': ((0, 208, 416), (0, 160, 416)), 'HALF': 208, 'EARLY': 5, 'B0': 800, 'CROSS': 'vvvvvaa', 'X2': 0,
+            'KSPLIT': 0, 'LOOK': 40, 'QT': ((0,), (1,), (2,), (3, 4), (5, 6)), 'LOW': 2})
 
 LANES = [["A", "B", M - 1, M - 2]] + [[m for m in range(top, top - 4, -1) if m > 0] for top in range(M - 3, 0, -4)]
 
@@ -36,16 +41,16 @@ TCW = NB * K + 64
 
 SCRATCH = {}
 for _d, _l in (
-        (BF, "UU:512 VV:512 X0:2048 X1:2048 ZZ:1664 ZW:512 Z64:1664 W64:384 T64:1664 U64:384 MW:384 MR:384 BT:512 "
+        (BF, "UU:512 VV:512 X0:2048 X1:2048 ZZ:2176 Z64:2176 T64:2176 MW:384 MR:384 BT:512 "
              "ZT:512 ONE:512 CR:416 CR4:416 CG:512 MK:416 RS:416 C2:128 CT:416 CT4:416 CS:416 CS4:416 SR1:512 SX:512 "
              "SK:512 EE:4096 TR:%d TC:%d" % (4 * TRW, 4 * TCW)),
         (F32, "KM:512 KS:416 KW:96 KSW:96 KB:416 KBW:96 AC:%d HS:512 TOT:32 VS:416 VW:96 W1:512 BV:96 E2:96 KC:96 NK:96 "
-              "PP:96 PS:96 SC:512 WV:96 YY:512" % (32 * S)),
-        (I32, "PI:16 UBI:8 KLI:26"), (U16, "UBL:8 KL:26 PKL:16 BL:4 OFH:26 OFM:26 OFL:26 OFW:6 PW:6 LL:104 LW:24")):
+              "PP:96 PS:96 SC:544 WV:96 YY:512" % (32 * S)),
+        (I32, "PI:16 UBI:8 KLI:26"), (U16, "UBL:8 KL:26 PKL:16 BL:4 OFH:26 OFM:26 OFL:26 OFW:6 PW:6 LL:136")):
     for _e in _l.split():
         SCRATCH[_e.split(":")[0]] = ("sbuf", [128, int(_e.split(":")[1])], _d)
-for _e in ("U:128 V:128 UB:128 W:512 X:512 ZZ:416 ZW:128 SR1:128 SX:128 SK:128 E:1024 TR:%d TC:%d B0:128 B1:128 B2:128 "
-           "LD0:144 LD1:144 LD2:144 PK0:240 PK1:240 PK2:240" % (TRW, TCW)).split():
+for _e in ("U:128 V:128 UB:128 W:512 X:512 ZZ:544 SR1:128 SX:128 SK:128 E:1024 TR:%d TC:%d B0:128 B1:128 B2:128 "
+           "LD0:144 LD1:144 LD2:144 PK0:144 PK1:144 PK2:144" % (TRW, TCW)).split():
     SCRATCH["q" + _e.split(":")[0]] = ("sbuf", [128, int(_e.split(":")[1])], X4)
     SCRATCH["s" + _e.split(":")[0]] = ("sbuf", [128, int(_e.split(":")[1])], U8)
 for _k in range(8):
@@ -59,13 +64,14 @@ for _n, _w in (("R16", 2), ("PKI", 16), ("PKJ", 16), ("BLI", 4), ("S6", 6), ("SR
 SCRATCH["KF"] = ("sbuf", [128, _at], F32)
 
 SEMAPHORES = ("sv sa st sg ldu ldx0 ldx1 ldx2 ldw ldv loc ole oa ob oc oy0 oy1 zl "
-              "rep0 rep1 rep2 shf0 shf1 shf2 arr0 arr1 arr2").split()
+              "rep0 rep1 rep2 rpa0 rpa1 rpa2 shf0 shf1 shf2 arr0 arr1 arr2").split()
 
 BIG = 1.5 * 2.0 ** 23
 ETA = 2.0 ** -110
 STEP = 2048.0
-CFG["T"] = (0.83, 0.0, 10.0, 90.0, 1600.0, 2500.0, 1.56, 3.8, 0.83)
-CFG["PS"] = 83.0
+CFG["T"] = (0.83, 5.0, 20.0, 90.0, 1500.0, 2400.0, 1.56, 3.8, 0.83)
+CFG["PS"] = 70.0
+CFG["WX"], CFG["WP"] = 110.0, 50.0
 
 
 def rank_program(g, core, T, topo):
@@ -119,7 +125,8 @@ def rank_program(g, core, T, topo):
                 for (k2, wr2, d) in touched.get(k[0], []):
                     if (wr or wr2) and d is not c and meets(k, k2):
                         free = d["q"] == q and not d["late"] and (not wr2 and not d["list"] or q == "t")
-                        c["after"][d["i"]] = max(c["after"].get(d["i"], 0.0), 0.0 if free else WAKE + d["late"])
+                        c["after"][d["i"]] = max(c["after"].get(d["i"], 0.0), 0.0 if free else d["late"] + (
+                            WAKE if d["q"] == q else CFG["WX"] + (CFG["WP"] if d["q"] == "t" else 0.0)))
         for keys, wr in ((reads, False), (writes, True)):
             for k in keys:
                 touched.setdefault(k[0], []).append((k, wr, c))
@@ -156,8 +163,21 @@ def rank_program(g, core, T, topo):
             order, ends = plan(way, ahead, [len(b) for b in behind], [0.0] * len(calls))
             length = max(ends[c["i"]] + c["late"] for c in calls)
             if best is None or length < best[0]:
-                best = (length, order)
+                best = (length, order, way)
             way = plan(ends, behind, [len(a) for a in ahead], [c["late"] for c in calls])[1]
+        seed = 12345
+        base = best[2]
+        for k in range(CFG.get("TRY", 0)):
+            way = []
+            for w in base:
+                seed = (seed * 1103515245 + 12345) % 2147483648
+                way.append(w + CFG["AMP"] * (seed / 2147483648.0 - 0.5) if seed % 7 == 0 else w)
+            order, ends = plan(way, ahead, [len(b) for b in behind], [0.0] * len(calls))
+            length = max(ends[c["i"]] + c["late"] for c in calls)
+            if length < best[0]:
+                best = (length, order, way)
+                base = way
+        CFG["LEN"] = best[0]
         for i in best[1]:
             calls[i]["run"]()
 
@@ -226,7 +246,7 @@ def rank_program(g, core, T, topo):
                 eng[q].dma_start(o[0], i[0]).then_inc(T.sem[sem], 16)
             total[sem] = 16 * len(pairs)
             record(q, reads, writes, sem, True)
-        note(q, run, reads, writes, 120.0 * len(pairs), late)
+        note(q, run, reads, writes, CFG.get("DI", 120.0) * len(pairs), late)
 
     def ap(x):
         return x[0] if isinstance(x, tuple) else x
@@ -346,10 +366,8 @@ def rank_program(g, core, T, topo):
     iota(A("CR"), [[0, M], [1, 16]], 0)
     iota(A("KLI"), [[16, M]], 15, 0, False)
     iota(A("CG"), [[1, 8], [0, 64]], 0)
-    iota(A("R16"), [[1, 2]], 0)
     iota(A("BLI", 0, 3), [[128, 3]], 0)
-    iota(A("PKI", 0, 7), [[2, 7]], 127)
-    iota(A("PKI", 7, 15), [[2, 8]], 128)
+    iota(A("PKI", 0, 9), [[2, 9]], 127)
     signs = sum(min(4, M - 4 * b) for b, on in enumerate(CFG["CROSS"]) if on == "a")
     iota(A("WC"), [[1, K]], C + 16 * 256 * signs)
     iota(A("VS"), [[1, C]], 0)
@@ -367,7 +385,7 @@ def rank_program(g, core, T, topo):
         zero("TR", 4 * (at + lo), 4 * (at + max(pad, 128 * (len(lanes) < 4))), CFG["ZM"])
     zero("TC", 0, 4 * blk(2), "v")
     zero("TC", 4 * blk(NB - 1), 4 * blk(NB), CFG["ZM"])
-    zero("ZW", 0, 128, CFG["ZM"])
+    zero("ZZ", 0, 128, CFG["ZM"])
     zero("BT", 0, 512, "v")
     memset(A("ONE"), 1.0)
     copy(A("UBL"), A("UBI"))
@@ -409,11 +427,10 @@ def rank_program(g, core, T, topo):
     ts(A("CT4"), A("CR4"), c_q4, 32768.0, ALU.is_gt, ALU.mult)
     lin(A("CS"), A("CT"), None, -31 * STEP)
     lin(A("CS4"), A("CT4"), None, -31744.0)
-    ts(A("PG", 6, 8), A("R16"), c_8, None, ALU.is_equal)
-    ts(A("PKJ", 0, 15), A("PKI", 0, 15), c_h, 139.0, ALU.add, ALU.min)
+    ts(g_i0, c_8, 0.0, None, ALU.is_equal)
+    ts(A("PKJ", 0, 9), A("PKI", 0, 9), c_h, 139.0, ALU.add, ALU.min)
     ts(A("BL", 0, 3), A("BLI", 0, 3), g_b1, None, ALU.add)
-    ts(A("PKL", 0, 7), A("PKJ", 0, 7), g_i0, None, ALU.mult)
-    ts(A("PKL", 7, 15), A("PKJ", 7, 15), g_i1, None, ALU.mult)
+    ts(A("PKL", 0, 9), A("PKJ", 0, 9), g_i0, None, ALU.mult)
 
     quant("U", 0, 128, "UU")
     pick("UB", 0, 128, "U", A("UBL"))
@@ -442,11 +459,13 @@ def rank_program(g, core, T, topo):
         note("g", run, [qb[1], sb[1]], [ql[1], sl[1]], 200.0, REMOTE * (1.5 if t == 0 else 1.0))
 
     def unpack(t, xx, f):
-        pick("PK%d" % t, 0, 240, "LD%d" % t, A("PKL", 0, 15), CFG["SP"])
-        for k in range(8):
-            mm(5, "E", 128 * k, "PK%d" % t, (8 - k) if k % 2 == 0 else (113 - k), 128, k == 0, k == 7)
-        for b in range(4):
-            f(A(xx, 4 * C + b, 2048, 4, 0, 16), A("P5", 0, K, 1, 32 * b, 32 * b + 16))
+        pick("PK%d" % t, 0, 144, "LD%d" % t, A("PKL", 0, 9), CFG["SP"])
+        for odd, bank in enumerate((5, 2)):
+            for k in range(0, 8, 2):
+                mm(bank, "E", 128 * (k + odd), "PK%d" % t, 8 - k, 128, k == 0, k == 6)
+            for b in range(4):
+                (act if f[odd] == "a" else copy)(A(xx, 4 * (C + odd) + b, 2048, 8, 0, 16),
+                                                 A("P%d" % bank, 0, K, 2, 32 * b, 32 * b + 16))
 
     where = {m: (at, ln) for (lanes, at, w, pad) in TILES for ln, m in enumerate(lanes)}
 
@@ -506,12 +525,13 @@ def rank_program(g, core, T, topo):
             else:
                 step("a", "TR", at, ln, "P6" if half // 16 - CFG["EARLY"] <= m < half // 16 else "P0", 0, "KS", m, m, 0.0)
 
-        boost[0] = CFG["BWT"]
+        boost[0] = CFG["BK"]
         if t > 0:
-            unpack(t - 1, xx, act if CFG["CP"] == "a" else copy)
+            unpack(t - 1, xx, CFG["CP"])
         quant("X", 384, 512, xx)
         mm(2, "UB", 0, "X", 384, 128)
         act(A("KW"), A("P2", 32, 128))
+        boost[0] = CFG["BWT"]
         own_keys("KSW", "P2", 0, K, 32, C)
         act(A("KBW"), A("KSW"), off=A("KL", 0, 6))
         tt(lane("TC", blk(0), 0, 0, K), A("P2", 32, 128), A("KBW"), ALU.is_ge)
@@ -578,54 +598,57 @@ def rank_program(g, core, T, topo):
             dmas("s", "ole", [(hbm(T.le[:, 0:C]), (T.W1[0:128:16, 0:C], A("W1", 0, C)[1])),
                               (hbm(T.le[:, C:512]), (T.E2[0:128:16, 0:K], A("E2")[1]))])
 
-        def take(dst, lst, c0, c1, on_scalar, at=0):
-            mid = c0 + on_scalar
+        cuts = CFG["CH"][t == NR - 1]
+        done = 0
+        for i in range(len(cuts)):
+            r0, r1 = (cuts[i - 1] if i else 0), cuts[i]
+            c0, c1 = (128 + r0 if i else 32), 128 + r1
+            m0 = min(c0, c1 - 128)
+            banks = ((0, 1, 2, 7), (3, 4, 5, 6))[i % 2]
+            boost[0] = (CFG["BW"][t == NR - 1], CFG["B0"] if t < NR - 1 else 0.0, 0.0, 0.0)[i]
+
+            def share(key, n):
+                return min(n, int(CFG[key][i] * n) // 8 * 8)
+            if i == 0:
+                scan(A("SC", 32, 128), A("CS4", 0, K), A("E2"), 0.0)
+            if r1 > r0:
+                scan(A("SC", 128 + r0, c1), A("CS4", 0, r1 - r0), A("W1", r0, r1), 0.0)
+            ts(A("LL", c0 // 4, c1 // 4), A("SC", c0 + 3, c1, 4), 4.0, g_lt, ALU.mult, ALU.add)
+            mid = c0 + share("GA", c1 - c0)
             if mid > c0:
-                act(A(dst, at + 4 * c0, at + 4 * mid), A(xx), off=A(lst, c0 // 4, mid // 4))
+                act(A("ZZ", 4 * c0, 4 * mid), A(xx), off=A("LL", c0 // 4, mid // 4))
             if mid < c1:
-                gather(A(dst, at + 4 * mid, at + 4 * c1), A(xx), A(lst, mid // 4, c1 // 4))
-
-        boost[0] = CFG["BW"][t == NR - 1]
-        scan(A("SC", C, 512), A("CS4", 0, K), A("E2"), 0.0)
-        ts(A("LW"), A("SC", C + 3, 512, 4), 4.0, g_lt, ALU.mult, ALU.add)
-        take("ZW", "LW", 0, K, CFG["GW"], 128)
-        quant("ZW", 0, 128)
-        wb = (0, 1, 2, 7)
-        for b in range(4):
-            mm(wb[b], "W", 128 * b, "ZW", 0, 128)
-        scaled("W64", 0, "ZW", 128, 4 * K, 4 * K * CFG["WA"][0], 64.0)
-        for b in range(4):
-            tt(A("U64", b, 4 * K, 4), A("P%d" % wb[b], 32, 128), A("W64", b, 4 * K, 4), ALU.add)
-        scaled("MW", 0, "U64", 0, 4 * K, 4 * K * CFG["WA"][1], 0.015625)
-        dmas("s", "rep%d" % t, [(A("MR", 0, 384, 1, 16 * k, 16 * k + 16), A("MW", 0, 384, 1, 112, 128)) for k in range(8)])
-        dmas("s", "shf%d" % t, [(A(xn, 4 * C, 2048, 1, 16, 128), A("MW", 0, 384, 1, 0, 112))])
-        send(t)
-        for i, (c0, c1, banks) in enumerate(((0, CFG["HALF"], (3, 4, 5, 6)), (CFG["HALF"], C, wb))):
-            H = c1 - c0
-            boost[0] = CFG["B0"] if i == 0 and t < NR - 1 else 0.0
-
-            def share(key):
-                return min(H, int(CFG[key][i] * H) // 8 * 8)
-            if i == 0 or CFG["L2"]:
-                l1 = c1 if CFG["L2"] else C
-                scan(A("SC", c0, l1), A("CS4", 0, l1 - c0), A("W1", c0, l1), 0.0)
-                ts(A("LL", c0 // 4, l1 // 4), A("SC", c0 + 3, l1, 4), 4.0, g_lt, ALU.mult, ALU.add)
-            take("ZZ", "LL", c0, c1, share("GA"))
-            quant("ZZ", c0, c1)
+                gather(A("ZZ", 4 * mid, 4 * c1), A(xx), A("LL", mid // 4, c1 // 4))
+            quant("ZZ", m0, c1)
             for b in range(4):
-                mm(banks[b], "W", 128 * b, "ZZ", c0, H)
-            scaled("Z64", 4 * c0, "ZZ", 4 * c0, 4 * H, 4 * share("ZA"), 64.0)
+                mm(banks[b], "W", 128 * b, "ZZ", m0, c1 - m0)
+            scaled("Z64", 4 * c0, "ZZ", 4 * c0, 4 * (c1 - c0), 4 * share("ZA", c1 - c0), 64.0)
             for b in range(4):
-                tt(A("T64", 4 * c0 + b, 4 * c1, 4), A("P%d" % banks[b], 0, H), A("Z64", 4 * c0 + b, 4 * c1, 4), ALU.add)
-            if CFG["XL"]:
-                for b in range(4):
-                    if b < 4 * CFG["XA"][i]:
-                        act(A(xn, 4 * c0 + b, 4 * c1, 4), A("T64", 4 * c0 + b, 4 * c1, 4), scale=0.015625)
-                    else:
-                        ts(A(xn, 4 * c0 + b, 4 * c1, 4), A("T64", 4 * c0 + b, 4 * c1, 4), 0.015625, None, ALU.mult)
-            else:
-                scaled(xn, 4 * c0, "T64", 4 * c0, 4 * H, 4 * share("XA"), 0.015625)
-            quant("X", c0, c1, xn)
+                tt(A("T64", 4 * c0 + b, 4 * c1, 4), A("P%d" % banks[b], c0 - m0, c1 - m0), A("Z64", 4 * c0 + b, 4 * c1, 4),
+                   ALU.add)
+            if i == 0:
+                scaled("MW", 0, "T64", 128, 4 * K, 4 * K * CFG["WA"], 0.015625)
+                rep = [(A("MR", 0, 384, 1, 16 * k, 16 * k + 16), A("MW", 0, 384, 1, 112, 128)) for k in range(8)]
+                n_a = CFG["RA"][t == NR - 1]
+                dmas("s", "rep%d" % t, rep[n_a:])
+                if n_a:
+                    dmas("a", "rpa%d" % t, rep[:n_a])
+                dmas("s", "shf%d" % t, [(A(xn, 4 * C, 2048, 1, 16, 128), A("MW", 0, 384, 1, 0, 112))])
+                send(t)
+            if r1 > r0:
+                if CFG["XL"]:
+                    for b in range(4):
+                        o, i_ = A(xn, 4 * r0 + b, 4 * r1, 4), A("T64", 512 + 4 * r0 + b, 512 + 4 * r1, 4)
+                        if b < 4 * CFG["XA"][i]:
+                            act(o, i_, scale=0.015625)
+                        else:
+                            ts(o, i_, 0.015625, None, ALU.mult)
+                else:
+                    scaled(xn, 4 * r0, "T64", 512 + 4 * r0, 4 * (r1 - r0), 4 * share("XA", r1 - r0), 0.015625)
+            if r1 - done >= 128 and (C - r1 >= 128 or r1 == C):
+                quant("X", done, r1, xn)
+                done = r1
+        boost[0] = 0.0
 
     xx = "X%d" % (NR % 2)
     mm(0, "V", 0, "X", 0, 384)
@@ -633,7 +656,7 @@ def rank_program(g, core, T, topo):
         (hbm(T.osc[4 * k:4 * k + 4, 0:384]), A("sX", 0, 384, 1, 32 * k, 32 * k + 4)) for k in range(4)])
     act(A("YY", 0, 384), A("P0", 0, 384))
     dmas("s", "oy0", [(hbm(T.y[:, 0:384]), A("YY", 0, 384))])
-    unpack(NR - 1, xx, copy)
+    unpack(NR - 1, xx, "av")
     quant("X", 384, 512, xx)
     mm(7, "V", 0, "X", 384, 128)
     scales = [(hbm(T.osc[4 * k:4 * k + 4, 384:512]), A("sX", 384, 512, 1, 32 * k, 32 * k + 4)) for k in range(4)]

@@ -2,85 +2,64 @@ from concourse.mybir import dt, AluOpType, ActivationFunctionType
 
 ALU = AluOpType
 ACT = ActivationFunctionType
-BF, F32, I32, U16, U8, X4 = "bfloat16", "float32", "int32", "uint16", "uint8", "float8_e4m3fn_x4"
+BF, F16, F32, I32, U16, U8, X4 = "bfloat16", "float16", "float32", "int32", "uint16", "uint8", "float8_e4m3fn_x4"
 NR = 3
 C, K = 416, 96
 M = C // 16
 S = 200
-CFG = {"TOP": 3, "LOW": 0, "CROSS": "vvvvvvv", "WW": "v", "GW": 96, "GA": (0.62, 1), "XA": (0.5, 1), "ZA": (0.5, 0.5),
-       "CP": "v", "SP": "a", "KSPLIT": 160, "DG": "v", "CUTS": (240, 112), "HALF": 208, "L2": 1, "XL": 0,
-       "QT": ((0,), (1,), (2,), (3,), (4,), (5, 6)), "QC": ((0, 2), (2, 4), (4, 7)), "WA": (1, 0), "KC": "v", "ZM": "v",
-       "LOOK": 70.0, "PASS": 4, "EARLY": 5, "X2": 0, "LQ": "sassss", "SHORT": 0.0, "SB": 120.0, "BWT": 0.0, "B0": 1000.0, "BW": (1000.0, 3000.0)}
-CFG.update({"CUTS": (240, 112), "WW": "a", "ZA": (0.62, 0.62), "KC": "a", "CROSS": "avvvvvv", "TOP": 4, "CP": "a",
-            "ZM": "a", 'QC': ((0, 4), (4, 7)), 'WA': (0, 0), 'XL': 1, 'XA': (0.62, 0.75), 'KSPLIT': 288,
-            "BWT": 1000.0, "EARLY": 3, "B0": 0.0})
-CFG.update({'LQ': 'ssssss', 'EARLY': 0, 'ZA': (0, 0.5, 0.5), "GA": (1, 0.62, 1), "XA": (0.5, 0.62, 0.75), "WA": 0,
-            "CH": ((0, 208, 416), (0, 208, 416)), "RA": (0, 0), "CP": "aa"})
-CFG.update({'CH': ((0, 160, 416), (0, 160, 416)), 'KSPLIT': 160, 'CROSS': 'vvvvvva', 'RA': (0, 2), 'BWT': 0, "XL": 0,
-            "BK": 3000.0})
-CFG.update({'CH': ((0, 208, 416), (0, 160, 416)), 'HALF': 208, 'EARLY': 5, 'B0': 800, 'CROSS': 'vvvvvaa', 'X2': 0,
-            'KSPLIT': 0, 'LOOK': 40, 'QT': ((0,), (1,), (2,), (3, 4), (5, 6)), 'LOW': 2})
-
-LANES = [["A", "B", M - 1, M - 2]] + [[m for m in range(top, top - 4, -1) if m > 0] for top in range(M - 3, 0, -4)]
-
-
-def layout(cuts):
-    ranges = [(n, a, b, k) for n, a, b, k in zip("HML", cuts + (0,), (C,) + cuts, (3, 7, 4))]
-    tiles, at = [], 0
-    for lanes in LANES:
-        w = C if lanes[0] == "A" else 16 * lanes[0]
-        pad = max([w] + [min(a + 128, b) for (n, a, b, k) in ranges if a < w])
-        tiles.append((lanes, at, w, pad))
-        at += pad
-    return ranges, tiles
-
-
-TRW = 2176
+HALF = 208
+TOP = (4, 5, 5)
+FROM_Z = 2
+EARLY = 3
+CROSS = "vvvvvaa"
+PIECES = ((0, 208, 416), (0, 208, 416), (0, 160, 416))
+GATHER = ((1, 0.62, 0.875), (1, 0.62, 0.875), (0.5, 1, 0.75))
+TIMES64, LANES_A = (0, 0.62, 0.75), (2, 3, 3)
+RANGES = (("H", 224, 416, 3), ("M", 96, 224, 7), ("L", 0, 96, 4))
+TILES = []
+TRW = 0
+for _l in [["A", M - 1, M - 2, M - 3]] + [[m for m in range(top, top - 4, -1) if m > 0] for top in range(M - 4, 0, -4)]:
+    _w = C if _l[0] == "A" else 16 * _l[0]
+    _p = max([_w] + [min(a + 128, b) for (_n, a, b, _k) in RANGES if a < _w])
+    TILES.append((_l, TRW, _w, _p))
+    TRW += _p
+TRW += 128
 NB = 9
 TCW = NB * K + 64
 
 SCRATCH = {}
 for _d, _l in (
-        (BF, "UU:512 VV:512 X0:2048 X1:2048 ZZ:2176 Z64:2176 T64:2176 MW:384 MR:384 BT:512 "
-             "ZT:512 ONE:512 CR:416 CR4:416 CG:512 MK:416 RS:416 C2:128 CT:416 CT4:416 CS:416 CS4:416 SR1:512 SX:512 "
-             "SK:512 EE:4096 TR:%d TC:%d" % (4 * TRW, 4 * TCW)),
-        (F32, "KM:512 KS:416 KW:96 KSW:96 KB:416 KBW:96 AC:%d HS:512 TOT:32 VS:416 VW:96 W1:512 BV:96 E2:96 KC:96 NK:96 "
-              "PP:96 PS:96 SC:544 WV:96 YY:512" % (32 * S)),
-        (I32, "PI:16 UBI:8 KLI:26"), (U16, "UBL:8 KL:26 PKL:16 BL:4 OFH:26 OFM:26 OFL:26 OFW:6 PW:6 LL:136")):
+        (BF, "UU:512 VV:512 X0:2048 X1:2048 ZZ:2176 Z64:2176 T64:2176 R64:384 U64:384 MW:384 MR:384 BT:512 ZT:512 "
+             "ONE:512 CR:416 CR4:416 CG:512 MK:416 RS:416 C2:128 GT:416 CT4:416 CS:96 CS4:416 SD:512 AB:1600 VS:416 "
+             "W1:512 BV:96 E2:96 SR1:512 SX:512 SK:512 EE:4096 TR:%d TC:%d" % (4 * TRW, 4 * TCW)),
+        (F32, "KM:512 KS:416 KW:96 KSW:96 CD:512 AC:%d HS:512 TOT:32 VW:96 KC:96 NK:96 PP:96 PS:96 WV:96 LE:512 YY:512 "
+              "PKI:16 PKJ:16 BLI:8 PF:16 PG:16 WC:96" % (32 * S)),
+        (F16, "SC:544"), (I32, "PI:16 UBI:8"), (U16, "UBL:8 PKL:16 BL:4 OFH:26 OFM:26 OFL:26 OFW:6 PW:6 LL:136")):
     for _e in _l.split():
         SCRATCH[_e.split(":")[0]] = ("sbuf", [128, int(_e.split(":")[1])], _d)
-for _e in ("U:128 V:128 UB:128 W:512 X:512 ZZ:544 SR1:128 SX:128 SK:128 E:1024 TR:%d TC:%d B0:128 B1:128 B2:128 "
-           "LD0:144 LD1:144 LD2:144 PK0:144 PK1:144 PK2:144" % (TRW, TCW)).split():
+for _e in ("U:128 V:128 F:128 UB:128 W:512 WR:512 X:512 ZZ:544 SR1:128 SX:128 SK:128 E:1024 TR:%d TC:%d B0:128 B1:128 "
+           "B2:128 LD0:144 LD1:144 LD2:144 PK0:144 PK1:144 PK2:144" % (TRW, TCW)).split():
     SCRATCH["q" + _e.split(":")[0]] = ("sbuf", [128, int(_e.split(":")[1])], X4)
     SCRATCH["s" + _e.split(":")[0]] = ("sbuf", [128, int(_e.split(":")[1])], U8)
 for _k in range(8):
     SCRATCH["P%d" % _k] = ("psum", [128, 512], F32)
-POOL = {}
-_at = 0
-for _n, _w in (("R16", 2), ("PKI", 16), ("PKJ", 16), ("BLI", 4), ("S6", 6), ("SR", 6), ("PF", 16), ("PG", 16),
-               ("WC", 96)):
-    POOL[_n] = (_at, _w)
-    _at += (_w + 7) // 8 * 8
-SCRATCH["KF"] = ("sbuf", [128, _at], F32)
 
-SEMAPHORES = ("sv sa st sg ldu ldx0 ldx1 ldx2 ldw ldv loc ole oa ob oc oy0 oy1 zl "
-              "rep0 rep1 rep2 rpa0 rpa1 rpa2 shf0 shf1 shf2 arr0 arr1 arr2").split()
+SEMAPHORES = ("sv sa st sg ldu ldx0 ldx1 ldx2 ldw ldv loc ole oa0 oa1 os ob oc oy0 oy1 oyw zl wr0 wr32 wr64 "
+              "rep0 rep1 rep2 rpa shf0 shf1 shf2 arr0 arr1 arr2").split()
 
 BIG = 1.5 * 2.0 ** 23
 ETA = 2.0 ** -110
 STEP = 2048.0
-CFG["T"] = (0.83, 5.0, 20.0, 90.0, 1500.0, 2400.0, 1.56, 3.8, 0.83)
-CFG["PS"] = 70.0
-CFG["WX"], CFG["WP"] = 110.0, 50.0
+CYC, CALL, ACALL, BANK, ISSUE, WAKE, AFTER_MM, LOCAL, REMOTE, GAT, SCA = (
+    0.83, 5.0, 20.0, 83.0, 120.0, 90.0, 50.0, 1500.0, 1800.0, 1.56, 3.8)
+CASES = ((1.0, 110.0), (0.9, 200.0), (1.25, 130.0))
+LOOKS = (30.0, 70.0, 120.0)
 
 
 def rank_program(g, core, T, topo):
     rank = T.rank_of(core)
     if rank is None:
         return
-    CYC, CALL, ACALL, WAKE, LOCAL, REMOTE, GAT, SCA, PE = CFG["T"]
-    TOP, LOW = CFG["TOP"], CFG["LOW"]
-    RANGES, TILES = layout(CFG["CUTS"])
     n_ranks = len(T.cores)
     eng = {"v": g.vector, "a": g.scalar, "t": g.tensor, "g": g, "s": g.sync}
     own = {"v": "sv", "a": "sa", "t": "st", "g": "sg"}
@@ -88,15 +67,12 @@ def rank_program(g, core, T, topo):
     known = {q: {} for q in eng}
     log = {}
     serial = [0]
-    part = [False]
     calls = []
     touched = {}
     boost = [0.0]
+    unpacks, lists_out = [], []
 
     def A(name, c0=0, c1=None, step=1, p0=0, p1=128):
-        if name in POOL:
-            at, w = POOL[name]
-            name, c0, c1 = "KF", at + c0, at + (w if c1 is None else c1)
         t = T[name]
         if c1 is None:
             c1 = t.shape[1]
@@ -117,30 +93,26 @@ def rank_program(g, core, T, topo):
         return True
 
     def note(q, run, reads, writes, busy, late=0.0):
-        c = {"q": q, "run": run, "busy": busy, "late": late, "after": {}, "next": [], "i": len(calls),
-             "list": any(SCRATCH[k[0]][2] == U16 for k in reads),
-             "boost": boost[0] + (CFG["SHORT"] if q == "a" and busy < CFG["SB"] else 0.0)}
+        c = {"q": q, "run": run, "busy": busy, "late": late, "after": {}, "i": len(calls), "boost": boost[0],
+             "list": any(SCRATCH[k[0]][2] == U16 for k in reads)}
         for keys, wr in ((reads, False), (writes, True)):
             for k in keys:
                 for (k2, wr2, d) in touched.get(k[0], []):
                     if (wr or wr2) and d is not c and meets(k, k2):
                         free = d["q"] == q and not d["late"] and (not wr2 and not d["list"] or q == "t")
-                        c["after"][d["i"]] = max(c["after"].get(d["i"], 0.0), 0.0 if free else d["late"] + (
-                            WAKE if d["q"] == q else CFG["WX"] + (CFG["WP"] if d["q"] == "t" else 0.0)))
+                        c["after"][d["i"]] = c["after"].get(d["i"], False) or not free
         for keys, wr in ((reads, False), (writes, True)):
             for k in keys:
                 touched.setdefault(k[0], []).append((k, wr, c))
-        for i in c["after"]:
-            calls[i]["next"].append(c)
         calls.append(c)
 
-    def plan(way, links, waits, lead):
+    def plan(way, links, waits, lead, look):
         left, at, ends, order = list(waits), list(lead), [0.0] * len(calls), []
         ready = {q: [c["i"] for c in calls if c["q"] == q and not left[c["i"]]] for q in eng}
         free = {q: 0.0 for q in eng}
         while len(order) < len(calls):
             t0, q = min((max(min(at[i] for i in ready[q]), free[q]), q) for q in eng if ready[q])
-            i = max((i for i in ready[q] if at[i] <= t0 + CFG["LOOK"]), key=lambda i: (way[i], -i))
+            i = max((i for i in ready[q] if at[i] <= t0 + look), key=lambda i: (way[i], -i))
             ready[q].remove(i)
             order.append(i)
             ends[i] = free[q] = max(at[i], free[q]) + calls[i]["busy"]
@@ -151,34 +123,53 @@ def rank_program(g, core, T, topo):
                     ready[calls[j]["q"]].append(j)
         return order, ends
 
+    def gaps(slow, cross):
+        return [[(j, (slow * calls[j]["late"] + (WAKE if calls[j]["q"] == c["q"] else cross + (
+            AFTER_MM if calls[j]["q"] == "t" else 0.0))) if wait else 0.0) for j, wait in c["after"].items()] for c in calls]
+
+    def length(order, behind, slow):
+        free, ends = {q: 0.0 for q in eng}, [0.0] * len(calls)
+        for i in order:
+            q = calls[i]["q"]
+            ends[i] = free[q] = max([free[q]] + [ends[j] + gap for (j, gap) in behind[i]]) + calls[i]["busy"]
+        return max(ends[c["i"]] + slow * c["late"] for c in calls)
+
+    def keeps(order):
+        at = {i: n for n, i in enumerate(order)}
+        return all(at[j] < at[c["i"]] for c in calls for j in c["after"])
+
     def issue():
-        ahead = [[(d["i"], d["after"][c["i"]]) for d in c["next"]] for c in calls]
-        behind = [list(c["after"].items()) for c in calls]
-        way = [0.0] * len(calls)
-        for c in reversed(calls):
-            way[c["i"]] = c["busy"] + max([c["late"]] + [way[j] + gap for (j, gap) in ahead[c["i"]]])
+        cases = [(slow, gaps(slow, cross)) for (slow, cross) in CASES]
         best = None
-        for k in range(CFG["PASS"]):
-            way = [c.get("first", way[c["i"]] + c["boost"]) for c in calls]
-            order, ends = plan(way, ahead, [len(b) for b in behind], [0.0] * len(calls))
-            length = max(ends[c["i"]] + c["late"] for c in calls)
-            if best is None or length < best[0]:
-                best = (length, order, way)
-            way = plan(ends, behind, [len(a) for a in ahead], [c["late"] for c in calls])[1]
-        seed = 12345
-        base = best[2]
-        for k in range(CFG.get("TRY", 0)):
-            way = []
-            for w in base:
-                seed = (seed * 1103515245 + 12345) % 2147483648
-                way.append(w + CFG["AMP"] * (seed / 2147483648.0 - 0.5) if seed % 7 == 0 else w)
-            order, ends = plan(way, ahead, [len(b) for b in behind], [0.0] * len(calls))
-            length = max(ends[c["i"]] + c["late"] for c in calls)
-            if length < best[0]:
-                best = (length, order, way)
-                base = way
-        CFG["LEN"] = best[0]
-        for i in best[1]:
+        for (slow, behind) in cases:
+            ahead = [[] for c in calls]
+            for c in calls:
+                for (j, gap) in behind[c["i"]]:
+                    ahead[j].append((c["i"], gap))
+            for look in LOOKS:
+                way = [0.0] * len(calls)
+                for c in reversed(calls):
+                    way[c["i"]] = c["busy"] + max([slow * c["late"]] + [way[j] + gap for (j, gap) in ahead[c["i"]]])
+                for k in range(2):
+                    way = [c.get("first", way[c["i"]] + c["boost"]) for c in calls]
+                    order, ends = plan(way, ahead, [len(b) for b in behind], [0.0] * len(calls), look)
+                    long = sum(length(order, b, s) for (s, b) in cases)
+                    if best is None or long < best[0]:
+                        best = (long, order)
+                    way = plan(ends, behind, [len(a) for a in ahead], [slow * c["late"] for c in calls], look)[1]
+        order = best[1]
+        for banks in unpacks:
+            places = [n for n, i in enumerate(order) if i in banks[0] + banks[1]]
+            last = order[places[-1]] in banks[1]
+            trial = list(order)
+            for n, i in zip(places, banks[1 - last] + banks[last]):
+                trial[n] = i
+            if keeps(trial):
+                order = trial
+        rest = [i for i in order if i not in lists_out[1:]]
+        n = rest.index(lists_out[0]) + 1
+        order = rest[:n] + lists_out[1:] + rest[n:]
+        for i in order:
             calls[i]["run"]()
 
     def need(q, deps):
@@ -226,18 +217,13 @@ def rank_program(g, core, T, topo):
         def run():
             need(q, collect(q, reads, writes, False))
             s = own[q]
-            if q == "g":
-                now = writes[0][2] - writes[0][1] < 128
-                if now or part[0]:
-                    need(q, [{"sem": s, "cnt": total[s], "clock": {}, "n": 0}])
-                part[0] = now
             total[s] = total.get(s, 0) + 1
             fn().then_inc(T.sem[s], 1)
             record(q, reads, writes, s, False)
         note(q, run, reads, writes, busy)
 
-    def dmas(q, sem, pairs, late=LOCAL):
-        reads = [i[1] for (o, i) in pairs if i[1]]
+    def dmas(q, sem, pairs, late=LOCAL, behind=()):
+        reads = [i[1] for (o, i) in pairs if i[1]] + [x[1] for x in behind]
         writes = [o[1] for (o, i) in pairs if o[1]]
 
         def run():
@@ -246,7 +232,7 @@ def rank_program(g, core, T, topo):
                 eng[q].dma_start(o[0], i[0]).then_inc(T.sem[sem], 16)
             total[sem] = 16 * len(pairs)
             record(q, reads, writes, sem, True)
-        note(q, run, reads, writes, CFG.get("DI", 120.0) * len(pairs), late)
+        note(q, run, reads, writes, ISSUE * len(pairs), late)
 
     def ap(x):
         return x[0] if isinstance(x, tuple) else x
@@ -259,10 +245,10 @@ def rank_program(g, core, T, topo):
 
     def span(out, *ins, both=False):
         sides = [out] + list(ins)
-        c = 0.5 if all(SCRATCH[x[1][0]][2] in (BF, U16) for x in sides) else 1.0
+        c = 0.5 if all(SCRATCH[x[1][0]][2] in (BF, U16, F16) for x in sides) else 1.0
         if both and not any(is_bank(x[1]) for x in ins):
             c *= 2
-        return CALL + CYC * max(64, c * count(out)) + (CFG["PS"] if any(is_bank(x[1]) for x in ins) else 0.0)
+        return CALL + CYC * max(64, c * count(out)) + (BANK if any(is_bank(x[1]) for x in ins) else 0.0)
 
     def memset(out, c):
         op("v", lambda: g.vector.memset(out[0], c), [], [out], span(out))
@@ -277,8 +263,8 @@ def rank_program(g, core, T, topo):
             fn = lambda: g.vector.tensor_scalar(out[0], in0[0], ap(s1), ap(s2), o0, o1)
         op("v", fn, [in0, s1, s2], [out], span(out, in0))
 
-    def tt(out, in0, in1, o):
-        op("v", lambda: g.vector.tensor_tensor(out[0], in0[0], in1[0], o), [in0, in1], [out],
+    def tt(out, in0, in1, o, behind=()):
+        op("v", lambda: g.vector.tensor_tensor(out[0], in0[0], in1[0], o), [in0, in1] + list(behind), [out],
            span(out, in0, in1, both=True))
 
     def scan(out, d0, d1, init, o0=ALU.add, o1=ALU.max):
@@ -287,6 +273,14 @@ def rank_program(g, core, T, topo):
 
     def gather(out, win, off):
         op("v", lambda: g.vector.tensor_copy(out[0], win[0].indirect(off[0])), [win, off], [out],
+           50 + GAT * CYC * count(out))
+
+    def gather_min(out, win, off, in1):
+        op("v", lambda: g.vector.tensor_tensor(out[0], win[0].indirect(off[0]), in1[0], ALU.min), [win, off, in1], [out],
+           50 + GAT * CYC * count(out))
+
+    def gather_times(out, win, off, c):
+        op("v", lambda: g.vector.tensor_scalar(out[0], win[0].indirect(off[0]), c, None, ALU.mult), [win, off], [out],
            50 + GAT * CYC * count(out))
 
     def scatter(win, off, in_):
@@ -304,27 +298,28 @@ def rank_program(g, core, T, topo):
             kw["accum_out"] = accum[0]
         busy = CYC * max(64, count(out)) if off is None else 65 + GAT * CYC * count(out)
         op("a", lambda: g.scalar.activation(out[0], src, func, **kw), [in_, bias, scale, off],
-           [out] + ([accum] if accum is not None else []), busy + ACALL + (min(CALL, 20.0) if accum is not None else 0))
+           [out] + ([accum] if accum is not None else []), busy + ACALL + (CALL if accum is not None else 0))
 
     def lin(out, in_, scale, bias):
         act(out, in_, ACT.Identity, bias, scale)
 
-    def quant(name, c0, c1, src=None):
-        qq, ss, in_ = A("q" + name, c0, c1), A("s" + name, c0, c1), A(src or name, 4 * c0, 4 * c1)
+    def quant(name, c0, c1, src=None, s0=None):
+        s0 = c0 if s0 is None else s0
+        qq, ss, in_ = A("q" + name, c0, c1), A("s" + name, c0, c1), A(src or name, 4 * s0, 4 * (s0 + c1 - c0))
         op("v", lambda: g.vector.quantize_mx(qq[0], ss[0], in_[0]), [in_], [qq, ss], 12 + 0.88 * (c1 - c0))
 
-    def pick(dst, d0, d1, src, off, on="a"):
+    def pick(dst, d0, d1, src, off):
         qo, qi, so, si = A("q" + dst, d0, d1), A("q" + src), A("s" + dst, d0, d1), A("s" + src)
         op("v", lambda: g.vector.tensor_copy(qo[0].bitcast(dt.uint32), qi[0].bitcast(dt.uint32).indirect(off[0])),
            [qi, off], [qo], 50 + GAT * CYC * (d1 - d0))
-        (act if on == "a" else gather)(so, si, off=off)
+        act(so, si, off=off)
 
     def mm(bank, st, s0, mv, m0, n, start=True, stop=True):
         out = A("P%d" % bank, 0, n)
         a, b = A("q" + st, s0, s0 + 128), A("s" + st, s0, s0 + 128)
         c, d = A("q" + mv, m0, m0 + n), A("s" + mv, m0, m0 + n)
         op("t", lambda: g.tensor.matmul_mx(out[0], a[0], b[0], c[0], d[0], start, stop), [a, b, c, d], [out],
-           PE * (n + 16))
+           CYC * (n + 16))
 
     def iota(out, pattern, base, cm=0, real=True):
         kw = {"allow_small_or_imprecise_dtypes": True} if real else {}
@@ -349,28 +344,30 @@ def rank_program(g, core, T, topo):
     def hbm(x):
         return (x, None)
 
-    cut = 4 * CFG["HALF"] if CFG["X2"] else 4 * C
-    loads = (("ldu", 2800.0, [(A("UU"), hbm(T.u[:]))]),
-             ("ldx0", 3900.0, [(A("X0", 0, cut), hbm(T.x[:, 0:cut]))]),
-             ("ldx2", 5000.0, [(A("X0", cut, 4 * C), hbm(T.x[:, cut:4 * C]))] if cut < 4 * C else []),
-             ("ldx1", 5600.0, [(A("X0", 4 * C, 2048), hbm(T.x[:, 4 * C:2048]))]),
-             ("ldw", 7500.0, [(bytes_of(A("qW")), hbm(T.wc[:])), (A("sW"), hbm(T.ws[:]))]),
-             ("ldv", 8500.0, [(A("VV"), hbm(T.v[:]))]))
-    for q, (sem, late, pairs) in zip(CFG["LQ"], loads):
-        if pairs:
-            dmas(q, sem, pairs, late)
-            calls[-1]["first"] = 1e6 - late
+    def columns(dst, d0, src, s0, n):
+        return [(bytes_of(A("q" + dst, d0, d0 + n)), bytes_of(A("q" + src, s0, s0 + n))),
+                (A("s" + dst, d0, d0 + n), A("s" + src, s0, s0 + n))]
+
+    for (sem, late, pairs) in (("ldu", 2380.0, [(A("UU"), hbm(T.u[:]))]),
+                               ("ldx0", 3315.0, [(A("X0", 0, 4 * HALF), hbm(T.x[:, 0:4 * HALF]))]),
+                               ("ldx2", 4250.0, [(A("X0", 4 * HALF, 4 * C), hbm(T.x[:, 4 * HALF:4 * C]))]),
+                               ("ldx1", 4760.0, [(A("X0", 4 * C, 2048), hbm(T.x[:, 4 * C:2048]))]),
+                               ("ldw", 6375.0, [(bytes_of(A("qW")), hbm(T.wc[:])), (A("sW"), hbm(T.ws[:]))]),
+                               ("ldv", 7225.0, [(A("VV"), hbm(T.v[:]))])):
+        dmas("s", sem, pairs, late)
+        calls[-1]["first"] = 1e6 - late
+    dmas("s", "wr0", [p for b in range(4) for k in (0, 16) for p in columns("WR", 128 * b + k, "W", 128 * b + 112, 16)])
+    calls[-1]["first"] = 1e5
 
     iota(col("PI", 0), [[0, 1]], 0, 1, False)
     iota(A("UBI"), [[16, 8]], 0, 0, False)
     iota(A("CR"), [[0, M], [1, 16]], 0)
-    iota(A("KLI"), [[16, M]], 15, 0, False)
     iota(A("CG"), [[1, 8], [0, 64]], 0)
     iota(A("BLI", 0, 3), [[128, 3]], 0)
     iota(A("PKI", 0, 9), [[2, 9]], 127)
-    signs = sum(min(4, M - 4 * b) for b, on in enumerate(CFG["CROSS"]) if on == "a")
-    iota(A("WC"), [[1, K]], C + 16 * 256 * signs)
-    iota(A("VS"), [[1, C]], 0)
+    signs = sum(min(4, M - 4 * b) for b, on in enumerate(CROSS) if on == "a")
+    iota(A("WC"), [[1, K]], C - 256 + 16 * 256 * signs)
+    iota(A("VS"), [[1, C]], -256)
     iota(A("CR4"), [[0, C // 4], [1, 4]], 0)
     memset(A("ZT"), 0.0)
 
@@ -381,52 +378,53 @@ def rank_program(g, core, T, topo):
             else:
                 memset(A(name, c, min(c1, c + 512)), 0.0)
     for (lanes, at, w, pad) in TILES:
-        lo = min([16 * m for m in lanes if m not in ("A", "B")]) if len(lanes) == 4 else 0
-        zero("TR", 4 * (at + lo), 4 * (at + max(pad, 128 * (len(lanes) < 4))), CFG["ZM"])
+        lo = 16 * lanes[-1] if len(lanes) == 4 else 0
+        zero("TR", 4 * (at + lo), 4 * (at + max(pad, 128 * (len(lanes) < 4))), "a")
     zero("TC", 0, 4 * blk(2), "v")
-    zero("TC", 4 * blk(NB - 1), 4 * blk(NB), CFG["ZM"])
-    zero("ZZ", 0, 128, CFG["ZM"])
+    zero("TC", 4 * blk(NB - 1), 4 * blk(NB), "a")
+    zero("ZZ", 0, 128, "a")
     zero("BT", 0, 512, "v")
     memset(A("ONE"), 1.0)
     copy(A("UBL"), A("UBI"))
-    copy(A("KL"), A("KLI"))
     for c, (sh, msk) in enumerate(((0, 15), (2, 3), (4, 7), (0, 3), (3, 1), (0, 7))):
         ts(col("PI", c + 1), col("PI", 0), sh, msk, ALU.logical_shift_right, ALU.bitwise_and)
     copy(A("PF", 0, 7), A("PI", 0, 7))
     c_q, c_q4, c_g, c_t, c_h, c_8 = [col("PF", c) for c in range(1, 7)]
-    g_off, g_thr, g_sub, g_o4, g_b0, g_b1, g_i0, g_i1, g_lt, g_row, g_wt = [col("PG", c) for c in range(11)]
+    g_off, g_d0, g_sub, g_o4, g_b0, g_b1, g_i0, g_dg, g_lt, g_row, g_wt, g_r0 = [col("PG", c) for c in range(12)]
     ts(A("MK"), A("CR"), c_q, None, ALU.is_equal)
     ts(A("RS"), A("CR"), 0.0, None, ALU.is_gt)
     quant("LD0", 0, 128, "ZT")
-    dmas("s", "zl", [p for k in range(1, NR) for p in (
-        (bytes_of(A("qLD%d" % k, 0, 128)), bytes_of(A("qLD0", 0, 128))), (A("sLD%d" % k, 0, 128), A("sLD0", 0, 128)))])
+    dmas("s", "zl", [p for k in range(1, NR) for p in columns("LD%d" % k, 0, "LD0", 0, 128)])
     ts(A("SR1"), A("CG"), c_g, -1.0, ALU.is_equal, ALU.mult)
     act(A("SK"), A("SR1"), scale=-256.0)
-    act(A("SX", 2, 512, 4), A("SR1", 2, 512, 4))
-    act(A("SX", 3, 512, 4), A("SR1", 3, 512, 4))
+    for ln in (1, 2, 3):
+        act(A("SX", ln, 512, 4), A("SR1", ln, 512, 4))
     act(A("C2"), A("SR1", 0, 512, 4), scale=-2.0)
     select(A("SX", 0, 512, 4), A("C2"), [[1, 128]], ALU.is_gt, 0, -1)
-    select(A("SX", 1, 512, 4), A("C2"), [[-1, 128]], ALU.is_gt, 0, 1)
     for name in ("SR1", "SX", "SK"):
         quant(name, 0, 128)
     for k in range(8):
         select(A("EE", 512 * k, 512 * k + 512), A("ONE"), [[-1000, 4], [-1, 32], [1000, 4]], ALU.is_equal, -16 * k, 1)
         quant("E", 128 * k, 128 * k + 128, "EE")
-    wv = 5 if CFG["WW"] == "v" else 0
-    memset(col("AC", S - 1), 16.0 * LOW)
-    memset(col("AC", S * M + S - 1), 16.0 * wv)
+    memset(col("AC", S - 1), 0.0)
+    memset(col("AC", S * M + S - 1), 0.0)
     lin(g_off, c_q, -STEP, 15 * STEP)
-    lin(g_o4, c_q4, 4096.0, -12288.0)
+    lin(g_o4, c_q4, 2048.0, 1024.0 - 6144.0)
     lin(g_b0, c_q4, 32.0, c_t)
     lin(g_sub, g_off, None, 1.0 + BIG)
-    lin(g_row, g_off, -1.0, 16.0 * (M - 1 + TOP))
+    lin(g_row, g_off, -1.0, 16.0 * (M - 1 + TOP[1]))
+    lin(g_r0, g_off, -1.0, 16.0 * (M - 1 + TOP[0]))
     lin(g_wt, g_off, -1.0, 16.0 * (K // 16 - 1))
     lin(g_b1, c_g, 4.0, g_b0)
     lin(g_lt, g_o4, None, c_t)
-    ts(A("CT"), A("CR"), c_q, 32 * STEP, ALU.is_gt, ALU.mult)
-    ts(A("CT4"), A("CR4"), c_q4, 32768.0, ALU.is_gt, ALU.mult)
-    lin(A("CS"), A("CT"), None, -31 * STEP)
-    lin(A("CS4"), A("CT4"), None, -31744.0)
+    ts(A("GT"), A("CR"), c_q, None, ALU.is_gt)
+    ts(A("CT4"), A("CR4"), c_q4, 2560.0, ALU.is_gt, ALU.mult)
+    lin(A("CS"), A("GT", 0, K), 32 * STEP, -31 * STEP)
+    lin(A("CD", 0, C), A("GT"), 32 * STEP, -31 * STEP)
+    lin(A("CD", C, 512), A("GT", 0, K), 32 * STEP, -31 * STEP)
+    lin(g_d0, c_q, -2.0, 32.0)
+    lin(g_dg, col("CS", 15), None, g_d0)
+    lin(A("CS4"), A("CT4"), None, -2048.0)
     ts(g_i0, c_8, 0.0, None, ALU.is_equal)
     ts(A("PKJ", 0, 9), A("PKI", 0, 9), c_h, 139.0, ALU.add, ALU.min)
     ts(A("BL", 0, 3), A("BLI", 0, 3), g_b1, None, ALU.add)
@@ -435,11 +433,10 @@ def rank_program(g, core, T, topo):
     quant("U", 0, 128, "UU")
     pick("UB", 0, 128, "U", A("UBL"))
     quant("V", 0, 128, "VV")
-    quant("X", 0, CFG["HALF"], "X0")
-    quant("X", CFG["HALF"], C, "X0")
+    quant("X", 0, HALF, "X0")
+    quant("X", HALF, C, "X0")
 
     def send(t):
-        gather(A("BT", 0, 48), A("MR"), A("BL", 0, 3))
         quant("B%d" % t, 0, 128, "BT")
         dst = T.cores[(rank + t + 1) % n_ranks]
         src = T.cores[(rank - t - 1) % n_ranks]
@@ -458,14 +455,16 @@ def rank_program(g, core, T, topo):
             record("r", [], [ql[1], sl[1]], arr, True)
         note("g", run, [qb[1], sb[1]], [ql[1], sl[1]], 200.0, REMOTE * (1.5 if t == 0 else 1.0))
 
-    def unpack(t, xx, f):
-        pick("PK%d" % t, 0, 144, "LD%d" % t, A("PKL", 0, 9), CFG["SP"])
+    def unpack(t, xx, engines):
+        pick("PK%d" % t, 0, 144, "LD%d" % t, A("PKL", 0, 9))
+        unpacks.append([])
         for odd, bank in enumerate((5, 2)):
+            unpacks[-1].append(list(range(len(calls), len(calls) + 4)))
             for k in range(0, 8, 2):
                 mm(bank, "E", 128 * (k + odd), "PK%d" % t, 8 - k, 128, k == 0, k == 6)
             for b in range(4):
-                (act if f[odd] == "a" else copy)(A(xx, 4 * (C + odd) + b, 2048, 8, 0, 16),
-                                                 A("P%d" % bank, 0, K, 2, 32 * b, 32 * b + 16))
+                (act if engines[odd] == "a" else copy)(A(xx, 4 * (C + odd) + b, 2048, 8, 0, 16),
+                                                       A("P%d" % bank, 0, K, 2, 32 * b, 32 * b + 16))
 
     where = {m: (at, ln) for (lanes, at, w, pad) in TILES for ln, m in enumerate(lanes)}
 
@@ -476,93 +475,86 @@ def rank_program(g, core, T, topo):
         tt(A("KM", k0 + c0, k0 + c1), A(bank, p0 + c0, p0 + c1), A("MK", c0, c1), ALU.mult)
         scan(A(dst, c0, c1), A("RS", c0, c1), A("KM", k0 + c0, k0 + c1), 0.0, ALU.mult, ALU.add)
 
-    def step(on, buf, at, ln, src, p0, keys, m, slot, start):
-        out, own_key, end = lane(buf, at, ln, 0, 16 * m), col(keys, 16 * m + 15), S * slot + S
-        if on == "a":
-            lin(out, A(src, p0, p0 + 16 * m), -1.0, own_key)
-            act(out, out, ACT.Sign, bias=ETA, accum=col("AC", end - 1))
-        else:
-            ts(out, A(src, p0, p0 + 16 * m), own_key, 2.0, ALU.is_le, ALU.mult)
-            scan(A("AC", end - 8 * m, end), lane(buf, at, ln, 0, 8 * m), lane(buf, at, ln, 8 * m, 16 * m),
-                 start - 16.0 * m, ALU.add, ALU.add)
+    def own_chunk(out, src, keys, c0, n):
+        tt(out, src, keys, ALU.is_ge)
+        scan(A("SD", c0, c0 + n), A("GT", 0, n), out, 0.0, ALU.mult, ALU.add)
+        lin(A("CD", c0 + 15, c0 + n, 16), A("SD", c0 + 15, c0 + n, 16), -2.0, g_dg)
+
+    def step_scalar(buf, at, ln, src, keys, m, slot):
+        out = lane(buf, at, ln, 0, 16 * m)
+        lin(out, A(src, 0, 16 * m), -1.0, col(keys, 16 * m + 15))
+        act(out, out, ACT.Sign, bias=ETA, accum=col("AC", S * slot + S - 1))
+
+    def step_vector(at, ln, m, start):
+        end = S * (m - M + 9)
+        ts(lane("TR", at, ln, 0, 16 * m), A("P1", 0, 16 * m), col("KS", 16 * m + 15), 2.0, ALU.is_le, ALU.mult)
+        scan(A("AB", end - 8 * m, end), lane("TR", at, ln, 0, 8 * m), lane("TR", at, ln, 8 * m, 16 * m),
+             start - 16.0 * m, ALU.add, ALU.add)
 
     def place(name, bank, c0, n, slot, off, win, vals, p0=0):
         k = n // 16
-        scan(A("HS", c0, c0 + n), A("CS", 0, n), A("P%d" % bank, p0, p0 + n), 0.0)
+        scan(A("HS", c0, c0 + n), A("CD", c0, c0 + n), A("P%d" % bank, p0, p0 + n), 0.0)
         tt(A("TOT", slot, slot + k), A("HS", c0 + 15, c0 + n, 16), A("AC", S * slot + S - 1, S * (slot + k), S), ALU.add)
         ts(A("OF" + name, 0, k), A("TOT", slot, slot + k), off, 0.5, ALU.add, ALU.mult)
         scatter(win, A("OF" + name, 0, k), vals)
 
     for t in range(NR):
         xx, xn = "X%d" % (t % 2), "X%d" % ((t + 1) % 2)
+        final = t == NR - 1
 
-        half = CFG["HALF"] if CFG["EARLY"] else 0
-        if half:
-            boost[0] = CFG["B0"]
-            mm(4, "UB", 0, "X", 0, half)
-            mm(6, "UB", 0, "X", 0, half)
-            own_keys("KS", "P4", 0, half)
-            boost[0] = 0.0
+        boost[0] = 800.0
+        mm(4, "UB", 0, "X", 0, HALF)
+        mm(6, "UB", 0, "X", 0, HALF)
+        own_keys("KS", "P4", 0, HALF)
+        boost[0] = 0.0
+        mm(7, "UB", 0, "X", HALF, C - HALF)
         mm(1, "UB", 0, "X", 0, C)
         mm(0, "UB", 0, "X", 0, C)
-        own_keys("KS", "P1", max(half, CFG["KSPLIT"]), C)
-        if CFG["KSPLIT"] > half:
-            own_keys("KS", "P1", half, CFG["KSPLIT"])
-        act(A("KB"), A("KS"), off=A("KL"))
-        if CFG["DG"] == "v":
-            tt(lane("TR", 0, 0, 0, C), A("P1", 0, C), A("KB"), ALU.is_ge)
-            tt(lane("TR", 0, 1, 0, C), A("P1", 0, C), A("KB"), ALU.is_gt)
-        else:
-            tt(lane("TR", 0, 0, 0, C), A("P1", 0, C), A("KB"), ALU.subtract)
-            ts(lane("TR", 0, 1, 0, C), lane("TR", 0, 0, 0, C), 0.0, None, ALU.is_gt)
-            ts(lane("TR", 0, 0, 0, C), lane("TR", 0, 0, 0, C), 0.0, None, ALU.is_ge)
+        own_keys("KS", "P7", HALF, C, -HALF)
+        own_chunk(lane("TR", 0, 0, 0, HALF), A("P4", 0, HALF), A("KS", 0, HALF), 0, HALF)
+        own_chunk(lane("TR", 0, 0, HALF, C), A("P1", HALF, C), A("KS", HALF, C), HALF, C - HALF)
         for m in range(M - 1, 0, -1):
             at, ln = where[m]
-            if m >= M - TOP:
-                step("v", "TR", at, ln, "P1", 0, "KS", m, m, 16.0 * (M - 1 - m - TOP))
-            elif m <= LOW:
-                step("v", "TR", at, ln, "P1", 0, "KS", m, m, 16.0 * (LOW - m))
+            if m >= M - TOP[t]:
+                step_vector(at, ln, m, 16.0 * (M - 1 - m - TOP[t]))
             else:
-                step("a", "TR", at, ln, "P6" if half // 16 - CFG["EARLY"] <= m < half // 16 else "P0", 0, "KS", m, m, 0.0)
+                step_scalar("TR", at, ln, "P6" if HALF // 16 - EARLY <= m < HALF // 16 else "P0", "KS", m, m)
+        act(A("AC", S * (M - TOP[t]) + S - 1, S * M, S), A("AB", S * (8 - TOP[t]) + S - 1, S * 8, S))
 
-        boost[0] = CFG["BK"]
         if t > 0:
-            unpack(t - 1, xx, CFG["CP"])
+            unpack(t - 1, xx, "aa")
+        if t == 1:
+            for n in (32, 64):
+                dmas("s", "wr%d" % n, [p for b in range(4) for p in columns("WR", 128 * b + n, "WR", 128 * b, n)],
+                     behind=[A("qLD0", 128, 140)])
         quant("X", 384, 512, xx)
         mm(2, "UB", 0, "X", 384, 128)
         act(A("KW"), A("P2", 32, 128))
-        boost[0] = CFG["BWT"]
         own_keys("KSW", "P2", 0, K, 32, C)
-        act(A("KBW"), A("KSW"), off=A("KL", 0, 6))
-        tt(lane("TC", blk(0), 0, 0, K), A("P2", 32, 128), A("KBW"), ALU.is_ge)
-        tt(lane("TC", blk(0), 1, 0, K), A("P2", 32, 128), A("KBW"), ALU.is_gt)
+        own_chunk(lane("TC", blk(0), 0, 0, K), A("P2", 32, 128), A("KSW"), C, K)
         for m in range(5, 0, -1):
-            step(CFG["WW"], "TC", blk(0 if m > 3 else 1), (7 - m) % 4, "KW", 0, "KSW", m, M + m, 16.0 * (5 - m))
+            step_scalar("TC", blk(0 if m > 2 else 1), (6 - m) % 4, "KW", "KSW", m, M + m)
         quant("TC", 0 if t == 0 else 32, blk(2) - 32)
         mm(6, "SX", 0, "TC", blk(0) - 32, 128, True, False)
         mm(6, "SR1", 0, "TC", blk(1) - 32, 128, False, True)
-        for b, on in enumerate(CFG["CROSS"]):
+        for b, on in enumerate(CROSS):
             ms = range(4 * b, min(4 * b + 4, M))
             for m in ms:
                 out = lane("TC", blk(2 + b), m % 4, 0, K)
                 if on == "v":
-                    ts(out, A("P2", 32, 128) if CFG.get("XP") else A("KW"), col("KS", 16 * m + 15), 2.0, ALU.is_ge, ALU.mult)
+                    ts(out, A("KW"), col("KS", 16 * m + 15), 2.0, ALU.is_ge, ALU.mult)
                 else:
                     lin(out, A("KW"), -1.0, col("KS", 16 * m + 15))
-            outs = [A("TC", 4 * blk(2 + b), 4 * blk(3 + b))] if len(ms) == 4 else [
-                lane("TC", blk(2 + b), m % 4, 0, K) for m in ms]
-            for out in outs:
-                if on == "a":
+            if on == "a":
+                for out in [A("TC", 4 * blk(2 + b), 4 * blk(3 + b))] if len(ms) == 4 else [
+                        lane("TC", blk(2 + b), m % 4, 0, K) for m in ms]:
                     act(out, out, ACT.Sign, bias=ETA, scale=-1.0)
-                elif on == "m":
-                    ts(out, out, 0.0, 2.0, ALU.is_le, ALU.mult)
-        for b0, b1 in CFG["QC"]:
+        for b0, b1 in ((0, 3), (3, 5), (5, 7)):
             quant("TC", blk(2 + b0) - (32 if t == 0 and b0 == 0 else 0), blk(2 + b1))
             for b in range(b0, b1):
                 mm(5, "SK", 0, "TC", blk(2 + b) - 32, 128, b == 0, b == 6)
 
-        boost[0] = 0.0
-        for run in CFG["QT"]:
+        for run in ((0,), (1,), (2,), (3,), (4,), (5, 6)):
             (_, at, w, pad) = TILES[run[-1]]
             end = max(at + (pad if t == 0 else w), TILES[run[0]][1] + 128)
             if run[-1] == len(TILES) - 1 and t == 0:
@@ -575,95 +567,89 @@ def rank_program(g, core, T, topo):
                         last = i + 1 == len(TILES) or TILES[i + 1][2] <= a
                         mm(bank, "SX" if i == 0 else "SR1", 0, "TR", at + a, max(128, min(b, w) - a), i == 0, last)
         for (name, a, b, bank) in RANGES:
-            place(name, bank, a, b - a, a // 16, g_row, A("W1", 0, C), A("VS", a, b))
+            place(name, bank, a, b - a, a // 16, g_row if t else g_r0, A("W1", 0, C), A("VS", a, b))
 
-        boost[0] = CFG["BWT"]
         tt(A("VW"), A("P5", 32, 128), A("WC"), ALU.add)
         place("W", 6, C, K, M, g_wt, A("WV"), A("VW"), 32)
-        if CFG["KC"] == "a":
-            lin(A("KC"), A("WV"), 2.0 ** -9, BIG)
-        else:
-            ts(A("KC"), A("WV"), 2.0 ** -9, BIG, ALU.mult, ALU.add)
+        lin(A("KC"), A("WV"), 2.0 ** -9, BIG + 1.0)
         lin(A("NK"), A("KC"), -512.0, 512.0 * (BIG + 1.0))
         scan(A("PP"), A("ONE", 0, K), A("KC"), BIG)
         scan(A("PS"), A("CS", 0, K), A("PP"), 0.0)
         ts(A("PW"), A("PS", 15, K, 16), g_sub, None, ALU.subtract)
         tt(A("BV"), A("WV"), A("NK"), ALU.add)
         act(A("W1", C, 512), A("ONE", 0, K), scale=1024.0)
-        win, off, own_id, out = A("W1"), A("PW"), A("BV"), A("E2")
-        op("v", lambda win=win, off=off, own_id=own_id, out=out: g.vector.tensor_tensor(
-            out[0], win[0].indirect(off[0]), own_id[0], ALU.min), [win, off, own_id], [out], 50 + GAT * CYC * K)
-        scatter(win, off, own_id)
-        if t == NR - 1:
-            dmas("s", "ole", [(hbm(T.le[:, 0:C]), (T.W1[0:128:16, 0:C], A("W1", 0, C)[1])),
-                              (hbm(T.le[:, C:512]), (T.E2[0:128:16, 0:K], A("E2")[1]))])
+        gather_min(A("E2"), A("W1"), A("PW"), A("BV"))
+        scatter(A("W1"), A("PW"), A("BV"))
 
-        cuts = CFG["CH"][t == NR - 1]
-        done = 0
-        for i in range(len(cuts)):
-            r0, r1 = (cuts[i - 1] if i else 0), cuts[i]
+        for i, r1 in enumerate(PIECES[t]):
+            r0 = PIECES[t][i - 1] if i else 0
             c0, c1 = (128 + r0 if i else 32), 128 + r1
             m0 = min(c0, c1 - 128)
             banks = ((0, 1, 2, 7), (3, 4, 5, 6))[i % 2]
-            boost[0] = (CFG["BW"][t == NR - 1], CFG["B0"] if t < NR - 1 else 0.0, 0.0, 0.0)[i]
-
-            def share(key, n):
-                return min(n, int(CFG[key][i] * n) // 8 * 8)
+            boost[0] = 0.0 if final else (1000.0, 800.0, 0.0)[i]
             if i == 0:
                 scan(A("SC", 32, 128), A("CS4", 0, K), A("E2"), 0.0)
-            if r1 > r0:
-                scan(A("SC", 128 + r0, c1), A("CS4", 0, r1 - r0), A("W1", r0, r1), 0.0)
+            else:
+                scan(A("SC", c0, c1), A("CS4", 0, r1 - r0), A("W1", r0, r1), 0.0)
             ts(A("LL", c0 // 4, c1 // 4), A("SC", c0 + 3, c1, 4), 4.0, g_lt, ALU.mult, ALU.add)
-            mid = c0 + share("GA", c1 - c0)
-            if mid > c0:
-                act(A("ZZ", 4 * c0, 4 * mid), A(xx), off=A("LL", c0 // 4, mid // 4))
+            mid = c0 + int(GATHER[t][i] * (c1 - c0)) // 8 * 8
+            act(A("ZZ", 4 * c0, 4 * mid), A(xx), off=A("LL", c0 // 4, mid // 4))
             if mid < c1:
                 gather(A("ZZ", 4 * mid, 4 * c1), A(xx), A("LL", mid // 4, c1 // 4))
             quant("ZZ", m0, c1)
             for b in range(4):
                 mm(banks[b], "W", 128 * b, "ZZ", m0, c1 - m0)
-            scaled("Z64", 4 * c0, "ZZ", 4 * c0, 4 * (c1 - c0), 4 * share("ZA", c1 - c0), 64.0)
+            scaled("Z64", 4 * c0, "ZZ", 4 * c0, 4 * (c1 - c0), 4 * (int(TIMES64[i] * (c1 - c0)) // 8 * 8), 64.0)
             for b in range(4):
                 tt(A("T64", 4 * c0 + b, 4 * c1, 4), A("P%d" % banks[b], c0 - m0, c1 - m0), A("Z64", 4 * c0 + b, 4 * c1, 4),
-                   ALU.add)
+                   ALU.add, [A("qB%d" % t, 0, 12)] if final and 4 * i + b >= 5 else [])
             if i == 0:
-                scaled("MW", 0, "T64", 128, 4 * K, 4 * K * CFG["WA"], 0.015625)
-                rep = [(A("MR", 0, 384, 1, 16 * k, 16 * k + 16), A("MW", 0, 384, 1, 112, 128)) for k in range(8)]
-                n_a = CFG["RA"][t == NR - 1]
-                dmas("s", "rep%d" % t, rep[n_a:])
-                if n_a:
-                    dmas("a", "rpa%d" % t, rep[:n_a])
+                scaled("MW", 0, "T64", 128, 4 * K, 0, 0.015625)
+                src = A("Z64", 128, 512, 1, 112, 128) if t >= FROM_Z else A("MW", 0, 384, 1, 112, 128)
+                rep = [(A("R64" if t >= FROM_Z else "MR", 0, 384, 1, 16 * k, 16 * k + 16), src) for k in range(8)]
+                dmas("s", "rep%d" % t, rep[2 * final:])
+                if final:
+                    dmas("a", "rpa", rep[:2])
                 dmas("s", "shf%d" % t, [(A(xn, 4 * C, 2048, 1, 16, 128), A("MW", 0, 384, 1, 0, 112))])
-                send(t)
-            if r1 > r0:
-                if CFG["XL"]:
+                if t >= FROM_Z:
                     for b in range(4):
-                        o, i_ = A(xn, 4 * r0 + b, 4 * r1, 4), A("T64", 512 + 4 * r0 + b, 512 + 4 * r1, 4)
-                        if b < 4 * CFG["XA"][i]:
-                            act(o, i_, scale=0.015625)
-                        else:
-                            ts(o, i_, 0.015625, None, ALU.mult)
+                        mm(3 + b, "WR", 128 * b, "ZZ", m0, c1 - m0)
+                        tt(A("U64", b, 4 * K, 4), A("P%d" % (3 + b), c0 - m0, c0 - m0 + K), A("R64", b, 4 * K, 4), ALU.add)
+                    gather_times(A("BT", 0, 48), A("U64"), A("BL", 0, 3), 0.015625)
+                    lists_out[:] = [len(calls)]
                 else:
-                    scaled(xn, 4 * r0, "T64", 512 + 4 * r0, 4 * (r1 - r0), 4 * share("XA", r1 - r0), 0.015625)
-            if r1 - done >= 128 and (C - r1 >= 128 or r1 == C):
-                quant("X", done, r1, xn)
-                done = r1
+                    gather(A("BT", 0, 48), A("MR"), A("BL", 0, 3))
+                send(t)
+            else:
+                for b in range(4):
+                    o, i_ = A(xn, 4 * r0 + b, 4 * r1, 4), A("T64", 512 + 4 * r0 + b, 512 + 4 * r1, 4)
+                    if b < LANES_A[i]:
+                        act(o, i_, scale=0.015625)
+                    else:
+                        ts(o, i_, 0.015625, None, ALU.mult)
+                quant("X", r0, r1, xn)
         boost[0] = 0.0
 
     xx = "X%d" % (NR % 2)
-    mm(0, "V", 0, "X", 0, 384)
-    dmas("s", "oa", [(hbm(T.oc[:, 0:1536]), bytes_of(A("qX", 0, 384)))] + [
-        (hbm(T.osc[4 * k:4 * k + 4, 0:384]), A("sX", 0, 384, 1, 32 * k, 32 * k + 4)) for k in range(4)])
-    act(A("YY", 0, 384), A("P0", 0, 384))
-    dmas("s", "oy0", [(hbm(T.y[:, 0:384]), A("YY", 0, 384))])
+    lists_out.extend(range(len(calls), len(calls) + 3))
+    lin(A("LE", 0, C), A("W1", 0, C), None, 256.0)
+    lin(A("LE", C, 512), A("E2"), None, 256.0)
+    dmas("s", "ole", [(hbm(T.le[:]), (T.LE[0:128:16, :], A("LE")[1]))], behind=[A("MW")])
+    for i in range(2):
+        c0, c1 = PIECES[-1][i], PIECES[-1][i + 1]
+        mm(i, "V", 0, "X", c0, c1 - c0)
+        dmas("s", "oa%d" % i, [(hbm(T.oc[:, 4 * c0:4 * c1]), bytes_of(A("qX", c0, c1)))])
+        act(A("YY", c0, c1), A("P%d" % i, 0, c1 - c0))
+        dmas("s", "oy%d" % i, [(hbm(T.y[:, c0:c1]), A("YY", c0, c1))])
+    dmas("s", "os", [(hbm(T.osc[4 * k:4 * k + 4, 0:C]), A("sX", 0, C, 1, 32 * k, 32 * k + 4)) for k in range(4)])
     unpack(NR - 1, xx, "av")
-    quant("X", 384, 512, xx)
-    mm(7, "V", 0, "X", 384, 128)
-    scales = [(hbm(T.osc[4 * k:4 * k + 4, 384:512]), A("sX", 384, 512, 1, 32 * k, 32 * k + 4)) for k in range(4)]
-    dmas("s", "ob", [(hbm(T.oc[:, 1536:2048]), bytes_of(A("qX", 384, 512)))] + scales[2:])
+    quant("F", 0, 128, xx, 384)
+    mm(7, "V", 0, "F", 0, 128)
+    scales = [(hbm(T.osc[4 * k:4 * k + 4, C:512]), A("sF", 32, 128, 1, 32 * k, 32 * k + 4)) for k in range(4)]
+    dmas("s", "ob", [(hbm(T.oc[:, 4 * C:2048]), bytes_of(A("qF", 32, 128)))] + scales[2:])
     dmas("a", "oc", scales[:2])
-    copy(A("YY", 384, 512), A("P7", 0, 128))
-    dmas("a", "oy1", [(hbm(T.y[:, 384:512]), A("YY", 384, 512))])
+    copy(A("YY", C, 512), A("P7", 32, 128))
+    dmas("a", "oyw", [(hbm(T.y[:, C:512]), A("YY", C, 512))])
 
     issue()
     for s, c in total.items():

@@ -7,18 +7,32 @@ NR = 3
 C, K = 416, 96
 M = C // 16
 S = 200
-HALF = 208
-TOP = (4, 5, 5)
-FROM_Z = 2
-EARLY = 3
-CROSS = "vvvvvaa"
-PIECES = ((0, 208, 416), (0, 208, 416), (0, 160, 416))
-GATHER = ((1, 0.62, 0.875), (1, 0.62, 0.875), (0.5, 1, 0.75))
-TIMES64, LANES_A = (0, 0.62, 0.75), (2, 3, 3)
-RANGES = (("H", 224, 416, 3), ("M", 96, 224, 7), ("L", 0, 96, 4))
+XO = 4 * K
+HALF = (208, 208, 208)
+TOP = (5, 6, 6)
+REP_A = (0, 0, 2)
+EARLY = (3, 6, 6)
+CROSS = ("vvvvvaa", "vvvvvaa", "vvvvvaa")
+SPLIT = (1, 1, 1)
+CROSSQ = ((0, 3), (3, 5), (5, 7))
+RUNS = ((1,), (2,), (3,), (4, 5), (6,))
+PIECES = ((208, 416), (208, 416), (0, 160, 416))
+GATHER = ((1, 0.5, 0.8), (1, 0.5, 0.8), (0.5, 1, 0.75))
+TIMES64 = ((1, 0, 1), (1, 0, 1), (0, 0.62, 0.75))
+LANES_A = (2, 3, 3)
+A_FIRST = 's1*3 s2 s1*2 c1 s2 s1 s2*3 s1 kw s2 x fill s2 x s1 x s1*2 s2 u1 s1 u1 x rH u1 s1 x u2*2 x s1*2 u1 u2 c2 u1 x u2 rH u2 x s2 x s2 cw s2 rW s2*2 s1 s2 s1 s2 s1*2 s2 rM s1*2 s2*4 rL kc*2'
+A_NEXT = 'g0 g1 g2 z0 p7*5 fill z2 s1*3 s2 s1*6 s2 pk s1 s2*2 s1 s2*2 un*8 s2*5 kw s1*2 x*2 rH x u1 c2 x u1*2 x u1 u2 rH u2*3 u1 s1 x*2 u2 x*2 s2 s1 s2*2 cw rW s2 s1*4 s2*4 c1 rM kc*2 rL'
+A_THIRD = 'g0 fill g1 z0 p7*4 g2 p7 z2 s1*4 s2 pk s1*2 s2 s1 s2*4 un s1 s2 un*7 s1*2 s2*2 s1 kw s2 x*4 s1 x rH u1 x u1*2 rH u1 x u2*2 x u2 c2 x u2 u1 s2 u2 s2 s1*4 c1 rW cw s2*3 s1*3 s2 rM s2*3 rL kc*2'
+A_LAST = 'g0 rep g1 p7*5 g2 z1 z2 m1*2 pk le m1 le m2*3 un*4 y f y f'
+V_FIRST = 'k1*2 c1 k2 c1 k2 w kw w*3 c2 x*2 kw ws*2 kw x t0 cw x*4 ws x c2 ws x*2 w x*2 t1 cw x*2 ws x*4 xq x*2 qw rH xq rH xq oH t2 rW t3 vw rW oW rM t4 rM t6 oM p rL p bv rL p oL e'
+V_NEXT = 'l0 in l0 l1*2 g1 q0 g2 q1 z1 q2 a1*3 b*2 a1 k1 a2*4 k1 k2 k1 c1 k2*2 w*2 c2 pk w ws*2 w*3 ws c1 ws*2 c2 ws kw t4 t0 t1 kw x*3 kw x*3 cw x*8 cw x xq x*5 rH qw xq rH xq oH t2 rW t3 vw rW oW rM t6 rM p oM rL bv p rL p oL e'
+V_THIRD = 'l0*2 in l1*2 q0 g1 q1 z1 g2 a1*3 q2 b a1 b k1 a2*4 k1 k2 k1 c1 k2*2 pk w*4 ws w c2 w ws kw ws c1 t0 ws c2 t1 kw ws x kw x*3 ws x cw x*2 t4 x*6 cw x*5 xq x*2 qw rH xq rH xq oH rW t2 rW vw t3 oW t6 rM p rM p rL oM rL p bv oL e'
+V_LAST = 'l0 in l0 l1 g0 l1 z0 q0 a0 g2 q1 z2 a0*3 z1 b*2 q2 a1*3 m0 a2 pk a2*2 a1 a2 un m1 un m2 un k1 un k2 f*2'
+ORDER = {"v": (V_FIRST, V_NEXT, V_THIRD, V_LAST), "a": (A_FIRST, A_NEXT, A_THIRD, A_LAST)}
+RANGES = (("H", 288, 416, 3), ("M", 160, 288, 7), ("L", 0, 160, 4))
 TILES = []
 TRW = 0
-for _l in [["A", M - 1, M - 2, M - 3]] + [[m for m in range(top, top - 4, -1) if m > 0] for top in range(M - 4, 0, -4)]:
+for _l in [["A", M - 1, M - 2, M - 3]] + [[m for m in range(top, top - 4, -1) if m > 0] for top in (22, 18, 14, 10, 2, 6)]:
     _w = C if _l[0] == "A" else 16 * _l[0]
     _p = max([_w] + [min(a + 128, b) for (_n, a, b, _k) in RANGES if a < _w])
     TILES.append((_l, TRW, _w, _p))
@@ -29,31 +43,32 @@ TCW = NB * K + 64
 
 SCRATCH = {}
 for _d, _l in (
-        (BF, "UU:512 VV:512 X0:2048 X1:2048 ZZ:2176 Z64:2176 T64:2176 R64:384 U64:384 MW:384 MR:384 BT:512 ZT:512 "
+        (BF, "UU:512 VV:512 X0:2432 X1:2432 ZZ:2176 Z64:2176 T64:2176 MR:384 BT:512 ZT:512 "
              "ONE:512 CR:416 CR4:416 CG:512 MK:416 RS:416 C2:128 GT:416 CT4:416 CS:96 CS4:416 SD:512 AB:1600 VS:416 "
-             "W1:512 BV:96 E2:96 SR1:512 SX:512 SK:512 EE:4096 TR:%d TC:%d" % (4 * TRW, 4 * TCW)),
+             "W1:512 BV:96 E2:96 SR1:512 SX:512 SK:512 EE:2112 TR:%d TC:%d" % (4 * TRW, 4 * TCW)),
         (F32, "KM:512 KS:416 KW:96 KSW:96 CD:512 AC:%d HS:512 TOT:32 VW:96 KC:96 NK:96 PP:96 PS:96 WV:96 LE:512 YY:512 "
-              "PKI:16 PKJ:16 BLI:8 PF:16 PG:16 WC:96" % (32 * S)),
-        (F16, "SC:544"), (I32, "PI:16 UBI:8"), (U16, "UBL:8 PKL:16 BL:4 OFH:26 OFM:26 OFL:26 OFW:6 PW:6 LL:136")):
+              "PKI:16 PKJ:16 BLI:8 PF:16 PG:16 P7A:384 P7B:48 WC0:96 WC1:96 WC2:96" % (32 * S)),
+        (F16, "SC:544"), (I32, "PI:16 UBI:8"), (U16, "UBL:8 PKL:16 BL:8 OFH:26 OFM:26 OFL:26 OFW:6 PW:6 LL:136")):
     for _e in _l.split():
         SCRATCH[_e.split(":")[0]] = ("sbuf", [128, int(_e.split(":")[1])], _d)
-for _e in ("U:128 V:128 F:128 UB:128 W:512 WR:512 X:512 ZZ:544 SR1:128 SX:128 SK:128 E:1024 TR:%d TC:%d B0:128 B1:128 "
+for _e in ("U:128 V:128 F:128 UB:128 W:512 WR:192 X:512 ZZ:544 SR1:128 SX:128 SK:128 E:528 TR:%d TC:%d B0:128 B1:128 "
            "B2:128 LD0:144 LD1:144 LD2:144 PK0:144 PK1:144 PK2:144" % (TRW, TCW)).split():
     SCRATCH["q" + _e.split(":")[0]] = ("sbuf", [128, int(_e.split(":")[1])], X4)
     SCRATCH["s" + _e.split(":")[0]] = ("sbuf", [128, int(_e.split(":")[1])], U8)
 for _k in range(8):
     SCRATCH["P%d" % _k] = ("psum", [128, 512], F32)
 
-SEMAPHORES = ("sv sa st sg ldu ldx0 ldx1 ldx2 ldw ldv loc ole oa0 oa1 os ob oc oy0 oy1 oyw zl wr0 wr32 wr64 "
-              "rep0 rep1 rep2 rpa shf0 shf1 shf2 arr0 arr1 arr2").split()
+SEMAPHORES = ("sv sa st sg ldu ldx0 ldx1 ldx2 ldw ldv loc ole oa0 oa1 os ob oc oy0 oy1 oyw zl wr0 wr1 "
+              "rep0 rep1 rep2 rpa0 rpa1 rpa2 shf0 shf1 shf2 arr0 arr1 arr2").split()
 
 BIG = 1.5 * 2.0 ** 23
 ETA = 2.0 ** -110
+DROP = 65536.0
 STEP = 2048.0
 CYC, CALL, ACALL, BANK, ISSUE, WAKE, AFTER_MM, LOCAL, REMOTE, GAT, SCA = (
     0.83, 5.0, 20.0, 83.0, 120.0, 90.0, 50.0, 1500.0, 1800.0, 1.56, 3.8)
-CASES = ((1.0, 110.0), (0.9, 200.0), (1.25, 130.0))
-LOOKS = (30.0, 70.0, 120.0)
+CASES = ((1.0, 200.0),)
+LOOKS = (70.0,)
 
 
 def rank_program(g, core, T, topo):
@@ -69,8 +84,10 @@ def rank_program(g, core, T, topo):
     serial = [0]
     calls = []
     touched = {}
-    boost = [0.0]
-    unpacks, lists_out = [], []
+    turn = [None, None]
+
+    def stage(cycle, name):
+        turn[:] = [None, (cycle, name)]
 
     def A(name, c0=0, c1=None, step=1, p0=0, p1=128):
         t = T[name]
@@ -93,7 +110,8 @@ def rank_program(g, core, T, topo):
         return True
 
     def note(q, run, reads, writes, busy, late=0.0):
-        c = {"q": q, "run": run, "busy": busy, "late": late, "after": {}, "i": len(calls), "boost": boost[0],
+        c = {"q": q, "run": run, "busy": busy, "late": late, "after": {}, "i": len(calls),
+             "turn": turn[0] if q in "vas" else None, "stage": turn[1],
              "list": any(SCRATCH[k[0]][2] == U16 for k in reads)}
         for keys, wr in ((reads, False), (writes, True)):
             for k in keys:
@@ -134,11 +152,22 @@ def rank_program(g, core, T, topo):
             ends[i] = free[q] = max([free[q]] + [ends[j] + gap for (j, gap) in behind[i]]) + calls[i]["busy"]
         return max(ends[c["i"]] + slow * c["late"] for c in calls)
 
-    def keeps(order):
-        at = {i: n for n, i in enumerate(order)}
-        return all(at[j] < at[c["i"]] for c in calls for j in c["after"])
-
     def issue():
+        for q in "va":
+            chain = []
+            for cycle in range(NR + 1):
+                left = {}
+                for c in calls:
+                    if c["q"] == q and c["stage"] and c["stage"][0] == cycle:
+                        left.setdefault(c["stage"][1], []).append(c)
+                for word in ORDER[q][cycle].split():
+                    name, n = (word.split("*") + ["1"])[:2]
+                    for k in range(int(n)):
+                        chain.append(left[name].pop(0))
+                        chain[-1]["turn"] = 1000.0 * cycle + len(chain) * 0.001
+                assert not any(left.values()), (q, cycle, {k: len(v) for k, v in left.items() if v})
+            for a, b in zip(chain, chain[1:]):
+                b["after"].setdefault(a["i"], False)
         cases = [(slow, gaps(slow, cross)) for (slow, cross) in CASES]
         best = None
         for (slow, behind) in cases:
@@ -148,27 +177,15 @@ def rank_program(g, core, T, topo):
                     ahead[j].append((c["i"], gap))
             for look in LOOKS:
                 way = [0.0] * len(calls)
-                for c in reversed(calls):
-                    way[c["i"]] = c["busy"] + max([slow * c["late"]] + [way[j] + gap for (j, gap) in ahead[c["i"]]])
-                for k in range(2):
-                    way = [c.get("first", way[c["i"]] + c["boost"]) for c in calls]
+                for k in range(3):
                     order, ends = plan(way, ahead, [len(b) for b in behind], [0.0] * len(calls), look)
                     long = sum(length(order, b, s) for (s, b) in cases)
                     if best is None or long < best[0]:
                         best = (long, order)
-                    way = plan(ends, behind, [len(a) for a in ahead], [slow * c["late"] for c in calls], look)[1]
+                    for i in reversed(order):
+                        way[i] = calls[i]["busy"] + max([slow * calls[i]["late"]] + [way[j] + gap for (j, gap) in ahead[i]])
+                    way = [way[c["i"]] if c["stage"] or c["turn"] is None else -c["turn"] for c in calls]
         order = best[1]
-        for banks in unpacks:
-            places = [n for n, i in enumerate(order) if i in banks[0] + banks[1]]
-            last = order[places[-1]] in banks[1]
-            trial = list(order)
-            for n, i in zip(places, banks[1 - last] + banks[last]):
-                trial[n] = i
-            if keeps(trial):
-                order = trial
-        rest = [i for i in order if i not in lists_out[1:]]
-        n = rest.index(lists_out[0]) + 1
-        order = rest[:n] + lists_out[1:] + rest[n:]
         for i in order:
             calls[i]["run"]()
 
@@ -275,8 +292,8 @@ def rank_program(g, core, T, topo):
         op("v", lambda: g.vector.tensor_copy(out[0], win[0].indirect(off[0])), [win, off], [out],
            50 + GAT * CYC * count(out))
 
-    def gather_min(out, win, off, in1):
-        op("v", lambda: g.vector.tensor_tensor(out[0], win[0].indirect(off[0]), in1[0], ALU.min), [win, off, in1], [out],
+    def gather_tt(out, win, off, in1, o):
+        op("v", lambda: g.vector.tensor_tensor(out[0], win[0].indirect(off[0]), in1[0], o), [win, off, in1], [out],
            50 + GAT * CYC * count(out))
 
     def gather_times(out, win, off, c):
@@ -344,20 +361,26 @@ def rank_program(g, core, T, topo):
     def hbm(x):
         return (x, None)
 
+    def state(name, c0=0, c1=512, p0=0, p1=128):
+        return A(name, XO + 4 * c0, XO + 4 * c1, 1, p0, p1)
+
     def columns(dst, d0, src, s0, n):
         return [(bytes_of(A("q" + dst, d0, d0 + n)), bytes_of(A("q" + src, s0, s0 + n))),
                 (A("s" + dst, d0, d0 + n), A("s" + src, s0, s0 + n))]
 
     for (sem, late, pairs) in (("ldu", 2380.0, [(A("UU"), hbm(T.u[:]))]),
-                               ("ldx0", 3315.0, [(A("X0", 0, 4 * HALF), hbm(T.x[:, 0:4 * HALF]))]),
-                               ("ldx2", 4250.0, [(A("X0", 4 * HALF, 4 * C), hbm(T.x[:, 4 * HALF:4 * C]))]),
-                               ("ldx1", 4760.0, [(A("X0", 4 * C, 2048), hbm(T.x[:, 4 * C:2048]))]),
+                               ("ldx0", 3315.0, [(state("X0", 0, HALF[0]), hbm(T.x[:, 0:4 * HALF[0]]))]),
+                               ("ldx2", 4250.0, [(state("X0", HALF[0], C), hbm(T.x[:, 4 * HALF[0]:4 * C]))]),
+                               ("ldx1", 4760.0, [(state("X0", C, 512), hbm(T.x[:, 4 * C:2048]))]),
                                ("ldw", 6375.0, [(bytes_of(A("qW")), hbm(T.wc[:])), (A("sW"), hbm(T.ws[:]))]),
                                ("ldv", 7225.0, [(A("VV"), hbm(T.v[:]))])):
+        turn[0] = late - 1e6
         dmas("s", sem, pairs, late)
-        calls[-1]["first"] = 1e6 - late
-    dmas("s", "wr0", [p for b in range(4) for k in (0, 16) for p in columns("WR", 128 * b + k, "W", 128 * b + 112, 16)])
-    calls[-1]["first"] = 1e5
+    dmas("s", "wr0", [p for b in range(4) for p in (
+        (bytes_of(A("qWR", 16 * b, 16 * b + 16)), hbm(T.wc[:, 512 * b + 448:512 * b + 512])),
+        (A("sWR", 16 * b, 16 * b + 16), hbm(T.ws[:, 128 * b + 112:128 * b + 128])))], 8000.0)
+    dmas("s", "wr1", columns("WR", 64, "WR", 0, 64) + columns("WR", 128, "WR", 0, 64))
+    turn[0] = None
 
     iota(col("PI", 0), [[0, 1]], 0, 1, False)
     iota(A("UBI"), [[16, 8]], 0, 0, False)
@@ -365,8 +388,9 @@ def rank_program(g, core, T, topo):
     iota(A("CG"), [[1, 8], [0, 64]], 0)
     iota(A("BLI", 0, 3), [[128, 3]], 0)
     iota(A("PKI", 0, 9), [[2, 9]], 127)
-    signs = sum(min(4, M - 4 * b) for b, on in enumerate(CROSS) if on == "a")
-    iota(A("WC"), [[1, K]], C - 256 + 16 * 256 * signs)
+    for k in range(NR):
+        signs = sum(min(4, M - 4 * b) for b, on in enumerate(CROSS[k]) if on == "a")
+        iota(A("WC%d" % k), [[1, K]], C - 256 + 16 * 256 * signs)
     iota(A("VS"), [[1, C]], -256)
     iota(A("CR4"), [[0, C // 4], [1, 4]], 0)
     memset(A("ZT"), 0.0)
@@ -389,8 +413,11 @@ def rank_program(g, core, T, topo):
     for c, (sh, msk) in enumerate(((0, 15), (2, 3), (4, 7), (0, 3), (3, 1), (0, 7))):
         ts(col("PI", c + 1), col("PI", 0), sh, msk, ALU.logical_shift_right, ALU.bitwise_and)
     copy(A("PF", 0, 7), A("PI", 0, 7))
-    c_q, c_q4, c_g, c_t, c_h, c_8 = [col("PF", c) for c in range(1, 7)]
-    g_off, g_d0, g_sub, g_o4, g_b0, g_b1, g_i0, g_dg, g_lt, g_row, g_wt, g_r0 = [col("PG", c) for c in range(12)]
+    tt(col("PI", 8), col("PI", 0), col("PI", 3), ALU.subtract)
+    ts(col("PI", 9), col("PI", 8), 0, 3, ALU.logical_shift_right, ALU.bitwise_and)
+    copy(col("PF", 7), col("PI", 9))
+    c_q, c_q4, c_g, c_t, c_h, c_8, c_r = [col("PF", c) for c in range(1, 8)]
+    g_off, g_d0, g_sub, g_o4, g_b0, g_b1, g_i0, g_dg, g_lt, g_wt, g_b2 = [col("PG", c) for c in range(11)]
     ts(A("MK"), A("CR"), c_q, None, ALU.is_equal)
     ts(A("RS"), A("CR"), 0.0, None, ALU.is_gt)
     quant("LD0", 0, 128, "ZT")
@@ -403,38 +430,44 @@ def rank_program(g, core, T, topo):
     select(A("SX", 0, 512, 4), A("C2"), [[1, 128]], ALU.is_gt, 0, -1)
     for name in ("SR1", "SX", "SK"):
         quant(name, 0, 128)
-    for k in range(8):
-        select(A("EE", 512 * k, 512 * k + 512), A("ONE"), [[-1000, 4], [-1, 32], [1000, 4]], ALU.is_equal, -16 * k, 1)
-        quant("E", 128 * k, 128 * k + 128, "EE")
+    zero("EE", 2048, 2112, "a")
+    for k in range(4):
+        select(A("EE", 512 * k, 512 * k + 512), A("ONE"), [[-1000, 4], [-1, 32], [1000, 4]], ALU.is_equal, -32 * k, 1)
+    quant("E", 0, 256, "EE")
+    quant("E", 256, 528, "EE")
     memset(col("AC", S - 1), 0.0)
     memset(col("AC", S * M + S - 1), 0.0)
     lin(g_off, c_q, -STEP, 15 * STEP)
     lin(g_o4, c_q4, 2048.0, 1024.0 - 6144.0)
-    lin(g_b0, c_q4, 32.0, c_t)
+    lin(g_b0, c_q4, 8.0, c_g)
     lin(g_sub, g_off, None, 1.0 + BIG)
-    lin(g_row, g_off, -1.0, 16.0 * (M - 1 + TOP[1]))
-    lin(g_r0, g_off, -1.0, 16.0 * (M - 1 + TOP[0]))
-    lin(g_wt, g_off, -1.0, 16.0 * (K // 16 - 1))
-    lin(g_b1, c_g, 4.0, g_b0)
+    g_row = [col("PG", 11 + TOP.index(n)) for n in TOP]
+    for k, n in enumerate(TOP):
+        if TOP.index(n) == k:
+            lin(g_row[k], g_off, -1.0, 16.0 * (M - 1 + n) + DROP)
+    lin(g_wt, g_off, -1.0, 16.0 * (K // 16 - 1) + DROP)
+    lin(g_b1, g_b0, 4.0, c_t)
+    lin(g_b2, g_b0, 4.0, c_r)
     lin(g_lt, g_o4, None, c_t)
     ts(A("GT"), A("CR"), c_q, None, ALU.is_gt)
     ts(A("CT4"), A("CR4"), c_q4, 2560.0, ALU.is_gt, ALU.mult)
     lin(A("CS"), A("GT", 0, K), 32 * STEP, -31 * STEP)
-    lin(A("CD", 0, C), A("GT"), 32 * STEP, -31 * STEP)
-    lin(A("CD", C, 512), A("GT", 0, K), 32 * STEP, -31 * STEP)
+    lin(A("CD", 0, C - 1), A("GT", 1, C), 32 * STEP, -31 * STEP)
+    lin(A("CD", C, 511), A("GT", 1, K), 32 * STEP, -31 * STEP)
     lin(g_d0, c_q, -2.0, 32.0)
     lin(g_dg, col("CS", 15), None, g_d0)
     lin(A("CS4"), A("CT4"), None, -2048.0)
     ts(g_i0, c_8, 0.0, None, ALU.is_equal)
     ts(A("PKJ", 0, 9), A("PKI", 0, 9), c_h, 139.0, ALU.add, ALU.min)
     ts(A("BL", 0, 3), A("BLI", 0, 3), g_b1, None, ALU.add)
+    ts(A("BL", 4, 7), A("BLI", 0, 3), g_b2, None, ALU.add)
     ts(A("PKL", 0, 9), A("PKJ", 0, 9), g_i0, None, ALU.mult)
 
     quant("U", 0, 128, "UU")
     pick("UB", 0, 128, "U", A("UBL"))
     quant("V", 0, 128, "VV")
-    quant("X", 0, HALF, "X0")
-    quant("X", HALF, C, "X0")
+    quant("X", 0, HALF[0], "X0", K)
+    quant("X", HALF[0], C, "X0", K + HALF[0])
 
     def send(t):
         quant("B%d" % t, 0, 128, "BT")
@@ -455,16 +488,19 @@ def rank_program(g, core, T, topo):
             record("r", [], [ql[1], sl[1]], arr, True)
         note("g", run, [qb[1], sb[1]], [ql[1], sl[1]], 200.0, REMOTE * (1.5 if t == 0 else 1.0))
 
-    def unpack(t, xx, engines):
+    def unpack(t, xx, engines, times):
         pick("PK%d" % t, 0, 144, "LD%d" % t, A("PKL", 0, 9))
-        unpacks.append([])
         for odd, bank in enumerate((5, 2)):
-            unpacks[-1].append(list(range(len(calls), len(calls) + 4)))
+            stage(t + 1, "un")
             for k in range(0, 8, 2):
-                mm(bank, "E", 128 * (k + odd), "PK%d" % t, 8 - k, 128, k == 0, k == 6)
+                mm(bank, "E", 64 * k + 16 * odd, "PK%d" % t, 8 - k, 128, k == 0, k == 6)
             for b in range(4):
-                (act if engines[odd] == "a" else copy)(A(xx, 4 * (C + odd) + b, 2048, 8, 0, 16),
-                                                       A("P%d" % bank, 0, K, 2, 32 * b, 32 * b + 16))
+                out = A(xx, XO + 4 * (C + odd) + b, XO + 2048, 8, 0, 16)
+                in_ = A("P%d" % bank, 0, K, 2, 32 * b, 32 * b + 16)
+                if engines[odd] == "a":
+                    act(out, in_, scale=times)
+                else:
+                    ts(out, in_, times, None, ALU.mult)
 
     where = {m: (at, ln) for (lanes, at, w, pad) in TILES for ln, m in enumerate(lanes)}
 
@@ -475,70 +511,87 @@ def rank_program(g, core, T, topo):
         tt(A("KM", k0 + c0, k0 + c1), A(bank, p0 + c0, p0 + c1), A("MK", c0, c1), ALU.mult)
         scan(A(dst, c0, c1), A("RS", c0, c1), A("KM", k0 + c0, k0 + c1), 0.0, ALU.mult, ALU.add)
 
-    def own_chunk(out, src, keys, c0, n):
+    def own_chunk(t, when, out, src, keys, c0, n):
+        stage(t, when)
         tt(out, src, keys, ALU.is_ge)
         scan(A("SD", c0, c0 + n), A("GT", 0, n), out, 0.0, ALU.mult, ALU.add)
-        lin(A("CD", c0 + 15, c0 + n, 16), A("SD", c0 + 15, c0 + n, 16), -2.0, g_dg)
+        lin(A("CD", c0 + 14, c0 + n, 16), A("SD", c0 + 15, c0 + n, 16), -2.0, g_dg)
 
-    def step_scalar(buf, at, ln, src, keys, m, slot):
+    def step_scalar(t, when, n, buf, at, ln, src, keys, m, slot):
         out = lane(buf, at, ln, 0, 16 * m)
+        stage(t, when + "1")
         lin(out, A(src, 0, 16 * m), -1.0, col(keys, 16 * m + 15))
+        stage(t, when + "2")
         act(out, out, ACT.Sign, bias=ETA, accum=col("AC", S * slot + S - 1))
 
-    def step_vector(at, ln, m, start):
+    def step_vector(t, m, start):
+        at, ln = where[m]
         end = S * (m - M + 9)
+        stage(t, "w")
         ts(lane("TR", at, ln, 0, 16 * m), A("P1", 0, 16 * m), col("KS", 16 * m + 15), 2.0, ALU.is_le, ALU.mult)
+        stage(t, "ws")
         scan(A("AB", end - 8 * m, end), lane("TR", at, ln, 0, 8 * m), lane("TR", at, ln, 8 * m, 16 * m),
              start - 16.0 * m, ALU.add, ALU.add)
 
-    def place(name, bank, c0, n, slot, off, win, vals, p0=0):
+    def place(t, when, then, name, bank, c0, n, slot, off, win, vals, p0=0):
         k = n // 16
-        scan(A("HS", c0, c0 + n), A("CD", c0, c0 + n), A("P%d" % bank, p0, p0 + n), 0.0)
-        tt(A("TOT", slot, slot + k), A("HS", c0 + 15, c0 + n, 16), A("AC", S * slot + S - 1, S * (slot + k), S), ALU.add)
-        ts(A("OF" + name, 0, k), A("TOT", slot, slot + k), off, 0.5, ALU.add, ALU.mult)
+        stage(t, when)
+        ks = min(k, max(0, M - TOP[t] - slot)) if slot < M else k
+        if ks:
+            lin(A("CD", c0 + 15, c0 + 16 * ks, 16), A("AC", S * slot + S - 1, S * (slot + ks), S), None, -DROP)
+        if ks < k:
+            lin(A("CD", c0 + 16 * ks + 15, c0 + n, 16), A("AB", S * (slot + ks - M + 9) - 1, S * (slot + k - M + 8), S),
+                None, -DROP)
+        scan(A("HS", c0, c0 + n), A("P%d" % bank, p0, p0 + n), A("CD", c0, c0 + n), -DROP, ALU.max, ALU.add)
+        ts(A("OF" + name, 0, k), A("HS", c0 + 15, c0 + n, 16), off, 0.5, ALU.add, ALU.mult)
+        stage(t, then)
         scatter(win, A("OF" + name, 0, k), vals)
 
     for t in range(NR):
         xx, xn = "X%d" % (t % 2), "X%d" % ((t + 1) % 2)
         final = t == NR - 1
 
-        boost[0] = 800.0
-        mm(4, "UB", 0, "X", 0, HALF)
-        mm(6, "UB", 0, "X", 0, HALF)
-        own_keys("KS", "P4", 0, HALF)
-        boost[0] = 0.0
-        mm(7, "UB", 0, "X", HALF, C - HALF)
-        mm(1, "UB", 0, "X", 0, C)
+        half = HALF[t]
+        stage(t, "k1")
+        mm(2, "UB", 0, "X", 0, half)
+        mm(7, "UB", 0, "X", 0, half)
+        own_keys("KS", "P2", 0, half)
+        stage(t, "k2")
+        mm(4, "UB", 0, "X", half, C - half)
         mm(0, "UB", 0, "X", 0, C)
-        own_keys("KS", "P7", HALF, C, -HALF)
-        own_chunk(lane("TR", 0, 0, 0, HALF), A("P4", 0, HALF), A("KS", 0, HALF), 0, HALF)
-        own_chunk(lane("TR", 0, 0, HALF, C), A("P1", HALF, C), A("KS", HALF, C), HALF, C - HALF)
-        for m in range(M - 1, 0, -1):
-            at, ln = where[m]
-            if m >= M - TOP[t]:
-                step_vector(at, ln, m, 16.0 * (M - 1 - m - TOP[t]))
-            else:
-                step_scalar("TR", at, ln, "P6" if HALF // 16 - EARLY <= m < HALF // 16 else "P0", "KS", m, m)
-        act(A("AC", S * (M - TOP[t]) + S - 1, S * M, S), A("AB", S * (8 - TOP[t]) + S - 1, S * 8, S))
+        mm(1, "UB", 0, "X", 0, C)
+        own_keys("KS", "P4", half, C, -half)
+        if SPLIT[t]:
+            own_chunk(t, "c1", lane("TR", 0, 0, 0, half), A("P2", 0, half), A("KS", 0, half), 0, half)
+            own_chunk(t, "c2", lane("TR", 0, 0, half, C), A("P1", half, C), A("KS", half, C), half, C - half)
+        else:
+            own_chunk(t, "c2", lane("TR", 0, 0, 0, C), A("P1", 0, C), A("KS"), 0, C)
+        for m in range(M - 1, M - 1 - TOP[t], -1):
+            step_vector(t, m, 16.0 * (M - 1 - m - TOP[t]))
+        early = list(range(half // 16 - 1, half // 16 - 1 - EARLY[t], -1))
+        early += [2, 1]
+        steps = early + [m for m in range(M - 1 - TOP[t], 0, -1) if m not in early]
+        for n, m in enumerate(steps):
+            step_scalar(t, "s", n, "TR", where[m][0], where[m][1], "P7" if m in early else "P0", "KS", m, m)
 
         if t > 0:
-            unpack(t - 1, xx, "aa")
-        if t == 1:
-            for n in (32, 64):
-                dmas("s", "wr%d" % n, [p for b in range(4) for p in columns("WR", 128 * b + n, "WR", 128 * b, n)],
-                     behind=[A("qLD0", 128, 140)])
-        quant("X", 384, 512, xx)
+            stage(t, "pk")
+            unpack(t - 1, xx, "aa", 64.0)
+        stage(t, "kw")
+        quant("X", 384, 512, xx, K + 384)
         mm(2, "UB", 0, "X", 384, 128)
         act(A("KW"), A("P2", 32, 128))
         own_keys("KSW", "P2", 0, K, 32, C)
-        own_chunk(lane("TC", blk(0), 0, 0, K), A("P2", 32, 128), A("KSW"), C, K)
+        own_chunk(t, "cw", lane("TC", blk(0), 0, 0, K), A("P2", 32, 128), A("KSW"), C, K)
         for m in range(5, 0, -1):
-            step_scalar("TC", blk(0 if m > 2 else 1), (6 - m) % 4, "KW", "KSW", m, M + m)
+            step_scalar(t, "u", 5 - m, "TC", blk(0 if m > 2 else 1), (6 - m) % 4, "KW", "KSW", m, M + m)
+        stage(t, "qw")
         quant("TC", 0 if t == 0 else 32, blk(2) - 32)
         mm(6, "SX", 0, "TC", blk(0) - 32, 128, True, False)
         mm(6, "SR1", 0, "TC", blk(1) - 32, 128, False, True)
-        for b, on in enumerate(CROSS):
+        for b, on in enumerate(CROSS[t]):
             ms = range(4 * b, min(4 * b + 4, M))
+            stage(t, "x")
             for m in ms:
                 out = lane("TC", blk(2 + b), m % 4, 0, K)
                 if on == "v":
@@ -549,92 +602,115 @@ def rank_program(g, core, T, topo):
                 for out in [A("TC", 4 * blk(2 + b), 4 * blk(3 + b))] if len(ms) == 4 else [
                         lane("TC", blk(2 + b), m % 4, 0, K) for m in ms]:
                     act(out, out, ACT.Sign, bias=ETA, scale=-1.0)
-        for b0, b1 in ((0, 3), (3, 5), (5, 7)):
+        stage(t, "xq")
+        for b0, b1 in CROSSQ:
             quant("TC", blk(2 + b0) - (32 if t == 0 and b0 == 0 else 0), blk(2 + b1))
             for b in range(b0, b1):
                 mm(5, "SK", 0, "TC", blk(2 + b) - 32, 128, b == 0, b == 6)
 
-        for run in ((0,), (1,), (2,), (3,), (4,), (5, 6)):
+        done = {i: max([steps.index(m) for m in TILES[i][0] if m in steps] + [-1]) for i in range(len(TILES))}
+        runs = [(0,)] + sorted(RUNS, key=lambda run: max(done[i] for i in run))
+        for n, run in enumerate(runs):
             (_, at, w, pad) = TILES[run[-1]]
             end = max(at + (pad if t == 0 else w), TILES[run[0]][1] + 128)
-            if run[-1] == len(TILES) - 1 and t == 0:
-                end = at + 128
+            stage(t, "t%d" % run[0])
             quant("TR", TILES[run[0]][1], end)
             for i in run:
                 (lanes, at, w, pad) = TILES[i]
+                later = [j for j in run if j > i] + [j for r in runs[n + 1:] for j in r]
                 for (name, a, b, bank) in RANGES:
                     if a < w:
-                        last = i + 1 == len(TILES) or TILES[i + 1][2] <= a
+                        last = all(TILES[j][2] <= a for j in later)
                         mm(bank, "SX" if i == 0 else "SR1", 0, "TR", at + a, max(128, min(b, w) - a), i == 0, last)
         for (name, a, b, bank) in RANGES:
-            place(name, bank, a, b - a, a // 16, g_row if t else g_r0, A("W1", 0, C), A("VS", a, b))
+            place(t, "r" + name, "o" + name, name, bank, a, b - a, a // 16, g_row[t], A("W1", 0, C), A("VS", a, b))
 
-        tt(A("VW"), A("P5", 32, 128), A("WC"), ALU.add)
-        place("W", 6, C, K, M, g_wt, A("WV"), A("VW"), 32)
+        stage(t, "vw")
+        tt(A("VW"), A("P5", 32, 128), A("WC%d" % t), ALU.add)
+        place(t, "rW", "oW", "W", 6, C, K, M, g_wt, A("WV"), A("VW"), 32)
+        stage(t, "kc")
         lin(A("KC"), A("WV"), 2.0 ** -9, BIG + 1.0)
         lin(A("NK"), A("KC"), -512.0, 512.0 * (BIG + 1.0))
+        stage(t, "p")
         scan(A("PP"), A("ONE", 0, K), A("KC"), BIG)
         scan(A("PS"), A("CS", 0, K), A("PP"), 0.0)
         ts(A("PW"), A("PS", 15, K, 16), g_sub, None, ALU.subtract)
-        tt(A("BV"), A("WV"), A("NK"), ALU.add)
+        stage(t, "bv")
+        scan(A("BV"), A("NK"), A("WV"), 0.0, ALU.min, ALU.add)
+        stage(t, "fill")
         act(A("W1", C, 512), A("ONE", 0, K), scale=1024.0)
-        gather_min(A("E2"), A("W1"), A("PW"), A("BV"))
+        stage(t, "e")
+        gather_tt(A("E2"), A("W1"), A("PW"), A("BV"), ALU.min)
+        stage(t + 1, "in")
         scatter(A("W1"), A("PW"), A("BV"))
 
+        down = 0.015625 if t else 1.0
         for i, r1 in enumerate(PIECES[t]):
             r0 = PIECES[t][i - 1] if i else 0
             c0, c1 = (128 + r0 if i else 32), 128 + r1
             m0 = min(c0, c1 - 128)
-            banks = ((0, 1, 2, 7), (3, 4, 5, 6))[i % 2]
-            boost[0] = 0.0 if final else (1000.0, 800.0, 0.0)[i]
+            banks = ((0, 1, 2, 7), (3, 4, 5, 6))[r1 == C]
             if i == 0:
+                stage(t + 1, "l0")
                 scan(A("SC", 32, 128), A("CS4", 0, K), A("E2"), 0.0)
-            else:
-                scan(A("SC", c0, c1), A("CS4", 0, r1 - r0), A("W1", r0, r1), 0.0)
-            ts(A("LL", c0 // 4, c1 // 4), A("SC", c0 + 3, c1, 4), 4.0, g_lt, ALU.mult, ALU.add)
-            mid = c0 + int(GATHER[t][i] * (c1 - c0)) // 8 * 8
-            act(A("ZZ", 4 * c0, 4 * mid), A(xx), off=A("LL", c0 // 4, mid // 4))
-            if mid < c1:
-                gather(A("ZZ", 4 * mid, 4 * c1), A(xx), A("LL", mid // 4, c1 // 4))
-            quant("ZZ", m0, c1)
+                ts(A("LL", 8, 32), A("SC", 35, 128, 4), 4.0, g_lt, ALU.mult, ALU.add)
+                stage(t + 1, "l1")
+                scan(A("SC", 128, 544), A("CS4"), A("W1", 0, C), 0.0)
+                ts(A("LL", 32, 136), A("SC", 131, 544, 4), 4.0, g_lt, ALU.mult, ALU.add)
+            for (a, e) in ([(32, 128)] if i == 0 else []) + ([(128 + r0, c1)] if r1 > r0 else []):
+                j = 0 if a == 32 else 2 if e == 128 + C else 1
+                mid = a + int(GATHER[t][j] * (e - a)) // 8 * 8
+                stage(t + 1, "g%d" % j)
+                if mid > a:
+                    act(A("ZZ", 4 * a, 4 * mid), state(xx), scale=down, off=A("LL", a // 4, mid // 4))
+                if mid < e:
+                    gather_times(A("ZZ", 4 * mid, 4 * e), state(xx), A("LL", mid // 4, e // 4), down)
+                stage(t + 1, "q%d" % j)
+                quant("ZZ", min(a, e - 128), e)
+                stage(t + 1, "z%d" % j)
+                scaled("Z64", 4 * a, "ZZ", 4 * a, 4 * (e - a), 4 * (int(TIMES64[t][j] * (e - a)) // 8 * 8), 64.0)
+                if j == 0:
+                    stage(t + 1, "rep")
+                    rep = [(A("MR", 0, XO, 1, 16 * k, 16 * k + 16), A("ZZ", 128, 512, 1, 112, 128)) for k in range(8)]
+                    dmas("s", "rep%d" % t, rep[REP_A[t]:])
+                    if REP_A[t]:
+                        dmas("a", "rpa%d" % t, rep[:REP_A[t]])
+                    stage(t + 1, "p7")
+                    for b in range(4):
+                        mm(3 + b, "WR", 16 * b, "ZZ", 0, 128)
+                        act(A("P7A", b, XO, 4), A("P%d" % (3 + b), 32, 128), scale=0.015625)
+                    act(A("P7B"), A("P7A"), off=A("BL", 4, 7))
+                    stage(t + 1, "b")
+                    gather_tt(A("BT", 0, 48), A("MR"), A("BL", 0, 3), A("P7B"), ALU.add)
+                    send(t)
             for b in range(4):
                 mm(banks[b], "W", 128 * b, "ZZ", m0, c1 - m0)
-            scaled("Z64", 4 * c0, "ZZ", 4 * c0, 4 * (c1 - c0), 4 * (int(TIMES64[i] * (c1 - c0)) // 8 * 8), 64.0)
+            stage(t + 1, "a%d" % j)
             for b in range(4):
-                tt(A("T64", 4 * c0 + b, 4 * c1, 4), A("P%d" % banks[b], c0 - m0, c1 - m0), A("Z64", 4 * c0 + b, 4 * c1, 4),
-                   ALU.add, [A("qB%d" % t, 0, 12)] if final and 4 * i + b >= 5 else [])
+                out = A("T64", 4 * c0 + b, 4 * c1, 4) if final else A(xn, 4 * c0 - 128 + b, 4 * c1 - 128, 4)
+                tt(out, A("P%d" % banks[b], c0 - m0, c1 - m0), A("Z64", 4 * c0 + b, 4 * c1, 4), ALU.add)
             if i == 0:
-                scaled("MW", 0, "T64", 128, 4 * K, 0, 0.015625)
-                src = A("Z64", 128, 512, 1, 112, 128) if t >= FROM_Z else A("MW", 0, 384, 1, 112, 128)
-                rep = [(A("R64" if t >= FROM_Z else "MR", 0, 384, 1, 16 * k, 16 * k + 16), src) for k in range(8)]
-                dmas("s", "rep%d" % t, rep[2 * final:])
+                stage(t + 1, "m0")
                 if final:
-                    dmas("a", "rpa", rep[:2])
-                dmas("s", "shf%d" % t, [(A(xn, 4 * C, 2048, 1, 16, 128), A("MW", 0, 384, 1, 0, 112))])
-                if t >= FROM_Z:
-                    for b in range(4):
-                        mm(3 + b, "WR", 128 * b, "ZZ", m0, c1 - m0)
-                        tt(A("U64", b, 4 * K, 4), A("P%d" % (3 + b), c0 - m0, c0 - m0 + K), A("R64", b, 4 * K, 4), ALU.add)
-                    gather_times(A("BT", 0, 48), A("U64"), A("BL", 0, 3), 0.015625)
-                    lists_out[:] = [len(calls)]
-                else:
-                    gather(A("BT", 0, 48), A("MR"), A("BL", 0, 3))
-                send(t)
-            else:
-                for b in range(4):
-                    o, i_ = A(xn, 4 * r0 + b, 4 * r1, 4), A("T64", 512 + 4 * r0 + b, 512 + 4 * r1, 4)
-                    if b < LANES_A[i]:
+                    scaled(xn, 0, "T64", 128, 4 * K, 0, 0.015625)
+                dmas("s", "shf%d" % t, [(state(xn, C, 512, 16, 128), A(xn, 0, XO, 1, 0, 112))])
+            if r1 > r0:
+                stage(t + 1, "m%d" % j)
+                for b in range(4 * final):
+                    o, i_ = A(xn, XO + 4 * r0 + b, XO + 4 * r1, 4), A("T64", 512 + 4 * r0 + b, 512 + 4 * r1, 4)
+                    if b < LANES_A[j]:
                         act(o, i_, scale=0.015625)
                     else:
                         ts(o, i_, 0.015625, None, ALU.mult)
-                quant("X", r0, r1, xn)
-        boost[0] = 0.0
+                stage(t + 1, "k%d" % j)
+                quant("X", r0, r1, xn, K + r0)
 
     xx = "X%d" % (NR % 2)
-    lists_out.extend(range(len(calls), len(calls) + 3))
+    stage(NR, "le")
     lin(A("LE", 0, C), A("W1", 0, C), None, 256.0)
     lin(A("LE", C, 512), A("E2"), None, 256.0)
-    dmas("s", "ole", [(hbm(T.le[:]), (T.LE[0:128:16, :], A("LE")[1]))], behind=[A("MW")])
+    dmas("s", "ole", [(hbm(T.le[:]), (T.LE[0:128:16, :], A("LE")[1]))], behind=[A("qB%d" % (NR - 1), 0, 12)])
+    stage(NR, "y")
     for i in range(2):
         c0, c1 = PIECES[-1][i], PIECES[-1][i + 1]
         mm(i, "V", 0, "X", c0, c1 - c0)
@@ -642,8 +718,10 @@ def rank_program(g, core, T, topo):
         act(A("YY", c0, c1), A("P%d" % i, 0, c1 - c0))
         dmas("s", "oy%d" % i, [(hbm(T.y[:, c0:c1]), A("YY", c0, c1))])
     dmas("s", "os", [(hbm(T.osc[4 * k:4 * k + 4, 0:C]), A("sX", 0, C, 1, 32 * k, 32 * k + 4)) for k in range(4)])
-    unpack(NR - 1, xx, "av")
-    quant("F", 0, 128, xx, 384)
+    stage(NR, "pk")
+    unpack(NR - 1, xx, "av", 1.0)
+    stage(NR, "f")
+    quant("F", 0, 128, xx, K + 384)
     mm(7, "V", 0, "F", 0, 128)
     scales = [(hbm(T.osc[4 * k:4 * k + 4, C:512]), A("sF", 32, 128, 1, 32 * k, 32 * k + 4)) for k in range(4)]
     dmas("s", "ob", [(hbm(T.oc[:, 4 * C:2048]), bytes_of(A("qF", 32, 128)))] + scales[2:])

@@ -9,26 +9,35 @@ M = C // 16
 S = 200
 XO = 4 * K
 HALF = (208, 208, 208)
-TOP = (5, 6, 6)
-REP_A = (0, 0, 2)
+TOP = (5, 5, 5)
+REP_A = (0, 0, 4)
 EARLY = (3, 6, 6)
-CROSS = ("vvvvvaa", "vvvvvaa", "vvvvvaa")
+CROSS = ("vvvvvaa", "vvvvvav", "vvvvvav")
 SPLIT = (1, 1, 1)
+LATE = (1, 1, 0)
+WBANK = (5, 2, 2)
+KBANK = (6, 5, 5)
 CROSSQ = ((0, 3), (3, 5), (5, 7))
 RUNS = ((1,), (2,), (3,), (4, 5), (6,))
-PIECES = ((208, 416), (208, 416), (0, 160, 416))
-GATHER = ((1, 0.5, 0.8), (1, 0.5, 0.8), (0.5, 1, 0.75))
-TIMES64 = ((1, 0, 1), (1, 0, 1), (0, 0.62, 0.75))
+PIECES = ((208, 416), (208, 416), (0, 208, 416))
+GATHER = ((1, 0.5, 0.8), (1, 0.5, 0.8), (0.5, 0.4, 0.75))
+TIMES64 = ((1, 0, 1), (1, 0, 1), (0, 0, 1))
 LANES_A = (2, 3, 3)
-A_FIRST = 's1*3 s2 s1*2 c1 s2 s1 s2*3 s1 kw s2 x fill s2 x s1 x s1*2 s2 u1 s1 u1 x rH u1 s1 x u2*2 x s1*2 u1 u2 c2 u1 x u2 rH u2 x s2 x s2 cw s2 rW s2*2 s1 s2 s1 s2 s1*2 s2 rM s1*2 s2*4 rL kc*2'
-A_NEXT = 'g0 g1 g2 z0 p7*5 fill z2 s1*3 s2 s1*6 s2 pk s1 s2*2 s1 s2*2 un*8 s2*5 kw s1*2 x*2 rH x u1 c2 x u1*2 x u1 u2 rH u2*3 u1 s1 x*2 u2 x*2 s2 s1 s2*2 cw rW s2 s1*4 s2*4 c1 rM kc*2 rL'
-A_THIRD = 'g0 fill g1 z0 p7*4 g2 p7 z2 s1*4 s2 pk s1*2 s2 s1 s2*4 un s1 s2 un*7 s1*2 s2*2 s1 kw s2 x*4 s1 x rH u1 x u1*2 rH u1 x u2*2 x u2 c2 x u2 u1 s2 u2 s2 s1*4 c1 rW cw s2*3 s1*3 s2 rM s2*3 rL kc*2'
-A_LAST = 'g0 rep g1 p7*5 g2 z1 z2 m1*2 pk le m1 le m2*3 un*4 y f y f'
-V_FIRST = 'k1*2 c1 k2 c1 k2 w kw w*3 c2 x*2 kw ws*2 kw x t0 cw x*4 ws x c2 ws x*2 w x*2 t1 cw x*2 ws x*4 xq x*2 qw rH xq rH xq oH t2 rW t3 vw rW oW rM t4 rM t6 oM p rL p bv rL p oL e'
-V_NEXT = 'l0 in l0 l1*2 g1 q0 g2 q1 z1 q2 a1*3 b*2 a1 k1 a2*4 k1 k2 k1 c1 k2*2 w*2 c2 pk w ws*2 w*3 ws c1 ws*2 c2 ws kw t4 t0 t1 kw x*3 kw x*3 cw x*8 cw x xq x*5 rH qw xq rH xq oH t2 rW t3 vw rW oW rM t6 rM p oM rL bv p rL p oL e'
-V_THIRD = 'l0*2 in l1*2 q0 g1 q1 z1 g2 a1*3 q2 b a1 b k1 a2*4 k1 k2 k1 c1 k2*2 pk w*4 ws w c2 w ws kw ws c1 t0 ws c2 t1 kw ws x kw x*3 ws x cw x*2 t4 x*6 cw x*5 xq x*2 qw rH xq rH xq oH rW t2 rW vw t3 oW t6 rM p rM p rL oM rL p bv oL e'
-V_LAST = 'l0 in l0 l1 g0 l1 z0 q0 a0 g2 q1 z2 a0*3 z1 b*2 q2 a1*3 m0 a2 pk a2*2 a1 a2 un m1 un m2 un k1 un k2 f*2'
-ORDER = {"v": (V_FIRST, V_NEXT, V_THIRD, V_LAST), "a": (A_FIRST, A_NEXT, A_THIRD, A_LAST)}
+A_FIRST = 'i*4 j i*7 u i*12 j i*4 kw s1*3 u1 s2 u2 u1 s2 s1 u2 s2 s1*3 s2 u1 x*2 u1 u2 s1 x s1 s2 x s1*2 c2 s2 u1 x s1 u2*2 s2 x*2 s2*2 s1 s2*2 rW x cw x rH s2 rH s2 s1*4 s2 s1 s2 rM s1 s2 c1 s1 s2*4 i fill kc i rL kc i*5'
+A_NEXT = 'g0 g1 p7*5 g2 z2 z0 fill s1*6 s2*3 s1 pk s1*2 s2 s1*2 un*2 s2 un*6 s2*5 s1 kw s2*2 rH u1 x u1 u2 x u1*2 rH u1 u2 c2 x*2 u2 s1 u2*2 s1*2 x s2 rW cw s1 s2 s1 s2*2 s1*3 s2 c1 s2*3 rM rL kc*2'
+A_THIRD = 'g0 g1 g2 p7*5 z2 z0 s1*3 s2 pk s1 s2 s1 s2*2 s1 s2 s1*2 un*3 s2 un s2 un s2 un*3 s1*2 s2 s1 s2 kw s2 u1 s1 x u1 s1 u2 u1 c2 x rH s2 u1 x rH x u1 u2 s2 u2*3 x s1*2 rW s1*2 cw s2 s1 s2*2 s1*2 s2*4 fill c1 rM rL kc*2'
+A_LAST = 'g0 rep g1 p7*5 g2 z2 m1*2 pk m1 m2*3 un le un*3 le y*2 f*2'
+T_FIRST = 'k1*2 kw*2 k2*3 t0 xq*2 qw t0 qw t1 xq t1 t0 xq*4 t1 t2 t3 t2 t3 t4*2 t6'
+T_NEXT = 'p7*4 a1*4 a2*4 k1*2 a0*3 k2*2 a0 k2 un*8 kw*2 t0*2 t1 t0 t4 t1 t4 xq*3 qw t1 qw xq*4 t2*2 t3*2 t6'
+T_THIRD = 'p7*2 a1 p7*2 a1*3 a2*3 k1 a2 k1 a0*4 k2*3 un*8 t0 kw*2 t0 t1 xq t0 t4 xq*2 qw t4 qw t1 xq*4 t1 t2*2 t3*2 t6'
+T_LAST = 'p7*4 a0*4 a1*4 a2*4 un*8 y*2 f'
+V_FIRST = 'i*20 u i u i k1 i*4 kw k1 i k1 kw k2 kw c1 x*3 k2 x cw k2 x i x c2 x*2 w*2 c2 x*2 w x*2 cw x*4 w x xq x*2 ws*2 w t0 ws qw x t1 ws*2 xq t2 xq c1 rW rH t3 rW rH vw oH oW t4 rM t6 rM p oM rL bv p rL p oL e'
+V_NEXT = 'l0 j l0 j*2 in l1 j l1 l2 q0 g1 l2 q1 z1 g2 a1 b a1 b a1 q2 a1 qe k1 a2*4 k1 k2 k1 a0*2 qe k2 c1 k2 a0 c1 a0 w pk w*2 ws w c2 ws w c2 ws*3 kw t0 t4 kw t1 kw x*2 cw x*10 cw x*5 xq x*3 qw rH x*2 xq rH xq oH rW t2 rW vw t3 oW t6 p rM p rM p rL oM rL bv oL e'
+V_THIRD = 'l0*2 in l1 l2 l1 l2 g1 q0 q1 z1 g2 a1 q2 a1*3 b*2 k1 a2*3 k1 a2 k1 k2 a0 c1 a0*2 c1 k2 pk k2 a0 c2 w*2 ws w*2 t0 kw w ws*3 kw c2 t4 kw t1 x*2 ws x cw x*2 cw x*9 xq x*5 qw rH x*3 xq rH xq oH rW t2 rW vw t3 oW t6 p rM p rM p rL oM rL bv oL e'
+V_LAST = 'l0*2 in g0 l1 q0 l1 l2 z0 l2 g1 a0*3 q1 b*2 g2 a0 z1 q2 a1*3 a2 m0 a1 pk a2 m1 a2*2 k1 m2 v k2 un*4 f*2'
+S_LAST = 'rep m0 oc le os oc f y y'
+ORDER = {"v": (V_FIRST, V_NEXT, V_THIRD, V_LAST), "a": (A_FIRST, A_NEXT, A_THIRD, A_LAST),
+         "t": (T_FIRST, T_NEXT, T_THIRD, T_LAST), "s": ("i*2", "rep m0", "rep m0", S_LAST)}
 RANGES = (("H", 288, 416, 3), ("M", 160, 288, 7), ("L", 0, 160, 4))
 TILES = []
 TRW = 0
@@ -44,21 +53,21 @@ TCW = NB * K + 64
 SCRATCH = {}
 for _d, _l in (
         (BF, "UU:512 VV:512 X0:2432 X1:2432 ZZ:2176 Z64:2176 T64:2176 MR:384 BT:512 ZT:512 "
-             "ONE:512 CR:416 CR4:416 CG:512 MK:416 RS:416 C2:128 GT:416 CT4:416 CS:96 CS4:416 SD:512 AB:1600 VS:416 "
-             "W1:512 BV:96 E2:96 SR1:512 SX:512 SK:512 EE:2112 TR:%d TC:%d" % (4 * TRW, 4 * TCW)),
+             "ONE:512 CR:416 CG:512 MK:416 RS:416 C2:128 GT:416 CT4:8 CS:96 CS2:96 UP:96 CS4:512 SD:512 AB:1600 VS:416 "
+             "W1:608 BV:96 SR1:512 SX:512 SK:512 EE:2112 TR:%d TC:%d" % (4 * TRW, 4 * TCW)),
         (F32, "KM:512 KS:416 KW:96 KSW:96 CD:512 AC:%d HS:512 TOT:32 VW:96 KC:96 NK:96 PP:96 PS:96 WV:96 LE:512 YY:512 "
               "PKI:16 PKJ:16 BLI:8 PF:16 PG:16 P7A:384 P7B:48 WC0:96 WC1:96 WC2:96" % (32 * S)),
         (F16, "SC:544"), (I32, "PI:16 UBI:8"), (U16, "UBL:8 PKL:16 BL:8 OFH:26 OFM:26 OFL:26 OFW:6 PW:6 LL:136")):
     for _e in _l.split():
         SCRATCH[_e.split(":")[0]] = ("sbuf", [128, int(_e.split(":")[1])], _d)
-for _e in ("U:128 V:128 F:128 UB:128 W:512 WR:192 X:512 ZZ:544 SR1:128 SX:128 SK:128 E:528 TR:%d TC:%d B0:128 B1:128 "
+for _e in ("U:128 V:128 F:128 UB:128 W:512 WR:192 X:512 ZZ:672 SR1:128 SX:128 SK:128 E:528 TR:%d TC:%d B0:128 B1:128 "
            "B2:128 LD0:144 LD1:144 LD2:144 PK0:144 PK1:144 PK2:144" % (TRW, TCW)).split():
     SCRATCH["q" + _e.split(":")[0]] = ("sbuf", [128, int(_e.split(":")[1])], X4)
     SCRATCH["s" + _e.split(":")[0]] = ("sbuf", [128, int(_e.split(":")[1])], U8)
 for _k in range(8):
     SCRATCH["P%d" % _k] = ("psum", [128, 512], F32)
 
-SEMAPHORES = ("sv sa st sg ldu ldx0 ldx1 ldx2 ldw ldv loc ole oa0 oa1 os ob oc oy0 oy1 oyw zl wr0 wr1 "
+SEMAPHORES = ("sv sa st sg ldu ldx0 ldx1 ldx2 ldw ldv loc ole oa0 oa1 os ob oc oy0 oy1 oyw zl zm wr0 wr1 "
               "rep0 rep1 rep2 rpa0 rpa1 rpa2 shf0 shf1 shf2 arr0 arr1 arr2").split()
 
 BIG = 1.5 * 2.0 ** 23
@@ -153,7 +162,7 @@ def rank_program(g, core, T, topo):
         return max(ends[c["i"]] + slow * c["late"] for c in calls)
 
     def issue():
-        for q in "va":
+        for q in ORDER:
             chain = []
             for cycle in range(NR + 1):
                 left = {}
@@ -168,6 +177,9 @@ def rank_program(g, core, T, topo):
                 assert not any(left.values()), (q, cycle, {k: len(v) for k, v in left.items() if v})
             for a, b in zip(chain, chain[1:]):
                 b["after"].setdefault(a["i"], False)
+        mine = [c for c in calls if c["q"] == "g"]
+        for a, b in zip(mine, mine[1:]):
+            b["after"].setdefault(a["i"], False)
         cases = [(slow, gaps(slow, cross)) for (slow, cross) in CASES]
         best = None
         for (slow, behind) in cases:
@@ -370,8 +382,8 @@ def rank_program(g, core, T, topo):
 
     for (sem, late, pairs) in (("ldu", 2380.0, [(A("UU"), hbm(T.u[:]))]),
                                ("ldx0", 3315.0, [(state("X0", 0, HALF[0]), hbm(T.x[:, 0:4 * HALF[0]]))]),
-                               ("ldx2", 4250.0, [(state("X0", HALF[0], C), hbm(T.x[:, 4 * HALF[0]:4 * C]))]),
-                               ("ldx1", 4760.0, [(state("X0", C, 512), hbm(T.x[:, 4 * C:2048]))]),
+                               ("ldx1", 3900.0, [(state("X0", 384, 512), hbm(T.x[:, 4 * 384:2048]))]),
+                               ("ldx2", 4700.0, [(state("X0", HALF[0], 384), hbm(T.x[:, 4 * HALF[0]:4 * 384]))]),
                                ("ldw", 6375.0, [(bytes_of(A("qW")), hbm(T.wc[:])), (A("sW"), hbm(T.ws[:]))]),
                                ("ldv", 7225.0, [(A("VV"), hbm(T.v[:]))])):
         turn[0] = late - 1e6
@@ -382,18 +394,9 @@ def rank_program(g, core, T, topo):
     dmas("s", "wr1", columns("WR", 64, "WR", 0, 64) + columns("WR", 128, "WR", 0, 64))
     turn[0] = None
 
-    iota(col("PI", 0), [[0, 1]], 0, 1, False)
-    iota(A("UBI"), [[16, 8]], 0, 0, False)
-    iota(A("CR"), [[0, M], [1, 16]], 0)
-    iota(A("CG"), [[1, 8], [0, 64]], 0)
-    iota(A("BLI", 0, 3), [[128, 3]], 0)
-    iota(A("PKI", 0, 9), [[2, 9]], 127)
-    for k in range(NR):
-        signs = sum(min(4, M - 4 * b) for b, on in enumerate(CROSS[k]) if on == "a")
-        iota(A("WC%d" % k), [[1, K]], C - 256 + 16 * 256 * signs)
-    iota(A("VS"), [[1, C]], -256)
-    iota(A("CR4"), [[0, C // 4], [1, 4]], 0)
-    memset(A("ZT"), 0.0)
+    stage(0, "i")
+    c_q, c_q4, c_g, c_t, c_h, c_8, c_r = [col("PF", c) for c in range(1, 8)]
+    g_off, g_d0, g_sub, g_o4, g_b0, g_b1, g_i0, g_dg, g_lt, g_wt, g_b2 = [col("PG", c) for c in range(11)]
 
     def zero(name, c0, c1, on):
         for c in range(c0, c1, 512):
@@ -401,72 +404,102 @@ def rank_program(g, core, T, topo):
                 act(A(name, c, min(c1, c + 512)), A("ZT", 0, min(c1, c + 512) - c))
             else:
                 memset(A(name, c, min(c1, c + 512)), 0.0)
-    for (lanes, at, w, pad) in TILES:
-        lo = 16 * lanes[-1] if len(lanes) == 4 else 0
-        zero("TR", 4 * (at + lo), 4 * (at + max(pad, 128 * (len(lanes) < 4))), "a")
-    zero("TC", 0, 4 * blk(2), "v")
-    zero("TC", 4 * blk(NB - 1), 4 * blk(NB), "a")
-    zero("ZZ", 0, 128, "a")
-    zero("BT", 0, 512, "v")
-    memset(A("ONE"), 1.0)
-    copy(A("UBL"), A("UBI"))
+
+    def sides(k):
+        select(A("EE", 512 * k, 512 * k + 512), A("ONE"), [[-1000, 4], [-1, 32], [1000, 4]], ALU.is_equal, -32 * k, 1)
+    memset(A("ZT"), 0.0)
+    iota(col("PI", 0), [[0, 1]], 0, 1, False)
+    iota(A("UBI"), [[16, 8]], 0, 0, False)
+    iota(A("CG"), [[1, 8], [0, 64]], 0)
+    iota(A("CR"), [[0, M], [1, 16]], 0)
     for c, (sh, msk) in enumerate(((0, 15), (2, 3), (4, 7), (0, 3), (3, 1), (0, 7))):
         ts(col("PI", c + 1), col("PI", 0), sh, msk, ALU.logical_shift_right, ALU.bitwise_and)
+    memset(A("ONE"), 1.0)
     copy(A("PF", 0, 7), A("PI", 0, 7))
     tt(col("PI", 8), col("PI", 0), col("PI", 3), ALU.subtract)
+    copy(A("UBL"), A("UBI"))
     ts(col("PI", 9), col("PI", 8), 0, 3, ALU.logical_shift_right, ALU.bitwise_and)
-    copy(col("PF", 7), col("PI", 9))
-    c_q, c_q4, c_g, c_t, c_h, c_8, c_r = [col("PF", c) for c in range(1, 8)]
-    g_off, g_d0, g_sub, g_o4, g_b0, g_b1, g_i0, g_dg, g_lt, g_wt, g_b2 = [col("PG", c) for c in range(11)]
-    ts(A("MK"), A("CR"), c_q, None, ALU.is_equal)
-    ts(A("RS"), A("CR"), 0.0, None, ALU.is_gt)
     quant("LD0", 0, 128, "ZT")
-    dmas("s", "zl", [p for k in range(1, NR) for p in columns("LD%d" % k, 0, "LD0", 0, 128)])
+    copy(col("PF", 7), col("PI", 9))
+    dmas("s", "zl", [p for name in ("LD1", "LD2", "ZZ") for p in columns(name, 0, "LD0", 0, 128)]
+         + [p for k in range(NR) for p in columns("PK%d" % k, 112, "LD0", 0, 32)])
+    dmas("s", "zm", [p for (lanes, at, w, pad) in TILES[:-1] if pad > w for p in columns("TR", at + w, "LD0", 0, pad - w)],
+         5000.0)
+    for (lanes, at, w, pad) in TILES[3:]:
+        lo = 16 * lanes[-1] if len(lanes) == 4 else 0
+        zero("TR", 4 * (at + lo), 4 * (at + (pad if lanes is TILES[-1][0] else w)), "a")
     ts(A("SR1"), A("CG"), c_g, -1.0, ALU.is_equal, ALU.mult)
-    act(A("SK"), A("SR1"), scale=-256.0)
+    act(A("C2"), A("SR1", 0, 512, 4), scale=-2.0)
     for ln in (1, 2, 3):
         act(A("SX", ln, 512, 4), A("SR1", ln, 512, 4))
-    act(A("C2"), A("SR1", 0, 512, 4), scale=-2.0)
+    act(A("SK"), A("SR1"), scale=-256.0)
+    iota(A("VS"), [[1, C]], -256)
     select(A("SX", 0, 512, 4), A("C2"), [[1, 128]], ALU.is_gt, 0, -1)
-    for name in ("SR1", "SX", "SK"):
-        quant(name, 0, 128)
-    zero("EE", 2048, 2112, "a")
+    iota(A("BLI", 0, 3), [[128, 3]], 0)
+    iota(A("PKI", 0, 9), [[2, 9]], 127)
+    for k in range(NR):
+        if CROSS.index(CROSS[k]) == k:
+            signs = sum(min(4, M - 4 * b) for b, on in enumerate(CROSS[k]) if on == "a")
+            iota(A("WC%d" % k), [[1, K]], C - 256 + 16 * 256 * signs)
     for k in range(4):
-        select(A("EE", 512 * k, 512 * k + 512), A("ONE"), [[-1000, 4], [-1, 32], [1000, 4]], ALU.is_equal, -32 * k, 1)
-    quant("E", 0, 256, "EE")
-    quant("E", 256, 528, "EE")
+        sides(k)
+    zero("TC", 0, 4 * blk(2), "v")
+    quant("SR1", 0, 128)
+    ts(A("MK"), A("CR"), c_q, None, ALU.is_equal)
+    ts(A("RS"), A("CR"), 0.0, None, ALU.is_gt)
+    ts(A("GT"), A("CR"), c_q, None, ALU.is_gt)
+    zero("BT", 0, 512, "v")
     memset(col("AC", S - 1), 0.0)
     memset(col("AC", S * M + S - 1), 0.0)
+    ts(g_i0, c_8, 0.0, None, ALU.is_equal)
+    for (lanes, at, w, pad) in TILES[:3]:
+        zero("TR", 4 * (at + 16 * lanes[-1]), 4 * (at + w), "a")
+    zero("TC", 4 * blk(NB - 1), 4 * blk(NB), "a")
+    lin(g_d0, c_q, -2.0, 32.0)
+    lin(A("CS"), A("GT", 0, K), 32 * STEP, -31 * STEP)
+    lin(A("CD", 0, C - 1), A("GT", 1, C), 32 * STEP, -31 * STEP)
+    lin(g_dg, col("CS", 15), None, g_d0)
+    lin(A("CD", C, 511), A("GT", 1, K), 32 * STEP, -31 * STEP)
     lin(g_off, c_q, -STEP, 15 * STEP)
     lin(g_o4, c_q4, 2048.0, 1024.0 - 6144.0)
     lin(g_b0, c_q4, 8.0, c_g)
-    lin(g_sub, g_off, None, 1.0 + BIG)
+    zero("ZZ", 0, 128, "a")
+    zero("EE", 2048, 2112, "a")
+    lin(g_sub, g_off, 0.5, (C - 256) / 512.0)
     g_row = [col("PG", 11 + TOP.index(n)) for n in TOP]
     for k, n in enumerate(TOP):
         if TOP.index(n) == k:
             lin(g_row[k], g_off, -1.0, 16.0 * (M - 1 + n) + DROP)
     lin(g_wt, g_off, -1.0, 16.0 * (K // 16 - 1) + DROP)
     lin(g_b1, g_b0, 4.0, c_t)
-    lin(g_b2, g_b0, 4.0, c_r)
+    lin(g_b2, c_r, float(K), g_b0)
     lin(g_lt, g_o4, None, c_t)
-    ts(A("GT"), A("CR"), c_q, None, ALU.is_gt)
-    ts(A("CT4"), A("CR4"), c_q4, 2560.0, ALU.is_gt, ALU.mult)
-    lin(A("CS"), A("GT", 0, K), 32 * STEP, -31 * STEP)
-    lin(A("CD", 0, C - 1), A("GT", 1, C), 32 * STEP, -31 * STEP)
-    lin(A("CD", C, 511), A("GT", 1, K), 32 * STEP, -31 * STEP)
-    lin(g_d0, c_q, -2.0, 32.0)
-    lin(g_dg, col("CS", 15), None, g_d0)
-    lin(A("CS4"), A("CT4"), None, -2048.0)
-    ts(g_i0, c_8, 0.0, None, ALU.is_equal)
-    ts(A("PKJ", 0, 9), A("PKI", 0, 9), c_h, 139.0, ALU.add, ALU.min)
+    quant("SK", 0, 128)
+    quant("SX", 0, 128)
+    ts(A("CT4", 0, 4), A("CR", 0, 4), c_q4, 2560.0, ALU.is_gt, ALU.mult)
+    lin(A("CT4", 4, 8), A("CT4", 0, 4), None, -2048.0)
+    for k in range(4):
+        lin(A("CS4", k, 512, 4), A("ZT", 0, 128), None, col("CT4", 4 + k))
+    stage(0, "j")
+    act(A("UP"), A("ONE", 0, K), scale=512.0)
+    act(A("CS2"), A("CS"), scale=256.0)
+    stage(1, "j")
+    ts(A("BL", 4, 7), A("BLI", 0, 3), 0.25, g_b2, ALU.mult, ALU.add)
     ts(A("BL", 0, 3), A("BLI", 0, 3), g_b1, None, ALU.add)
-    ts(A("BL", 4, 7), A("BLI", 0, 3), g_b2, None, ALU.add)
+    ts(A("PKJ", 0, 9), A("PKI", 0, 9), c_h, 139.0, ALU.add, ALU.min)
     ts(A("PKL", 0, 9), A("PKJ", 0, 9), g_i0, None, ALU.mult)
+    stage(1, "qe")
+    quant("E", 0, 256, "EE")
+    quant("E", 256, 528, "EE")
 
+    stage(0, "u")
     quant("U", 0, 128, "UU")
     pick("UB", 0, 128, "U", A("UBL"))
+    stage(NR, "v")
     quant("V", 0, 128, "VV")
+    stage(0, "k1")
     quant("X", 0, HALF[0], "X0", K)
+    stage(0, "k2")
     quant("X", HALF[0], C, "X0", K + HALF[0])
 
     def send(t):
@@ -488,9 +521,19 @@ def rank_program(g, core, T, topo):
             record("r", [], [ql[1], sl[1]], arr, True)
         note("g", run, [qb[1], sb[1]], [ql[1], sl[1]], 200.0, REMOTE * (1.5 if t == 0 else 1.0))
 
-    def unpack(t, xx, engines, times):
-        pick("PK%d" % t, 0, 144, "LD%d" % t, A("PKL", 0, 9))
-        for odd, bank in enumerate((5, 2)):
+    def seven(t, banks):
+        stage(t + 1, "p7")
+        for r, bank in enumerate(banks):
+            mm(bank, "WR", 16 * r, "ZZ", 128, 128)
+            act(A("P7A", K * r, K * r + K), A("P%d" % bank, 32, 128), scale=0.015625)
+        act(A("P7B"), A("P7A"), off=A("BL", 4, 7))
+        stage(t + 1, "b")
+        gather_tt(A("BT", 0, 48), A("MR"), A("BL", 0, 3), A("P7B"), ALU.add)
+        send(t)
+
+    def unpack(t, xx, engines, times, banks):
+        pick("PK%d" % t, 0, 112, "LD%d" % t, A("PKL", 0, 7))
+        for odd, bank in enumerate(banks):
             stage(t + 1, "un")
             for k in range(0, 8, 2):
                 mm(bank, "E", 64 * k + 16 * odd, "PK%d" % t, 8 - k, 128, k == 0, k == 6)
@@ -576,13 +619,14 @@ def rank_program(g, core, T, topo):
 
         if t > 0:
             stage(t, "pk")
-            unpack(t - 1, xx, "aa", 64.0)
+            unpack(t - 1, xx, "aa", 64.0, (5, 2))
         stage(t, "kw")
-        quant("X", 384, 512, xx, K + 384)
-        mm(2, "UB", 0, "X", 384, 128)
-        act(A("KW"), A("P2", 32, 128))
-        own_keys("KSW", "P2", 0, K, 32, C)
-        own_chunk(t, "cw", lane("TC", blk(0), 0, 0, K), A("P2", 32, 128), A("KSW"), C, K)
+        quant("F", 0, 128, xx, K + 384)
+        mm(WBANK[t], "UB", 0, "F", 0, 128)
+        mm(KBANK[t], "UB", 0, "F", 0, 128)
+        act(A("KW"), A("P%d" % KBANK[t], 32, 128))
+        own_keys("KSW", "P%d" % WBANK[t], 0, K, 32, C)
+        own_chunk(t, "cw", lane("TC", blk(0), 0, 0, K), A("P%d" % WBANK[t], 32, 128), A("KSW"), C, K)
         for m in range(5, 0, -1):
             step_scalar(t, "u", 5 - m, "TC", blk(0 if m > 2 else 1), (6 - m) % 4, "KW", "KSW", m, M + m)
         stage(t, "qw")
@@ -612,7 +656,7 @@ def rank_program(g, core, T, topo):
         runs = [(0,)] + sorted(RUNS, key=lambda run: max(done[i] for i in run))
         for n, run in enumerate(runs):
             (_, at, w, pad) = TILES[run[-1]]
-            end = max(at + (pad if t == 0 else w), TILES[run[0]][1] + 128)
+            end = max(at + w, TILES[run[0]][1] + 128)
             stage(t, "t%d" % run[0])
             quant("TR", TILES[run[0]][1], end)
             for i in run:
@@ -623,40 +667,40 @@ def rank_program(g, core, T, topo):
                         last = all(TILES[j][2] <= a for j in later)
                         mm(bank, "SX" if i == 0 else "SR1", 0, "TR", at + a, max(128, min(b, w) - a), i == 0, last)
         for (name, a, b, bank) in RANGES:
-            place(t, "r" + name, "o" + name, name, bank, a, b - a, a // 16, g_row[t], A("W1", 0, C), A("VS", a, b))
+            place(t, "r" + name, "o" + name, name, bank, a, b - a, a // 16, g_row[t], A("W1", K, 512), A("VS", a, b))
 
         stage(t, "vw")
-        tt(A("VW"), A("P5", 32, 128), A("WC%d" % t), ALU.add)
+        tt(A("VW"), A("P5", 32, 128), A("WC%d" % CROSS.index(CROSS[t])), ALU.add)
         place(t, "rW", "oW", "W", 6, C, K, M, g_wt, A("WV"), A("VW"), 32)
         stage(t, "kc")
         lin(A("KC"), A("WV"), 2.0 ** -9, BIG + 1.0)
         lin(A("NK"), A("KC"), -512.0, 512.0 * (BIG + 1.0))
         stage(t, "p")
-        scan(A("PP"), A("ONE", 0, K), A("KC"), BIG)
-        scan(A("PS"), A("CS", 0, K), A("PP"), 0.0)
-        ts(A("PW"), A("PS", 15, K, 16), g_sub, None, ALU.subtract)
+        scan(A("PP"), A("UP"), A("WV"), -1024.0)
+        scan(A("PS"), A("CS2"), A("PP"), 0.0)
+        ts(A("PW"), A("PS", 15, K, 16), 2.0 ** -9, g_sub, ALU.mult, ALU.subtract)
         stage(t, "bv")
         scan(A("BV"), A("NK"), A("WV"), 0.0, ALU.min, ALU.add)
         stage(t, "fill")
-        act(A("W1", C, 512), A("ONE", 0, K), scale=1024.0)
+        act(A("W1", 512, 512 + K), A("ONE", 0, K), scale=1024.0)
         stage(t, "e")
-        gather_tt(A("E2"), A("W1"), A("PW"), A("BV"), ALU.min)
+        gather_tt(A("W1", 0, K), A("W1", K, 512 + K), A("PW"), A("BV"), ALU.min)
         stage(t + 1, "in")
-        scatter(A("W1"), A("PW"), A("BV"))
+        scatter(A("W1", K, 512 + K), A("PW"), A("BV"))
 
         down = 0.015625 if t else 1.0
         for i, r1 in enumerate(PIECES[t]):
             r0 = PIECES[t][i - 1] if i else 0
             c0, c1 = (128 + r0 if i else 32), 128 + r1
+            if LATE[t]:
+                c0 = 128 + r0
             m0 = min(c0, c1 - 128)
-            banks = ((0, 1, 2, 7), (3, 4, 5, 6))[r1 == C]
-            if i == 0:
-                stage(t + 1, "l0")
-                scan(A("SC", 32, 128), A("CS4", 0, K), A("E2"), 0.0)
-                ts(A("LL", 8, 32), A("SC", 35, 128, 4), 4.0, g_lt, ALU.mult, ALU.add)
-                stage(t + 1, "l1")
-                scan(A("SC", 128, 544), A("CS4"), A("W1", 0, C), 0.0)
-                ts(A("LL", 32, 136), A("SC", 131, 544, 4), 4.0, g_lt, ALU.mult, ALU.add)
+            banks = ((0, 1, 2, 7), (3, 6, 4, 5))[r1 == C]
+            cut = K + PIECES[t][-2]
+            for n, (a, e) in enumerate([] if i else [(0, K), (K, cut), (cut, 512)]):
+                stage(t + 1, "l%d" % n)
+                scan(A("SC", 32 + a, 32 + e), A("CS4", 0, e - a), A("W1", a, e), 0.0)
+                ts(A("LL", 8 + a // 4, 8 + e // 4), A("SC", 35 + a, 32 + e, 4), 4.0, g_lt, ALU.mult, ALU.add)
             for (a, e) in ([(32, 128)] if i == 0 else []) + ([(128 + r0, c1)] if r1 > r0 else []):
                 j = 0 if a == 32 else 2 if e == 128 + C else 1
                 mid = a + int(GATHER[t][j] * (e - a)) // 8 * 8
@@ -666,7 +710,7 @@ def rank_program(g, core, T, topo):
                 if mid < e:
                     gather_times(A("ZZ", 4 * mid, 4 * e), state(xx), A("LL", mid // 4, e // 4), down)
                 stage(t + 1, "q%d" % j)
-                quant("ZZ", min(a, e - 128), e)
+                quant("ZZ", 128 + min(a, e - 128), 128 + e, "ZZ", min(a, e - 128))
                 stage(t + 1, "z%d" % j)
                 scaled("Z64", 4 * a, "ZZ", 4 * a, 4 * (e - a), 4 * (int(TIMES64[t][j] * (e - a)) // 8 * 8), 64.0)
                 if j == 0:
@@ -675,21 +719,22 @@ def rank_program(g, core, T, topo):
                     dmas("s", "rep%d" % t, rep[REP_A[t]:])
                     if REP_A[t]:
                         dmas("a", "rpa%d" % t, rep[:REP_A[t]])
-                    stage(t + 1, "p7")
-                    for b in range(4):
-                        mm(3 + b, "WR", 16 * b, "ZZ", 0, 128)
-                        act(A("P7A", b, XO, 4), A("P%d" % (3 + b), 32, 128), scale=0.015625)
-                    act(A("P7B"), A("P7A"), off=A("BL", 4, 7))
-                    stage(t + 1, "b")
-                    gather_tt(A("BT", 0, 48), A("MR"), A("BL", 0, 3), A("P7B"), ALU.add)
-                    send(t)
-            for b in range(4):
-                mm(banks[b], "W", 128 * b, "ZZ", m0, c1 - m0)
+                    seven(t, (3, 6, 4, 5))
             stage(t + 1, "a%d" % j)
+            for b in range(4):
+                mm(banks[b], "W", 128 * b, "ZZ", 128 + m0, c1 - m0)
             for b in range(4):
                 out = A("T64", 4 * c0 + b, 4 * c1, 4) if final else A(xn, 4 * c0 - 128 + b, 4 * c1 - 128, 4)
                 tt(out, A("P%d" % banks[b], c0 - m0, c1 - m0), A("Z64", 4 * c0 + b, 4 * c1, 4), ALU.add)
-            if i == 0:
+            if LATE[t] and r1 == C:
+                stage(t + 1, "a0")
+                for b in (0, 2):
+                    mm(banks[b // 2], "W", 128 * b + 128, "ZZ", 0, 256, True, False)
+                    mm(banks[b // 2], "W", 128 * b, "ZZ", 128, 128, False, True)
+                for b in range(4):
+                    tt(A(xn, b, XO, 4), A("P%d" % banks[b // 2], 128 * (b % 2) + 32, 128 * (b % 2) + 128),
+                       A("Z64", 128 + b, 512, 4), ALU.add)
+            if r1 == C if LATE[t] else i == 0:
                 stage(t + 1, "m0")
                 if final:
                     scaled(xn, 0, "T64", 128, 4 * K, 0, 0.015625)
@@ -707,26 +752,29 @@ def rank_program(g, core, T, topo):
 
     xx = "X%d" % (NR % 2)
     stage(NR, "le")
-    lin(A("LE", 0, C), A("W1", 0, C), None, 256.0)
-    lin(A("LE", C, 512), A("E2"), None, 256.0)
+    lin(A("LE", 0, C), A("W1", K, 512), None, 256.0)
+    lin(A("LE", C, 512), A("W1", 0, K), None, 256.0)
     dmas("s", "ole", [(hbm(T.le[:]), (T.LE[0:128:16, :], A("LE")[1]))], behind=[A("qB%d" % (NR - 1), 0, 12)])
     stage(NR, "y")
     for i in range(2):
         c0, c1 = PIECES[-1][i], PIECES[-1][i + 1]
-        mm(i, "V", 0, "X", c0, c1 - c0)
+        stage(NR, "oc")
         dmas("s", "oa%d" % i, [(hbm(T.oc[:, 4 * c0:4 * c1]), bytes_of(A("qX", c0, c1)))])
+        stage(NR, "y")
+        mm(i, "V", 0, "X", c0, c1 - c0)
         act(A("YY", c0, c1), A("P%d" % i, 0, c1 - c0))
         dmas("s", "oy%d" % i, [(hbm(T.y[:, c0:c1]), A("YY", c0, c1))])
+    stage(NR, "os")
     dmas("s", "os", [(hbm(T.osc[4 * k:4 * k + 4, 0:C]), A("sX", 0, C, 1, 32 * k, 32 * k + 4)) for k in range(4)])
     stage(NR, "pk")
-    unpack(NR - 1, xx, "av", 1.0)
+    unpack(NR - 1, xx, "av", 1.0, (7, 2))
     stage(NR, "f")
     quant("F", 0, 128, xx, K + 384)
-    mm(7, "V", 0, "F", 0, 128)
+    mm(3, "V", 0, "F", 0, 128)
     scales = [(hbm(T.osc[4 * k:4 * k + 4, C:512]), A("sF", 32, 128, 1, 32 * k, 32 * k + 4)) for k in range(4)]
     dmas("s", "ob", [(hbm(T.oc[:, 4 * C:2048]), bytes_of(A("qF", 32, 128)))] + scales[2:])
     dmas("a", "oc", scales[:2])
-    copy(A("YY", C, 512), A("P7", 32, 128))
+    copy(A("YY", C, 512), A("P3", 32, 128))
     dmas("a", "oyw", [(hbm(T.y[:, C:512]), A("YY", C, 512))])
 
     issue()

@@ -7,37 +7,46 @@ NR = 3
 C, K = 416, 96
 M = C // 16
 S = 200
-XO = 4 * K
-HALF = (208, 208, 208)
-TOP = (5, 5, 5)
-REP_A = (0, 0, 4)
-EARLY = (3, 6, 6)
-CROSS = ("vvvvvaa", "vvvvvav", "vvvvvav")
+CUT = (208, 208, 208)
+HALF = (128,) + CUT[:-1]
+RUN = max(max(h, C - h) for h in HALF)
 SPLIT = (1, 1, 1)
-LATE = (1, 1, 0)
-WBANK = (5, 2, 2)
+BY_DMA = ((0,), (0,), (0,))
+PRODUCTS = (((0, (3, 6, 4, 5)), (1, (0, 1, 2, 7)), (2, (3, 6, 4, 5))),) * 3
+ON_VECTOR = ((25, 24, 23, 22, 21), (25, 24, 23, 22, 21, 12), (25, 24, 23, 22, 21, 12))
+EARLY = ((7, 6, 5, 4, 3, 2, 1), (11, 10, 9, 8, 7, 2, 1), (11, 10, 9, 8, 7, 2, 1))
+REP_A = (0, 0, 4)
+CROSS = ("vvvvvaa", "vvvvvav", "vvvvvav")
+WBANK = (5, 6, 6)
 KBANK = (6, 5, 5)
 CROSSQ = ((0, 3), (3, 5), (5, 7))
-RUNS = ((1,), (2,), (3,), (4, 5), (6,))
-PIECES = ((208, 416), (208, 416), (0, 208, 416))
-GATHER = ((1, 0.5, 0.8), (1, 0.5, 0.8), (0.5, 0.4, 0.75))
+RUNS = (((0,), (1,), (6,), (2,), (3,), (4, 5)),) + (((0,), (1,), (4, 5), (2,), (3,), (6,)),) * 2
+GATHER = ((1, 0.5, 0.8), (1, 0.5, 0.8), (0.5, 0.4, 1))
 TIMES64 = ((1, 0, 1), (1, 0, 1), (0, 0, 1))
-LANES_A = (2, 3, 3)
-A_FIRST = 'i*4 j i*7 u i*12 j i*4 kw s1*3 u1 s2 u2 u1 s2 s1 u2 s2 s1*3 s2 u1 x*2 u1 u2 s1 x s1 s2 x s1*2 c2 s2 u1 x s1 u2*2 s2 x*2 s2*2 s1 s2*2 rW x cw x rH s2 rH s2 s1*4 s2 s1 s2 rM s1 s2 c1 s1 s2*4 i fill kc i rL kc i*5'
-A_NEXT = 'g0 g1 p7*5 g2 z2 z0 fill s1*6 s2*3 s1 pk s1*2 s2 s1*2 un*2 s2 un*6 s2*5 s1 kw s2*2 rH u1 x u1 u2 x u1*2 rH u1 u2 c2 x*2 u2 s1 u2*2 s1*2 x s2 rW cw s1 s2 s1 s2*2 s1*3 s2 c1 s2*3 rM rL kc*2'
-A_THIRD = 'g0 g1 g2 p7*5 z2 z0 s1*3 s2 pk s1 s2 s1 s2*2 s1 s2 s1*2 un*3 s2 un s2 un s2 un*3 s1*2 s2 s1 s2 kw s2 u1 s1 x u1 s1 u2 u1 c2 x rH s2 u1 x rH x u1 u2 s2 u2*3 x s1*2 rW s1*2 cw s2 s1 s2*2 s1*2 s2*4 fill c1 rM rL kc*2'
-A_LAST = 'g0 rep g1 p7*5 g2 z2 m1*2 pk m1 m2*3 un le un*3 le y*2 f*2'
-T_FIRST = 'k1*2 kw*2 k2*3 t0 xq*2 qw t0 qw t1 xq t1 t0 xq*4 t1 t2 t3 t2 t3 t4*2 t6'
-T_NEXT = 'p7*4 a1*4 a2*4 k1*2 a0*3 k2*2 a0 k2 un*8 kw*2 t0*2 t1 t0 t4 t1 t4 xq*3 qw t1 qw xq*4 t2*2 t3*2 t6'
-T_THIRD = 'p7*2 a1 p7*2 a1*3 a2*3 k1 a2 k1 a0*4 k2*3 un*8 t0 kw*2 t0 t1 xq t0 t4 xq*2 qw t4 qw t1 xq*4 t1 t2*2 t3*2 t6'
-T_LAST = 'p7*4 a0*4 a1*4 a2*4 un*8 y*2 f'
-V_FIRST = 'i*20 u i u i k1 i*4 kw k1 i k1 kw k2 kw c1 x*3 k2 x cw k2 x i x c2 x*2 w*2 c2 x*2 w x*2 cw x*4 w x xq x*2 ws*2 w t0 ws qw x t1 ws*2 xq t2 xq c1 rW rH t3 rW rH vw oH oW t4 rM t6 rM p oM rL bv p rL p oL e'
-V_NEXT = 'l0 j l0 j*2 in l1 j l1 l2 q0 g1 l2 q1 z1 g2 a1 b a1 b a1 q2 a1 qe k1 a2*4 k1 k2 k1 a0*2 qe k2 c1 k2 a0 c1 a0 w pk w*2 ws w c2 ws w c2 ws*3 kw t0 t4 kw t1 kw x*2 cw x*10 cw x*5 xq x*3 qw rH x*2 xq rH xq oH rW t2 rW vw t3 oW t6 p rM p rM p rL oM rL bv oL e'
-V_THIRD = 'l0*2 in l1 l2 l1 l2 g1 q0 q1 z1 g2 a1 q2 a1*3 b*2 k1 a2*3 k1 a2 k1 k2 a0 c1 a0*2 c1 k2 pk k2 a0 c2 w*2 ws w*2 t0 kw w ws*3 kw c2 t4 kw t1 x*2 ws x cw x*2 cw x*9 xq x*5 qw rH x*3 xq rH xq oH rW t2 rW vw t3 oW t6 p rM p rM p rL oM rL bv oL e'
-V_LAST = 'l0*2 in g0 l1 q0 l1 l2 z0 l2 g1 a0*3 q1 b*2 g2 a0 z1 q2 a1*3 a2 m0 a1 pk a2 m1 a2*2 k1 m2 v k2 un*4 f*2'
-S_LAST = 'rep m0 oc le os oc f y y'
-ORDER = {"v": (V_FIRST, V_NEXT, V_THIRD, V_LAST), "a": (A_FIRST, A_NEXT, A_THIRD, A_LAST),
-         "t": (T_FIRST, T_NEXT, T_THIRD, T_LAST), "s": ("i*2", "rep m0", "rep m0", S_LAST)}
+ZERO = "gggggaag"
+UNPACK = "av"
+ORDER = {
+    "v": ("iz nw iu ix*5 iz ix is nw is*3 ig im*2 is u it u k1 iy ik kw k1*2 kw c1 kw k2 cw x0*3 x1*2 c1 x1 k2 x1 cw k2 t6 x0 w21 qw x3 w23 w25 x2 c2 w24 w21 w22 t0 x3 x4 w25 x2 x3 x2 w22 c2 x4 t1 x2 w24 w23 x4*2 xq x3 rW rH xq rH xq oH rW t2 vw t3 oW p rM t4 rM p oM rL p rL bv oL e",
+          "ir l0*2 in ir l1 l2 ir l1 ie l2 q0 g1 ib*2 q1 z1 g2 a1 b a1 b a1 q2 a1 ie k1 a2*2 k1 a2*2 k1 k2 w12 qe c1 k2 c1 k2 w12 w23 w21 w22 pk w24 c2 w22 w25 w23 w24 c2 w25 kw t0 t4 w21 kw t1 kw x1 x2 x4 x0 x2 x0 x1 x4*2 cw x0 x4 x2*2 x1 x0 x1 x6 x3 cw rH xq x3*3 rH qw x6 xq*2 oH rW t2 rW vw t3 oW t6 p rM p rM p rL oM rL bv oL e",
+          "l0*2 in l1 l2 l1 l2 q0 g1 v q1 z1 g2 a1*2 q2 a1*2 b k1 b a2*2 k1 a2*2 k1 k2 w12 c1 w12 k2 pk k2 c1 w23 w21 w22 w21 w25 c2 kw w24 w23 w22 w25 kw t0 c2 kw w24 x3 x2 x4*2 x1 x6 x0 t1 x3*3 x4 t4 x1 x0 x2 x0 cw x0 x2 cw x1*2 x2 qw x4 xq rH x6 xq rH xq oH rW t2 rW vw t3 oW t6 p rM p rM p rL oM rL bv oL e",
+          "l0*2 in g0 l1 q0 l1 l2 g1 z0 l2 q1 z1 b a0 b a1*3 a0 q2 a1 a0*2 k1 a2*3 pk a2 k2 un*4 f*2"),
+    "a": ("n6 n5 na iy*2 id iy ik id iy u ic io*2 ip ic io*2 id s3 s1 s6 kw s7 s5 s4 u3 u2 u4 u1 s2 s5 s3 s6 s1 s2 s4 u5 u2 u4 u3 cw u1 u5 x6 s20 s16 s18 s14 x5 x6 s20 s18 rW s19 s17 s14 s19 s15 s12 s11 s17 rH x6 x5*3 s13 c2 x6 rH x5 s15 s10 s16 s11 s13 s12 s9 s10 s8 s7 rM s9 s8 c1 it rL kc il ib ie il it ib kc it fill it*2",
+          "g0 ib g1 p7*5 g2 a0*2 z2 a0 fill a0 s11 s2 s10 s8 s7 s1 s11 s10 s9 s8 s2 s15 s18 s9 pk s1 s20 s19 un*8 s7 s20 s19 c2 s18 s6 kw s17 s16 u4 rH u3 s4 x5 u5 s14 u3 u1 u2 u5 rH x5 u4 u2 x5*2 s16 u1 x5 s15 s13 rW cw s17 s14 s13 s3 s5 s6 s4 s3 s5 rM c1 rM*2 kc rL kc",
+          "g0 g1 p7*2 g2 p7*2 a0*2 p7 z2 a0*2 s10 s8 s7 s11 s10 s1 pk s9 s11 s2 s9 s18 un s19 un*7 s19 s20 s18 s17 s14 kw s20 x5 s2 s8 x5*2 s7 u3 u4 s1 u2 u1 rH s16 u3 u5 x5 s4 u1 rH u4 u2 u5 x5 c2 s3 s13 s15 s17 rW s16 cw s15 s13 s14 s5 s6 s4 s5 s3 s6 rM*2 c1 rM rL kc fill kc",
+          "g0 rep g1 p7*5 g2 z2 d0 pk le y un*4 le y f*2"),
+    "t": ("k1*2 kw*2 k2*3 qw t0*2 qw t1*2 xq*2 t0 xq*5 t1 t6 t2 t3 t2 t3 t4*2",
+          "p7*4 a0*2 a1*4 a0*2 a2*2 k1 a2*2 k1 k2*3 un*2 kw*2 t0 t1 t0*2 t1*2 t4 xq*3 qw*2 xq*2 t4 xq*2 t2 t3 t2 t3 t6",
+          "p7*4 a0 a1*2 a0 a1*2 a0*2 a2*2 k1 a2*2 k1 k2*3 un*2 kw*2 t0*2 t1*2 t0 t1 t4 qw xq*2 qw xq*5 t2 t4 t2 t3*2 t6",
+          "p7*4 a0 a1*2 a0 a1*2 a0*2 a2*4 y un*2 y f"),
+    "s": ("ld*6 iz*2 wr",
+          "rep m0",
+          "rep m0",
+          "rep d0 oc y oc os y le f"),
+    "g": ("ix iu is im iy n1 n2 nx iv n4 n0 n3 ie iv qe*3 ip ib iv qe*2 nz*2 lv",
+          "b d0",
+          "b d0",
+          "b"),
+}
 RANGES = (("H", 288, 416, 3), ("M", 160, 288, 7), ("L", 0, 160, 4))
 TILES = []
 TRW = 0
@@ -52,32 +61,29 @@ TCW = NB * K + 64
 
 SCRATCH = {}
 for _d, _l in (
-        (BF, "UU:512 VV:512 X0:2432 X1:2432 ZZ:2176 Z64:2176 T64:2176 MR:384 BT:512 ZT:512 "
-             "ONE:512 CR:416 CG:512 MK:416 RS:416 C2:128 GT:416 CT4:8 CS:96 CS2:96 UP:96 CS4:512 SD:512 AB:1600 VS:416 "
-             "W1:608 BV:96 SR1:512 SX:512 SK:512 EE:2112 TR:%d TC:%d" % (4 * TRW, 4 * TCW)),
-        (F32, "KM:512 KS:416 KW:96 KSW:96 CD:512 AC:%d HS:512 TOT:32 VW:96 KC:96 NK:96 PP:96 PS:96 WV:96 LE:512 YY:512 "
-              "PKI:16 PKJ:16 BLI:8 PF:16 PG:16 P7A:384 P7B:48 WC0:96 WC1:96 WC2:96" % (32 * S)),
+        (BF, "UU:512 VV:512 X0:2048 X1:2048 ZZ:2176 Z64:2176 MR:384 MW:384 BT:512 ZT:512 "
+             "CG:128 C2:128 CT4:8 CS:96 CS2:96 UP:96 CS4:512 SD:512 AB:1600 VS:416 W1:608 BV:96 SR1:512 SX:512 SK:512 "
+             "EE:576 TR:%d TC:%d CR:%d MK:%d RS:%d GT:%d" % (4 * TRW, 4 * TCW, RUN, RUN, RUN, RUN)),
+        (F32, "KM:512 KS:416 KW:96 KSW:96 CD:512 AC:%d HS:512 VW:96 KC:96 NK:96 PP:96 PS:96 WV:96 LE:512 YY:512 "
+              "PKI:16 PKJ:16 BLI:8 PF:16 PG:16 P7A:384 P7B:48 PA0:384 PA1:1664 PA2:1664 WC0:96 WC1:96 WC2:96" % (32 * S)),
         (F16, "SC:544"), (I32, "PI:16 UBI:8"), (U16, "UBL:8 PKL:16 BL:8 OFH:26 OFM:26 OFL:26 OFW:6 PW:6 LL:136")):
     for _e in _l.split():
         SCRATCH[_e.split(":")[0]] = ("sbuf", [128, int(_e.split(":")[1])], _d)
-for _e in ("U:128 V:128 F:128 UB:128 W:512 WR:192 X:512 ZZ:672 SR1:128 SX:128 SK:128 E:528 TR:%d TC:%d B0:128 B1:128 "
-           "B2:128 LD0:144 LD1:144 LD2:144 PK0:144 PK1:144 PK2:144" % (TRW, TCW)).split():
+for _e in ("U:128 V:128 F:128 UB:128 W:512 WR:192 X:512 ZZ:544 SR1:128 SX:128 SK:128 E:144 TR:%d TC:%d B0:128 B1:128 "
+           "B2:128 LD0:144 LD1:144 LD2:144 PK0:128 PK1:128 PK2:128" % (TRW, TCW)).split():
     SCRATCH["q" + _e.split(":")[0]] = ("sbuf", [128, int(_e.split(":")[1])], X4)
     SCRATCH["s" + _e.split(":")[0]] = ("sbuf", [128, int(_e.split(":")[1])], U8)
 for _k in range(8):
     SCRATCH["P%d" % _k] = ("psum", [128, 512], F32)
 
-SEMAPHORES = ("sv sa st sg ldu ldx0 ldx1 ldx2 ldw ldv loc ole oa0 oa1 os ob oc oy0 oy1 oyw zl zm wr0 wr1 "
-              "rep0 rep1 rep2 rpa0 rpa1 rpa2 shf0 shf1 shf2 arr0 arr1 arr2").split()
+SEMAPHORES = "sv sa st sg ldu ldx0 ldx1 ldx2 ldw ldv loc ole oa0 oa1 os ob oc oy0 oy1 oyw zl zm wr0 wr1".split() + [
+    "%s%d" % (_s, _t) for _s in ("rep", "rpa", "shf", "arr", "ad0", "ad1", "ad2") for _t in range(NR)]
 
 BIG = 1.5 * 2.0 ** 23
 ETA = 2.0 ** -110
 DROP = 65536.0
 STEP = 2048.0
-CYC, CALL, ACALL, BANK, ISSUE, WAKE, AFTER_MM, LOCAL, REMOTE, GAT, SCA = (
-    0.83, 5.0, 20.0, 83.0, 120.0, 90.0, 50.0, 1500.0, 1800.0, 1.56, 3.8)
-CASES = ((1.0, 200.0),)
-LOOKS = (70.0,)
+DOWN = 0.015625
 
 
 def rank_program(g, core, T, topo):
@@ -93,10 +99,10 @@ def rank_program(g, core, T, topo):
     serial = [0]
     calls = []
     touched = {}
-    turn = [None, None]
+    turn = [None]
 
     def stage(cycle, name):
-        turn[:] = [None, (cycle, name)]
+        turn[0] = (cycle, name)
 
     def A(name, c0=0, c1=None, step=1, p0=0, p1=128):
         t = T[name]
@@ -118,88 +124,40 @@ def rank_program(g, core, T, topo):
             return False
         return True
 
-    def note(q, run, reads, writes, busy, late=0.0):
-        c = {"q": q, "run": run, "busy": busy, "late": late, "after": {}, "i": len(calls),
-             "turn": turn[0] if q in "vas" else None, "stage": turn[1],
-             "list": any(SCRATCH[k[0]][2] == U16 for k in reads)}
+    def note(q, run, reads, writes):
+        c = {"q": q, "run": run, "after": set(), "i": len(calls), "stage": turn[0]}
         for keys, wr in ((reads, False), (writes, True)):
             for k in keys:
                 for (k2, wr2, d) in touched.get(k[0], []):
-                    if (wr or wr2) and d is not c and meets(k, k2):
-                        free = d["q"] == q and not d["late"] and (not wr2 and not d["list"] or q == "t")
-                        c["after"][d["i"]] = c["after"].get(d["i"], False) or not free
+                    if (wr or wr2 or is_bank(k) and d["q"] != q) and d is not c and meets(k, k2):
+                        c["after"].add(d["i"])
         for keys, wr in ((reads, False), (writes, True)):
             for k in keys:
                 touched.setdefault(k[0], []).append((k, wr, c))
         calls.append(c)
 
-    def plan(way, links, waits, lead, look):
-        left, at, ends, order = list(waits), list(lead), [0.0] * len(calls), []
-        ready = {q: [c["i"] for c in calls if c["q"] == q and not left[c["i"]]] for q in eng}
-        free = {q: 0.0 for q in eng}
-        while len(order) < len(calls):
-            t0, q = min((max(min(at[i] for i in ready[q]), free[q]), q) for q in eng if ready[q])
-            i = max((i for i in ready[q] if at[i] <= t0 + look), key=lambda i: (way[i], -i))
-            ready[q].remove(i)
-            order.append(i)
-            ends[i] = free[q] = max(at[i], free[q]) + calls[i]["busy"]
-            for (j, gap) in links[i]:
-                at[j] = max(at[j], ends[i] + gap)
-                left[j] -= 1
-                if not left[j]:
-                    ready[calls[j]["q"]].append(j)
-        return order, ends
-
-    def gaps(slow, cross):
-        return [[(j, (slow * calls[j]["late"] + (WAKE if calls[j]["q"] == c["q"] else cross + (
-            AFTER_MM if calls[j]["q"] == "t" else 0.0))) if wait else 0.0) for j, wait in c["after"].items()] for c in calls]
-
-    def length(order, behind, slow):
-        free, ends = {q: 0.0 for q in eng}, [0.0] * len(calls)
-        for i in order:
-            q = calls[i]["q"]
-            ends[i] = free[q] = max([free[q]] + [ends[j] + gap for (j, gap) in behind[i]]) + calls[i]["busy"]
-        return max(ends[c["i"]] + slow * c["late"] for c in calls)
-
     def issue():
+        chains = []
         for q in ORDER:
-            chain = []
+            chains.append([])
             for cycle in range(NR + 1):
                 left = {}
                 for c in calls:
-                    if c["q"] == q and c["stage"] and c["stage"][0] == cycle:
+                    if c["q"] == q and c["stage"][0] == cycle:
                         left.setdefault(c["stage"][1], []).append(c)
                 for word in ORDER[q][cycle].split():
                     name, n = (word.split("*") + ["1"])[:2]
                     for k in range(int(n)):
-                        chain.append(left[name].pop(0))
-                        chain[-1]["turn"] = 1000.0 * cycle + len(chain) * 0.001
+                        chains[-1].append(left[name].pop(0))
                 assert not any(left.values()), (q, cycle, {k: len(v) for k, v in left.items() if v})
-            for a, b in zip(chain, chain[1:]):
-                b["after"].setdefault(a["i"], False)
-        mine = [c for c in calls if c["q"] == "g"]
-        for a, b in zip(mine, mine[1:]):
-            b["after"].setdefault(a["i"], False)
-        cases = [(slow, gaps(slow, cross)) for (slow, cross) in CASES]
-        best = None
-        for (slow, behind) in cases:
-            ahead = [[] for c in calls]
-            for c in calls:
-                for (j, gap) in behind[c["i"]]:
-                    ahead[j].append((c["i"], gap))
-            for look in LOOKS:
-                way = [0.0] * len(calls)
-                for k in range(3):
-                    order, ends = plan(way, ahead, [len(b) for b in behind], [0.0] * len(calls), look)
-                    long = sum(length(order, b, s) for (s, b) in cases)
-                    if best is None or long < best[0]:
-                        best = (long, order)
-                    for i in reversed(order):
-                        way[i] = calls[i]["busy"] + max([slow * calls[i]["late"]] + [way[j] + gap for (j, gap) in ahead[i]])
-                    way = [way[c["i"]] if c["stage"] or c["turn"] is None else -c["turn"] for c in calls]
-        order = best[1]
-        for i in order:
-            calls[i]["run"]()
+        done = set()
+        while any(chains):
+            before = len(done)
+            for chain in chains:
+                while chain and chain[0]["after"] <= done:
+                    chain[0]["run"]()
+                    done.add(chain.pop(0)["i"])
+            assert len(done) > before
 
     def need(q, deps):
         for h in sorted(deps, key=lambda h: -h["n"]):
@@ -239,7 +197,7 @@ def rank_program(g, core, T, topo):
         for k in writes:
             log.setdefault(k[0], []).append((k, True, q, h))
 
-    def op(q, fn, reads, writes, busy):
+    def op(q, fn, reads, writes):
         reads = [r[1] for r in reads if isinstance(r, tuple)]
         writes = [w[1] for w in writes]
 
@@ -249,19 +207,19 @@ def rank_program(g, core, T, topo):
             total[s] = total.get(s, 0) + 1
             fn().then_inc(T.sem[s], 1)
             record(q, reads, writes, s, False)
-        note(q, run, reads, writes, busy)
+        note(q, run, reads, writes)
 
-    def dmas(q, sem, pairs, late=LOCAL, behind=()):
+    def dmas(q, sem, pairs, behind=(), **how):
         reads = [i[1] for (o, i) in pairs if i[1]] + [x[1] for x in behind]
         writes = [o[1] for (o, i) in pairs if o[1]]
 
         def run():
             need(q, collect(q, reads, writes, True))
             for (o, i) in pairs:
-                eng[q].dma_start(o[0], i[0]).then_inc(T.sem[sem], 16)
+                eng[q].dma_start(o[0], i[0], **how).then_inc(T.sem[sem], 16)
             total[sem] = 16 * len(pairs)
             record(q, reads, writes, sem, True)
-        note(q, run, reads, writes, ISSUE * len(pairs), late)
+        note(q, run, reads, writes)
 
     def ap(x):
         return x[0] if isinstance(x, tuple) else x
@@ -269,52 +227,33 @@ def rank_program(g, core, T, topo):
     def bytes_of(x):
         return (x[0].bitcast(dt.uint8), x[1])
 
-    def count(x):
-        return len(range(x[1][3], x[1][4], x[1][5]))
-
-    def span(out, *ins, both=False):
-        sides = [out] + list(ins)
-        c = 0.5 if all(SCRATCH[x[1][0]][2] in (BF, U16, F16) for x in sides) else 1.0
-        if both and not any(is_bank(x[1]) for x in ins):
-            c *= 2
-        return CALL + CYC * max(64, c * count(out)) + (BANK if any(is_bank(x[1]) for x in ins) else 0.0)
-
     def memset(out, c):
-        op("v", lambda: g.vector.memset(out[0], c), [], [out], span(out))
+        op("v", lambda: g.vector.memset(out[0], c), [], [out])
 
     def copy(out, in_):
-        op("v", lambda: g.vector.tensor_copy(out[0], in_[0]), [in_], [out], span(out, in_))
+        op("v", lambda: g.vector.tensor_copy(out[0], in_[0]), [in_], [out])
 
     def ts(out, in0, s1, s2, o0, o1=None):
         if o1 is None:
             fn = lambda: g.vector.tensor_scalar(out[0], in0[0], ap(s1), None, o0)
         else:
             fn = lambda: g.vector.tensor_scalar(out[0], in0[0], ap(s1), ap(s2), o0, o1)
-        op("v", fn, [in0, s1, s2], [out], span(out, in0))
+        op("v", fn, [in0, s1, s2], [out])
 
-    def tt(out, in0, in1, o, behind=()):
-        op("v", lambda: g.vector.tensor_tensor(out[0], in0[0], in1[0], o), [in0, in1] + list(behind), [out],
-           span(out, in0, in1, both=True))
+    def tt(out, in0, in1, o):
+        op("v", lambda: g.vector.tensor_tensor(out[0], in0[0], in1[0], o), [in0, in1], [out])
 
     def scan(out, d0, d1, init, o0=ALU.add, o1=ALU.max):
-        op("v", lambda: g.vector.tensor_tensor_scan(out[0], d0[0], d1[0], init, o0, o1), [d0, d1], [out],
-           span(out, d0, d1))
-
-    def gather(out, win, off):
-        op("v", lambda: g.vector.tensor_copy(out[0], win[0].indirect(off[0])), [win, off], [out],
-           50 + GAT * CYC * count(out))
+        op("v", lambda: g.vector.tensor_tensor_scan(out[0], d0[0], d1[0], init, o0, o1), [d0, d1], [out])
 
     def gather_tt(out, win, off, in1, o):
-        op("v", lambda: g.vector.tensor_tensor(out[0], win[0].indirect(off[0]), in1[0], o), [win, off, in1], [out],
-           50 + GAT * CYC * count(out))
+        op("v", lambda: g.vector.tensor_tensor(out[0], win[0].indirect(off[0]), in1[0], o), [win, off, in1], [out])
 
     def gather_times(out, win, off, c):
-        op("v", lambda: g.vector.tensor_scalar(out[0], win[0].indirect(off[0]), c, None, ALU.mult), [win, off], [out],
-           50 + GAT * CYC * count(out))
+        op("v", lambda: g.vector.tensor_scalar(out[0], win[0].indirect(off[0]), c, None, ALU.mult), [win, off], [out])
 
     def scatter(win, off, in_):
-        op("v", lambda: g.vector.tensor_copy(win[0].indirect(off[0]), in_[0]), [in_, off], [win],
-           50 + SCA * CYC * count(in_))
+        op("v", lambda: g.vector.tensor_copy(win[0].indirect(off[0]), in_[0]), [in_, off], [win])
 
     def act(out, in_, func=ACT.Copy, bias=None, scale=None, accum=None, off=None):
         src = in_[0] if off is None else in_[0].indirect(off[0])
@@ -325,9 +264,8 @@ def rank_program(g, core, T, topo):
             kw["scale"] = ap(scale)
         if accum is not None:
             kw["accum_out"] = accum[0]
-        busy = CYC * max(64, count(out)) if off is None else 65 + GAT * CYC * count(out)
         op("a", lambda: g.scalar.activation(out[0], src, func, **kw), [in_, bias, scale, off],
-           [out] + ([accum] if accum is not None else []), busy + ACALL + (CALL if accum is not None else 0))
+           [out] + ([accum] if accum is not None else []))
 
     def lin(out, in_, scale, bias):
         act(out, in_, ACT.Identity, bias, scale)
@@ -335,28 +273,26 @@ def rank_program(g, core, T, topo):
     def quant(name, c0, c1, src=None, s0=None):
         s0 = c0 if s0 is None else s0
         qq, ss, in_ = A("q" + name, c0, c1), A("s" + name, c0, c1), A(src or name, 4 * s0, 4 * (s0 + c1 - c0))
-        op("v", lambda: g.vector.quantize_mx(qq[0], ss[0], in_[0]), [in_], [qq, ss], 12 + 0.88 * (c1 - c0))
+        op("v", lambda: g.vector.quantize_mx(qq[0], ss[0], in_[0]), [in_], [qq, ss])
 
     def pick(dst, d0, d1, src, off):
         qo, qi, so, si = A("q" + dst, d0, d1), A("q" + src), A("s" + dst, d0, d1), A("s" + src)
         op("v", lambda: g.vector.tensor_copy(qo[0].bitcast(dt.uint32), qi[0].bitcast(dt.uint32).indirect(off[0])),
-           [qi, off], [qo], 50 + GAT * CYC * (d1 - d0))
+           [qi, off], [qo])
         act(so, si, off=off)
 
     def mm(bank, st, s0, mv, m0, n, start=True, stop=True):
         out = A("P%d" % bank, 0, n)
         a, b = A("q" + st, s0, s0 + 128), A("s" + st, s0, s0 + 128)
         c, d = A("q" + mv, m0, m0 + n), A("s" + mv, m0, m0 + n)
-        op("t", lambda: g.tensor.matmul_mx(out[0], a[0], b[0], c[0], d[0], start, stop), [a, b, c, d], [out],
-           CYC * (n + 16))
+        op("t", lambda: g.tensor.matmul_mx(out[0], a[0], b[0], c[0], d[0], start, stop), [a, b, c, d], [out])
 
     def iota(out, pattern, base, cm=0, real=True):
         kw = {"allow_small_or_imprecise_dtypes": True} if real else {}
-        op("g", lambda: g.iota(out[0], pattern, base, cm, **kw), [], [out], 130 + 2 * CYC * count(out))
+        op("g", lambda: g.iota(out[0], pattern, base, cm, **kw), [], [out])
 
-    def select(out, in_, pattern, cmp, base, cm):
-        op("g", lambda: g.affine_select(out[0], in_[0], pattern, cmp, 0.0, base, cm), [in_], [out],
-           170 + 2 * CYC * count(out))
+    def select(out, in_, pattern, cmp, fill, base, cm):
+        op("g", lambda: g.affine_select(out[0], in_[0], pattern, cmp, fill, base, cm), [in_], [out])
 
     def col(name, c):
         return A(name, c, c + 1)
@@ -374,133 +310,150 @@ def rank_program(g, core, T, topo):
         return (x, None)
 
     def state(name, c0=0, c1=512, p0=0, p1=128):
-        return A(name, XO + 4 * c0, XO + 4 * c1, 1, p0, p1)
+        return A(name, 4 * c0, 4 * c1, 1, p0, p1)
 
     def columns(dst, d0, src, s0, n):
         return [(bytes_of(A("q" + dst, d0, d0 + n)), bytes_of(A("q" + src, s0, s0 + n))),
                 (A("s" + dst, d0, d0 + n), A("s" + src, s0, s0 + n))]
 
-    for (sem, late, pairs) in (("ldu", 2380.0, [(A("UU"), hbm(T.u[:]))]),
-                               ("ldx0", 3315.0, [(state("X0", 0, HALF[0]), hbm(T.x[:, 0:4 * HALF[0]]))]),
-                               ("ldx1", 3900.0, [(state("X0", 384, 512), hbm(T.x[:, 4 * 384:2048]))]),
-                               ("ldx2", 4700.0, [(state("X0", HALF[0], 384), hbm(T.x[:, 4 * HALF[0]:4 * 384]))]),
-                               ("ldw", 6375.0, [(bytes_of(A("qW")), hbm(T.wc[:])), (A("sW"), hbm(T.ws[:]))]),
-                               ("ldv", 7225.0, [(A("VV"), hbm(T.v[:]))])):
-        turn[0] = late - 1e6
-        dmas("s", sem, pairs, late)
+    stage(0, "ld")
+    dmas("s", "ldu", [(A("UU"), hbm(T.u[:]))])
+    dmas("s", "ldx0", [(state("X0", 0, HALF[0]), hbm(T.x[:, 0:4 * HALF[0]]))])
+    dmas("s", "ldx1", [(state("X0", 384, 512), hbm(T.x[:, 4 * 384:2048]))])
+    dmas("s", "ldx2", [(state("X0", HALF[0], 384), hbm(T.x[:, 4 * HALF[0]:4 * 384]))])
+    dmas("s", "ldw", [(bytes_of(A("qW")), hbm(T.wc[:])), (A("sW"), hbm(T.ws[:]))])
     dmas("s", "wr0", [p for b in range(4) for p in (
         (bytes_of(A("qWR", 16 * b, 16 * b + 16)), hbm(T.wc[:, 512 * b + 448:512 * b + 512])),
-        (A("sWR", 16 * b, 16 * b + 16), hbm(T.ws[:, 128 * b + 112:128 * b + 128])))], 8000.0)
+        (A("sWR", 16 * b, 16 * b + 16), hbm(T.ws[:, 128 * b + 112:128 * b + 128])))])
+    stage(0, "wr")
     dmas("s", "wr1", columns("WR", 64, "WR", 0, 64) + columns("WR", 128, "WR", 0, 64))
-    turn[0] = None
 
-    stage(0, "i")
-    c_q, c_q4, c_g, c_t, c_h, c_8, c_r = [col("PF", c) for c in range(1, 8)]
-    g_off, g_d0, g_sub, g_o4, g_b0, g_b1, g_i0, g_dg, g_lt, g_wt, g_b2 = [col("PG", c) for c in range(11)]
+    c_q, c_q4, c_g, c_t, c_k, c_r = [col("PF", c) for c in range(1, 7)]
+    g_off, g_d0, g_sub, g_o4, g_b0, g_b1, g_i0, g_dg, g_lt, g_wt, g_b2, g_row = [col("PG", c) for c in range(12)]
 
     def zero(name, c0, c1, on):
         for c in range(c0, c1, 512):
             if on == "a":
                 act(A(name, c, min(c1, c + 512)), A("ZT", 0, min(c1, c + 512) - c))
+            elif on == "g":
+                iota(A(name, c, min(c1, c + 512)), [[0, min(c1, c + 512) - c]], 0)
             else:
                 memset(A(name, c, min(c1, c + 512)), 0.0)
 
-    def sides(k):
-        select(A("EE", 512 * k, 512 * k + 512), A("ONE"), [[-1000, 4], [-1, 32], [1000, 4]], ALU.is_equal, -32 * k, 1)
-    memset(A("ZT"), 0.0)
+    stage(0, "ix")
     iota(col("PI", 0), [[0, 1]], 0, 1, False)
-    iota(A("UBI"), [[16, 8]], 0, 0, False)
-    iota(A("CG"), [[1, 8], [0, 64]], 0)
-    iota(A("CR"), [[0, M], [1, 16]], 0)
-    for c, (sh, msk) in enumerate(((0, 15), (2, 3), (4, 7), (0, 3), (3, 1), (0, 7))):
+    for c, (sh, msk) in enumerate(((0, 15), (2, 3), (4, 7), (0, 3), (5, 3))):
         ts(col("PI", c + 1), col("PI", 0), sh, msk, ALU.logical_shift_right, ALU.bitwise_and)
-    memset(A("ONE"), 1.0)
-    copy(A("PF", 0, 7), A("PI", 0, 7))
+    copy(A("PF", 0, 6), A("PI", 0, 6))
+    stage(1, "ir")
     tt(col("PI", 8), col("PI", 0), col("PI", 3), ALU.subtract)
-    copy(A("UBL"), A("UBI"))
     ts(col("PI", 9), col("PI", 8), 0, 3, ALU.logical_shift_right, ALU.bitwise_and)
+    copy(c_r, col("PI", 9))
+    stage(0, "iu")
+    iota(A("UBI"), [[16, 8]], 0, 0, False)
+    copy(A("UBL"), A("UBI"))
+    stage(0, "iz")
+    memset(A("ZT"), 0.0)
     quant("LD0", 0, 128, "ZT")
-    copy(col("PF", 7), col("PI", 9))
-    dmas("s", "zl", [p for name in ("LD1", "LD2", "ZZ") for p in columns(name, 0, "LD0", 0, 128)]
-         + [p for k in range(NR) for p in columns("PK%d" % k, 112, "LD0", 0, 32)])
-    dmas("s", "zm", [p for (lanes, at, w, pad) in TILES[:-1] if pad > w for p in columns("TR", at + w, "LD0", 0, pad - w)],
-         5000.0)
-    for (lanes, at, w, pad) in TILES[3:]:
+    dmas("s", "zm", [p for (lanes, at, w, pad) in TILES[:-1] if pad > w for p in columns("TR", at + w, "LD0", 0, pad - w)])
+    dmas("s", "zl", [p for name in ("LD1", "LD2") for p in columns(name, 0, "LD0", 0, 16)]
+         + [p for k in range(NR) for p in columns("PK%d" % k, 48, "LD0", 0, 80)])
+    for i, (lanes, at, w, pad) in enumerate(TILES):
+        stage(0, "n%d" % i)
         lo = 16 * lanes[-1] if len(lanes) == 4 else 0
-        zero("TR", 4 * (at + lo), 4 * (at + (pad if lanes is TILES[-1][0] else w)), "a")
-    ts(A("SR1"), A("CG"), c_g, -1.0, ALU.is_equal, ALU.mult)
+        zero("TR", 4 * (at + lo), 4 * (at + (pad if i == len(TILES) - 1 else w)), ZERO[i])
+    stage(0, "nw")
+    zero("TC", 0, 4 * blk(2), "v")
+    stage(0, "nx")
+    zero("TC", 4 * blk(NB - 1), 4 * blk(NB), ZERO[7])
+    stage(0, "nz")
+    zero("ZZ", 0, 128, "g")
+    zero("BT", 0, 512, "g")
+    stage(0, "na")
+    act(A("AC", S - 1, S * M + S, S * M), A("ZT", 0, 2))
+    stage(0, "im")
+    iota(A("CR"), [[0, RUN // 16], [1, 16]], 0)
+    ts(A("MK"), A("CR"), c_q, None, ALU.is_equal)
+    ts(A("RS"), A("CR"), 0.0, None, ALU.is_gt)
+    stage(0, "ig")
+    ts(A("GT"), A("CR"), c_q, None, ALU.is_gt)
+    stage(0, "is")
+    iota(A("CG"), [[1, 8], [0, 16]], 0)
+    for ln in range(4):
+        ts(A("SR1", ln, 512, 4), A("CG"), c_g, -1.0, ALU.is_equal, ALU.mult)
+    quant("SR1", 0, 128)
+    stage(0, "iy")
     act(A("C2"), A("SR1", 0, 512, 4), scale=-2.0)
     for ln in (1, 2, 3):
-        act(A("SX", ln, 512, 4), A("SR1", ln, 512, 4))
+        act(A("SX", ln, 512, 4), A("SR1", 0, 512, 4))
+    select(A("SX", 0, 512, 4), A("C2"), [[1, 128]], ALU.is_gt, 0.0, 0, -1)
+    quant("SX", 0, 128)
+    stage(0, "ik")
     act(A("SK"), A("SR1"), scale=-256.0)
+    quant("SK", 0, 128)
+    stage(0, "iv")
     iota(A("VS"), [[1, C]], -256)
-    select(A("SX", 0, 512, 4), A("C2"), [[1, 128]], ALU.is_gt, 0, -1)
-    iota(A("BLI", 0, 3), [[128, 3]], 0)
-    iota(A("PKI", 0, 9), [[2, 9]], 127)
     for k in range(NR):
         if CROSS.index(CROSS[k]) == k:
             signs = sum(min(4, M - 4 * b) for b, on in enumerate(CROSS[k]) if on == "a")
             iota(A("WC%d" % k), [[1, K]], C - 256 + 16 * 256 * signs)
-    for k in range(4):
-        sides(k)
-    zero("TC", 0, 4 * blk(2), "v")
-    quant("SR1", 0, 128)
-    ts(A("MK"), A("CR"), c_q, None, ALU.is_equal)
-    ts(A("RS"), A("CR"), 0.0, None, ALU.is_gt)
-    ts(A("GT"), A("CR"), c_q, None, ALU.is_gt)
-    zero("BT", 0, 512, "v")
-    memset(col("AC", S - 1), 0.0)
-    memset(col("AC", S * M + S - 1), 0.0)
-    ts(g_i0, c_8, 0.0, None, ALU.is_equal)
-    for (lanes, at, w, pad) in TILES[:3]:
-        zero("TR", 4 * (at + 16 * lanes[-1]), 4 * (at + w), "a")
-    zero("TC", 4 * blk(NB - 1), 4 * blk(NB), "a")
+    stage(0, "id")
     lin(g_d0, c_q, -2.0, 32.0)
     lin(A("CS"), A("GT", 0, K), 32 * STEP, -31 * STEP)
-    lin(A("CD", 0, C - 1), A("GT", 1, C), 32 * STEP, -31 * STEP)
     lin(g_dg, col("CS", 15), None, g_d0)
-    lin(A("CD", C, 511), A("GT", 1, K), 32 * STEP, -31 * STEP)
+    stage(0, "ic")
+    for c in range(0, 512, RUN):
+        n = min(RUN, 512 - c)
+        lin(A("CD", c, c + n - 1), A("GT", 1, n), 32 * STEP, -31 * STEP)
+    stage(0, "io")
     lin(g_off, c_q, -STEP, 15 * STEP)
-    lin(g_o4, c_q4, 2048.0, 1024.0 - 6144.0)
-    lin(g_b0, c_q4, 8.0, c_g)
-    zero("ZZ", 0, 128, "a")
-    zero("EE", 2048, 2112, "a")
-    lin(g_sub, g_off, 0.5, (C - 256) / 512.0)
-    g_row = [col("PG", 11 + TOP.index(n)) for n in TOP]
-    for k, n in enumerate(TOP):
-        if TOP.index(n) == k:
-            lin(g_row[k], g_off, -1.0, 16.0 * (M - 1 + n) + DROP)
+    lin(g_row, g_off, -1.0, 16.0 * (M - 1) + DROP)
     lin(g_wt, g_off, -1.0, 16.0 * (K // 16 - 1) + DROP)
-    lin(g_b1, g_b0, 4.0, c_t)
-    lin(g_b2, c_r, float(K), g_b0)
+    lin(g_sub, g_off, 0.5, (C - 256) / 512.0)
+    stage(0, "ip")
+    iota(A("UP"), [[0, K]], 512)
+    act(A("CS2"), A("CS"), scale=256.0)
+    stage(0, "il")
+    lin(g_o4, c_q4, 2048.0, 1024.0 - 6144.0)
     lin(g_lt, g_o4, None, c_t)
-    quant("SK", 0, 128)
-    quant("SX", 0, 128)
+    stage(0, "it")
     ts(A("CT4", 0, 4), A("CR", 0, 4), c_q4, 2560.0, ALU.is_gt, ALU.mult)
     lin(A("CT4", 4, 8), A("CT4", 0, 4), None, -2048.0)
     for k in range(4):
         lin(A("CS4", k, 512, 4), A("ZT", 0, 128), None, col("CT4", 4 + k))
-    stage(0, "j")
-    act(A("UP"), A("ONE", 0, K), scale=512.0)
-    act(A("CS2"), A("CS"), scale=256.0)
-    stage(1, "j")
+    stage(0, "ib")
+    iota(A("BLI", 0, 3), [[128, 3]], 0)
+    lin(g_b0, c_q4, 8.0, c_g)
+    lin(g_b1, g_b0, 4.0, c_t)
+    stage(1, "ib")
+    lin(g_b2, c_r, float(K), g_b0)
     ts(A("BL", 4, 7), A("BLI", 0, 3), 0.25, g_b2, ALU.mult, ALU.add)
     ts(A("BL", 0, 3), A("BLI", 0, 3), g_b1, None, ALU.add)
-    ts(A("PKJ", 0, 9), A("PKI", 0, 9), c_h, 139.0, ALU.add, ALU.min)
-    ts(A("PKL", 0, 9), A("PKJ", 0, 9), g_i0, None, ALU.mult)
+    stage(0, "ie")
+    iota(A("PKI", 0, 3), [[4, 3]], 128)
+    lin(A("PKJ", 0, 3), A("PKI", 0, 3), None, c_q4)
+    stage(1, "ie")
+    tt(g_i0, c_t, c_k, ALU.is_equal)
+    ts(A("PKL", 0, 3), A("PKJ", 0, 3), g_i0, None, ALU.mult)
+    stage(0, "qe")
+    for k in range(4):
+        select(A("EE", 0, 512), A("EE", 0, 512) if k else A("ZT"), [[-1000, 4], [-1, 32], [1000, 4]], ALU.not_equal, 1.0,
+               -32 * k, 1)
+    zero("EE", 512, 576, "g")
     stage(1, "qe")
-    quant("E", 0, 256, "EE")
-    quant("E", 256, 528, "EE")
+    quant("E", 0, 144, "EE")
+    stage(0, "lv")
+    dmas("g", "ldv", [(A("VV"), hbm(T.v[:]))])
 
     stage(0, "u")
     quant("U", 0, 128, "UU")
     pick("UB", 0, 128, "U", A("UBL"))
-    stage(NR, "v")
+    stage(NR - 1, "v")
     quant("V", 0, 128, "VV")
     stage(0, "k1")
-    quant("X", 0, HALF[0], "X0", K)
+    quant("X", 0, HALF[0], "X0")
     stage(0, "k2")
-    quant("X", HALF[0], C, "X0", K + HALF[0])
+    quant("X", HALF[0], C, "X0")
 
     def send(t):
         quant("B%d" % t, 0, 128, "BT")
@@ -519,31 +472,30 @@ def rank_program(g, core, T, topo):
             total["loc"] = total.get("loc", 0) + 2 * len(topo.engines(core, dst))
             total[arr] = 2 * len(topo.engines(src, core))
             record("r", [], [ql[1], sl[1]], arr, True)
-        note("g", run, [qb[1], sb[1]], [ql[1], sl[1]], 200.0, REMOTE * (1.5 if t == 0 else 1.0))
+        note("g", run, [qb[1], sb[1]], [ql[1], sl[1]])
 
-    def seven(t, banks):
+    def seven(t, banks, scale):
         stage(t + 1, "p7")
         for r, bank in enumerate(banks):
-            mm(bank, "WR", 16 * r, "ZZ", 128, 128)
-            act(A("P7A", K * r, K * r + K), A("P%d" % bank, 32, 128), scale=0.015625)
+            mm(bank, "WR", 16 * r, "ZZ", 0, 128)
+            act(A("P7A", K * r, K * r + K), A("P%d" % bank, 32, 128), scale=scale)
         act(A("P7B"), A("P7A"), off=A("BL", 4, 7))
         stage(t + 1, "b")
         gather_tt(A("BT", 0, 48), A("MR"), A("BL", 0, 3), A("P7B"), ALU.add)
         send(t)
 
-    def unpack(t, xx, engines, times, banks):
-        pick("PK%d" % t, 0, 112, "LD%d" % t, A("PKL", 0, 7))
+    def unpack(t, xx, engines, banks):
+        pick("PK%d" % t, 0, 48, "LD%d" % t, A("PKL", 0, 3))
         for odd, bank in enumerate(banks):
             stage(t + 1, "un")
-            for k in range(0, 8, 2):
-                mm(bank, "E", 64 * k + 16 * odd, "PK%d" % t, 8 - k, 128, k == 0, k == 6)
+            mm(bank, "E", 16 * odd, "PK%d" % t, 0, 128)
             for b in range(4):
-                out = A(xx, XO + 4 * (C + odd) + b, XO + 2048, 8, 0, 16)
-                in_ = A("P%d" % bank, 0, K, 2, 32 * b, 32 * b + 16)
+                out = A(xx, 4 * (C + odd) + b, 2048, 8, 0, 16)
+                in_ = A("P%d" % bank, 0, 48, 1, 32 * b, 32 * b + 16)
                 if engines[odd] == "a":
-                    act(out, in_, scale=times)
+                    act(out, in_)
                 else:
-                    ts(out, in_, times, None, ALU.mult)
+                    copy(out, in_)
 
     where = {m: (at, ln) for (lanes, at, w, pad) in TILES for ln, m in enumerate(lanes)}
 
@@ -551,8 +503,8 @@ def rank_program(g, core, T, topo):
         return A(buf, 4 * (at + c0) + ln, 4 * (at + c1), 4)
 
     def own_keys(dst, bank, c0, c1, p0=0, k0=0):
-        tt(A("KM", k0 + c0, k0 + c1), A(bank, p0 + c0, p0 + c1), A("MK", c0, c1), ALU.mult)
-        scan(A(dst, c0, c1), A("RS", c0, c1), A("KM", k0 + c0, k0 + c1), 0.0, ALU.mult, ALU.add)
+        tt(A("KM", k0 + c0, k0 + c1), A(bank, p0 + c0, p0 + c1), A("MK", 0, c1 - c0), ALU.mult)
+        scan(A(dst, c0, c1), A("RS", 0, c1 - c0), A("KM", k0 + c0, k0 + c1), 0.0, ALU.mult, ALU.add)
 
     def own_chunk(t, when, out, src, keys, c0, n):
         stage(t, when)
@@ -560,31 +512,39 @@ def rank_program(g, core, T, topo):
         scan(A("SD", c0, c0 + n), A("GT", 0, n), out, 0.0, ALU.mult, ALU.add)
         lin(A("CD", c0 + 14, c0 + n, 16), A("SD", c0 + 15, c0 + n, 16), -2.0, g_dg)
 
-    def step_scalar(t, when, n, buf, at, ln, src, keys, m, slot):
+    def step_scalar(t, when, buf, at, ln, src, keys, m, slot):
         out = lane(buf, at, ln, 0, 16 * m)
-        stage(t, when + "1")
+        stage(t, "%s%d" % (when, m))
         lin(out, A(src, 0, 16 * m), -1.0, col(keys, 16 * m + 15))
-        stage(t, when + "2")
         act(out, out, ACT.Sign, bias=ETA, accum=col("AC", S * slot + S - 1))
 
-    def step_vector(t, m, start):
+    def above(t, m):
+        return sum(n > m for n in ON_VECTOR[t])
+
+    def end_of(t, m):
+        return S * (sorted(ON_VECTOR[t]).index(m) + 1)
+
+    def step_vector(t, m, src):
         at, ln = where[m]
-        end = S * (m - M + 9)
-        stage(t, "w")
-        ts(lane("TR", at, ln, 0, 16 * m), A("P1", 0, 16 * m), col("KS", 16 * m + 15), 2.0, ALU.is_le, ALU.mult)
-        stage(t, "ws")
+        end = end_of(t, m)
+        stage(t, "w%d" % m)
+        ts(lane("TR", at, ln, 0, 16 * m), A(src, 0, 16 * m), col("KS", 16 * m + 15), 2.0, ALU.is_le, ALU.mult)
         scan(A("AB", end - 8 * m, end), lane("TR", at, ln, 0, 8 * m), lane("TR", at, ln, 8 * m, 16 * m),
-             start - 16.0 * m, ALU.add, ALU.add)
+             16.0 * (above(t, m) - m), ALU.add, ALU.add)
 
     def place(t, when, then, name, bank, c0, n, slot, off, win, vals, p0=0):
         k = n // 16
         stage(t, when)
-        ks = min(k, max(0, M - TOP[t] - slot)) if slot < M else k
-        if ks:
-            lin(A("CD", c0 + 15, c0 + 16 * ks, 16), A("AC", S * slot + S - 1, S * (slot + ks), S), None, -DROP)
-        if ks < k:
-            lin(A("CD", c0 + 16 * ks + 15, c0 + n, 16), A("AB", S * (slot + ks - M + 9) - 1, S * (slot + k - M + 8), S),
-                None, -DROP)
+        m0 = slot
+        for m in range(slot, slot + k):
+            on = m in ON_VECTOR[t]
+            if m + 1 == slot + k or on != (m + 1 in ON_VECTOR[t]):
+                out = A("CD", c0 + 16 * (m0 - slot) + 15, c0 + 16 * (m + 1 - slot), 16)
+                if on:
+                    lin(out, A("AB", end_of(t, m0) - 1, end_of(t, m), S), None, -DROP)
+                else:
+                    lin(out, A("AC", S * m0 + S - 1, S * (m + 1), S), None, 16.0 * above(t, m) - DROP)
+                m0 = m + 1
         scan(A("HS", c0, c0 + n), A("P%d" % bank, p0, p0 + n), A("CD", c0, c0 + n), -DROP, ALU.max, ALU.add)
         ts(A("OF" + name, 0, k), A("HS", c0 + 15, c0 + n, 16), off, 0.5, ALU.add, ALU.mult)
         stage(t, then)
@@ -592,7 +552,6 @@ def rank_program(g, core, T, topo):
 
     for t in range(NR):
         xx, xn = "X%d" % (t % 2), "X%d" % ((t + 1) % 2)
-        final = t == NR - 1
 
         half = HALF[t]
         stage(t, "k1")
@@ -601,41 +560,36 @@ def rank_program(g, core, T, topo):
         own_keys("KS", "P2", 0, half)
         stage(t, "k2")
         mm(4, "UB", 0, "X", half, C - half)
-        mm(0, "UB", 0, "X", 0, C)
         mm(1, "UB", 0, "X", 0, C)
+        mm(0, "UB", 0, "X", 0, C)
         own_keys("KS", "P4", half, C, -half)
-        if SPLIT[t]:
-            own_chunk(t, "c1", lane("TR", 0, 0, 0, half), A("P2", 0, half), A("KS", 0, half), 0, half)
-            own_chunk(t, "c2", lane("TR", 0, 0, half, C), A("P1", half, C), A("KS", half, C), half, C - half)
-        else:
-            own_chunk(t, "c2", lane("TR", 0, 0, 0, C), A("P1", 0, C), A("KS"), 0, C)
-        for m in range(M - 1, M - 1 - TOP[t], -1):
-            step_vector(t, m, 16.0 * (M - 1 - m - TOP[t]))
-        early = list(range(half // 16 - 1, half // 16 - 1 - EARLY[t], -1))
-        early += [2, 1]
-        steps = early + [m for m in range(M - 1 - TOP[t], 0, -1) if m not in early]
-        for n, m in enumerate(steps):
-            step_scalar(t, "s", n, "TR", where[m][0], where[m][1], "P7" if m in early else "P0", "KS", m, m)
+        own_chunk(t, "c1", lane("TR", 0, 0, 0, half), A("P2", 0, half), A("KS", 0, half), 0, half)
+        own_chunk(t, "c2", lane("TR", 0, 0, half, C), A("P1", half, C), A("KS", half, C), half, C - half)
+        for m in range(M - 1, 0, -1):
+            if m in ON_VECTOR[t]:
+                step_vector(t, m, "P2" if 16 * m < half else "P1")
+            else:
+                step_scalar(t, "s", "TR", where[m][0], where[m][1], "P7" if m in EARLY[t] else "P0", "KS", m, m)
 
         if t > 0:
             stage(t, "pk")
-            unpack(t - 1, xx, "aa", 64.0, (5, 2))
+            unpack(t - 1, xx, "aa", (5, 6))
         stage(t, "kw")
-        quant("F", 0, 128, xx, K + 384)
+        quant("F", 0, 128, xx, 384)
         mm(WBANK[t], "UB", 0, "F", 0, 128)
         mm(KBANK[t], "UB", 0, "F", 0, 128)
         act(A("KW"), A("P%d" % KBANK[t], 32, 128))
         own_keys("KSW", "P%d" % WBANK[t], 0, K, 32, C)
         own_chunk(t, "cw", lane("TC", blk(0), 0, 0, K), A("P%d" % WBANK[t], 32, 128), A("KSW"), C, K)
         for m in range(5, 0, -1):
-            step_scalar(t, "u", 5 - m, "TC", blk(0 if m > 2 else 1), (6 - m) % 4, "KW", "KSW", m, M + m)
+            step_scalar(t, "u", "TC", blk(0 if m > 2 else 1), (6 - m) % 4, "KW", "KSW", m, M + m)
         stage(t, "qw")
         quant("TC", 0 if t == 0 else 32, blk(2) - 32)
         mm(6, "SX", 0, "TC", blk(0) - 32, 128, True, False)
         mm(6, "SR1", 0, "TC", blk(1) - 32, 128, False, True)
         for b, on in enumerate(CROSS[t]):
             ms = range(4 * b, min(4 * b + 4, M))
-            stage(t, "x")
+            stage(t, "x%d" % b)
             for m in ms:
                 out = lane("TC", blk(2 + b), m % 4, 0, K)
                 if on == "v":
@@ -652,22 +606,19 @@ def rank_program(g, core, T, topo):
             for b in range(b0, b1):
                 mm(5, "SK", 0, "TC", blk(2 + b) - 32, 128, b == 0, b == 6)
 
-        done = {i: max([steps.index(m) for m in TILES[i][0] if m in steps] + [-1]) for i in range(len(TILES))}
-        runs = [(0,)] + sorted(RUNS, key=lambda run: max(done[i] for i in run))
-        for n, run in enumerate(runs):
+        for n, run in enumerate(RUNS[t]):
             (_, at, w, pad) = TILES[run[-1]]
-            end = max(at + w, TILES[run[0]][1] + 128)
             stage(t, "t%d" % run[0])
-            quant("TR", TILES[run[0]][1], end)
+            quant("TR", TILES[run[0]][1], max(at + w, TILES[run[0]][1] + 128))
             for i in run:
                 (lanes, at, w, pad) = TILES[i]
-                later = [j for j in run if j > i] + [j for r in runs[n + 1:] for j in r]
+                later = [j for j in run if j > i] + [j for r in RUNS[t][n + 1:] for j in r]
                 for (name, a, b, bank) in RANGES:
                     if a < w:
                         last = all(TILES[j][2] <= a for j in later)
                         mm(bank, "SX" if i == 0 else "SR1", 0, "TR", at + a, max(128, min(b, w) - a), i == 0, last)
         for (name, a, b, bank) in RANGES:
-            place(t, "r" + name, "o" + name, name, bank, a, b - a, a // 16, g_row[t], A("W1", K, 512), A("VS", a, b))
+            place(t, "r" + name, "o" + name, name, bank, a, b - a, a // 16, g_row, A("W1", K, 512), A("VS", a, b))
 
         stage(t, "vw")
         tt(A("VW"), A("P5", 32, 128), A("WC%d" % CROSS.index(CROSS[t])), ALU.add)
@@ -682,82 +633,75 @@ def rank_program(g, core, T, topo):
         stage(t, "bv")
         scan(A("BV"), A("NK"), A("WV"), 0.0, ALU.min, ALU.add)
         stage(t, "fill")
-        act(A("W1", 512, 512 + K), A("ONE", 0, K), scale=1024.0)
+        act(A("W1", 512, 512 + K), A("UP"), scale=2.0)
         stage(t, "e")
         gather_tt(A("W1", 0, K), A("W1", K, 512 + K), A("PW"), A("BV"), ALU.min)
         stage(t + 1, "in")
         scatter(A("W1", K, 512 + K), A("PW"), A("BV"))
 
-        down = 0.015625 if t else 1.0
-        for i, r1 in enumerate(PIECES[t]):
-            r0 = PIECES[t][i - 1] if i else 0
-            c0, c1 = (128 + r0 if i else 32), 128 + r1
-            if LATE[t]:
-                c0 = 128 + r0
-            m0 = min(c0, c1 - 128)
-            banks = ((0, 1, 2, 7), (3, 6, 4, 5))[r1 == C]
-            cut = K + PIECES[t][-2]
-            for n, (a, e) in enumerate([] if i else [(0, K), (K, cut), (cut, 512)]):
-                stage(t + 1, "l%d" % n)
-                scan(A("SC", 32 + a, 32 + e), A("CS4", 0, e - a), A("W1", a, e), 0.0)
-                ts(A("LL", 8 + a // 4, 8 + e // 4), A("SC", 35 + a, 32 + e, 4), 4.0, g_lt, ALU.mult, ALU.add)
-            for (a, e) in ([(32, 128)] if i == 0 else []) + ([(128 + r0, c1)] if r1 > r0 else []):
-                j = 0 if a == 32 else 2 if e == 128 + C else 1
-                mid = a + int(GATHER[t][j] * (e - a)) // 8 * 8
-                stage(t + 1, "g%d" % j)
-                if mid > a:
-                    act(A("ZZ", 4 * a, 4 * mid), state(xx), scale=down, off=A("LL", a // 4, mid // 4))
-                if mid < e:
-                    gather_times(A("ZZ", 4 * mid, 4 * e), state(xx), A("LL", mid // 4, e // 4), down)
-                stage(t + 1, "q%d" % j)
-                quant("ZZ", 128 + min(a, e - 128), 128 + e, "ZZ", min(a, e - 128))
+        pieces = ((32, 128), (128, 128 + CUT[t]), (128 + CUT[t], 128 + C))
+        for j, (a, e) in enumerate(pieces if SPLIT[t] else (pieces[0], (128, 128 + C))):
+            stage(t + 1, "l%d" % j)
+            scan(A("SC", a, e), A("CS4", 0, e - a), A("W1", a - 32, e - 32), 0.0)
+            ts(A("LL", a // 4, e // 4), A("SC", a + 3, e, 4), 4.0, g_lt, ALU.mult, ALU.add)
+        for j, (a, e) in enumerate(pieces):
+            n, lead, by_dma = e - a, max(0, 128 - e + a), j in BY_DMA[t]
+            zz, z0 = (xn, a - 128) if j and by_dma else ("ZZ", a)
+            down = 1.0 if by_dma else DOWN
+            mid = int(GATHER[t][j] * n) // 8 * 8
+            stage(t + 1, "g%d" % j)
+            if mid > 0:
+                act(A(zz, 4 * z0, 4 * (z0 + mid)), state(xx), scale=down, off=A("LL", a // 4, (a + mid) // 4))
+            if mid < n:
+                gather_times(A(zz, 4 * (z0 + mid), 4 * (z0 + n)), state(xx), A("LL", (a + mid) // 4, e // 4), down)
+            stage(t + 1, "q%d" % j)
+            quant("ZZ", a - lead, e, zz, z0 - lead)
+            if not by_dma or t == NR - 1:
                 stage(t + 1, "z%d" % j)
-                scaled("Z64", 4 * a, "ZZ", 4 * a, 4 * (e - a), 4 * (int(TIMES64[t][j] * (e - a)) // 8 * 8), 64.0)
-                if j == 0:
-                    stage(t + 1, "rep")
-                    rep = [(A("MR", 0, XO, 1, 16 * k, 16 * k + 16), A("ZZ", 128, 512, 1, 112, 128)) for k in range(8)]
-                    dmas("s", "rep%d" % t, rep[REP_A[t]:])
-                    if REP_A[t]:
-                        dmas("a", "rpa%d" % t, rep[:REP_A[t]])
-                    seven(t, (3, 6, 4, 5))
+                scaled("Z64", 4 * a, "ZZ", 4 * a, 4 * n, 4 * (int(TIMES64[t][j] * n) // 8 * 8), 64.0)
+            if j == 0:
+                stage(t + 1, "rep")
+                rep = [(A("MR", 0, 4 * K, 1, 16 * k, 16 * k + 16), A("ZZ", 128, 512, 1, 112, 128)) for k in range(8)]
+                dmas("s", "rep%d" % t, rep[REP_A[t]:])
+                if REP_A[t]:
+                    dmas("a", "rpa%d" % t, rep[:REP_A[t]])
+                if t < NR - 1:
+                    stage(t + 1, "m0")
+                    dmas("s", "shf%d" % t, [(state(xn, C, 512, 16, 128), A("ZZ", 128, 512, 1, 0, 112))])
+                seven(t, (3, 6, 4, 5), DOWN)
+        for j, banks in PRODUCTS[t]:
+            a, e = pieces[j]
+            n, lead, by_dma = e - a, max(0, 128 - e + a), j in BY_DMA[t]
             stage(t + 1, "a%d" % j)
             for b in range(4):
-                mm(banks[b], "W", 128 * b, "ZZ", 128 + m0, c1 - m0)
+                mm(banks[b], "W", 128 * b, "ZZ", a - lead, n + lead)
             for b in range(4):
-                out = A("T64", 4 * c0 + b, 4 * c1, 4) if final else A(xn, 4 * c0 - 128 + b, 4 * c1 - 128, 4)
-                tt(out, A("P%d" % banks[b], c0 - m0, c1 - m0), A("Z64", 4 * c0 + b, 4 * c1, 4), ALU.add)
-            if LATE[t] and r1 == C:
-                stage(t + 1, "a0")
-                for b in (0, 2):
-                    mm(banks[b // 2], "W", 128 * b + 128, "ZZ", 0, 256, True, False)
-                    mm(banks[b // 2], "W", 128 * b, "ZZ", 128, 128, False, True)
-                for b in range(4):
-                    tt(A(xn, b, XO, 4), A("P%d" % banks[b // 2], 128 * (b % 2) + 32, 128 * (b % 2) + 128),
-                       A("Z64", 128 + b, 512, 4), ALU.add)
-            if r1 == C if LATE[t] else i == 0:
-                stage(t + 1, "m0")
-                if final:
-                    scaled(xn, 0, "T64", 128, 4 * K, 0, 0.015625)
-                dmas("s", "shf%d" % t, [(state(xn, C, 512, 16, 128), A(xn, 0, XO, 1, 0, 112))])
-            if r1 > r0:
-                stage(t + 1, "m%d" % j)
-                for b in range(4 * final):
-                    o, i_ = A(xn, XO + 4 * r0 + b, XO + 4 * r1, 4), A("T64", 512 + 4 * r0 + b, 512 + 4 * r1, 4)
-                    if b < LANES_A[j]:
-                        act(o, i_, scale=0.015625)
-                    else:
-                        ts(o, i_, 0.015625, None, ALU.mult)
+                made = A("P%d" % banks[b], lead, lead + n)
+                if j == 0 and t == NR - 1:
+                    tt(A("MW", b, 4 * K, 4), made, A("Z64", 128 + b, 512, 4), ALU.add)
+                elif by_dma:
+                    act(A("PA%d" % j, b, 4 * n, 4), made, scale=DOWN)
+                else:
+                    tt(A(xn, 4 * (a - 128) + b, 4 * (e - 128), 4), made, A("Z64", 4 * a + b, 4 * e, 4), ALU.add)
+            stage(t + 1, "d%d" % j)
+            if j == 0 and t == NR - 1:
+                act(A("MW"), A("MW"), scale=DOWN)
+                dmas("s", "shf%d" % t, [(state(xn, C, 512, 16, 128), A("MW", 0, 4 * K, 1, 0, 112))])
+            elif by_dma:
+                out, in_ = (state(xn, a - 128, e - 128), A("PA%d" % j, 0, 4 * n)) if j else (
+                    state(xn, C, 512, 16, 128), A("PA0", 0, 4 * K, 1, 0, 112))
+                dmas("g", "ad%d%d" % (j, t), [(out, in_)], accum_op=ALU.add)
+            if j:
                 stage(t + 1, "k%d" % j)
-                quant("X", r0, r1, xn, K + r0)
+                quant("X", a - 128, e - 128, xn)
 
     xx = "X%d" % (NR % 2)
     stage(NR, "le")
     lin(A("LE", 0, C), A("W1", K, 512), None, 256.0)
     lin(A("LE", C, 512), A("W1", 0, K), None, 256.0)
     dmas("s", "ole", [(hbm(T.le[:]), (T.LE[0:128:16, :], A("LE")[1]))], behind=[A("qB%d" % (NR - 1), 0, 12)])
-    stage(NR, "y")
     for i in range(2):
-        c0, c1 = PIECES[-1][i], PIECES[-1][i + 1]
+        c0, c1 = (0, CUT[-1], C)[i:i + 2]
         stage(NR, "oc")
         dmas("s", "oa%d" % i, [(hbm(T.oc[:, 4 * c0:4 * c1]), bytes_of(A("qX", c0, c1)))])
         stage(NR, "y")
@@ -767,9 +711,9 @@ def rank_program(g, core, T, topo):
     stage(NR, "os")
     dmas("s", "os", [(hbm(T.osc[4 * k:4 * k + 4, 0:C]), A("sX", 0, C, 1, 32 * k, 32 * k + 4)) for k in range(4)])
     stage(NR, "pk")
-    unpack(NR - 1, xx, "av", 1.0, (7, 2))
+    unpack(NR - 1, xx, UNPACK, (7, 2))
     stage(NR, "f")
-    quant("F", 0, 128, xx, K + 384)
+    quant("F", 0, 128, xx, 384)
     mm(3, "V", 0, "F", 0, 128)
     scales = [(hbm(T.osc[4 * k:4 * k + 4, C:512]), A("sF", 32, 128, 1, 32 * k, 32 * k + 4)) for k in range(4)]
     dmas("s", "ob", [(hbm(T.oc[:, 4 * C:2048]), bytes_of(A("qF", 32, 128)))] + scales[2:])

from concourse.mybir import dt, AluOpType, ActivationFunctionType

ALU = AluOpType
ACT = ActivationFunctionType
BF, F16, F32, I32, U16, U8, X4 = "bfloat16", "float16", "float32", "int32", "uint16", "uint8", "float8_e4m3fn_x4"
NR = 3
C, K = 416, 96
M = C // 16
S = 200
CUT = (208, 208, 208)
HALF = (128,) + CUT[:-1]
RUN = max(max(h, C - h) for h in HALF)
SPLIT = (1, 1, 1)
BY_DMA = ((0,), (0,), (0,))
PRODUCTS = (((0, (3, 6, 4, 5)), (1, (0, 1, 2, 7)), (2, (3, 6, 4, 5))),) * 3
ON_VECTOR = ((25, 24, 23, 22, 21), (25, 24, 23, 22, 21, 12), (25, 24, 23, 22, 21, 12))
EARLY = ((7, 6, 5, 4, 3, 2, 1), (11, 10, 9, 8, 7, 2, 1), (11, 10, 9, 8, 7, 2, 1))
REP_A = (0, 0, 4)
CROSS = ("vvvvvaa", "vvvvvav", "vvvvvav")
WBANK = (5, 6, 6)
KBANK = (6, 5, 5)
CROSSQ = ((0, 3), (3, 5), (5, 7))
RUNS = (((0,), (1,), (6,), (2,), (3,), (4, 5)),) + (((0,), (1,), (4, 5), (2,), (3,), (6,)),) * 2
GATHER = ((1, 0.5, 0.8), (1, 0.5, 0.8), (0.5, 0.4, 1))
TIMES64 = ((1, 0, 1), (1, 0, 1), (0, 0, 1))
ZERO = "gggggaag"
UNPACK = "av"
ORDER = {
    "v": ("iz nw iu ix*5 iz ix is nw is*3 ig im*2 is u it u k1 iy ik kw k1*2 kw c1 kw k2 cw x0*3 x1*2 c1 x1 k2 x1 cw k2 t6 x0 w21 qw x3 w23 w25 x2 c2 w24 w21 w22 t0 x3 x4 w25 x2 x3 x2 w22 c2 x4 t1 x2 w24 w23 x4*2 xq x3 rW rH xq rH xq oH rW t2 vw t3 oW p rM t4 rM p oM rL p rL bv oL e",
          "ir l0*2 in ir l1 l2 ir l1 ie l2 q0 g1 ib*2 q1 z1 g2 a1 b a1 b a1 q2 a1 ie k1 a2*2 k1 a2*2 k1 k2 w12 qe c1 k2 c1 k2 w12 w23 w21 w22 pk w24 c2 w22 w25 w23 w24 c2 w25 kw t0 t4 w21 kw t1 kw x1 x2 x4 x0 x2 x0 x1 x4*2 cw x0 x4 x2*2 x1 x0 x1 x6 x3 cw rH xq x3*3 rH qw x6 xq*2 oH rW t2 rW vw t3 oW t6 p rM p rM p rL oM rL bv oL e",
          "l0*2 in l1 l2 l1 l2 q0 g1 v q1 z1 g2 a1*2 q2 a1*2 b k1 b a2*2 k1 a2*2 k1 k2 w12 c1 w12 k2 pk k2 c1 w23 w21 w22 w21 w25 c2 kw w24 w23 w22 w25 kw t0 c2 kw w24 x3 x2 x4*2 x1 x6 x0 t1 x3*3 x4 t4 x1 x0 x2 x0 cw x0 x2 cw x1*2 x2 qw x4 xq rH x6 xq rH xq oH rW t2 rW vw t3 oW t6 p rM p rM p rL oM rL bv oL e",
          "l0*2 in g0 l1 q0 l1 l2 g1 z0 l2 q1 z1 b a0 b a1*3 a0 q2 a1 a0*2 k1 a2*3 pk a2 k2 un*4 f*2"),
    "a": ("n6 n5 na iy*2 id iy ik id iy u ic io*2 ip ic io*2 id s3 s1 s6 kw s7 s5 s4 u3 u2 u4 u1 s2 s5 s3 s6 s1 s2 s4 u5 u2 u4 u3 cw u1 u5 x6 s20 s16 s18 s14 x5 x6 s20 s18 rW s19 s17 s14 s19 s15 s12 s11 s17 rH x6 x5*3 s13 c2 x6 rH x5 s15 s10 s16 s11 s13 s12 s9 s10 s8 s7 rM s9 s8 c1 it rL kc il ib ie il it ib kc it fill it*2",
          "g0 ib g1 p7*5 g2 a0*2 z2 a0 fill a0 s11 s2 s10 s8 s7 s1 s11 s10 s9 s8 s2 s15 s18 s9 pk s1 s20 s19 un*8 s7 s20 s19 c2 s18 s6 kw s17 s16 u4 rH u3 s4 x5 u5 s14 u3 u1 u2 u5 rH x5 u4 u2 x5*2 s16 u1 x5 s15 s13 rW cw s17 s14 s13 s3 s5 s6 s4 s3 s5 rM c1 rM*2 kc rL kc",
          "g0 g1 p7*2 g2 p7*2 a0*2 p7 z2 a0*2 s10 s8 s7 s11 s10 s1 pk s9 s11 s2 s9 s18 un s19 un*7 s19 s20 s18 s17 s14 kw s20 x5 s2 s8 x5*2 s7 u3 u4 s1 u2 u1 rH s16 u3 u5 x5 s4 u1 rH u4 u2 u5 x5 c2 s3 s13 s15 s17 rW s16 cw s15 s13 s14 s5 s6 s4 s5 s3 s6 rM*2 c1 rM rL kc fill kc",
          "g0 rep g1 p7*5 g2 z2 d0 pk le y un*4 le y f*2"),
    "t": ("k1*2 kw*2 k2*3 qw t0*2 qw t1*2 xq*2 t0 xq*5 t1 t6 t2 t3 t2 t3 t4*2",
          "p7*4 a0*2 a1*4 a0*2 a2*2 k1 a2*2 k1 k2*3 un*2 kw*2 t0 t1 t0*2 t1*2 t4 xq*3 qw*2 xq*2 t4 xq*2 t2 t3 t2 t3 t6",
          "p7*4 a0 a1*2 a0 a1*2 a0*2 a2*2 k1 a2*2 k1 k2*3 un*2 kw*2 t0*2 t1*2 t0 t1 t4 qw xq*2 qw xq*5 t2 t4 t2 t3*2 t6",
          "p7*4 a0 a1*2 a0 a1*2 a0*2 a2*4 y un*2 y f"),
    "s": ("ld*6 iz*2 wr",
          "rep m0",
          "rep m0",
          "rep d0 oc y oc os y le f"),
    "g": ("ix iu is im iy n1 n2 nx iv n4 n0 n3 ie iv qe*3 ip ib iv qe*2 nz*2 lv",
          "b d0",
          "b d0",
          "b"),
}
RANGES = (("H", 288, 416, 3), ("M", 160, 288, 7), ("L", 0, 160, 4))
TILES = []
TRW = 0
for _l in [["A", M - 1, M - 2, M - 3]] + [[m for m in range(top, top - 4, -1) if m > 0] for top in (22, 18, 14, 10, 2, 6)]:
    _w = C if _l[0] == "A" else 16 * _l[0]
    _p = max([_w] + [min(a + 128, b) for (_n, a, b, _k) in RANGES if a < _w])
    TILES.append((_l, TRW, _w, _p))
    TRW += _p
TRW += 128
NB = 9
TCW = NB * K + 64

SCRATCH = {}
for _d, _l in (
        (BF, "UU:512 VV:512 X0:2048 X1:2048 ZZ:2176 Z64:2176 MR:384 MW:384 BT:512 ZT:512 "
             "CG:128 C2:128 CT4:8 CS:96 CS2:96 UP:96 CS4:512 SD:512 AB:1600 VS:416 W1:608 BV:96 SR1:512 SX:512 SK:512 "
             "EE:576 TR:%d TC:%d CR:%d MK:%d RS:%d GT:%d" % (4 * TRW, 4 * TCW, RUN, RUN, RUN, RUN)),
        (F32, "KM:512 KS:416 KW:96 KSW:96 CD:512 AC:%d HS:512 VW:96 KC:96 NK:96 PP:96 PS:96 WV:96 LE:512 YY:512 "
              "PKI:16 PKJ:16 BLI:8 PF:16 PG:16 P7A:384 P7B:48 PA0:384 PA1:1664 PA2:1664 WC0:96 WC1:96 WC2:96" % (32 * S)),
        (F16, "SC:544"), (I32, "PI:16 UBI:8"), (U16, "UBL:8 PKL:16 BL:8 OFH:26 OFM:26 OFL:26 OFW:6 PW:6 LL:136")):
    for _e in _l.split():
        SCRATCH[_e.split(":")[0]] = ("sbuf", [128, int(_e.split(":")[1])], _d)
for _e in ("U:128 V:128 F:128 UB:128 W:512 WR:192 X:512 ZZ:544 SR1:128 SX:128 SK:128 E:144 TR:%d TC:%d B0:128 B1:128 "
           "B2:128 LD0:144 LD1:144 LD2:144 PK0:128 PK1:128 PK2:128" % (TRW, TCW)).split():
    SCRATCH["q" + _e.split(":")[0]] = ("sbuf", [128, int(_e.split(":")[1])], X4)
    SCRATCH["s" + _e.split(":")[0]] = ("sbuf", [128, int(_e.split(":")[1])], U8)
for _k in range(8):
    SCRATCH["P%d" % _k] = ("psum", [128, 512], F32)

SEMAPHORES = "sv sa st sg ldu ldx0 ldx1 ldx2 ldw ldv loc ole oa0 oa1 os ob oc oy0 oy1 oyw zl zm wr0 wr1".split() + [
    "%s%d" % (_s, _t) for _s in ("rep", "rpa", "shf", "arr", "ad0", "ad1", "ad2") for _t in range(NR)]

BIG = 1.5 * 2.0 ** 23
ETA = 2.0 ** -110
DROP = 65536.0
STEP = 2048.0
DOWN = 0.015625


def rank_program(g, core, T, topo):
    rank = T.rank_of(core)
    if rank is None:
        return
    n_ranks = len(T.cores)
    eng = {"v": g.vector, "a": g.scalar, "t": g.tensor, "g": g, "s": g.sync}
    own = {"v": "sv", "a": "sa", "t": "st", "g": "sg"}
    total = {}
    known = {q: {} for q in eng}
    log = {}
    serial = [0]
    calls = []
    touched = {}
    turn = [None]

    def stage(cycle, name):
        turn[0] = (cycle, name)

    def A(name, c0=0, c1=None, step=1, p0=0, p1=128):
        t = T[name]
        if c1 is None:
            c1 = t.shape[1]
        ap = t[p0:p1, c0:c1] if step == 1 else t[p0:p1, c0:c1:step]
        return (ap, (name, p0, p1, c0, c1, step))

    def is_bank(k):
        return k[0][0] == "P" and k[0][1:].isdigit()

    def meets(a, b):
        if is_bank(a):
            return True
        if a[2] <= b[1] or b[2] <= a[1] or a[4] <= b[3] or b[4] <= a[3]:
            return False
        s = min(a[5], b[5])
        if s > 1 and a[5] % s == 0 and b[5] % s == 0 and a[3] % s != b[3] % s:
            return False
        return True

    def note(q, run, reads, writes):
        c = {"q": q, "run": run, "after": set(), "i": len(calls), "stage": turn[0]}
        for keys, wr in ((reads, False), (writes, True)):
            for k in keys:
                for (k2, wr2, d) in touched.get(k[0], []):
                    if (wr or wr2 or is_bank(k) and d["q"] != q) and d is not c and meets(k, k2):
                        c["after"].add(d["i"])
        for keys, wr in ((reads, False), (writes, True)):
            for k in keys:
                touched.setdefault(k[0], []).append((k, wr, c))
        calls.append(c)

    def issue():
        chains = []
        for q in ORDER:
            chains.append([])
            for cycle in range(NR + 1):
                left = {}
                for c in calls:
                    if c["q"] == q and c["stage"][0] == cycle:
                        left.setdefault(c["stage"][1], []).append(c)
                for word in ORDER[q][cycle].split():
                    name, n = (word.split("*") + ["1"])[:2]
                    for k in range(int(n)):
                        chains[-1].append(left[name].pop(0))
                assert not any(left.values()), (q, cycle, {k: len(v) for k, v in left.items() if v})
        done = set()
        while any(chains):
            before = len(done)
            for chain in chains:
                while chain and chain[0]["after"] <= done:
                    chain[0]["run"]()
                    done.add(chain.pop(0)["i"])
            assert len(done) > before

    def need(q, deps):
        for h in sorted(deps, key=lambda h: -h["n"]):
            if known[q].get(h["sem"], 0) < h["cnt"]:
                eng[q].wait_ge(T.sem[h["sem"]], h["cnt"])
                known[q][h["sem"]] = h["cnt"]
                for s, c in h["clock"].items():
                    if known[q].get(s, 0) < c:
                        known[q][s] = c

    def collect(q, reads, writes, dma):
        deps = {}
        for keys, wr in ((reads, False), (writes, True)):
            for k in keys:
                bank = is_bank(k)
                for (k2, wr2, q2, h) in log.get(k[0], []):
                    if not meets(k, k2):
                        continue
                    if bank:
                        if q2 == q:
                            continue
                    elif not (wr or wr2):
                        continue
                    elif q2 == q and not dma and not h["dma"] and not wr2 and not h["list"]:
                        continue
                    old = deps.get(h["sem"])
                    if old is None or old["cnt"] < h["cnt"]:
                        deps[h["sem"]] = h
        return list(deps.values())

    def record(q, reads, writes, sem, dma):
        serial[0] += 1
        h = {"sem": sem, "cnt": total[sem], "clock": dict(known[q]) if q in known else {}, "dma": dma, "n": serial[0],
             "list": any(SCRATCH[k[0]][2] == U16 for k in reads)}
        for k in reads:
            log.setdefault(k[0], []).append((k, False, q, h))
        for k in writes:
            log.setdefault(k[0], []).append((k, True, q, h))

    def op(q, fn, reads, writes):
        reads = [r[1] for r in reads if isinstance(r, tuple)]
        writes = [w[1] for w in writes]

        def run():
            need(q, collect(q, reads, writes, False))
            s = own[q]
            total[s] = total.get(s, 0) + 1
            fn().then_inc(T.sem[s], 1)
            record(q, reads, writes, s, False)
        note(q, run, reads, writes)

    def dmas(q, sem, pairs, behind=(), **how):
        reads = [i[1] for (o, i) in pairs if i[1]] + [x[1] for x in behind]
        writes = [o[1] for (o, i) in pairs if o[1]]

        def run():
            need(q, collect(q, reads, writes, True))
            for (o, i) in pairs:
                eng[q].dma_start(o[0], i[0], **how).then_inc(T.sem[sem], 16)
            total[sem] = 16 * len(pairs)
            record(q, reads, writes, sem, True)
        note(q, run, reads, writes)

    def ap(x):
        return x[0] if isinstance(x, tuple) else x

    def bytes_of(x):
        return (x[0].bitcast(dt.uint8), x[1])

    def memset(out, c):
        op("v", lambda: g.vector.memset(out[0], c), [], [out])

    def copy(out, in_):
        op("v", lambda: g.vector.tensor_copy(out[0], in_[0]), [in_], [out])

    def ts(out, in0, s1, s2, o0, o1=None):
        if o1 is None:
            fn = lambda: g.vector.tensor_scalar(out[0], in0[0], ap(s1), None, o0)
        else:
            fn = lambda: g.vector.tensor_scalar(out[0], in0[0], ap(s1), ap(s2), o0, o1)
        op("v", fn, [in0, s1, s2], [out])

    def tt(out, in0, in1, o):
        op("v", lambda: g.vector.tensor_tensor(out[0], in0[0], in1[0], o), [in0, in1], [out])

    def scan(out, d0, d1, init, o0=ALU.add, o1=ALU.max):
        op("v", lambda: g.vector.tensor_tensor_scan(out[0], d0[0], d1[0], init, o0, o1), [d0, d1], [out])

    def gather_tt(out, win, off, in1, o):
        op("v", lambda: g.vector.tensor_tensor(out[0], win[0].indirect(off[0]), in1[0], o), [win, off, in1], [out])

    def gather_times(out, win, off, c):
        op("v", lambda: g.vector.tensor_scalar(out[0], win[0].indirect(off[0]), c, None, ALU.mult), [win, off], [out])

    def scatter(win, off, in_):
        op("v", lambda: g.vector.tensor_copy(win[0].indirect(off[0]), in_[0]), [in_, off], [win])

    def act(out, in_, func=ACT.Copy, bias=None, scale=None, accum=None, off=None):
        src = in_[0] if off is None else in_[0].indirect(off[0])
        kw = {}
        if bias is not None:
            kw["bias"] = ap(bias)
        if scale is not None:
            kw["scale"] = ap(scale)
        if accum is not None:
            kw["accum_out"] = accum[0]
        op("a", lambda: g.scalar.activation(out[0], src, func, **kw), [in_, bias, scale, off],
           [out] + ([accum] if accum is not None else []))

    def lin(out, in_, scale, bias):
        act(out, in_, ACT.Identity, bias, scale)

    def quant(name, c0, c1, src=None, s0=None):
        s0 = c0 if s0 is None else s0
        qq, ss, in_ = A("q" + name, c0, c1), A("s" + name, c0, c1), A(src or name, 4 * s0, 4 * (s0 + c1 - c0))
        op("v", lambda: g.vector.quantize_mx(qq[0], ss[0], in_[0]), [in_], [qq, ss])

    def pick(dst, d0, d1, src, off):
        qo, qi, so, si = A("q" + dst, d0, d1), A("q" + src), A("s" + dst, d0, d1), A("s" + src)
        op("v", lambda: g.vector.tensor_copy(qo[0].bitcast(dt.uint32), qi[0].bitcast(dt.uint32).indirect(off[0])),
           [qi, off], [qo])
        act(so, si, off=off)

    def mm(bank, st, s0, mv, m0, n, start=True, stop=True):
        out = A("P%d" % bank, 0, n)
        a, b = A("q" + st, s0, s0 + 128), A("s" + st, s0, s0 + 128)
        c, d = A("q" + mv, m0, m0 + n), A("s" + mv, m0, m0 + n)
        op("t", lambda: g.tensor.matmul_mx(out[0], a[0], b[0], c[0], d[0], start, stop), [a, b, c, d], [out])

    def iota(out, pattern, base, cm=0, real=True):
        kw = {"allow_small_or_imprecise_dtypes": True} if real else {}
        op("g", lambda: g.iota(out[0], pattern, base, cm, **kw), [], [out])

    def select(out, in_, pattern, cmp, fill, base, cm):
        op("g", lambda: g.affine_select(out[0], in_[0], pattern, cmp, fill, base, cm), [in_], [out])

    def col(name, c):
        return A(name, c, c + 1)

    def scaled(dst, d0, src, s0, n, on_scalar, c):
        if on_scalar > 0:
            act(A(dst, d0, d0 + on_scalar), A(src, s0, s0 + on_scalar), scale=c)
        if on_scalar < n:
            ts(A(dst, d0 + on_scalar, d0 + n), A(src, s0 + on_scalar, s0 + n), c, None, ALU.mult)

    def blk(b):
        return 32 + K * b + (32 if b >= 2 else 0)

    def hbm(x):
        return (x, None)

    def state(name, c0=0, c1=512, p0=0, p1=128):
        return A(name, 4 * c0, 4 * c1, 1, p0, p1)

    def columns(dst, d0, src, s0, n):
        return [(bytes_of(A("q" + dst, d0, d0 + n)), bytes_of(A("q" + src, s0, s0 + n))),
                (A("s" + dst, d0, d0 + n), A("s" + src, s0, s0 + n))]

    stage(0, "ld")
    dmas("s", "ldu", [(A("UU"), hbm(T.u[:]))])
    dmas("s", "ldx0", [(state("X0", 0, HALF[0]), hbm(T.x[:, 0:4 * HALF[0]]))])
    dmas("s", "ldx1", [(state("X0", 384, 512), hbm(T.x[:, 4 * 384:2048]))])
    dmas("s", "ldx2", [(state("X0", HALF[0], 384), hbm(T.x[:, 4 * HALF[0]:4 * 384]))])
    dmas("s", "ldw", [(bytes_of(A("qW")), hbm(T.wc[:])), (A("sW"), hbm(T.ws[:]))])
    dmas("s", "wr0", [p for b in range(4) for p in (
        (bytes_of(A("qWR", 16 * b, 16 * b + 16)), hbm(T.wc[:, 512 * b + 448:512 * b + 512])),
        (A("sWR", 16 * b, 16 * b + 16), hbm(T.ws[:, 128 * b + 112:128 * b + 128])))])
    stage(0, "wr")
    dmas("s", "wr1", columns("WR", 64, "WR", 0, 64) + columns("WR", 128, "WR", 0, 64))

    c_q, c_q4, c_g, c_t, c_k, c_r = [col("PF", c) for c in range(1, 7)]
    g_off, g_d0, g_sub, g_o4, g_b0, g_b1, g_i0, g_dg, g_lt, g_wt, g_b2, g_row = [col("PG", c) for c in range(12)]

    def zero(name, c0, c1, on):
        for c in range(c0, c1, 512):
            if on == "a":
                act(A(name, c, min(c1, c + 512)), A("ZT", 0, min(c1, c + 512) - c))
            elif on == "g":
                iota(A(name, c, min(c1, c + 512)), [[0, min(c1, c + 512) - c]], 0)
            else:
                memset(A(name, c, min(c1, c + 512)), 0.0)

    stage(0, "ix")
    iota(col("PI", 0), [[0, 1]], 0, 1, False)
    for c, (sh, msk) in enumerate(((0, 15), (2, 3), (4, 7), (0, 3), (5, 3))):
        ts(col("PI", c + 1), col("PI", 0), sh, msk, ALU.logical_shift_right, ALU.bitwise_and)
    copy(A("PF", 0, 6), A("PI", 0, 6))
    stage(1, "ir")
    tt(col("PI", 8), col("PI", 0), col("PI", 3), ALU.subtract)
    ts(col("PI", 9), col("PI", 8), 0, 3, ALU.logical_shift_right, ALU.bitwise_and)
    copy(c_r, col("PI", 9))
    stage(0, "iu")
    iota(A("UBI"), [[16, 8]], 0, 0, False)
    copy(A("UBL"), A("UBI"))
    stage(0, "iz")
    memset(A("ZT"), 0.0)
    quant("LD0", 0, 128, "ZT")
    dmas("s", "zm", [p for (lanes, at, w, pad) in TILES[:-1] if pad > w for p in columns("TR", at + w, "LD0", 0, pad - w)])
    dmas("s", "zl", [p for name in ("LD1", "LD2") for p in columns(name, 0, "LD0", 0, 16)]
         + [p for k in range(NR) for p in columns("PK%d" % k, 48, "LD0", 0, 80)])
    for i, (lanes, at, w, pad) in enumerate(TILES):
        stage(0, "n%d" % i)
        lo = 16 * lanes[-1] if len(lanes) == 4 else 0
        zero("TR", 4 * (at + lo), 4 * (at + (pad if i == len(TILES) - 1 else w)), ZERO[i])
    stage(0, "nw")
    zero("TC", 0, 4 * blk(2), "v")
    stage(0, "nx")
    zero("TC", 4 * blk(NB - 1), 4 * blk(NB), ZERO[7])
    stage(0, "nz")
    zero("ZZ", 0, 128, "g")
    zero("BT", 0, 512, "g")
    stage(0, "na")
    act(A("AC", S - 1, S * M + S, S * M), A("ZT", 0, 2))
    stage(0, "im")
    iota(A("CR"), [[0, RUN // 16], [1, 16]], 0)
    ts(A("MK"), A("CR"), c_q, None, ALU.is_equal)
    ts(A("RS"), A("CR"), 0.0, None, ALU.is_gt)
    stage(0, "ig")
    ts(A("GT"), A("CR"), c_q, None, ALU.is_gt)
    stage(0, "is")
    iota(A("CG"), [[1, 8], [0, 16]], 0)
    for ln in range(4):
        ts(A("SR1", ln, 512, 4), A("CG"), c_g, -1.0, ALU.is_equal, ALU.mult)
    quant("SR1", 0, 128)
    stage(0, "iy")
    act(A("C2"), A("SR1", 0, 512, 4), scale=-2.0)
    for ln in (1, 2, 3):
        act(A("SX", ln, 512, 4), A("SR1", 0, 512, 4))
    select(A("SX", 0, 512, 4), A("C2"), [[1, 128]], ALU.is_gt, 0.0, 0, -1)
    quant("SX", 0, 128)
    stage(0, "ik")
    act(A("SK"), A("SR1"), scale=-256.0)
    quant("SK", 0, 128)
    stage(0, "iv")
    iota(A("VS"), [[1, C]], -256)
    for k in range(NR):
        if CROSS.index(CROSS[k]) == k:
            signs = sum(min(4, M - 4 * b) for b, on in enumerate(CROSS[k]) if on == "a")
            iota(A("WC%d" % k), [[1, K]], C - 256 + 16 * 256 * signs)
    stage(0, "id")
    lin(g_d0, c_q, -2.0, 32.0)
    lin(A("CS"), A("GT", 0, K), 32 * STEP, -31 * STEP)
    lin(g_dg, col("CS", 15), None, g_d0)
    stage(0, "ic")
    for c in range(0, 512, RUN):
        n = min(RUN, 512 - c)
        lin(A("CD", c, c + n - 1), A("GT", 1, n), 32 * STEP, -31 * STEP)
    stage(0, "io")
    lin(g_off, c_q, -STEP, 15 * STEP)
    lin(g_row, g_off, -1.0, 16.0 * (M - 1) + DROP)
    lin(g_wt, g_off, -1.0, 16.0 * (K // 16 - 1) + DROP)
    lin(g_sub, g_off, 0.5, (C - 256) / 512.0)
    stage(0, "ip")
    iota(A("UP"), [[0, K]], 512)
    act(A("CS2"), A("CS"), scale=256.0)
    stage(0, "il")
    lin(g_o4, c_q4, 2048.0, 1024.0 - 6144.0)
    lin(g_lt, g_o4, None, c_t)
    stage(0, "it")
    ts(A("CT4", 0, 4), A("CR", 0, 4), c_q4, 2560.0, ALU.is_gt, ALU.mult)
    lin(A("CT4", 4, 8), A("CT4", 0, 4), None, -2048.0)
    for k in range(4):
        lin(A("CS4", k, 512, 4), A("ZT", 0, 128), None, col("CT4", 4 + k))
    stage(0, "ib")
    iota(A("BLI", 0, 3), [[128, 3]], 0)
    lin(g_b0, c_q4, 8.0, c_g)
    lin(g_b1, g_b0, 4.0, c_t)
    stage(1, "ib")
    lin(g_b2, c_r, float(K), g_b0)
    ts(A("BL", 4, 7), A("BLI", 0, 3), 0.25, g_b2, ALU.mult, ALU.add)
    ts(A("BL", 0, 3), A("BLI", 0, 3), g_b1, None, ALU.add)
    stage(0, "ie")
    iota(A("PKI", 0, 3), [[4, 3]], 128)
    lin(A("PKJ", 0, 3), A("PKI", 0, 3), None, c_q4)
    stage(1, "ie")
    tt(g_i0, c_t, c_k, ALU.is_equal)
    ts(A("PKL", 0, 3), A("PKJ", 0, 3), g_i0, None, ALU.mult)
    stage(0, "qe")
    for k in range(4):
        select(A("EE", 0, 512), A("EE", 0, 512) if k else A("ZT"), [[-1000, 4], [-1, 32], [1000, 4]], ALU.not_equal, 1.0,
               -32 * k, 1)
    zero("EE", 512, 576, "g")
    stage(1, "qe")
    quant("E", 0, 144, "EE")
    stage(0, "lv")
    dmas("g", "ldv", [(A("VV"), hbm(T.v[:]))])

    stage(0, "u")
    quant("U", 0, 128, "UU")
    pick("UB", 0, 128, "U", A("UBL"))
    stage(NR - 1, "v")
    quant("V", 0, 128, "VV")
    stage(0, "k1")
    quant("X", 0, HALF[0], "X0")
    stage(0, "k2")
    quant("X", HALF[0], C, "X0")

    def send(t):
        quant("B%d" % t, 0, 128, "BT")
        dst = T.cores[(rank + t + 1) % n_ranks]
        src = T.cores[(rank - t - 1) % n_ranks]
        rid, pid, _ = topo.addr(dst)
        qb, sb = A("qB%d" % t, 0, 12), A("sB%d" % t, 0, 12)
        ql, sl = A("qLD%d" % t, 128, 140), A("sLD%d" % t, 128, 140)
        arr = "arr%d" % t

        def run():
            need("g", collect("g", [qb[1], sb[1]], [], True))
            g.remote_dma(ql[0].bitcast(dt.uint8), qb[0].bitcast(dt.uint8), T.sem[arr], T.sem.loc, pid, rid,
                         topo.mask(core, dst))
            g.remote_dma(sl[0], sb[0], T.sem[arr], T.sem.loc, pid, rid, topo.mask(core, dst))
            total["loc"] = total.get("loc", 0) + 2 * len(topo.engines(core, dst))
            total[arr] = 2 * len(topo.engines(src, core))
            record("r", [], [ql[1], sl[1]], arr, True)
        note("g", run, [qb[1], sb[1]], [ql[1], sl[1]])

    def seven(t, banks, scale):
        stage(t + 1, "p7")
        for r, bank in enumerate(banks):
            mm(bank, "WR", 16 * r, "ZZ", 0, 128)
            act(A("P7A", K * r, K * r + K), A("P%d" % bank, 32, 128), scale=scale)
        act(A("P7B"), A("P7A"), off=A("BL", 4, 7))
        stage(t + 1, "b")
        gather_tt(A("BT", 0, 48), A("MR"), A("BL", 0, 3), A("P7B"), ALU.add)
        send(t)

    def unpack(t, xx, engines, banks):
        pick("PK%d" % t, 0, 48, "LD%d" % t, A("PKL", 0, 3))
        for odd, bank in enumerate(banks):
            stage(t + 1, "un")
            mm(bank, "E", 16 * odd, "PK%d" % t, 0, 128)
            for b in range(4):
                out = A(xx, 4 * (C + odd) + b, 2048, 8, 0, 16)
                in_ = A("P%d" % bank, 0, 48, 1, 32 * b, 32 * b + 16)
                if engines[odd] == "a":
                    act(out, in_)
                else:
                    copy(out, in_)

    where = {m: (at, ln) for (lanes, at, w, pad) in TILES for ln, m in enumerate(lanes)}

    def lane(buf, at, ln, c0, c1):
        return A(buf, 4 * (at + c0) + ln, 4 * (at + c1), 4)

    def own_keys(dst, bank, c0, c1, p0=0, k0=0):
        tt(A("KM", k0 + c0, k0 + c1), A(bank, p0 + c0, p0 + c1), A("MK", 0, c1 - c0), ALU.mult)
        scan(A(dst, c0, c1), A("RS", 0, c1 - c0), A("KM", k0 + c0, k0 + c1), 0.0, ALU.mult, ALU.add)

    def own_chunk(t, when, out, src, keys, c0, n):
        stage(t, when)
        tt(out, src, keys, ALU.is_ge)
        scan(A("SD", c0, c0 + n), A("GT", 0, n), out, 0.0, ALU.mult, ALU.add)
        lin(A("CD", c0 + 14, c0 + n, 16), A("SD", c0 + 15, c0 + n, 16), -2.0, g_dg)

    def step_scalar(t, when, buf, at, ln, src, keys, m, slot):
        out = lane(buf, at, ln, 0, 16 * m)
        stage(t, "%s%d" % (when, m))
        lin(out, A(src, 0, 16 * m), -1.0, col(keys, 16 * m + 15))
        act(out, out, ACT.Sign, bias=ETA, accum=col("AC", S * slot + S - 1))

    def above(t, m):
        return sum(n > m for n in ON_VECTOR[t])

    def end_of(t, m):
        return S * (sorted(ON_VECTOR[t]).index(m) + 1)

    def step_vector(t, m, src):
        at, ln = where[m]
        end = end_of(t, m)
        stage(t, "w%d" % m)
        ts(lane("TR", at, ln, 0, 16 * m), A(src, 0, 16 * m), col("KS", 16 * m + 15), 2.0, ALU.is_le, ALU.mult)
        scan(A("AB", end - 8 * m, end), lane("TR", at, ln, 0, 8 * m), lane("TR", at, ln, 8 * m, 16 * m),
             16.0 * (above(t, m) - m), ALU.add, ALU.add)

    def place(t, when, then, name, bank, c0, n, slot, off, win, vals, p0=0):
        k = n // 16
        stage(t, when)
        m0 = slot
        for m in range(slot, slot + k):
            on = m in ON_VECTOR[t]
            if m + 1 == slot + k or on != (m + 1 in ON_VECTOR[t]):
                out = A("CD", c0 + 16 * (m0 - slot) + 15, c0 + 16 * (m + 1 - slot), 16)
                if on:
                    lin(out, A("AB", end_of(t, m0) - 1, end_of(t, m), S), None, -DROP)
                else:
                    lin(out, A("AC", S * m0 + S - 1, S * (m + 1), S), None, 16.0 * above(t, m) - DROP)
                m0 = m + 1
        scan(A("HS", c0, c0 + n), A("P%d" % bank, p0, p0 + n), A("CD", c0, c0 + n), -DROP, ALU.max, ALU.add)
        ts(A("OF" + name, 0, k), A("HS", c0 + 15, c0 + n, 16), off, 0.5, ALU.add, ALU.mult)
        stage(t, then)
        scatter(win, A("OF" + name, 0, k), vals)

    for t in range(NR):
        xx, xn = "X%d" % (t % 2), "X%d" % ((t + 1) % 2)

        half = HALF[t]
        stage(t, "k1")
        mm(2, "UB", 0, "X", 0, half)
        mm(7, "UB", 0, "X", 0, half)
        own_keys("KS", "P2", 0, half)
        stage(t, "k2")
        mm(4, "UB", 0, "X", half, C - half)
        mm(1, "UB", 0, "X", 0, C)
        mm(0, "UB", 0, "X", 0, C)
        own_keys("KS", "P4", half, C, -half)
        own_chunk(t, "c1", lane("TR", 0, 0, 0, half), A("P2", 0, half), A("KS", 0, half), 0, half)
        own_chunk(t, "c2", lane("TR", 0, 0, half, C), A("P1", half, C), A("KS", half, C), half, C - half)
        for m in range(M - 1, 0, -1):
            if m in ON_VECTOR[t]:
                step_vector(t, m, "P2" if 16 * m < half else "P1")
            else:
                step_scalar(t, "s", "TR", where[m][0], where[m][1], "P7" if m in EARLY[t] else "P0", "KS", m, m)

        if t > 0:
            stage(t, "pk")
            unpack(t - 1, xx, "aa", (5, 6))
        stage(t, "kw")
        quant("F", 0, 128, xx, 384)
        mm(WBANK[t], "UB", 0, "F", 0, 128)
        mm(KBANK[t], "UB", 0, "F", 0, 128)
        act(A("KW"), A("P%d" % KBANK[t], 32, 128))
        own_keys("KSW", "P%d" % WBANK[t], 0, K, 32, C)
        own_chunk(t, "cw", lane("TC", blk(0), 0, 0, K), A("P%d" % WBANK[t], 32, 128), A("KSW"), C, K)
        for m in range(5, 0, -1):
            step_scalar(t, "u", "TC", blk(0 if m > 2 else 1), (6 - m) % 4, "KW", "KSW", m, M + m)
        stage(t, "qw")
        quant("TC", 0 if t == 0 else 32, blk(2) - 32)
        mm(6, "SX", 0, "TC", blk(0) - 32, 128, True, False)
        mm(6, "SR1", 0, "TC", blk(1) - 32, 128, False, True)
        for b, on in enumerate(CROSS[t]):
            ms = range(4 * b, min(4 * b + 4, M))
            stage(t, "x%d" % b)
            for m in ms:
                out = lane("TC", blk(2 + b), m % 4, 0, K)
                if on == "v":
                    ts(out, A("KW"), col("KS", 16 * m + 15), 2.0, ALU.is_ge, ALU.mult)
                else:
                    lin(out, A("KW"), -1.0, col("KS", 16 * m + 15))
            if on == "a":
                for out in [A("TC", 4 * blk(2 + b), 4 * blk(3 + b))] if len(ms) == 4 else [
                        lane("TC", blk(2 + b), m % 4, 0, K) for m in ms]:
                    act(out, out, ACT.Sign, bias=ETA, scale=-1.0)
        stage(t, "xq")
        for b0, b1 in CROSSQ:
            quant("TC", blk(2 + b0) - (32 if t == 0 and b0 == 0 else 0), blk(2 + b1))
            for b in range(b0, b1):
                mm(5, "SK", 0, "TC", blk(2 + b) - 32, 128, b == 0, b == 6)

        for n, run in enumerate(RUNS[t]):
            (_, at, w, pad) = TILES[run[-1]]
            stage(t, "t%d" % run[0])
            quant("TR", TILES[run[0]][1], max(at + w, TILES[run[0]][1] + 128))
            for i in run:
                (lanes, at, w, pad) = TILES[i]
                later = [j for j in run if j > i] + [j for r in RUNS[t][n + 1:] for j in r]
                for (name, a, b, bank) in RANGES:
                    if a < w:
                        last = all(TILES[j][2] <= a for j in later)
                        mm(bank, "SX" if i == 0 else "SR1", 0, "TR", at + a, max(128, min(b, w) - a), i == 0, last)
        for (name, a, b, bank) in RANGES:
            place(t, "r" + name, "o" + name, name, bank, a, b - a, a // 16, g_row, A("W1", K, 512), A("VS", a, b))

        stage(t, "vw")
        tt(A("VW"), A("P5", 32, 128), A("WC%d" % CROSS.index(CROSS[t])), ALU.add)
        place(t, "rW", "oW", "W", 6, C, K, M, g_wt, A("WV"), A("VW"), 32)
        stage(t, "kc")
        lin(A("KC"), A("WV"), 2.0 ** -9, BIG + 1.0)
        lin(A("NK"), A("KC"), -512.0, 512.0 * (BIG + 1.0))
        stage(t, "p")
        scan(A("PP"), A("UP"), A("WV"), -1024.0)
        scan(A("PS"), A("CS2"), A("PP"), 0.0)
        ts(A("PW"), A("PS", 15, K, 16), 2.0 ** -9, g_sub, ALU.mult, ALU.subtract)
        stage(t, "bv")
        scan(A("BV"), A("NK"), A("WV"), 0.0, ALU.min, ALU.add)
        stage(t, "fill")
        act(A("W1", 512, 512 + K), A("UP"), scale=2.0)
        stage(t, "e")
        gather_tt(A("W1", 0, K), A("W1", K, 512 + K), A("PW"), A("BV"), ALU.min)
        stage(t + 1, "in")
        scatter(A("W1", K, 512 + K), A("PW"), A("BV"))

        pieces = ((32, 128), (128, 128 + CUT[t]), (128 + CUT[t], 128 + C))
        for j, (a, e) in enumerate(pieces if SPLIT[t] else (pieces[0], (128, 128 + C))):
            stage(t + 1, "l%d" % j)
            scan(A("SC", a, e), A("CS4", 0, e - a), A("W1", a - 32, e - 32), 0.0)
            ts(A("LL", a // 4, e // 4), A("SC", a + 3, e, 4), 4.0, g_lt, ALU.mult, ALU.add)
        for j, (a, e) in enumerate(pieces):
            n, lead, by_dma = e - a, max(0, 128 - e + a), j in BY_DMA[t]
            zz, z0 = (xn, a - 128) if j and by_dma else ("ZZ", a)
            down = 1.0 if by_dma else DOWN
            mid = int(GATHER[t][j] * n) // 8 * 8
            stage(t + 1, "g%d" % j)
            if mid > 0:
                act(A(zz, 4 * z0, 4 * (z0 + mid)), state(xx), scale=down, off=A("LL", a // 4, (a + mid) // 4))
            if mid < n:
                gather_times(A(zz, 4 * (z0 + mid), 4 * (z0 + n)), state(xx), A("LL", (a + mid) // 4, e // 4), down)
            stage(t + 1, "q%d" % j)
            quant("ZZ", a - lead, e, zz, z0 - lead)
            if not by_dma or t == NR - 1:
                stage(t + 1, "z%d" % j)
                scaled("Z64", 4 * a, "ZZ", 4 * a, 4 * n, 4 * (int(TIMES64[t][j] * n) // 8 * 8), 64.0)
            if j == 0:
                stage(t + 1, "rep")
                rep = [(A("MR", 0, 4 * K, 1, 16 * k, 16 * k + 16), A("ZZ", 128, 512, 1, 112, 128)) for k in range(8)]
                dmas("s", "rep%d" % t, rep[REP_A[t]:])
                if REP_A[t]:
                    dmas("a", "rpa%d" % t, rep[:REP_A[t]])
                if t < NR - 1:
                    stage(t + 1, "m0")
                    dmas("s", "shf%d" % t, [(state(xn, C, 512, 16, 128), A("ZZ", 128, 512, 1, 0, 112))])
                seven(t, (3, 6, 4, 5), DOWN)
        for j, banks in PRODUCTS[t]:
            a, e = pieces[j]
            n, lead, by_dma = e - a, max(0, 128 - e + a), j in BY_DMA[t]
            stage(t + 1, "a%d" % j)
            for b in range(4):
                mm(banks[b], "W", 128 * b, "ZZ", a - lead, n + lead)
            for b in range(4):
                made = A("P%d" % banks[b], lead, lead + n)
                if j == 0 and t == NR - 1:
                    tt(A("MW", b, 4 * K, 4), made, A("Z64", 128 + b, 512, 4), ALU.add)
                elif by_dma:
                    act(A("PA%d" % j, b, 4 * n, 4), made, scale=DOWN)
                else:
                    tt(A(xn, 4 * (a - 128) + b, 4 * (e - 128), 4), made, A("Z64", 4 * a + b, 4 * e, 4), ALU.add)
            stage(t + 1, "d%d" % j)
            if j == 0 and t == NR - 1:
                act(A("MW"), A("MW"), scale=DOWN)
                dmas("s", "shf%d" % t, [(state(xn, C, 512, 16, 128), A("MW", 0, 4 * K, 1, 0, 112))])
            elif by_dma:
                out, in_ = (state(xn, a - 128, e - 128), A("PA%d" % j, 0, 4 * n)) if j else (
                    state(xn, C, 512, 16, 128), A("PA0", 0, 4 * K, 1, 0, 112))
                dmas("g", "ad%d%d" % (j, t), [(out, in_)], accum_op=ALU.add)
            if j:
                stage(t + 1, "k%d" % j)
                quant("X", a - 128, e - 128, xn)

    xx = "X%d" % (NR % 2)
    stage(NR, "le")
    lin(A("LE", 0, C), A("W1", K, 512), None, 256.0)
    lin(A("LE", C, 512), A("W1", 0, K), None, 256.0)
    dmas("s", "ole", [(hbm(T.le[:]), (T.LE[0:128:16, :], A("LE")[1]))], behind=[A("qB%d" % (NR - 1), 0, 12)])
    for i in range(2):
        c0, c1 = (0, CUT[-1], C)[i:i + 2]
        stage(NR, "oc")
        dmas("s", "oa%d" % i, [(hbm(T.oc[:, 4 * c0:4 * c1]), bytes_of(A("qX", c0, c1)))])
        stage(NR, "y")
        mm(i, "V", 0, "X", c0, c1 - c0)
        act(A("YY", c0, c1), A("P%d" % i, 0, c1 - c0))
        dmas("s", "oy%d" % i, [(hbm(T.y[:, c0:c1]), A("YY", c0, c1))])
    stage(NR, "os")
    dmas("s", "os", [(hbm(T.osc[4 * k:4 * k + 4, 0:C]), A("sX", 0, C, 1, 32 * k, 32 * k + 4)) for k in range(4)])
    stage(NR, "pk")
    unpack(NR - 1, xx, UNPACK, (7, 2))
    stage(NR, "f")
    quant("F", 0, 128, xx, 384)
    mm(3, "V", 0, "F", 0, 128)
    scales = [(hbm(T.osc[4 * k:4 * k + 4, C:512]), A("sF", 32, 128, 1, 32 * k, 32 * k + 4)) for k in range(4)]
    dmas("s", "ob", [(hbm(T.oc[:, 4 * C:2048]), bytes_of(A("qF", 32, 128)))] + scales[2:])
    dmas("a", "oc", scales[:2])
    copy(A("YY", C, 512), A("P3", 32, 128))
    dmas("a", "oyw", [(hbm(T.y[:, C:512]), A("YY", C, 512))])

    issue()
    for s, c in total.items():
        if known["g"].get(s, 0) < c:
            g.wait_ge(T.sem[s], c)
